import numpy as np, ml_dtypes
CORES = [2,3,42,43,82,83,122,123]
N = 8
BF = ml_dtypes.bfloat16
def gentries(a):
    return np.ascontiguousarray(a.reshape(8, 16, -1).transpose(0, 2, 1)).reshape(8, -1)
def gtable(e):
    e = np.asarray(e); return np.ascontiguousarray(e.reshape(8, -1, 16).transpose(0, 2, 1)).reshape(128, -1).astype(np.int32)
W, M, B, T, P, QU, TH = 4096, 512, 192, 5, 1, 11, 254
def parts(rng):
    d = {}
    d["pr"] = (224 * rng.random((N, 8, 1, W)) ** 3 + 32 * rng.random((N, 8, 16, W))).astype(np.int64)
    d["ad"] = (np.exp2(rng.integers(2, 8, (N, 8, 1, W))) * rng.random((N, 8, 16, W))).astype(np.int64)
    d["mc"] = rng.integers(0, W, (N, 8, 16, M))
    d["gl"] = (224 * rng.random((N, 8, 1, M)) + 32 * rng.random((N, 8, 16, M))).astype(np.int64)
    d["z"] = (224 * rng.random((N, 8, 1, B)) + 32 * rng.random((N, 8, 16, B))).astype(np.int64)
    d["m"] = rng.integers(0, M, (N, 8, B))
    d["dv"] = (np.exp2(rng.integers(2, 8, (N, 8, 1, T * P))) * rng.random((N, 8, 16, T * P))).astype(np.int64)
    d["wt"] = rng.integers(0, 256, (N, 8, 16, 1))
    return d
def flat(a):
    return np.ascontiguousarray(np.reshape(a, (N, 128, -1)))
def pack(d):
    h = {k: flat(d[k]).astype(np.float32).astype(BF) for k in ("pr", "ad", "gl", "z", "dv", "wt")}
    return {"pr": h["pr"], "ad": h["ad"], "mc": flat(d["mc"]).astype(np.int32), "gl": h["gl"], "z0": h["z"], "m0": np.stack([gtable(a) for a in d["m"]]), "dv": h["dv"], "wt": h["wt"]}
def setup_inputs(rng):
    return pack(parts(rng))
def sized(rng, hi, *shape):
    return np.minimum((float(hi + 1) ** rng.random(shape[:-2] + (1, shape[-1])) * rng.random(shape)).astype(np.int64), hi)
def setup_inputs_spread(rng):
    d = parts(rng)
    d["pr"] = sized(rng, 255, N, 8, 16, W); d["ad"] = sized(rng, 127, N, 8, 16, W); d["dv"] = sized(rng, 255, N, 8, 16, T * P); d["wt"] = sized(rng, 255, N, 8, 16, 1)
    a = sized(rng, 255, N, 8, 16, M); d["gl"] = np.where(rng.random((N, 8, 1, M)) < 0.5, 255 - a, a)
    a = sized(rng, 255, N, 8, 16, B); d["z"] = np.where(rng.random((N, 8, 1, B)) < 0.6, rng.integers(0, 256, (N, 8, 16, B)), a)
    d["mc"] = np.minimum((W * rng.random((N, 8, 16, M)) ** 3).astype(np.int64), W - 1)
    d["m"] = np.minimum((M * rng.random((N, 8, B)) ** 2).astype(np.int64), M - 1)
    return pack(d)
def mix(rng, hi, *shape):
    q = rng.choice(np.array([0.0, 0.1, 0.5, 0.8, 0.9, 1.0]), shape[:-2] + (1, shape[-1]))
    return (rng.random(shape) < q).astype(np.int64) * hi
def setup_inputs_ends(rng):
    d = {"pr": mix(rng, 255, N, 8, 16, W), "ad": mix(rng, 127, N, 8, 16, W), "mc": mix(rng, W - 1, N, 8, 16, M), "gl": mix(rng, 255, N, 8, 16, M), "z": mix(rng, 255, N, 8, 16, B),
         "m": (M - 1) * rng.integers(0, 2, (N, 8, B)), "dv": mix(rng, 255, N, 8, 16, T * P), "wt": mix(rng, 255, N, 8, 16, 1)}
    pr, ad, mc, gl, z, m, dv, wt = [d[k] for k in ("pr", "ad", "mc", "gl", "z", "m", "dv", "wt")]; a = N - 1
    wt[:, 0, :8] = 0; wt[:, 0, 8:] = 255
    gl[0, :, :, 0] = 0; gl[0, :, :, M - 1] = 0
    gl[1, :, :, 0] = 0; gl[1, :, :, M - 1] = 255; m[1] = 0; m[1, 7, B - 1] = M - 1; z[1, 7, :, B - 1] = 0; dv[1, 7, :, :P] = 0
    pr[a, 7, :, 0] = 255; ad[a, 7, :, 0] = 127; ad[a, 7, :, W - 1] = 0; gl[a, 7, :, 0] = 255; gl[a, 7, :, M - 1] = 255
    mc[a, 7, :, 0] = 0; mc[a, 7, :, M - 1] = W - 1
    wt[a, 7] = 0; wt[a, 7, 15] = 255; wt[a, 7, 13:15] = 1
    for i in (0, 1, B - 2, B - 1): z[a, 7, :, i] = 255
    m[a, 7, 1] = 0; m[a, 7, B - 2] = 0; m[a, 7, B - 1] = M - 1
    m[a, 7, :B - 1] = np.where(np.all(z[a, 7, 13:, :B - 1] == 255, axis=0), 0, m[a, 7, :B - 1])
    wt[a, 6] = 255; gl[a, 6, :, 0] = 0; z[a, 6, :, 0] = 255; z[a, 6, :, B - 1] = 255; z[a, 6, :, 1] = 0; z[a, 6, :, B - 2] = 0
    m[a, 6, 0] = 0; m[a, 6, 1] = 0; m[a, 6, B - 2] = 0; m[a, 6, B - 1] = M - 1
    return pack(d)
def setup_inputs_corners(rng):
    d = parts(rng); pr, ad, mc, gl, z, m, dv, wt = [d[k] for k in ("pr", "ad", "mc", "gl", "z", "m", "dv", "wt")]
    m[:, 0] = 0; m[:, 1] = M - 1; m[:, 2] = np.arange(B); m[:, 3] = M - 1 - np.arange(B)
    wt[:, 0] = 0; wt[:, 1] = 255; dv[:, 4] = 255; dv[:, 5] = 0
    one = rng.integers(0, W, (N, 1, M)); one[:, 0, 0] = 0; one[:, 0, M - 1] = W - 1; mc[:, 4] = one; m[:, 4, 0] = 0; m[:, 4, B - 1] = M - 1
    gl[:, 5] = np.maximum(gl[:, 5], 1); goal = np.take_along_axis(gl[:, 5], m[:, 5][:, None, :], 2)
    c = rng.choice(np.array([0, QU - 1, QU, QU + 1, 16]), (N, 1, B)); place = np.argsort(np.argsort(rng.random((N, 16, B)), axis=1), axis=1)
    z[:, 5] = goal - (place >= c)
    ad[:, 6] = TH // 16; ad[:, 6, 15] = TH - 15 * (TH // 16) + rng.integers(-1, 2, (N, W))
    pr[:, 6] = np.maximum(pr[:, 6], 40); gl[:, 6] = np.maximum(gl[:, 6], 200); z[:, 6] = np.where(rng.random((N, 1, B)) < 0.7, 255, z[:, 6])
    pr[:, 7] = 255; gl[:, 7] = 255; z[:, 7] = 255 * rng.integers(0, 2, (N, 1, B)); wt[:, 7] = (255 * (np.arange(N) & 1)).reshape(N, 1, 1)
    return pack(d)
def setup_inputs_crowd(rng):
    d = parts(rng); pr, gl, z, m, dv, wt = [d[k] for k in ("pr", "gl", "z", "m", "dv", "wt")]
    gl[:, :6] = 0; m[:, :4] = np.argsort(rng.random((N, 4, M)), axis=-1)[..., :B]
    wt[:, :4] = 0; wt[:, :4, 0] = 1; wt[:, :4, 1] = 255
    c = np.full((N, 4, B), M - 1); c[:, 1, 0] = 0; c[:, 3] = rng.choice(np.array([0, 1, M // 2, M - 1]), (N, B))
    v = (c - 37 * m[:, :4]) & (M - 1); z[:, :4, 0] = v - 255 * (v // 255); z[:, :4, 1] = v // 255
    for i in range(N): gl[i, 2, :, m[i, 2, 0]] = 255
    z[:, 2, 2:, 0] = 100; dv[:, 2, :, :P] = 1
    for g in (4, 5):
        z[:, g] = z[:, g, :, :1].copy(); m[:, g] = m[:, g, :1].copy()
    z[:, 5, :, B - 1] = 255 - z[:, 5, :, 0]
    gl[:, 6] = 255
    pr[:, 7] = 255; gl[:, 7] = 255; z[:, 7] = 0; z[:, 7, :, B - 1] = 255; m[:, 7] = m[:, 7, :1].copy()
    return pack(d)
def setup_inputs_few(rng):
    d = parts(rng); d["z"] = np.minimum(d["z"], 254); d["dv"] = np.maximum(d["dv"], 1)
    mc, gl, z, m, wt = [d[k] for k in ("mc", "gl", "z", "m", "wt")]
    gl[1::2] = 255; z[1::2, 7, :, B - 1] = 255
    full = rng.permutation(np.array([0, 1, 3, 4]))
    for i in range(0, N, 2):
        g = int(full[(i // 2) & 3]); gl[i, g] = 0; m[i, g] = rng.permutation(M)[:B]
        wt[i, g] = 0; wt[i, g, 0] = 1; wt[i, g, 1] = 255
        a = rng.choice(np.array([11, 13, 23, 25, 27, 29]), B); u = W - 32 + a
        z[i, g, 1] = u // 255; z[i, g, 0] = u - 255 * (u // 255)
        mc[i, g, 15, m[i, g]] = W - 32 + ((-(a ** 7)) & 31)
    return pack(d)
def check_inputs(d):
    bad = []
    for k, hi in (("pr", 255), ("ad", 127), ("mc", W - 1), ("gl", 255), ("z0", 255), ("m0", M - 1), ("dv", 255), ("wt", 255)):
        a = np.asarray(d[k]).astype(np.float64)
        if not (np.min(a) >= 0 and np.max(a) <= hi): bad.append("range of " + k)
        elif np.any(a != np.floor(a)): bad.append("whole numbers of " + k)
    return bad
def reference(pr, ad, mc, gl, z0, m0, dv, wt):
    need_of, add_of, goal_of, z, dist, weight = [a.astype(np.float32).astype(np.int64).reshape(N, 8, 16, -1) for a in (pr, ad, gl, z0, dv, wt)]
    tb = mc.astype(np.int64).reshape(N, 8, 16, M); m = np.stack([gentries(a) for a in m0]).astype(np.int64)
    seen = [0] * N
    for t in range(T):
        for q in range(N):
            s = (q - t) % N; zz = z[s]; mm = m[s]
            o = np.take_along_axis(tb[q], mm[:, None, :], 2)
            ix = o.reshape(8, 1, 16 * B)
            p = np.take_along_axis(need_of[q], ix, 2).reshape(8, 16, 16, B); a = np.take_along_axis(add_of[q], ix, 2).reshape(8, 16, 16, B)
            K = [None] * 16 + [np.take_along_axis(goal_of[q], mm[:, None, :], 2)]
            for k in range(15, -1, -1): K[k] = np.maximum(p[:, :, k], K[k + 1] - a[:, :, k])
            K = np.stack(K)
            for j in range(P):
                met = np.add.reduce((zz[None] >= K).astype(np.int64), axis=2)
                best = np.max(np.where(met >= QU + (seen[q] & 1), np.arange(17).reshape(17, 1, 1), -1), axis=0)
                ak = np.take_along_axis(a, np.clip(best, 0, 15)[:, None, None, :], 2)[:, :, 0]
                new = np.abs(np.minimum(255, zz + ak) - dist[q, :, :, t * P + j][:, :, None])
                zz = np.where(((best >= 0) & (best < 16))[:, None, :], new, zz)
            goal = best == 16
            u = np.add.reduce(weight[q] * zz, axis=1) & (W - 1); to = (u + 37 * mm) & (M - 1)
            use = np.add.reduce(np.minimum(a, K[1:].transpose(1, 2, 0, 3)), axis=1)
            fresh = (((o * u[:, None, :]) >> 5) + o + 37 * np.arange(16).reshape(1, 16, 1)) & (W - 1)
            o = np.where(use < TH, fresh, o)
            for g in range(8):
                who = np.flatnonzero(goal[g]); where, first = np.unique(to[g, who], return_index=True)
                tb[q, g][:, where] = o[g][:, who[first]]
            z[s] = zz; m[s] = np.where(goal | (best < 0), to, mm); seen[q] = int(np.count_nonzero(goal))
    back = [(q - (T - 1)) % N for q in range(N)]
    return {"ymc": tb.reshape(N, 128, M).astype(np.float32), "yz": z[back].reshape(N, 128, B).astype(np.float32), "ym": np.stack([gtable(m[s]) for s in back]).astype(np.float32)}

@@ -1,0 +1,466 @@
+from concourse.mybir import dt, AluOpType, AxisListType, ActivationFunctionType
+
+A = AluOpType
+AF = ActivationFunctionType
+STEPS = 5
+B16 = "bfloat16"
+F32 = "float32"
+F16 = "float16"
+I32 = "int32"
+U16 = "uint16"
+BANKS = ["p%d" % b for b in range(8)]
+SCRATCH = {}
+for _names, _cols, _type in (
+        ("prw adw", 4096, B16), ("glw imw", 512, B16), ("mci", 512, I32), ("mcf yms", 512, F32), ("tb", 704, F32),
+        ("mi", 12, I32), ("dvs", 5, B16), ("wts", 1, B16),
+        ("d0 d1 ss", 6144, B16), ("ind", 3072, B16), ("ol", 192, U16), ("gg mb na15 r15 gi indk oh zdb xx wn", 192, B16),
+        ("zt", 256, B16), ("tg", 384, F16), ("ui ua", 384, I32), ("tgs", 24, F32), ("mlf kl tol ya yb mn", 12, F32),
+        ("acc", 1, F32), ("ai ai2", 1, I32), ("thr", 8, F32), ("si", 192, F16), ("sl la", 12, U16), ("es er", 24, F32), ("xs xr", 12, F32),
+        ("yy yzs of fd fw", 192, F32), ("f1 f2 f3 f4", 192, I32),
+        ("pi kki gri", 1, I32), ("pf kkf grf k37 kw jc jt", 1, F32), ("iw", 192, F32), ("ig cj onf", 128, F32), ("ie ce", 1536, B16),
+        ("cid cidn c296 cb cbh tma tmb ctm cg4 cnb wb wb8", 128, B16), ("sel selk seln", 2048, B16), ("dg dd", 640, B16),
+        ("ic bl", 12, F32), ("b32 one12", 12, B16), ("b512", 12, F16), ("ns", 192, F16), ("c255", 192, B16)):
+    for _n in _names.split():
+        SCRATCH[_n] = ("sbuf", [128, _cols], _type)
+SCRATCH["eb"] = ("sbuf", [128, 12, 208], B16)
+SCRATCH["mk"] = ("sbuf", [128, 12, 16], B16)
+for _t in range(STEPS):
+    SCRATCH["zb%d" % _t] = ("sbuf", [128, 192], B16)
+    SCRATCH["ml%d" % _t] = ("sbuf", [128, 12], U16)
+    if _t:
+        SCRATCH["zs%d" % _t] = ("sbuf", [128, 192], B16)
+        SCRATCH["ms%d" % _t] = ("sbuf", [128, 12], U16)
+del SCRATCH["ms1"]
+for _b in BANKS:
+    SCRATCH[_b] = ("psum", [128, 512], F32)
+LOADS = ["mc", "m0", "z0", "ad", "gl", "pr", "wt", "dv"]
+SEMAPHORES = ["cv", "cs", "ct", "cg", "outz", "outm", "outa", "outb", "snd"] + ["ld_" + n for n in LOADS]
+SEMAPHORES += ["er"] + ["mr%d" % t for t in range(1, STEPS)] + ["zr%d" % t for t in range(1, STEPS)]
+
+
+def scheduler(g, T):
+    queues = {"g": g, "v": g.vector, "s": g.scalar, "t": g.tensor, "y": g.sync}
+    ops = []
+    wr, rd, bank = {}, {}, {}
+
+    def op(q, fn, r=(), w=(), ext=None):
+        i = len(ops)
+        deps = set()
+        for x in list(r) + list(w):
+            if x in BANKS:
+                h = bank.setdefault(x, {})
+                deps.update(h[k] for k in h if k != q or (q != "t" and x in w))
+                h[q] = i
+        for x in r:
+            if x not in BANKS:
+                if x in wr:
+                    deps.add(wr[x])
+                rd.setdefault(x, {})[q] = i
+        for x in w:
+            if x not in BANKS:
+                if x in wr:
+                    deps.add(wr[x])
+                deps.update(rd.get(x, {}).values())
+                wr[x] = i
+                rd[x] = {}
+        deps.discard(i)
+        ops.append({"q": q, "fn": fn, "deps": deps, "ext": ext})
+
+    def emit():
+        pos, known, snap, need, waits = {}, {}, [], set(), []
+        for i, o in enumerate(ops):
+            q = o["q"]
+            pos[q] = pos.get(q, 0) + 1
+            o["pos"] = pos[q]
+            k = known.setdefault(q, {})
+            mine = []
+            for d in sorted(o["deps"], reverse=True):
+                e = ops[d]["ext"]
+                key, val = (e[0], e[1]) if e else (ops[d]["q"], ops[d]["pos"])
+                if k.get(key, 0) >= val:
+                    continue
+                mine.append(d)
+                need.add(d)
+                for a, b in snap[d].items():
+                    k[a] = max(k.get(a, 0), b)
+                k[key] = max(k.get(key, 0), val)
+            waits.append(mine)
+            snap.append(dict(k))
+        last = {}
+        for i, o in enumerate(ops):
+            if not o["ext"]:
+                last[o["q"]] = i
+        need.update(last.values())
+        count = {}
+        for i, o in enumerate(ops):
+            if i in need and not o["ext"]:
+                count[o["q"]] = count.get(o["q"], 0) + 1
+                o["tok"] = ("c" + o["q"], count[o["q"]])
+        for i, o in enumerate(ops):
+            if o["fn"] is None:
+                continue
+            Q = queues[o["q"]]
+            best = {}
+            for d in waits[i]:
+                s, n = (ops[d]["ext"] or ops[d]["tok"])[:2]
+                best[s] = max(best.get(s, 0), n)
+            for s, n in best.items():
+                Q.wait_ge(T.sem[s], n)
+            ins = o["fn"](Q)
+            if o["ext"]:
+                if o["ext"][2]:
+                    ins.then_inc(T.sem[o["ext"][0]], 16)
+            elif i in need:
+                ins.then_inc(T.sem["c" + o["q"]], 1)
+        for q, n in count.items():
+            g.wait_ge(T.sem["c" + q], n)
+
+    return op, emit
+
+
+def regs(name, a, b):
+    return ["%s.%d" % (name, c) for c in range(a, b)]
+
+
+def rank_program(g, core, T, topo):
+    rank = T.rank_of(core)
+    if rank is None:
+        return
+    op, emit = scheduler(g, T)
+    n_ranks = len(T.cores)
+    nxt = T.cores[(rank + 1) % n_ranks]
+    n_eng = 8
+    mask_out = sum(1 << e for e in topo.engines(core, nxt)[:n_eng])
+    rid, pid = topo.addr(nxt)[:2]
+
+    def V(fn, r=(), w=()):
+        op("v", fn, r, w)
+
+    def S(fn, r=(), w=()):
+        op("s", fn, r, w)
+
+    def P(fn, r=(), w=()):
+        op("t", fn, r, w)
+
+    def G(fn, r=(), w=()):
+        op("g", fn, r, w)
+
+    def ts(out, in0, s1, s2, *o):
+        return lambda Q: Q.tensor_scalar(out, in0, s1, s2, *o)
+
+    def tt(out, a, b, o):
+        return lambda Q: Q.tensor_tensor(out, a, b, o)
+
+    def cp(out, a):
+        return lambda Q: Q.tensor_copy(out, a)
+
+    def act(out, a, f, **k):
+        return lambda Q: Q.activation(out, a, f, **k)
+
+    def ms(out, c):
+        return lambda Q: Q.memset(out, c)
+
+    def mm(out, a, b, start=True, stop=True):
+        return lambda Q: Q.matmul(out, a, b, start, stop)
+
+    def iota(out, pattern, base=0, cm=0):
+        return lambda Q: Q.iota(out, pattern, base, cm, allow_small_or_imprecise_dtypes=True)
+
+    def load(q, name, buf):
+        op(q, lambda Q: Q.dma_start(T[buf][:], T[name][:]), [], [buf], ("ld_" + name, 16, True))
+
+    load("y", "mc", "mci")
+    load("s", "m0", "mi")
+    load("y", "ad", "adw")
+    load("s", "pr", "prw")
+    load("y", "gl", "glw")
+    load("y", "z0", "zb0")
+    load("y", "wt", "wts")
+    load("y", "dv", "dvs")
+
+    G(lambda Q: Q.iota(T.pi[:], [[0, 1]], 0, 1), [], ["pi"])
+    G(iota(T.ig[:], [[1, 8], [0, 16]]), [], ["ig"])
+    G(iota(T.iw[:], [[1, 192]]), [], ["iw"])
+    G(iota(T.ie[:], [[1, 96], [0, 16]]), [], ["ie"])
+    G(iota(T.ic[:], [[16, 12]]), [], ["ic"])
+    G(iota(T.imw[:, 0:256], [[1, 256]]), [], ["imwa"])
+    G(iota(T.imw[:, 256:512], [[1, 256]], -256), [], ["imwb"])
+    V(ms(T.d0[:, 1::2], 0.0), [], ["d0z"])
+    V(ms(T.sel[:], 0.0), [], ["selz"])
+    V(ts(T.kki[:], T.pi[:], 15, None, A.bitwise_and), ["pi"], ["kki"])
+    V(ts(T.gri[:], T.pi[:], 4, None, A.arith_shift_right), ["pi"], ["gri"])
+    V(cp(T.pf[:], T.pi[:]), ["pi"], ["pf"])
+    V(cp(T.kkf[:], T.kki[:]), ["kki"], ["kkf"])
+    V(cp(T.grf[:], T.gri[:]), ["gri"], ["grf"])
+    V(ts(T.kw[:], T.kkf[:], 2.0, -1.0, A.mult, A.add), ["kkf"], ["kw"])
+    V(ts(T.cb[:], T.ig[:], T.grf[:], None, A.is_equal), ["ig", "grf"], ["cb"])
+    for i in range(16):
+        V(cp(T.sel[:, 129 * i:129 * i + 113:16], T.cb[:, 0::16]), ["cb", "selz"], ["sel"] if i == 15 else [])
+    S(act(T.d1[:, 0::2], T.d0[:, 1::2], AF.Copy), ["d0z"], ["d1z"])
+    S(act(T.seln[:], T.sel[:], AF.Copy, scale=-1.0), ["sel"], ["seln"])
+    S(act(T.selk[:], T.sel[:], AF.Copy, scale=T.kw[:]), ["sel", "kw"], ["selk"])
+    V(ts(T.k37[:], T.kkf[:], -37.0, 555.0, A.mult, A.add), ["kkf"], ["k37"])
+    V(tt(T.jt[:], T.pf[:], T.kw[:], A.subtract), ["pf", "kw"], ["jt"])
+    V(ts(T.jc[:], T.jt[:], 14.0, None, A.add), ["jt"], ["jc"])
+    V(ts(T.cj[:], T.iw[:, 0:128], T.jc[:], None, A.is_equal), ["iw", "jc"], ["cj"])
+    V(cp(T.mcf[:], T.mci[:]), ["mci"], ["mcf"])
+    P(mm(T.p0[:], T.cj[:], T.mcf[:]), ["cj", "mcf"], ["p0"])
+    V(cp(T.ml0[:], T.mi[:]), ["mi"], ["ml0"])
+    V(ts(T.cid[:], T.iw[:, 0:128], T.pf[:], None, A.is_equal), ["iw", "pf"], ["cid"])
+    V(cp(T.tb[:, 0:512], T.p0[:]), ["p0"], ["tb"])
+
+    def consts():
+        V(ts(T.ce[:], T.ie[:], T.pf[:], None, A.is_equal), ["ie", "pf"], ["ce"])
+        V(ts(T.cidn[:], T.cid[:], -1.0, None, A.mult), ["cid"], ["cidn"])
+        V(ts(T.c296[:], T.cid[:], 296.0, None, A.mult), ["cid"], ["c296"])
+        V(ts(T.cg4[:], T.cb[:], -4.0, None, A.mult), ["cb"], ["cg4"])
+        V(ts(T.cbh[:], T.cb[:], 0.5, None, A.mult), ["cb"], ["cbh"])
+        V(ts(T.cnb[:], T.cb[:], -16.0, None, A.mult), ["cb"], ["cnb"])
+        V(ms(T.thr[:], 11.0), [], ["thr0"])
+        for c in range(12):
+            V(ts(T.mk[:, c, :], T.iw[:, 0:16], T.kkf[:], None, A.is_gt), ["iw", "kkf"], ["mk"] if c == 11 else [])
+        V(ts(T.tma[:], T.iw[:, 0:128], T.pf[:], 2.0, A.is_gt, A.mult), ["iw", "pf"], ["tma"])
+        V(tt(T.tmb[:], T.tma[:], T.cb[:], A.mult), ["tma", "cb"], ["tmb"])
+        V(tt(T.ctm[:], T.tmb[:], T.cid[:], A.subtract), ["tmb", "cid"], ["ctm"])
+        V(ts(T.bl[:], T.ic[:], T.kkf[:], None, A.add), ["ic", "kkf"], ["bl"])
+        V(ts(T.b32[:], T.bl[:], 32.0, None, A.mult), ["bl"], ["b32"])
+        V(ts(T.b512[:], T.bl[:], 512.0, 16.0, A.add, A.mult), ["bl"], ["b512"])
+        V(ms(T.one12[:], 1.0), [], ["one12"])
+        V(ts(T.ns[:], T.iw[:], -1.0, -513.0, A.mult, A.add), ["iw"], ["ns"])
+        V(ms(T.c255[:], -15.9375), [], ["c255"])
+        V(ms(T.onf[:], 1.0), [], ["onf"])
+        V(ts(T.wb[:], T.cb[:], T.wts[:], None, A.mult), ["cb", "wts"], ["wb"])
+        V(ts(T.wb8[:], T.cb[:], T.wts[:], 8.0, A.mult, A.mult), ["cb", "wts"], ["wb8"])
+        for t in range(STEPS):
+            V(ts(T.dg[:, 128 * t:128 * t + 128], T.cid[:], T.dvs[:, t:t + 1], None, A.mult), ["cid", "dvs"], ["dg%d" % t])
+
+    def distances():
+        for t in range(STEPS):
+            P(mm(T.p2[:, 128 * (t % 4):128 * (t % 4) + 128], T.cb[:], T.dg[:, 128 * t:128 * t + 128]), ["cb", "dg%d" % t], ["p2"])
+            if t == 3:
+                S(act(T.dd[:, 0:512], T.p2[:], AF.Copy), ["p2"], ["dda"])
+        S(act(T.dd[:, 512:640], T.p2[:, 0:128], AF.Copy), ["p2"], ["ddb"])
+
+    def listmm(pb, col, width, mats, buf, total, base=(), names=None):
+        def fn(Q):
+            out = T[pb][:, col:col + width]
+            first = True
+            for b in base:
+                Q.matmul(out, T.cid[:], T[b][:], first, False)
+                first = False
+            for i in range(16):
+                ins = Q.matmul(out, T[mats][:, 128 * i:128 * i + 128], T[buf][:, i:total:16], first, i == 15)
+                first = False
+            return ins
+        P(fn, ["cid", mats] + (names or [buf]) + list(base), [pb])
+
+    def step(t):
+        lastt = t == STEPS - 1
+        ml, z, th = "ml%d" % t, "zb%d" % t, "thr%d" % t
+        if t:
+            op(None, None, [], [ml if t > 1 else "xr"], ("mr%d" % t, n_eng, False))
+            op(None, None, [], [z], ("zr%d" % t, n_eng, False))
+        tol, mlf = (T.tol[:], T.mlf[:]) if t else (T.es[:, 0:12], T.es[:, 12:24])
+        if t == 1:
+            op(None, None, [], ["er"], ("er", n_eng, False))
+            V(tt(T.ya[:], T.er[:, 0:12], T.xr[:], A.subtract), ["er", "xr"], ["ya"])
+            V(tt(T.yb[:], T.xr[:], T.er[:, 12:24], A.min), ["er", "xr"], ["yb"])
+            V(tt(T.mn[:], T.ya[:], T.yb[:], A.max), ["ya", "yb"], ["mn"])
+            V(cp(T[ml][:], T.mn[:]), ["mn"], [ml])
+
+        def na(a, b):
+            S(act(T.d0[:, 1024 * a:1024 * b:2], T.adw[:].indirect(T.ol[:, 32 * a:32 * b]), AF.Copy, scale=-1.0), ["adw", "ol"], regs("d0", a, b))
+            S(act(T.na15[:, 32 * a:32 * b], T.d0[:, 1024 * a:1024 * b:32], AF.Copy), regs("d0", a, b), regs("na15", a, b))
+
+        def pg(q, a, b):
+            out, win = T.d1[:, 1024 * a + 1:1024 * b:2], T.prw[:].indirect(T.ol[:, 32 * a:32 * b])
+            op(q, cp(out, win) if q == "v" else act(out, win, AF.Copy), ["prw", "ol"], regs("d1", a, b))
+
+        def scan(a, b):
+            k = slice(1024 * a, 1024 * b, 32)
+            c = slice(32 * a, 32 * b)
+            V(tt(T.d1[:, k], T.gg[:, c], T.d0[:, k], A.add), ["gg"] + regs("d0", a, b), regs("d1", a, b))
+            V(ms(T.d0[:, k], -1024.0), [], regs("d0", a, b))
+            j = slice(1024 * a, 1024 * b)
+            V(lambda Q: Q.tensor_tensor_scan(T.ss[:, j], T.d0[:, j], T.d1[:, j], 0.0, A.add, A.max),
+              ["d0z", "d1z"] + regs("d0", a, b) + regs("d1", a, b), regs("ss", a, b))
+
+        def relu15(a, b):
+            V(ts(T.r15[:, 32 * a:32 * b], T.d1[:, 1024 * a:1024 * b:32], 0.0, None, A.max), regs("d1", a, b), regs("r15", a, b))
+
+        def zexp(c):
+            pb = "p%d" % (c % 2)
+            P(mm(T[pb][:], T.zt[0:96, 128 * (c // 3):128 * (c // 3) + 128], T.ce[0:96, 512 * (c % 3):512 * (c % 3) + 512]), ["zt", "ce"], [pb])
+
+        def cmp(c):
+            pb = "p%d" % (c % 2)
+            V(tt(T.ind[:, 512 * c:512 * c + 512], T.ss[:, 1024 * c + 1:1024 * c + 1024:2], T[pb][:], A.is_le), regs("ss", c, c + 1) + [pb], regs("ind", c, c + 1))
+
+        def cnt(a, b):
+            def fn(Q):
+                out = T.p3[:, 32 * a:32 * b]
+                Q.matmul(out, T.cg4[:], T.tg[:, 192 + 32 * a:192 + 32 * b], True, False)
+                for k in range(16):
+                    ins = Q.matmul(out, T.sel[:, 128 * k:128 * k + 128], T.ind[:, 512 * a + k:512 * b:16], False, k == 15)
+                return ins
+            P(fn, ["sel", "cg4", "tgg"] + regs("ind", a, b), ["p3"])
+
+        def use(a, b):
+            def fn(Q):
+                out = T.p4[:, 32 * a:32 * b]
+                Q.matmul(out, T.sel[:, 0:128], T.gg[:, 32 * a:32 * b], True, False)
+                Q.matmul(out, T.seln[:, 0:128], T.r15[:, 32 * a:32 * b], False, False)
+                for k in range(1, 16):
+                    Q.matmul(out, T.sel[:, 128 * k:128 * k + 128], T.ss[:, 1024 * a + 2 * k - 1:1024 * b:32], False, False)
+                    ins = Q.matmul(out, T.seln[:, 128 * k:128 * k + 128], T.ss[:, 1024 * a + 2 * k:1024 * b:32], False, k == 15)
+                return ins
+            P(fn, ["sel", "seln", "gg"] + regs("r15", a, b) + regs("ss", a, b), ["p4"])
+
+        def dups(a, b):
+            for c in range(a, b):
+                V(ts(T.eb[:, c, 0:192 - 16 * c], T.tg[:, 16 * c:192], T.kl[:, c:c + 1], None, A.is_equal), ["tgt", "kl"], ["eb%d" % c])
+
+        def send(name, src, dst, k, names=None):
+            op("g", lambda Q: Q.remote_dma(T[dst][:], T[src][:], T.sem[name], T.sem.snd, pid, rid, mask_out), names or [src], [], ("snd", n_eng * (k + 1), False))
+
+        S(act(T.gg[:], T.glw[:].indirect(T[ml][:]), AF.Copy), ["glw", ml], ["gg"])
+        S(act(T.mb[:], T.imw[:].indirect(T[ml][:]), AF.Copy), ["imwa", "imwb", ml], ["mb"])
+        V(cp(T.ol[:], T.tb[:, 0:512].indirect(T[ml][:])), ["tb", ml], ["ol"])
+        if t == 0:
+            consts()
+        V(cp(mlf, T[ml][:]), [ml], ["mlf"] + ["esm"] * (t == 0))
+        na(0, 2)
+        pg("v", 0, 2)
+        P(mm(T.p5[0:96, 0:128], T[z][:, 0:96], T.cid[:]), [z, "cid"], ["p5"])
+        P(mm(T.p5[0:96, 128:256], T[z][:, 96:192], T.cid[:]), [z, "cid"], ["p5"])
+        P(mm(T.p6[:, 0:192], T.cid[:], T[z][:], True, False), [z, "cid"], ["p6"])
+        P(mm(T.p6[:, 0:192], T.cidn[:], T.gg[:], False, True), ["cidn", "gg"], ["p6"])
+        S(act(T.zt[0:96, :], T.p5[0:96, 0:256], AF.Copy), ["p5"], ["zt"])
+        S(act(T.gi[:], T.p6[:, 0:192], AF.Sign, bias=0.5), ["p6"], ["gi"])
+        na(2, 4)
+        S(act(T.of[:], T.tb[:, 0:512].indirect(T[ml][:]), AF.Copy), ["tb", ml], ["of"])
+        zexp(0)
+        zexp(1)
+        P(mm(T.p5[:, 256:448], T.cbh[:], T.gi[:]), ["cbh", "gi"], ["p5"])
+        P(mm(T.p6[:, 0:192], T.wb[:], T[z][:]), ["wb", z], ["p6"])
+        P(mm(T.p6[:, 192:384], T.wb8[:], T[z][:], True, False), ["wb8", z], ["p6"])
+        P(mm(T.p6[:, 192:384], T.c296[:], T.mb[:], False, True), ["c296", "mb"], ["p6"])
+        scan(0, 2)
+        V(ts(T.tg[:, 192:384], T.p5[:, 256:448], 8.0, T.thr[:, t:t + 1], A.add, A.is_ge), ["p5", th], ["tgg"])
+        V(cp(T.ui[:], T.p6[:, 0:384]), ["p6"], ["ui"])
+        V(ts(T.ua[:], T.ui[:], 4095, None, A.bitwise_and), ["ui"], ["ua"])
+        V(ts(T.tg[:, 0:192], T.ua[:, 192:384], 0.125, 1.0, A.mult, A.add), ["ua"], ["tgt"])
+        if t == 0:
+            distances()
+        cmp(0)
+        cmp(1)
+        listmm("p7", 0, 24, "sel", "tg", 384, (), ["tgg", "tgt"])
+        S(act(T.p2[:, 0:192], T.of[:], AF.Copy), ["of"], ["p2"])
+        S(act(T.p2[:, 192:384], T.of[:], AF.Identity, bias=T.k37[:]), ["of", "k37"], ["p2"])
+        pg("s", 2, 3)
+        S(act(T.tgs[:, 0:12], T.p7[:, 0:12], AF.Copy, scale=0.0625), ["p7"], ["tgsa"])
+        S(act(T.tgs[:, 12:24], T.p7[:, 12:24], AF.Copy, scale=0.0625, accum_out=T.acc[:]), ["p7"], ["tgsb", "acc"])
+        S(act(tol, T.p7[:, 0:12], AF.Copy, scale=0.0625, bias=-1.0), ["p7"], ["tol"] + ["est"] * (t == 0))
+        if t == 0:
+            send("er", "es", "er", 0, ["est", "esm"])
+        if not lastt:
+            P(mm(T.p7[:, 64:65], T.onf[:], T.acc[:]), ["onf", "acc"], ["p7"])
+        pg("s", 3, 4)
+        zexp(2)
+        zexp(3)
+        cnt(0, 2)
+        V(tt(T.f1[:], T.ua[:, 0:192], T.p2[:, 0:192], A.mult), ["p2", "ua"], ["f1"])
+        V(ts(T.f2[:], T.f1[:], 5, None, A.arith_shift_right), ["f1"], ["f2"])
+        V(tt(T.kl[:], T.tgs[:, 0:12], T.tgs[:, 12:24], A.mult), ["tgsa", "tgsb"], ["kl"])
+        dups(0, 8)
+        relu15(0, 2)
+        use(0, 2)
+        na(4, 6)
+        pg("s", 4, 5)
+        pg("s", 5, 6)
+        scan(2, 4)
+        cmp(2)
+        cmp(3)
+        zexp(4)
+        zexp(5)
+        P(mm(T.p6[:, 0:192], T.cid[:], T.tg[:, 0:192], True, False), ["cid", "tgt"], ["p6"])
+        P(mm(T.p6[:, 0:192], T.cid[:], T.ns[:], False, True), ["cid", "ns"], ["p6"])
+        cnt(2, 4)
+        relu15(2, 4)
+        use(2, 4)
+        if not lastt:
+            V(cp(T.ai[:], T.p7[:, 64:65]), ["p7"], ["ai"])
+            V(ts(T.ai2[:], T.ai[:], 1, None, A.bitwise_and), ["ai"], ["ai2"])
+            V(ts(T.thr[:, t + 1:t + 2], T.ai2[:], 11.0, None, A.add), ["ai2"], ["thr%d" % (t + 1)])
+        scan(4, 5)
+        cmp(4)
+        scan(5, 6)
+        cmp(5)
+        relu15(4, 6)
+        cnt(4, 6)
+        S(act(T.d0[:, 0::32], T.na15[:], AF.Copy), regs("na15", 0, 6), regs("d0", 0, 6))
+        dups(8, 12)
+        V(ts(T.indk[:], T.p3[:, 0:192], T.thr[:, t:t + 1], 1024.0, A.is_ge, A.mult), ["p3", th], ["indk"])
+        listmm("p7", 96, 12, "sel", "indk", 192)
+        P(mm(T.p6[:, 192:384], T.ctm[:], T.indk[:]), ["ctm", "indk"], ["p6"])
+        V(tt(T.eb[:, :, 0:16], T.eb[:, :, 0:16], T.mk[:], A.mult), ["mk"] + ["eb%d" % c for c in range(12)], ["eb"])
+
+        def lost(Q):
+            Q.matmul(T.p5[:, 0:192], T.cnb[:], T.tg[:, 192:384], True, False)
+            for c in range(12):
+                ins = Q.matmul(T.p5[:, 16 * c:192], T.cb[:], T.eb[:, c, 0:192 - 16 * c], False, c == 11)
+            return ins
+        P(lost, ["cnb", "cb", "tgg", "eb"] + ["eb%d" % c for c in range(12)], ["p5"])
+        if t:
+            V(tt(T.ya[:], tol, T.p7[:, 96:108], A.subtract), ["tol", "p7"], ["ya"])
+            V(tt(T.yb[:], T.p7[:, 96:108], mlf, A.min), ["p7", "mlf"], ["yb"])
+            V(tt(T.mn[:], T.ya[:], T.yb[:], A.max), ["ya", "yb"], ["mn"])
+        if t == 0:
+            V(cp(T.xs[:], T.p7[:, 96:108]), ["p7"], ["xs"])
+            send("mr1", "xs", "xr", 1)
+        elif not lastt:
+            V(cp(T["ms%d" % (t + 1)][:], T.mn[:]), ["mn"], ["ms%d" % (t + 1)])
+            send("mr%d" % (t + 1), "ms%d" % (t + 1), "ml%d" % (t + 1), 2 * t + 1)
+        else:
+            op("y", lambda Q: Q.dma_start(T.ym[:], T.mn[:]), ["mn"], ["ym"], ("outm", 16, True))
+        S(act(T.oh[:], T.p6[:, 192:384], AF.Relu, scale=-0.0009765625), ["p6"], ["oh"])
+        listmm("p6", 384, 12, "selk", "oh", 192, ("b32", "one12"))
+        dd = T.dd[:, 128 * t:128 * t + 128]
+        P(mm(T.p0[:, 0:192], dd, T.oh[:]), ["dda", "ddb", "oh"], ["p0"])
+        P(mm(T.p0[:, 192:384], dd, T.oh[:], True, False), ["dda", "ddb", "oh"], ["p0"])
+        P(mm(T.p0[:, 192:384], T.cb[:], T.c255[:], False, True), ["cb", "c255"], ["p0"])
+        use(4, 6)
+        S(act(T.wn[:], T.p5[:, 0:192], AF.Relu, bias=-255.0, scale=-1.0), ["p5"], ["wn"])
+        V(tt(T.f3[:], T.f2[:], T.p2[:, 192:384], A.add), ["f2", "p2"], ["f3"])
+        V(ts(T.f4[:], T.f3[:], 4095, None, A.bitwise_and), ["f3"], ["f4"])
+        V(tt(T.fd[:], T.f4[:], T.p2[:, 0:192], A.subtract), ["f4", "p2"], ["fd"])
+        V(tt(T.si[:], T.wn[:], T.p6[:, 0:192], A.mult), ["wn", "p6"], ["si"])
+        listmm("p5", 448, 12, "sel", "si", 192, ("b512",))
+        V(cp(T.la[:], T.p6[:, 384:396]), ["p6"], ["la"])
+        V(tt(T.zdb[:], T[z][:], T.p0[:, 0:192], A.subtract), [z, "p0"], ["zdb"])
+        V(tt(T.yy[:], T.d0[:].indirect(T.la[:]), T.zdb[:], A.subtract), ["la", "zdb", "d0z"] + regs("d0", 0, 6), ["yy"])
+        V(tt(T.xx[:], T.yy[:], T.p0[:, 192:384], A.max), ["yy", "p0"], ["xx"])
+        if not lastt:
+            S(act(T["zs%d" % (t + 1)][:], T.xx[:], AF.Abs), ["xx"], ["zs%d" % (t + 1)])
+            send("zr%d" % (t + 1), "zs%d" % (t + 1), "zb%d" % (t + 1), 2 * t + 2)
+        else:
+            S(act(T.yzs[:], T.xx[:], AF.Abs), ["xx"], ["yzs"])
+            op("s", lambda Q: Q.dma_start(T.yz[:], T.yzs[:]), ["yzs"], ["yz"], ("outz", 16, True))
+        V(ts(T.p4[:, 192:384], T.p4[:, 0:192], 254.0, None, A.is_lt), ["p4"], ["p4", "ls"])
+        V(tt(T.fw[:], T.fd[:], T.p4[:, 192:384], A.mult), ["ls", "fd", "p4"], ["fw"])
+        V(ts(T.sl[:], T.p5[:, 448:460], 0.0625, None, A.mult), ["p5"], ["sl"])
+        V(tt(T.tb[:].indirect(T.sl[:]), T.fw[:], T.of[:], A.add), ["fw", "of", "sl"], ["tb"])
+
+    for t in range(STEPS):
+        step(t)
+
+    P(mm(T.p1[:, 0:256], T.cj[:], T.tb[:, 0:256]), ["cj", "tb"], ["p1"])
+    P(mm(T.p2[:, 0:256], T.cj[:], T.tb[:, 256:512]), ["cj", "tb"], ["p2"])
+    V(cp(T.yms[:, 0:256], T.p1[:, 0:256]), ["p1"], ["yma"])
+    S(act(T.yms[:, 256:512], T.p2[:, 0:256], AF.Copy), ["p2"], ["ymb"])
+    op("y", lambda Q: Q.dma_start(T.ymc[:, 0:256], T.yms[:, 0:256]), ["yma"], ["oa"], ("outa", 16, True))
+    op("s", lambda Q: Q.dma_start(T.ymc[:, 256:512], T.yms[:, 256:512]), ["ymb"], ["ob"], ("outb", 16, True))
+    emit()
+    for s in ("outm", "outz", "outa", "outb"):
+        g.wait_ge(T.sem[s], 16)
+    g.wait_ge(T.sem.snd, n_eng * (2 * (STEPS - 1) + 1))

@@ -8,65 +8,137 @@ F32 = "float32"
 F16 = "float16"
 I32 = "int32"
 U16 = "uint16"
+BLOCKS = [(128, 192), (64, 128), (0, 64)]
+MODS = [(64, 192), (0, 64)]
+NEWS = [(0, 192)]
+USES = [(64, 192), (0, 64)]
+NEEDS = [[(128, 192, "v"), (64, 128, "v"), (0, 64, "s")], [(128, 192, "v"), (64, 128, "s"), (0, 64, "s")]]
+ADDS = [[(128, 192, "s"), (64, 128, "v"), (0, 64, "s")], [(128, 192, "s"), (64, 128, "s"), (0, 64, "s")]]
+Q_MET = "vvv"
+Q_CLIP, Q_ML, Q_OF, Q_SAVE, Q_MOD, Q_R15 = "v", "v", "g", "g", "s", "v"
+SAVE = 32 * max(b - a for a, b in BLOCKS)
 BANKS = ["p%d" % b for b in range(8)]
 SCRATCH = {}
 for _names, _cols, _type in (
-        ("prw adw", 4096, B16), ("glw imw", 512, B16), ("mci", 512, I32), ("mcf yms", 512, F32), ("tb", 704, F32),
+        ("prw adw", 4096, B16), ("glw imw", 512, B16), ("mci", 512, I32), ("tb", 704, F32),
         ("mi", 12, I32), ("dvs", 5, B16), ("wts", 1, B16),
-        ("d0 d1 ss", 6144, B16), ("ind", 3072, B16), ("ol", 192, U16), ("gg mb na15 r15 gi indk oh zdb xx wn", 192, B16),
-        ("zt", 256, B16), ("tg", 384, F16), ("ui ua", 384, I32), ("tgs", 24, F32), ("mlf kl tol ya yb mn", 12, F32),
-        ("acc", 1, F32), ("ai ai2", 1, I32), ("thr", 8, F32), ("si", 192, F16), ("sl la", 12, U16), ("es er", 24, F32), ("xs xr", 12, F32),
-        ("yy yzs of fd fw", 192, F32), ("f1 f2 f3 f4", 192, I32),
-        ("pi kki gri", 1, I32), ("pf kkf grf k37 kw jc jt", 1, F32), ("iw", 192, F32), ("ig cj onf", 128, F32), ("ie ce", 1536, B16),
-        ("cid cidn c296 cb cbh tma tmb ctm cg4 cnb wb wb8", 128, B16), ("sel selk seln", 2048, B16), ("dg dd", 640, B16),
-        ("ic bl", 12, F32), ("b32 one12", 12, B16), ("b512", 12, F16), ("ns", 192, F16), ("c255", 192, B16)):
+        ("d1 ss", 6144, B16), ("ind", 3072, B16), ("ol", 192, U16), ("gg mb gi sg xx wn", 192, B16), ("oh", 384, B16),
+        ("zt", 128 * len(BLOCKS), B16), ("st", 128, B16), ("q1 q3 yy", 192, F16), ("mal ngl", 12, B16), ("kl tm ys", 12, F32),
+        ("acc", 4, F32), ("ai ai2", 1, I32), ("aif", 1, F32), ("thr", 16, F32), ("ml sl la", 12, U16),
+        ("yzs of fd fw", 192, F32), ("f1 f2 f3 f4", 192, I32),
+        ("pi kki gri odi", 1, I32), ("pf kkf grf k37 kw kwa ohb odf qb1 qb3 pw", 1, F32), ("pwi", 16, F32), ("th0", 3, F32),
+        ("iw", 192, F32), ("ig onf", 128, F32), ("ie ce", SAVE // 2, B16),
+        ("cid cidn cidh c37 cb cbh cb2 cb4 cbn cbn4 cbw cq1 cq3 tma ctm wb onb", 128, B16), ("isl sel selk seln", 2048, B16),
+        ("dg dd", 640, B16), ("ic bl b256", 12, F32), ("bas", 24, B16), ("lim", 192, B16)):
     for _n in _names.split():
         SCRATCH[_n] = ("sbuf", [128, _cols], _type)
-SCRATCH["eb"] = ("sbuf", [128, 12, 208], B16)
-SCRATCH["mk"] = ("sbuf", [128, 12, 16], B16)
+for _b, (_a, _e) in enumerate(BLOCKS):
+    SCRATCH["d0%d" % _b] = ("sbuf", [128, SAVE + 32 * (_e - _a)], B16)
+SCRATCH["tg"] = ("sbuf", [128, 2, 192], B16)
+SCRATCH["eb"] = ("sbuf", [128, 12, 192], B16)
 for _t in range(STEPS):
     SCRATCH["zb%d" % _t] = ("sbuf", [128, 192], B16)
-    SCRATCH["ml%d" % _t] = ("sbuf", [128, 12], U16)
-    if _t:
+    SCRATCH["mf%d" % _t] = ("sbuf", [128, 12], F32)
+    SCRATCH["ms%d" % _t] = ("sbuf", [128, 12], F32)
+    if _t < STEPS - 1:
         SCRATCH["zs%d" % _t] = ("sbuf", [128, 192], B16)
-        SCRATCH["ms%d" % _t] = ("sbuf", [128, 12], U16)
-del SCRATCH["ms1"]
 for _b in BANKS:
     SCRATCH[_b] = ("psum", [128, 512], F32)
 LOADS = ["mc", "m0", "z0", "ad", "gl", "pr", "wt", "dv"]
-SEMAPHORES = ["cv", "cs", "ct", "cg", "outz", "outm", "outa", "outb", "snd"] + ["ld_" + n for n in LOADS]
-SEMAPHORES += ["er"] + ["mr%d" % t for t in range(1, STEPS)] + ["zr%d" % t for t in range(1, STEPS)]
+SEMAPHORES = ["cv", "cs", "ct", "cg", "outz", "outm", "outa", "snd"] + ["ld_" + n for n in LOADS]
+SEMAPHORES += ["%s%d_%d" % (x, t, b) for x in ("mr", "zr") for t in range(1, STEPS) for b in range(len(BLOCKS))]
+
+CYCLE, PE_CYCLE, CALL, WAKE, LOOK = 0.83, 0.42, 20.0, 70.0, 0.0
+GATHER, SCATTER, SEND, FLIGHT = 1.56, 3.8, 600.0, {"m": 1700.0, "z": 2250.0}
+FIRST = 3600.0
+ORDER, DAG = [], []
+PERIOD = 16.3
+DUE = {'lists': (-17.7, 5.5, -44.5), 'ops': (5.3, 9.7, 22.1), 'adds': (-5.9, 10.0, 13.9), 'needs': (39.4, 13.2, 41.6), 'scan': (-0.9, -24.3, -0.3), 'goal': (-56.1, -25.9, 28.4), 'mod': (-7.0, 9.7, 7.7), 'first': (-4.6, -15.3, -14.4), 'count': (16.2,), 'lost': (38.5,), 'new': (-25.1, -31.6, 34.1), 'use': (1.5, 3.5, -18.0), 'write': (24.7, 29.1, 13.2), 'met': (-3.4, 6.4, 18.0), 'cmp': (-33.5, -13.1, 13.6), 'pass': (-26.6, 0.6, -21.5), 'move': (11.3, 1.8, 10.5)}
 
 
-def scheduler(g, T):
+def scheduler(g, T, now):
     queues = {"g": g, "v": g.vector, "s": g.scalar, "t": g.tensor, "y": g.sync}
-    ops = []
-    wr, rd, bank = {}, {}, {}
+    calls = []
 
-    def op(q, fn, r=(), w=(), ext=None):
-        i = len(ops)
-        deps = set()
-        for x in list(r) + list(w):
-            if x in BANKS:
-                h = bank.setdefault(x, {})
-                deps.update(h[k] for k in h if k != q or (q != "t" and x in w))
-                h[q] = i
-        for x in r:
-            if x not in BANKS:
+    def op(q, call, r=(), w=(), ext=None, after=None):
+        calls.append({"q": q, "fn": call[0], "ns": call[1], "late": call[2] if len(call) > 2 else 0.0, "r": list(r), "w": list(w), "ext": ext,
+                      "after": after, "due": now[0], "cls": tuple(now[1:]), "banks": {x[:2] for x in list(r) + list(w) if x[:2] in BANKS}})
+        return len(calls) - 1
+
+    def needs(ops, banks):
+        wr, rd, bank = {}, {}, {}
+        for i, o in enumerate(ops):
+            deps = set()
+            if banks:
+                for x in o["banks"]:
+                    h = bank.setdefault(x, {})
+                    deps.update(h[k] for k in h if k != o["q"])
+                    h[o["q"]] = i
+            for x in o["r"]:
                 if x in wr:
                     deps.add(wr[x])
-                rd.setdefault(x, {})[q] = i
-        for x in w:
-            if x not in BANKS:
+                rd.setdefault(x, []).append(i)
+            for x in o["w"]:
                 if x in wr:
                     deps.add(wr[x])
-                deps.update(rd.get(x, {}).values())
+                deps.update(rd.get(x, []))
                 wr[x] = i
-                rd[x] = {}
-        deps.discard(i)
-        ops.append({"q": q, "fn": fn, "deps": deps, "ext": ext})
+                rd[x] = []
+            deps.discard(i)
+            o["deps"] = deps
+
+    def place(due, pre, users, look):
+        left = [len(p) for p in pre]
+        can = [0.0] * len(calls)
+        ready = {}
+        for i, n in enumerate(left):
+            if n == 0:
+                ready.setdefault(calls[i]["q"], []).append(i)
+        free, bank, start, out = {}, {}, {}, []
+
+        def first(i):
+            o = calls[i]
+            t = max(can[i], free.get(o["q"], 0.0))
+            for x in o["banks"]:
+                for k, e in bank.get(x, {}).items():
+                    if k != o["q"] and e + WAKE > t:
+                        t = e + WAKE
+            return t
+        while len(out) < len(calls):
+            t, q = min((min(first(i) for i in r), str(q)) for q, r in ready.items() if r)
+            q = None if q == "None" else q
+            i = min((j for j in ready[q] if first(j) <= t + look), key=lambda j: (due[j], j))
+            o = calls[i]
+            start[i] = first(i)
+            end = start[i] + o["ns"]
+            if q:
+                free[q] = end
+            for x in o["banks"]:
+                bank.setdefault(x, {})[q] = end
+            out.append(i)
+            ready[q].remove(i)
+            for u in users[i]:
+                can[u] = max(can[u], end + (0.0 if calls[u]["after"] == i else o["late"] + WAKE))
+                left[u] -= 1
+                if left[u] == 0:
+                    ready.setdefault(calls[u]["q"], []).append(u)
+        return out, start
+
+    def order():
+        if not ORDER:
+            needs(calls, False)
+            pre = [set(o["deps"]) | ({o["after"]} if o["after"] is not None else set()) for o in calls]
+            users = [set() for _ in calls]
+            for i, p in enumerate(pre):
+                for d in p:
+                    users[d].add(i)
+            DAG.append((calls, pre, users, place))
+            ORDER[:] = place([o["due"] for o in calls], pre, users, LOOK)[0]
+        return [calls[i] for i in ORDER]
 
     def emit():
+        ops = order()
+        needs(ops, True)
         pos, known, snap, need, waits = {}, {}, [], set(), []
         for i, o in enumerate(ops):
             q = o["q"]
@@ -76,8 +148,8 @@ def scheduler(g, T):
             mine = []
             for d in sorted(o["deps"], reverse=True):
                 e = ops[d]["ext"]
-                key, val = (e[0], e[1]) if e else (ops[d]["q"], ops[d]["pos"])
-                if k.get(key, 0) >= val:
+                key, val = (e[0], 1) if e else (ops[d]["q"], ops[d]["pos"])
+                if k.get(key, 0) >= val or key == q == "t":
                     continue
                 mine.append(d)
                 need.add(d)
@@ -119,14 +191,26 @@ def scheduler(g, T):
 
 
 def regs(name, a, b):
-    return ["%s.%d" % (name, c) for c in range(a, b)]
+    return ["%s.%d" % (name, c) for c in range(a // 32, (b + 31) // 32)]
+
+
+def every(name):
+    return regs(name, 0, 192)
+
+
+def size(ap):
+    n = 1
+    for x in ap.shape[1:]:
+        n *= x
+    return n
 
 
 def rank_program(g, core, T, topo):
     rank = T.rank_of(core)
     if rank is None:
         return
-    op, emit = scheduler(g, T)
+    now = [0.0, -1, None, 0]
+    op, emit = scheduler(g, T, now)
     n_ranks = len(T.cores)
     nxt = T.cores[(rank + 1) % n_ranks]
     n_eng = 8
@@ -145,322 +229,334 @@ def rank_program(g, core, T, topo):
     def G(fn, r=(), w=()):
         op("g", fn, r, w)
 
-    def ts(out, in0, s1, s2, *o):
-        return lambda Q: Q.tensor_scalar(out, in0, s1, s2, *o)
+    def ns(n, rate=1.0):
+        return max(64, n * rate) * CYCLE + CALL
 
-    def tt(out, a, b, o):
-        return lambda Q: Q.tensor_tensor(out, a, b, o)
+    def ts(out, in0, s1, s2, *o, rate=1.0):
+        return (lambda Q: Q.tensor_scalar(out, in0, s1, s2, *o)), ns(size(out), rate)
 
-    def cp(out, a):
-        return lambda Q: Q.tensor_copy(out, a)
+    def tt(out, a, b, o, rate=1.0):
+        return (lambda Q: Q.tensor_tensor(out, a, b, o)), ns(size(b), rate)
+
+    def cp(out, a, rate=1.0):
+        return (lambda Q: Q.tensor_copy(out, a)), ns(size(out), rate)
 
     def act(out, a, f, **k):
-        return lambda Q: Q.activation(out, a, f, **k)
+        return (lambda Q: Q.activation(out, a, f, **k)), ns(size(out)) + 100.0 * ("accum_out" in k)
 
     def ms(out, c):
-        return lambda Q: Q.memset(out, c)
+        return (lambda Q: Q.memset(out, c)), ns(size(out), 0.5)
 
-    def mm(out, a, b, start=True, stop=True):
-        return lambda Q: Q.matmul(out, a, b, start, stop)
+    def gather(call, n, rate=GATHER):
+        return call[0], 60 + n * rate * CYCLE + CALL
+
+    def mm(out, *terms):
+        def fn(Q):
+            for i, x in enumerate(terms):
+                ins = Q.matmul(x[2] if len(x) > 2 else out, x[0], x[1], i == 0, i == len(terms) - 1)
+            return ins
+        return fn, sum(max(min(64, size(x[0])), size(x[1])) for x in terms) * PE_CYCLE
 
     def iota(out, pattern, base=0, cm=0):
-        return lambda Q: Q.iota(out, pattern, base, cm, allow_small_or_imprecise_dtypes=True)
+        return (lambda Q: Q.iota(out, pattern, base, cm, allow_small_or_imprecise_dtypes=True)), 130 + 2 * size(out) * CYCLE
 
-    def load(q, name, buf):
-        op(q, lambda Q: Q.dma_start(T[buf][:], T[name][:]), [], [buf], ("ld_" + name, 16, True))
+    def move(q, out, a, r, w):
+        if q == "g":
+            G(((lambda Q: Q.affine_select(out, a, [[0, size(out)]], A.is_ge, 0.0, 0, 0)), 170 + 2 * size(out) * CYCLE), r, w)
+        elif q == "v":
+            V(cp(out, a), r, w)
+        else:
+            S(act(out, a, AF.Copy), r, w)
 
-    load("y", "mc", "mci")
-    load("s", "m0", "mi")
-    load("y", "ad", "adw")
-    load("s", "pr", "prw")
-    load("y", "gl", "glw")
-    load("y", "z0", "zb0")
-    load("y", "wt", "wts")
-    load("y", "dv", "dvs")
+    behind = {}
 
-    G(lambda Q: Q.iota(T.pi[:], [[0, 1]], 0, 1), [], ["pi"])
+    def dma(q, out, a, r, w, sem, late):
+        behind[q] = op(q, ((lambda Q: Q.dma_start(out, a)), 100.0, late), r, w, (sem, 16, True), behind.get(q))
+
+    for q, name, buf, late in (("s", "m0", "mi", 1600), ("y", "mc", "mci", 3300), ("y", "ad", "adw", 7400), ("s", "gl", "glw", 2100), ("s", "z0", "zb0", 2300),
+                               ("s", "wt", "wts", 2300), ("s", "dv", "dvs", 2300), ("y", "pr", "prw", 11500)):
+        dma(q, T[buf][:], T[name][:], [], regs("z0", 0, 192) if name == "z0" else [buf], "ld_" + name, late)
+
+    now[0] = -100.0
+    G(((lambda Q: Q.iota(T.pi[:], [[0, 1]], 0, 1)), 140.0), [], ["pi"])
     G(iota(T.ig[:], [[1, 8], [0, 16]]), [], ["ig"])
     G(iota(T.iw[:], [[1, 192]]), [], ["iw"])
-    G(iota(T.ie[:], [[1, 96], [0, 16]]), [], ["ie"])
     G(iota(T.ic[:], [[16, 12]]), [], ["ic"])
     G(iota(T.imw[:, 0:256], [[1, 256]]), [], ["imwa"])
     G(iota(T.imw[:, 256:512], [[1, 256]], -256), [], ["imwb"])
-    V(ms(T.d0[:, 1::2], 0.0), [], ["d0z"])
-    V(ms(T.sel[:], 0.0), [], ["selz"])
+    G(iota(T.isl[:], [[-100, 16], [1, 8], [100, 16]]), [], ["isl"])
+    G(iota(T.ie[:], [[1, SAVE // 32], [0, 16]]), [], ["ie"])
+    for b, (a, e) in enumerate(BLOCKS):
+        V(ms(T["d0%d" % b][:, 0:32 * (e - a):2], 0.0), [], ["d0z%d" % b])
+        S(act(T.d1[:, 32 * a + 1:32 * e:2], T["d0%d" % b][:, 0:32 * (e - a):2], AF.Copy), ["d0z%d" % b], regs("r15", a, e))
     V(ts(T.kki[:], T.pi[:], 15, None, A.bitwise_and), ["pi"], ["kki"])
     V(ts(T.gri[:], T.pi[:], 4, None, A.arith_shift_right), ["pi"], ["gri"])
-    V(cp(T.pf[:], T.pi[:]), ["pi"], ["pf"])
-    V(cp(T.kkf[:], T.kki[:]), ["kki"], ["kkf"])
-    V(cp(T.grf[:], T.gri[:]), ["gri"], ["grf"])
-    V(ts(T.kw[:], T.kkf[:], 2.0, -1.0, A.mult, A.add), ["kkf"], ["kw"])
+    V(ts(T.odi[:], T.pi[:], 1, None, A.bitwise_and), ["pi"], ["odi"])
+    for a, b in (("pf", "pi"), ("kkf", "kki"), ("grf", "gri"), ("odf", "odi")):
+        V(cp(T[a][:], T[b][:]), [b], [a])
     V(ts(T.cb[:], T.ig[:], T.grf[:], None, A.is_equal), ["ig", "grf"], ["cb"])
-    for i in range(16):
-        V(cp(T.sel[:, 129 * i:129 * i + 113:16], T.cb[:, 0::16]), ["cb", "selz"], ["sel"] if i == 15 else [])
-    S(act(T.d1[:, 0::2], T.d0[:, 1::2], AF.Copy), ["d0z"], ["d1z"])
+    V(ts(T.sel[:], T.isl[:], T.grf[:], None, A.is_equal, rate=0.5), ["isl", "grf"], ["sel"])
+    V(ts(T.kwa[:], T.kkf[:], 15.0, SAVE - 31.0, A.is_equal, A.mult), ["kkf"], ["kwa"])
+    V(ts(T.kw[:], T.kkf[:], 2.0, 1.0, A.mult, A.add), ["kkf"], ["kw"])
+    V(tt(T.kw[:], T.kw[:], T.kwa[:], A.add), ["kw", "kwa"], ["kw"])
     S(act(T.seln[:], T.sel[:], AF.Copy, scale=-1.0), ["sel"], ["seln"])
     S(act(T.selk[:], T.sel[:], AF.Copy, scale=T.kw[:]), ["sel", "kw"], ["selk"])
-    V(ts(T.k37[:], T.kkf[:], -37.0, 555.0, A.mult, A.add), ["kkf"], ["k37"])
-    V(tt(T.jt[:], T.pf[:], T.kw[:], A.subtract), ["pf", "kw"], ["jt"])
-    V(ts(T.jc[:], T.jt[:], 14.0, None, A.add), ["jt"], ["jc"])
-    V(ts(T.cj[:], T.iw[:, 0:128], T.jc[:], None, A.is_equal), ["iw", "jc"], ["cj"])
-    V(cp(T.mcf[:], T.mci[:]), ["mci"], ["mcf"])
-    P(mm(T.p0[:], T.cj[:], T.mcf[:]), ["cj", "mcf"], ["p0"])
-    V(cp(T.ml0[:], T.mi[:]), ["mi"], ["ml0"])
+    V(ts(T.k37[:], T.kkf[:], 37.0, None, A.mult), ["kkf"], ["k37"])
+    V(ts(T.ohb[:], T.kkf[:], -14.5, 1024.0, A.add, A.mult), ["kkf"], ["ohb"])
+    V(ts(T.qb1[:], T.odf[:], 2560.0, -1280.5 + 2.0 ** -13, A.mult, A.add), ["odf"], ["qb1"])
+    V(ts(T.qb3[:], T.odf[:], 2560.0, -1280.5 + 2.0 ** -10, A.mult, A.add), ["odf"], ["qb3"])
     V(ts(T.cid[:], T.iw[:, 0:128], T.pf[:], None, A.is_equal), ["iw", "pf"], ["cid"])
-    V(cp(T.tb[:, 0:512], T.p0[:]), ["p0"], ["tb"])
+    V(ts(T.ce[:], T.ie[:], T.pf[:], None, A.is_equal, rate=0.5), ["ie", "pf"], ["ce"])
+    for name, src, c in (("cidn", "cid", -1.0), ("cidh", "cid", 0.5), ("c37", "cid", 37.0), ("cbh", "cb", 0.5), ("cb2", "cb", -2.0), ("cb4", "cb", 4.0),
+                         ("cbn", "cb", -4.0), ("cbn4", "cb", -0.25), ("cq1", "cb", -256.0), ("cq3", "cb", -32.0)):
+        V(ts(T[name][:], T[src][:], c, None, A.mult), [src], [name])
+    V(ts(T.tma[:], T.iw[:, 0:128], T.pf[:], None, A.is_lt), ["iw", "pf"], ["tma"])
+    V(tt(T.tma[:], T.tma[:], T.cb[:], A.mult), ["tma", "cb"], ["tma"])
+    V(tt(T.ctm[:], T.cidh[:], T.tma[:], A.subtract), ["tma", "cidh"], ["ctm"])
+    V(ms(T.onb[:], 1.0), [], ["onb"])
+    V(ms(T.onf[:], 1.0), [], ["onf"])
+    V(ms(T.fw[:], 0.5), [], every("fw"))
+    V(ms(T.fw[:, 0::16], 0.0), [], every("fw"))
+    V(ms(T.fd[:], 0.0), [], every("fd"))
+    V(ms(T.fd[:, 0::16], -0.125), [], every("fd"))
+    V(((lambda Q: Q.tensor_tensor_scan(T.lim[:], T.fw[:], T.fd[:], 0.0, A.mult, A.add)), ns(192)), every("fw") + every("fd"), ["lim"])
+    V(ts(T.pwi[:], T.iw[:, 0:16], T.kkf[:], -8.0, A.is_equal, A.mult), ["iw", "kkf"], ["pwi"])
+    V(tt(T.pwi[:], T.pwi[:], T.lim[:, 0:16], A.mult), ["pwi", "lim"], ["pwi"])
+    V(((lambda Q: Q.tensor_reduce(T.pw[:], T.pwi[:], AxisListType.X, A.add)), ns(16)), ["pwi"], ["pw"])
+    V(ts(T.cbw[:], T.cb[:], T.pw[:], None, A.mult), ["cb", "pw"], ["cbw"])
+    V(ts(T.bl[:], T.ic[:], T.kkf[:], None, A.add), ["ic", "kkf"], ["bl"])
+    V(ts(T.b256[:], T.bl[:], 256.0, None, A.add), ["bl"], ["b256"])
+    for b, (a, e) in enumerate(BLOCKS):
+        n = (e - a) // 16
+        V(ms(T.bas[:, a // 8:a // 8 + n], -256.0), [], ["basa%d" % b])
+        V(ts(T.bas[:, a // 8 + n:a // 8 + 2 * n], T.bl[:, 0:n], 32768.0, None, A.mult), ["bl"], ["basb%d" % b])
+    for i, c in enumerate((-2.5, -42.5, -34.5)):
+        V(ms(T.th0[:, i:i + 1], c), [], ["th0%d" % i])
+    V(ts(T.wb[:], T.cb[:], T.wts[:], None, A.mult), ["cb", "wts"], ["wb"])
+    for t in range(STEPS):
+        V(ts(T.dg[:, 128 * t:128 * t + 128], T.cid[:], T.dvs[:, t:t + 1], None, A.mult), ["cid", "dvs"], ["dg%d" % t])
+    P(mm(T.p0[:], (T.cb[:], T.dg[:, 0:512])), ["cb", "dg0", "dg1", "dg2", "dg3"], ["p0"])
+    P(mm(T.p1[:, 0:128], (T.cb[:], T.dg[:, 512:640])), ["cb", "dg4"], ["p1"])
+    S(act(T.dd[:, 0:512], T.p0[:], AF.Copy, scale=2.0 ** -10), ["p0"], ["dd0", "dd1", "dd2", "dd3"])
+    S(act(T.dd[:, 512:640], T.p1[:, 0:128], AF.Copy, scale=2.0 ** -10), ["p1"], ["dd4"])
+    V(cp(T.tb[:, 0:512], T.mci[:]), ["mci"], ["tb"])
+    V(cp(T.mf0[:], T.mi[:]), ["mi"], regs("m0", 0, 192))
 
-    def consts():
-        V(ts(T.ce[:], T.ie[:], T.pf[:], None, A.is_equal), ["ie", "pf"], ["ce"])
-        V(ts(T.cidn[:], T.cid[:], -1.0, None, A.mult), ["cid"], ["cidn"])
-        V(ts(T.c296[:], T.cid[:], 296.0, None, A.mult), ["cid"], ["c296"])
-        V(ts(T.cg4[:], T.cb[:], -4.0, None, A.mult), ["cb"], ["cg4"])
-        V(ts(T.cbh[:], T.cb[:], 0.5, None, A.mult), ["cb"], ["cbh"])
-        V(ts(T.cnb[:], T.cb[:], -16.0, None, A.mult), ["cb"], ["cnb"])
-        V(ms(T.thr[:], 11.0), [], ["thr0"])
-        for c in range(12):
-            V(ts(T.mk[:, c, :], T.iw[:, 0:16], T.kkf[:], None, A.is_gt), ["iw", "kkf"], ["mk"] if c == 11 else [])
-        V(ts(T.tma[:], T.iw[:, 0:128], T.pf[:], 2.0, A.is_gt, A.mult), ["iw", "pf"], ["tma"])
-        V(tt(T.tmb[:], T.tma[:], T.cb[:], A.mult), ["tma", "cb"], ["tmb"])
-        V(tt(T.ctm[:], T.tmb[:], T.cid[:], A.subtract), ["tmb", "cid"], ["ctm"])
-        V(ts(T.bl[:], T.ic[:], T.kkf[:], None, A.add), ["ic", "kkf"], ["bl"])
-        V(ts(T.b32[:], T.bl[:], 32.0, None, A.mult), ["bl"], ["b32"])
-        V(ts(T.b512[:], T.bl[:], 512.0, 16.0, A.add, A.mult), ["bl"], ["b512"])
-        V(ms(T.one12[:], 1.0), [], ["one12"])
-        V(ts(T.ns[:], T.iw[:], -1.0, -513.0, A.mult, A.add), ["iw"], ["ns"])
-        V(ms(T.c255[:], -15.9375), [], ["c255"])
-        V(ms(T.onf[:], 1.0), [], ["onf"])
-        V(ts(T.wb[:], T.cb[:], T.wts[:], None, A.mult), ["cb", "wts"], ["wb"])
-        V(ts(T.wb8[:], T.cb[:], T.wts[:], 8.0, A.mult, A.mult), ["cb", "wts"], ["wb8"])
-        for t in range(STEPS):
-            V(ts(T.dg[:, 128 * t:128 * t + 128], T.cid[:], T.dvs[:, t:t + 1], None, A.mult), ["cid", "dvs"], ["dg%d" % t])
+    def listmm(out, mats, buf, a, b, base=()):
+        return mm(out, *(list(base) + [(T[mats][:, 128 * i:128 * i + 128], T[buf][:, a + i:b:16]) for i in range(16)]))
 
-    def distances():
-        for t in range(STEPS):
-            P(mm(T.p2[:, 128 * (t % 4):128 * (t % 4) + 128], T.cb[:], T.dg[:, 128 * t:128 * t + 128]), ["cb", "dg%d" % t], ["p2"])
-            if t == 3:
-                S(act(T.dd[:, 0:512], T.p2[:], AF.Copy), ["p2"], ["dda"])
-        S(act(T.dd[:, 512:640], T.p2[:, 0:128], AF.Copy), ["p2"], ["ddb"])
+    sends = [0]
 
-    def listmm(pb, col, width, mats, buf, total, base=(), names=None):
-        def fn(Q):
-            out = T[pb][:, col:col + width]
-            first = True
-            for b in base:
-                Q.matmul(out, T.cid[:], T[b][:], first, False)
-                first = False
-            for i in range(16):
-                ins = Q.matmul(out, T[mats][:, 128 * i:128 * i + 128], T[buf][:, i:total:16], first, i == 15)
-                first = False
-            return ins
-        P(fn, ["cid", mats] + (names or [buf]) + list(base), [pb])
+    def send(name, src, dst, r, w):
+        sends[0] += 1
+        i = op("g", ((lambda Q: Q.remote_dma(dst, src, T.sem[name], T.sem.snd, pid, rid, mask_out)), SEND), r, [], ("snd%d" % sends[0], 0, False))
+        op(None, (None, 0.0, FLIGHT[name[0]] + FIRST * (sends[0] == 1)), [], w, (name, n_eng, False), i)
+
+    def back(a, b):
+        return slice(b - 1, a - 1 if a else None, -1)
+
+    def home(a):
+        b = [i for i, x in enumerate(BLOCKS) if x[0] <= a < x[1]][0]
+        return b, T["d0%d" % b], BLOCKS[b][0]
+
+    def quotient(out, a, scale, bias, r, w):
+        if Q_MOD == "s":
+            S(act(out, a, AF.Identity, scale=scale, bias=bias), r, w)
+        else:
+            V(ts(out, a, scale, bias, A.mult, A.add), r, w)
 
     def step(t):
         lastt = t == STEPS - 1
-        ml, z, th = "ml%d" % t, "zb%d" % t, "thr%d" % t
-        if t:
-            op(None, None, [], [ml if t > 1 else "xr"], ("mr%d" % t, n_eng, False))
-            op(None, None, [], [z], ("zr%d" % t, n_eng, False))
-        tol, mlf = (T.tol[:], T.mlf[:]) if t else (T.es[:, 0:12], T.es[:, 12:24])
-        if t == 1:
-            op(None, None, [], ["er"], ("er", n_eng, False))
-            V(tt(T.ya[:], T.er[:, 0:12], T.xr[:], A.subtract), ["er", "xr"], ["ya"])
-            V(tt(T.yb[:], T.xr[:], T.er[:, 12:24], A.min), ["er", "xr"], ["yb"])
-            V(tt(T.mn[:], T.ya[:], T.yb[:], A.max), ["ya", "yb"], ["mn"])
-            V(cp(T[ml][:], T.mn[:]), ["mn"], [ml])
+        mf, z = T["mf%d" % t], T["zb%d" % t]
+        mfn, zn = "m%d" % t, "z%d" % t
+        th = [T.thr[:, 3 * t + i:3 * t + i + 1] if t else T.th0[:, i:i + 1] for i in range(3)]
+        thn = ["thr%d" % t] if t else ["th00", "th01", "th02"]
 
-        def na(a, b):
-            S(act(T.d0[:, 1024 * a:1024 * b:2], T.adw[:].indirect(T.ol[:, 32 * a:32 * b]), AF.Copy, scale=-1.0), ["adw", "ol"], regs("d0", a, b))
-            S(act(T.na15[:, 32 * a:32 * b], T.d0[:, 1024 * a:1024 * b:32], AF.Copy), regs("d0", a, b), regs("na15", a, b))
+        def when(what, a=0):
+            now[1:] = [t, what, home(a)[0] if len(DUE[what]) > 1 else 0]
+            now[0] = PERIOD * t + DUE[what][now[3]]
 
-        def pg(q, a, b):
-            out, win = T.d1[:, 1024 * a + 1:1024 * b:2], T.prw[:].indirect(T.ol[:, 32 * a:32 * b])
-            op(q, cp(out, win) if q == "v" else act(out, win, AF.Copy), ["prw", "ol"], regs("d1", a, b))
+        for b, (a, e) in enumerate(BLOCKS):
+            c = slice(a // 16, e // 16)
+            when("lists", a)
+            move(Q_ML if t else "v", T.ml[:, c], mf[:, c] if t else T.mi[:, c], regs(mfn, a, e) if t else ["mi"], regs("ml", a, e))
+            S(gather(act(T.gg[:, a:e], T.glw[:].indirect(T.ml[:, c]), AF.Copy), e - a), ["glw"] + regs("ml", a, e), regs("gg", a, e))
+            S(gather(act(T.mb[:, a:e], T.imw[:].indirect(T.ml[:, c]), AF.Copy), e - a), ["imwa", "imwb"] + regs("ml", a, e), regs("mb", a, e))
+            when("ops", a)
+            win = T.tb[:, 0:512] if t else T.mci[:]
+            V(gather(cp(T.ol[:, a:e], win.indirect(T.ml[:, c])), e - a), ["tb" if t else "mci"] + regs("ml", a, e), regs("ol", a, e))
 
-        def scan(a, b):
-            k = slice(1024 * a, 1024 * b, 32)
-            c = slice(32 * a, 32 * b)
-            V(tt(T.d1[:, k], T.gg[:, c], T.d0[:, k], A.add), ["gg"] + regs("d0", a, b), regs("d1", a, b))
-            V(ms(T.d0[:, k], -1024.0), [], regs("d0", a, b))
-            j = slice(1024 * a, 1024 * b)
-            V(lambda Q: Q.tensor_tensor_scan(T.ss[:, j], T.d0[:, j], T.d1[:, j], 0.0, A.add, A.max),
-              ["d0z", "d1z"] + regs("d0", a, b) + regs("d1", a, b), regs("ss", a, b))
+        for a, e, q in ADDS[min(t, 1)]:
+            b, d0, o = home(a)
+            when("adds", a)
+            out, win = d0[:, 32 * (a - o) + 1:32 * (e - o):2], T.adw[:].indirect(T.ol[:, a:e])
+            call = ts(out, win, -1.0, None, A.mult) if q == "v" else act(out, win, AF.Copy, scale=-1.0)
+            op(q, gather(call, 16 * (e - a)), ["adw"] + regs("ol", a, e), regs("d0", a, e) + regs("cut", a, e))
+        for a, e, q in NEEDS[min(t, 1)]:
+            when("needs", a)
+            out, win = T.d1[:, 32 * a:32 * e:2], T.prw[:].indirect(T.ol[:, a:e])
+            op(q, gather(cp(out, win) if q == "v" else act(out, win, AF.Copy), 16 * (e - a)), ["prw"] + regs("ol", a, e), regs("d1", a, e))
+        for b, (a, e) in enumerate(BLOCKS):
+            d0, n = T["d0%d" % b], e - a
+            when("scan", a)
+            first, kept = d0[:, 31:32 * n:32], d0[:, SAVE:SAVE + 32 * n:32]
+            P(mm(T.p4[:, 384:384 + n], (T.cid[:], T.gg[:, a:e]), (T.cid[:], first)), ["cid"] + regs("gg", a, e) + regs("cut", a, e), ["p4.r"])
+            if Q_R15 == "v":
+                V(ts(T.d1[:, 32 * a + 31:32 * e:32], T.p4[:, 384:384 + n], 0.0, None, A.max), ["p4.r"], regs("r15", a, e))
+            else:
+                S(act(T.d1[:, 32 * a + 31:32 * e:32], T.p4[:, 384:384 + n], AF.Relu), ["p4.r"], regs("r15", a, e))
+            move(Q_SAVE, kept, first, regs("cut", a, e), regs("a15", a, e))
+            if Q_SAVE == "g":
+                G(iota(first, [[0, n]], -1024), [], regs("cut", a, e))
+            else:
+                V(ms(first, -1024.0), [], regs("cut", a, e))
+            j, k = back(32 * a, 32 * e), back(0, 32 * n)
+            V(((lambda Q, j=j, k=k, d0=d0: Q.tensor_tensor_scan(T.ss[:, j], d0[:, k], T.d1[:, j], 0.0, A.add, A.max)), ns(32 * n, 0.5)),
+              ["d0z%d" % b] + regs("d0", a, e) + regs("cut", a, e) + regs("d1", a, e) + regs("r15", a, e), regs("ss", a, e))
 
-        def relu15(a, b):
-            V(ts(T.r15[:, 32 * a:32 * b], T.d1[:, 1024 * a:1024 * b:32], 0.0, None, A.max), regs("d1", a, b), regs("r15", a, b))
+        for b, (a, e) in enumerate(BLOCKS):
+            when("goal", a)
+            P(mm(T.p5[:, 128 + a:128 + e], (T.cid[:], z[:, a:e]), (T.cidn[:], T.gg[:, a:e])), ["cid", "cidn"] + regs(zn, a, e) + regs("gg", a, e), regs("p5.d", a, e))
+            S(act(T.gi[:, a:e], T.p5[:, 128 + a:128 + e], AF.Sign, bias=0.5), regs("p5.d", a, e), regs("gi", a, e))
+            P(mm(T.p5[:, 320 + a:320 + e], (T.cbh[:], T.gi[:, a:e])), ["cbh"] + regs("gi", a, e), regs("p5.c", a, e))
+            S(act(T.tg[:, 1, a:e], T.p5[:, 320 + a:320 + e], AF.Sign, bias=th[0]), regs("p5.c", a, e) + thn, regs("goal", a, e))
 
-        def zexp(c):
-            pb = "p%d" % (c % 2)
-            P(mm(T[pb][:], T.zt[0:96, 128 * (c // 3):128 * (c // 3) + 128], T.ce[0:96, 512 * (c % 3):512 * (c % 3) + 512]), ["zt", "ce"], [pb])
-
-        def cmp(c):
-            pb = "p%d" % (c % 2)
-            V(tt(T.ind[:, 512 * c:512 * c + 512], T.ss[:, 1024 * c + 1:1024 * c + 1024:2], T[pb][:], A.is_le), regs("ss", c, c + 1) + [pb], regs("ind", c, c + 1))
-
-        def cnt(a, b):
-            def fn(Q):
-                out = T.p3[:, 32 * a:32 * b]
-                Q.matmul(out, T.cg4[:], T.tg[:, 192 + 32 * a:192 + 32 * b], True, False)
-                for k in range(16):
-                    ins = Q.matmul(out, T.sel[:, 128 * k:128 * k + 128], T.ind[:, 512 * a + k:512 * b:16], False, k == 15)
-                return ins
-            P(fn, ["sel", "cg4", "tgg"] + regs("ind", a, b), ["p3"])
-
-        def use(a, b):
-            def fn(Q):
-                out = T.p4[:, 32 * a:32 * b]
-                Q.matmul(out, T.sel[:, 0:128], T.gg[:, 32 * a:32 * b], True, False)
-                Q.matmul(out, T.seln[:, 0:128], T.r15[:, 32 * a:32 * b], False, False)
-                for k in range(1, 16):
-                    Q.matmul(out, T.sel[:, 128 * k:128 * k + 128], T.ss[:, 1024 * a + 2 * k - 1:1024 * b:32], False, False)
-                    ins = Q.matmul(out, T.seln[:, 128 * k:128 * k + 128], T.ss[:, 1024 * a + 2 * k:1024 * b:32], False, k == 15)
-                return ins
-            P(fn, ["sel", "seln", "gg"] + regs("r15", a, b) + regs("ss", a, b), ["p4"])
-
-        def dups(a, b):
-            for c in range(a, b):
-                V(ts(T.eb[:, c, 0:192 - 16 * c], T.tg[:, 16 * c:192], T.kl[:, c:c + 1], None, A.is_equal), ["tgt", "kl"], ["eb%d" % c])
-
-        def send(name, src, dst, k, names=None):
-            op("g", lambda Q: Q.remote_dma(T[dst][:], T[src][:], T.sem[name], T.sem.snd, pid, rid, mask_out), names or [src], [], ("snd", n_eng * (k + 1), False))
-
-        S(act(T.gg[:], T.glw[:].indirect(T[ml][:]), AF.Copy), ["glw", ml], ["gg"])
-        S(act(T.mb[:], T.imw[:].indirect(T[ml][:]), AF.Copy), ["imwa", "imwb", ml], ["mb"])
-        V(cp(T.ol[:], T.tb[:, 0:512].indirect(T[ml][:])), ["tb", ml], ["ol"])
-        if t == 0:
-            consts()
-        V(cp(mlf, T[ml][:]), [ml], ["mlf"] + ["esm"] * (t == 0))
-        na(0, 2)
-        pg("v", 0, 2)
-        P(mm(T.p5[0:96, 0:128], T[z][:, 0:96], T.cid[:]), [z, "cid"], ["p5"])
-        P(mm(T.p5[0:96, 128:256], T[z][:, 96:192], T.cid[:]), [z, "cid"], ["p5"])
-        P(mm(T.p6[:, 0:192], T.cid[:], T[z][:], True, False), [z, "cid"], ["p6"])
-        P(mm(T.p6[:, 0:192], T.cidn[:], T.gg[:], False, True), ["cidn", "gg"], ["p6"])
-        S(act(T.zt[0:96, :], T.p5[0:96, 0:256], AF.Copy), ["p5"], ["zt"])
-        S(act(T.gi[:], T.p6[:, 0:192], AF.Sign, bias=0.5), ["p6"], ["gi"])
-        na(2, 4)
-        S(act(T.of[:], T.tb[:, 0:512].indirect(T[ml][:]), AF.Copy), ["tb", ml], ["of"])
-        zexp(0)
-        zexp(1)
-        P(mm(T.p5[:, 256:448], T.cbh[:], T.gi[:]), ["cbh", "gi"], ["p5"])
-        P(mm(T.p6[:, 0:192], T.wb[:], T[z][:]), ["wb", z], ["p6"])
-        P(mm(T.p6[:, 192:384], T.wb8[:], T[z][:], True, False), ["wb8", z], ["p6"])
-        P(mm(T.p6[:, 192:384], T.c296[:], T.mb[:], False, True), ["c296", "mb"], ["p6"])
-        scan(0, 2)
-        V(ts(T.tg[:, 192:384], T.p5[:, 256:448], 8.0, T.thr[:, t:t + 1], A.add, A.is_ge), ["p5", th], ["tgg"])
-        V(cp(T.ui[:], T.p6[:, 0:384]), ["p6"], ["ui"])
-        V(ts(T.ua[:], T.ui[:], 4095, None, A.bitwise_and), ["ui"], ["ua"])
-        V(ts(T.tg[:, 0:192], T.ua[:, 192:384], 0.125, 1.0, A.mult, A.add), ["ua"], ["tgt"])
-        if t == 0:
-            distances()
-        cmp(0)
-        cmp(1)
-        listmm("p7", 0, 24, "sel", "tg", 384, (), ["tgg", "tgt"])
-        S(act(T.p2[:, 0:192], T.of[:], AF.Copy), ["of"], ["p2"])
-        S(act(T.p2[:, 192:384], T.of[:], AF.Identity, bias=T.k37[:]), ["of", "k37"], ["p2"])
-        pg("s", 2, 3)
-        S(act(T.tgs[:, 0:12], T.p7[:, 0:12], AF.Copy, scale=0.0625), ["p7"], ["tgsa"])
-        S(act(T.tgs[:, 12:24], T.p7[:, 12:24], AF.Copy, scale=0.0625, accum_out=T.acc[:]), ["p7"], ["tgsb", "acc"])
-        S(act(tol, T.p7[:, 0:12], AF.Copy, scale=0.0625, bias=-1.0), ["p7"], ["tol"] + ["est"] * (t == 0))
-        if t == 0:
-            send("er", "es", "er", 0, ["est", "esm"])
+        for i, (a, e) in enumerate(MODS):
+            when("mod", a)
+            c, l0, w = slice(a // 16, e // 16), 384 + a // 8, (e - a) // 16
+            x = [(T.wb[:], z[:, a:e]), (T.cq1[:], T.q1[:, a:e]), (T.c37[:], T.mb[:, a:e]), (T.cq3[:], T.q3[:, a:e])]
+            xn = [["wb"] + regs(zn, a, e), ["cq1"] + regs("q1", a, e), ["c37"] + regs("mb", a, e), ["cq3"] + regs("q3", a, e)]
+            P(mm(T.p6[:, a:e], *x[:1]), xn[0], regs("p6.x", a, e))
+            quotient(T.q1[:, a:e], T.p6[:, a:e], 2.0 ** -12, T.qb1[:], regs("p6.x", a, e) + ["qb1"], regs("q1", a, e))
+            P(mm(T.p7[:, a:e], *x[:3]), sum(xn[:3], []), regs("p7.x", a, e))
+            P(mm(T.p6[:, 192 + a:192 + e], *x[:2]), sum(xn[:2], []), regs("p6.u", a, e))
+            quotient(T.q3[:, a:e], T.p7[:, a:e], 2.0 ** -9, T.qb3[:], regs("p7.x", a, e) + ["qb3"], regs("q3", a, e))
+            P(mm(T.p7[:, 192 + a:192 + e], *x), sum(xn, []), regs("p7.m", a, e))
+            S(act(T.tg[:, 0, a:e], T.p7[:, 192 + a:192 + e], AF.Copy, bias=-256.0), regs("p7.m", a, e), regs("to", a, e))
+            P(mm(T.p6[:, l0:l0 + 2 * w], *[(T.sel[:, 128 * j:128 * j + 128], T.tg[:, :, a + j:e:16]) for j in range(16)]),
+              ["sel"] + regs("to", a, e) + regs("goal", a, e), regs("p6.l", a, e))
+            S(act(T.mal[:, c], T.p6[:, l0:l0 + w], AF.Copy, scale=0.0625), regs("p6.l", a, e), regs("mal", a, e))
+            S(act(T.ngl[:, c], T.p6[:, l0 + w:l0 + 2 * w], AF.Copy, scale=-32.0, bias=512.0, accum_out=T.acc[:, i:i + 1]), regs("p6.l", a, e),
+              regs("ngl", a, e) + ["acc%d" % i])
+            when("first", a)
+            V(tt(T.kl[:, c], T.mal[:, c], T.ngl[:, c], A.add), regs("mal", a, e) + regs("ngl", a, e), regs("kl", a, e))
+            for k in range(a // 16, e // 16):
+                V(ts(T.eb[:, k, 0:192 - 16 * k], T.tg[:, 0, 16 * k:192], T.kl[:, k:k + 1], None, A.is_equal, rate=0.5), regs("to", a, 192) + regs("kl", a, e), ["eb%d" % k])
         if not lastt:
-            P(mm(T.p7[:, 64:65], T.onf[:], T.acc[:]), ["onf", "acc"], ["p7"])
-        pg("s", 3, 4)
-        zexp(2)
-        zexp(3)
-        cnt(0, 2)
-        V(tt(T.f1[:], T.ua[:, 0:192], T.p2[:, 0:192], A.mult), ["p2", "ua"], ["f1"])
-        V(ts(T.f2[:], T.f1[:], 5, None, A.arith_shift_right), ["f1"], ["f2"])
-        V(tt(T.kl[:], T.tgs[:, 0:12], T.tgs[:, 12:24], A.mult), ["tgsa", "tgsb"], ["kl"])
-        dups(0, 8)
-        relu15(0, 2)
-        use(0, 2)
-        na(4, 6)
-        pg("s", 4, 5)
-        pg("s", 5, 6)
-        scan(2, 4)
-        cmp(2)
-        cmp(3)
-        zexp(4)
-        zexp(5)
-        P(mm(T.p6[:, 0:192], T.cid[:], T.tg[:, 0:192], True, False), ["cid", "tgt"], ["p6"])
-        P(mm(T.p6[:, 0:192], T.cid[:], T.ns[:], False, True), ["cid", "ns"], ["p6"])
-        cnt(2, 4)
-        relu15(2, 4)
-        use(2, 4)
-        if not lastt:
-            V(cp(T.ai[:], T.p7[:, 64:65]), ["p7"], ["ai"])
+            when("count")
+            sums = mm(T.p6[:, 408:409], *[(T.onf[:], T.acc[:, i:i + 1]) for i in range(len(MODS))])
+            P((sums[0], 4 * sums[1]), ["onf"] + ["acc%d" % i for i in range(len(MODS))], ["p6.a"])
+            V(ts(T.ai[:], T.p6[:, 408:409], 2.0 ** -10, None, A.mult), ["p6.a"], ["ai"])
             V(ts(T.ai2[:], T.ai[:], 1, None, A.bitwise_and), ["ai"], ["ai2"])
-            V(ts(T.thr[:, t + 1:t + 2], T.ai2[:], 11.0, None, A.add), ["ai2"], ["thr%d" % (t + 1)])
-        scan(4, 5)
-        cmp(4)
-        scan(5, 6)
-        cmp(5)
-        relu15(4, 6)
-        cnt(4, 6)
-        S(act(T.d0[:, 0::32], T.na15[:], AF.Copy), regs("na15", 0, 6), regs("d0", 0, 6))
-        dups(8, 12)
-        V(ts(T.indk[:], T.p3[:, 0:192], T.thr[:, t:t + 1], 1024.0, A.is_ge, A.mult), ["p3", th], ["indk"])
-        listmm("p7", 96, 12, "sel", "indk", 192)
-        P(mm(T.p6[:, 192:384], T.ctm[:], T.indk[:]), ["ctm", "indk"], ["p6"])
-        V(tt(T.eb[:, :, 0:16], T.eb[:, :, 0:16], T.mk[:], A.mult), ["mk"] + ["eb%d" % c for c in range(12)], ["eb"])
+            V(cp(T.aif[:], T.ai2[:]), ["ai2"], ["aif"])
+            V(ts(T.thr[:, 3 * t + 3:3 * t + 6], T.th0[:], T.aif[:], None, A.subtract), ["aif", "th00", "th01", "th02"], ["thr%d" % (t + 1)])
 
-        def lost(Q):
-            Q.matmul(T.p5[:, 0:192], T.cnb[:], T.tg[:, 192:384], True, False)
-            for c in range(12):
-                ins = Q.matmul(T.p5[:, 16 * c:192], T.cb[:], T.eb[:, c, 0:192 - 16 * c], False, c == 11)
-            return ins
-        P(lost, ["cnb", "cb", "tgg", "eb"] + ["eb%d" % c for c in range(12)], ["p5"])
-        if t:
-            V(tt(T.ya[:], tol, T.p7[:, 96:108], A.subtract), ["tol", "p7"], ["ya"])
-            V(tt(T.yb[:], T.p7[:, 96:108], mlf, A.min), ["p7", "mlf"], ["yb"])
-            V(tt(T.mn[:], T.ya[:], T.yb[:], A.max), ["ya", "yb"], ["mn"])
-        if t == 0:
-            V(cp(T.xs[:], T.p7[:, 96:108]), ["p7"], ["xs"])
-            send("mr1", "xs", "xr", 1)
-        elif not lastt:
-            V(cp(T["ms%d" % (t + 1)][:], T.mn[:]), ["mn"], ["ms%d" % (t + 1)])
-            send("mr%d" % (t + 1), "ms%d" % (t + 1), "ml%d" % (t + 1), 2 * t + 1)
-        else:
-            op("y", lambda Q: Q.dma_start(T.ym[:], T.mn[:]), ["mn"], ["ym"], ("outm", 16, True))
-        S(act(T.oh[:], T.p6[:, 192:384], AF.Relu, scale=-0.0009765625), ["p6"], ["oh"])
-        listmm("p6", 384, 12, "selk", "oh", 192, ("b32", "one12"))
-        dd = T.dd[:, 128 * t:128 * t + 128]
-        P(mm(T.p0[:, 0:192], dd, T.oh[:]), ["dda", "ddb", "oh"], ["p0"])
-        P(mm(T.p0[:, 192:384], dd, T.oh[:], True, False), ["dda", "ddb", "oh"], ["p0"])
-        P(mm(T.p0[:, 192:384], T.cb[:], T.c255[:], False, True), ["cb", "c255"], ["p0"])
-        use(4, 6)
-        S(act(T.wn[:], T.p5[:, 0:192], AF.Relu, bias=-255.0, scale=-1.0), ["p5"], ["wn"])
-        V(tt(T.f3[:], T.f2[:], T.p2[:, 192:384], A.add), ["f2", "p2"], ["f3"])
-        V(ts(T.f4[:], T.f3[:], 4095, None, A.bitwise_and), ["f3"], ["f4"])
-        V(tt(T.fd[:], T.f4[:], T.p2[:, 0:192], A.subtract), ["f4", "p2"], ["fd"])
-        V(tt(T.si[:], T.wn[:], T.p6[:, 0:192], A.mult), ["wn", "p6"], ["si"])
-        listmm("p5", 448, 12, "sel", "si", 192, ("b512",))
-        V(cp(T.la[:], T.p6[:, 384:396]), ["p6"], ["la"])
-        V(tt(T.zdb[:], T[z][:], T.p0[:, 0:192], A.subtract), [z, "p0"], ["zdb"])
-        V(tt(T.yy[:], T.d0[:].indirect(T.la[:]), T.zdb[:], A.subtract), ["la", "zdb", "d0z"] + regs("d0", 0, 6), ["yy"])
-        V(tt(T.xx[:], T.yy[:], T.p0[:, 192:384], A.max), ["yy", "p0"], ["xx"])
-        if not lastt:
-            S(act(T["zs%d" % (t + 1)][:], T.xx[:], AF.Abs), ["xx"], ["zs%d" % (t + 1)])
-            send("zr%d" % (t + 1), "zs%d" % (t + 1), "zb%d" % (t + 1), 2 * t + 2)
-        else:
-            S(act(T.yzs[:], T.xx[:], AF.Abs), ["xx"], ["yzs"])
-            op("s", lambda Q: Q.dma_start(T.yz[:], T.yzs[:]), ["yzs"], ["yz"], ("outz", 16, True))
-        V(ts(T.p4[:, 192:384], T.p4[:, 0:192], 254.0, None, A.is_lt), ["p4"], ["p4", "ls"])
-        V(tt(T.fw[:], T.fd[:], T.p4[:, 192:384], A.mult), ["ls", "fd", "p4"], ["fw"])
-        V(ts(T.sl[:], T.p5[:, 448:460], 0.0625, None, A.mult), ["p5"], ["sl"])
-        V(tt(T.tb[:].indirect(T.sl[:]), T.fw[:], T.of[:], A.add), ["fw", "of", "sl"], ["tb"])
+        when("lost")
+        P(mm(T.p7[:, 0:192], (T.cbn4[:], T.tg[:, 1, :]), (T.cb[:], T.lim[:]), (T.cbw[:], T.eb[:, :, 0:16]),
+             *[(T.cb4[:], T.eb[:, c, 16:192 - 16 * c], T.p7[:, 16 * c + 16:192]) for c in range(11)]),
+          ["cbn4", "cb", "cbw", "cb4", "lim"] + every("goal") + ["eb%d" % c for c in range(12)], every("p7.x"))
+        S(act(T.wn[:], T.p7[:, 0:192], AF.Relu, scale=2.0 ** 26, bias=2.0 ** 28 + 1024.0), every("p7.x"), ["wn"])
+        P(listmm(T.p6[:, 416:428], "sel", "wn", 0, 192, [(T.cid[:], T.mal[:])]), ["sel", "cid", "wn"] + every("mal"), ["p6.s"])
+        V(tt(T.ys[:], T.b256[:], T.p6[:, 416:428], A.min), ["b256", "p6.s"], ["ys"])
+        V(ts(T.sl[:], T.ys[:], 256.0, None, A.add), ["ys"], ["sl"])
+
+        for a, e in NEWS:
+            when("new", a)
+            if Q_OF == "s":
+                S(gather(act(T.of[:, a:e], T.tb[:, 0:512].indirect(T.ml[:, a // 16:e // 16]), AF.Copy), e - a), ["tb"] + regs("ml", a, e), regs("of", a, e))
+            else:
+                move(Q_OF, T.of[:, a:e], T.ol[:, a:e], regs("ol", a, e), regs("of", a, e))
+            S(act(T.p2[:, a:e], T.of[:, a:e], AF.Copy), regs("of", a, e), regs("p2.o", a, e))
+            S(act(T.p2[:, 192 + a:192 + e], T.of[:, a:e], AF.Identity, bias=T.k37[:]), regs("of", a, e) + ["k37"], regs("p2.k", a, e))
+            V(tt(T.f1[:, a:e], T.of[:, a:e], T.p6[:, 192 + a:192 + e], A.mult), regs("of", a, e) + regs("p6.u", a, e), regs("f1", a, e))
+            V(ts(T.f2[:, a:e], T.f1[:, a:e], 5, None, A.arith_shift_right), regs("f1", a, e), regs("f2", a, e))
+            V(tt(T.f3[:, a:e], T.f2[:, a:e], T.p2[:, 192 + a:192 + e], A.add), regs("f2", a, e) + regs("p2.k", a, e), regs("f3", a, e))
+            V(ts(T.f4[:, a:e], T.f3[:, a:e], 4095, None, A.bitwise_and), regs("f3", a, e), regs("f4", a, e))
+            V(tt(T.fd[:, a:e], T.f4[:, a:e], T.p2[:, a:e], A.subtract), regs("f4", a, e) + regs("p2.o", a, e), regs("fd", a, e))
+
+        for a, e in USES:
+            n = e - a
+            c = slice(a // 16, e // 16)
+            when("use", a)
+            ends = [(T.ss[:, 32 * a + 2 * k + 2:32 * e:32] if k < 15 else T.gg[:, a:e], T.ss[:, 32 * a + 2 * k + 1:32 * e:32]) for k in range(16)]
+            mask = T.p4[:, 192 + a:192 + e]
+            if n > 64:
+                def turned(Q, ends=ends, n=n):
+                    for k, (hi, lo) in enumerate(ends):
+                        Q.matmul(T.p4[0:n, k:128:16], hi, T.sel[:, 0:128:16], True, False)
+                        ins = Q.matmul(T.p4[0:n, k:128:16], lo, T.seln[:, 0:128:16], False, True)
+                    return ins
+                P((turned, 32 * 64 * PE_CYCLE), ["sel", "seln"] + regs("gg", a, e) + regs("ss", a, e), ["p4.t"])
+                S(act(T.st[0:n, :], T.p4[0:n, 0:128], AF.Sign, scale=-1.0, bias=253.5), ["p4.t"], ["st"])
+                P(mm(mask, (T.st[0:n, :], T.cidh[0:n, 0:n]), (T.onb[0:n, :], T.cidh[0:n, 0:n])), ["st", "cidh", "onb"], regs("p4.m", a, e))
+            else:
+                P(mm(T.p4[:, 128:128 + n], *[(T[m][:, 128 * k:128 * k + 128], x[i]) for k, x in enumerate(ends) for i, m in enumerate(("sel", "seln"))]),
+                  ["sel", "seln"] + regs("gg", a, e) + regs("ss", a, e), ["p4.u"])
+                V(ts(mask, T.p4[:, 128:128 + n], 254.0, None, A.is_lt), ["p4.u"], regs("p4.m", a, e))
+            when("write", a)
+            V(tt(T.fw[:, a:e], T.fd[:, a:e], mask, A.mult), regs("fd", a, e) + regs("p4.m", a, e), regs("fw", a, e))
+            V(gather(tt(T.tb[:].indirect(T.sl[:, c]), T.fw[:, a:e], T.of[:, a:e], A.add), n, SCATTER), ["sl"] + regs("of", a, e) + regs("fw", a, e), ["tb"])
+
+        for b, (a, e) in enumerate(BLOCKS):
+            n = e - a
+            c = slice(a // 16, e // 16)
+            d0 = T["d0%d" % b]
+            when("met", a)
+            zt = T.zt[0:n, 128 * b:128 * b + 128]
+            P(mm(T.p5[0:n, 0:128], (z[:, a:e], T.cid[:])), ["cid"] + regs(zn, a, e), ["p5.t"])
+            S(act(zt, T.p5[0:n, 0:128], AF.Copy), ["p5.t"], ["zt%d" % b])
+            when("cmp", a)
+            for s in range(a, e, 32):
+                pb = "p%d" % (s // 32 % 2)
+                spread, kk = (zt, T.ce[0:n, 16 * (s - a):16 * (s - a) + 512]), T.ss[:, 32 * s:32 * s + 1024:2]
+                if Q_MET[b] == "v":
+                    P(mm(T[pb][:], spread), ["zt%d" % b, "ce"], [pb])
+                    V(tt(T.ind[:, 16 * s:16 * s + 512], kk, T[pb][:], A.is_le), regs("ss", s, s + 32) + [pb], regs("ind", s, s + 32))
+                else:
+                    P(mm(T[pb][:], spread, (T.cidn[:], kk)), ["zt%d" % b, "ce", "cidn"] + regs("ss", s, s + 32), [pb])
+                    S(act(T.ind[:, 16 * s:16 * s + 512], T[pb][:], AF.Sign, bias=0.5), [pb], regs("ind", s, s + 32))
+            when("pass", a)
+            off = "cb2" if Q_MET[b] == "v" else "cbn"
+            P(mm(T.p3[:, a:e], (T[off][:], T.tg[:, 1, a:e]), *[(T.sel[:, 128 * k:128 * k + 128], T.ind[:, 16 * a + k:16 * e:16]) for k in range(16)]),
+              ["sel", off] + regs("goal", a, e) + regs("ind", a, e), regs("p3.c", a, e))
+            if Q_MET[b] == "v":
+                S(act(T.sg[:, a:e], T.p3[:, a:e], AF.Sign, bias=th[1]), regs("p3.c", a, e) + thn, regs("sg", a, e))
+            else:
+                S(act(T.sg[:, a:e], T.p3[:, a:e], AF.Sign, scale=0.5, bias=th[2]), regs("p3.c", a, e) + thn, regs("sg", a, e))
+            P(mm(T.p3[:, 192:192 + n], (T.ctm[:], T.sg[:, a:e])), ["ctm"] + regs("sg", a, e), ["p3.y"])
+            P(mm(T.p3[:, 192 + n:192 + 2 * n], (T.ctm[:], T.sg[:, a:e])), ["ctm"] + regs("sg", a, e), ["p3.w"])
+            S(act(T.oh[:, 2 * a:2 * e], T.p3[:, 192:192 + 2 * n], AF.Relu, scale=1024.0, bias=T.ohb[:]), ["p3.y", "p3.w", "ohb"], regs("oh", a, e))
+            l0, w = 384 + a // 8, n // 16
+            P(listmm(T.p7[:, l0:l0 + 2 * w], "selk", "oh", 2 * a, 2 * e, [(T.cid[:], T.bas[:, a // 8:e // 8]), (T.cidn[:], T.mal[:, c], T.p7[:, l0:l0 + w])]),
+              ["selk", "cid", "cidn", "basa%d" % b, "basb%d" % b] + regs("mal", a, e) + regs("oh", a, e), regs("p7.l", a, e))
+            V(tt(T.tm[:, c], mf[:, c], T.p7[:, l0:l0 + w], A.min), regs(mfn, a, e) + regs("p7.l", a, e), regs("tm", a, e))
+            S(act(T["ms%d" % t][:, c], T.tm[:, c], AF.Abs), regs("tm", a, e), regs("ms%d" % t, a, e))
+            if not lastt:
+                send("mr%d_%d" % (t + 1, b), T["ms%d" % t][:, c], T["mf%d" % (t + 1)][:, c], regs("ms%d" % t, a, e), regs("m%d" % (t + 1), a, e))
+            when("move", a)
+            V(ts(T.la[:, c], T.p7[:, l0 + w:l0 + 2 * w], 2.0 ** -10, None, A.mult), regs("p7.l", a, e), regs("la", a, e))
+            V(gather(tt(T.yy[:, a:e], d0[:].indirect(T.la[:, c]), z[:, a:e], A.subtract), n),
+              ["d0z%d" % b] + regs("la", a, e) + regs(zn, a, e) + regs("d0", a, e) + regs("cut", a, e) + regs("a15", a, e), regs("yy", a, e))
+            if Q_CLIP == "v":
+                V(ts(T.xx[:, a:e], T.yy[:, a:e], -255.0, None, A.max, rate=0.5), regs("yy", a, e), regs("xx", a, e))
+            else:
+                S(act(T.xx[:, a:e], T.yy[:, a:e], AF.Relu, bias=255.0), regs("yy", a, e), regs("xx", a, e))
+            P(mm(T.p2[:, 384:384 + n], (T.dd[:, 128 * t:128 * t + 128], T.oh[:, 2 * a:2 * a + n]), (T.cid[:], T.xx[:, a:e])),
+              ["dd%d" % t, "cid"] + regs("oh", a, e) + regs("xx", a, e), ["p2.z"])
+            zs = T.yzs if lastt else T["zs%d" % t]
+            S(act(zs[:, a:e], T.p2[:, 384:384 + n], AF.Abs, bias=0.0 if Q_CLIP == "v" else -255.0), ["p2.z"], regs("zs%d" % t, a, e))
+            if not lastt:
+                send("zr%d_%d" % (t + 1, b), zs[:, a:e], T["zb%d" % (t + 1)][:, a:e], regs("zs%d" % t, a, e), regs("z%d" % (t + 1), a, e))
 
     for t in range(STEPS):
         step(t)
-
-    P(mm(T.p1[:, 0:256], T.cj[:], T.tb[:, 0:256]), ["cj", "tb"], ["p1"])
-    P(mm(T.p2[:, 0:256], T.cj[:], T.tb[:, 256:512]), ["cj", "tb"], ["p2"])
-    V(cp(T.yms[:, 0:256], T.p1[:, 0:256]), ["p1"], ["yma"])
-    S(act(T.yms[:, 256:512], T.p2[:, 0:256], AF.Copy), ["p2"], ["ymb"])
-    op("y", lambda Q: Q.dma_start(T.ymc[:, 0:256], T.yms[:, 0:256]), ["yma"], ["oa"], ("outa", 16, True))
-    op("s", lambda Q: Q.dma_start(T.ymc[:, 256:512], T.yms[:, 256:512]), ["ymb"], ["ob"], ("outb", 16, True))
+    t = STEPS - 1
+    now[:] = [1000.0, -1, None, 0]
+    dma("y", T.ym[:], T["ms%d" % t][:], regs("ms%d" % t, 0, 192), ["ym"], "outm", 1600)
+    dma("s", T.yz[:], T.yzs[:], regs("zs%d" % t, 0, 192), ["yz"], "outz", 2000)
+    behind.clear()
+    dma("y", T.ymc[:], T.tb[:, 0:512], ["tb"], ["ymc"], "outa", 2600)
     emit()
-    for s in ("outm", "outz", "outa", "outb"):
+    for s in ("outm", "outz", "outa"):
         g.wait_ge(T.sem[s], 16)
-    g.wait_ge(T.sem.snd, n_eng * (2 * (STEPS - 1) + 1))
+    g.wait_ge(T.sem.snd, n_eng * sends[0])

@@ -10,50 +10,51 @@ I32 = "int32"
 U16 = "uint16"
 BLOCKS = [(128, 192), (64, 128), (0, 64)]
 MODS = [(64, 192), (0, 64)]
-NEWS = [(0, 192)]
+GOALS = MODS
+TURNS = MODS
 USES = [(64, 192), (0, 64)]
-NEEDS = [[(128, 192, "v"), (64, 128, "v"), (0, 64, "s")], [(128, 192, "v"), (64, 128, "s"), (0, 64, "s")]]
-ADDS = [[(128, 192, "s"), (64, 128, "v"), (0, 64, "s")], [(128, 192, "s"), (64, 128, "s"), (0, 64, "s")]]
-Q_MET = "vvv"
-Q_CLIP, Q_ML, Q_OF, Q_SAVE, Q_MOD, Q_R15 = "v", "v", "g", "g", "s", "v"
-SAVE = 32 * max(b - a for a, b in BLOCKS)
+NEEDS = ["v s vs", "v vs s"]
+ADDS = ["s v vs", "s s s"]
+ON_V = "".split()
+Q_ML, Q_SAVE, Q_CUT, Q_MAL = "ggvg"
+ROWS = [0, 256, 448, 576]
+SAVE = 32 * 64
+MAGIC = 1.5 * 2.0 ** 24
 BANKS = ["p%d" % b for b in range(8)]
 SCRATCH = {}
 for _names, _cols, _type in (
         ("prw adw", 4096, B16), ("glw imw", 512, B16), ("mci", 512, I32), ("tb", 704, F32),
-        ("mi", 12, I32), ("dvs", 5, B16), ("wts", 1, B16),
-        ("d1 ss", 6144, B16), ("ind", 3072, B16), ("ol", 192, U16), ("gg mb gi sg xx wn", 192, B16), ("oh", 384, B16),
-        ("zt", 128 * len(BLOCKS), B16), ("st", 128, B16), ("q1 q3 yy", 192, F16), ("mal ngl", 12, B16), ("kl tm ys", 12, F32),
-        ("acc", 4, F32), ("ai ai2", 1, I32), ("aif", 1, F32), ("thr", 16, F32), ("ml sl la", 12, U16),
-        ("yzs of fd fw", 192, F32), ("f1 f2 f3 f4", 192, I32),
-        ("pi kki gri odi", 1, I32), ("pf kkf grf k37 kw kwa ohb odf qb1 qb3 pw", 1, F32), ("pwi", 16, F32), ("th0", 3, F32),
-        ("iw", 192, F32), ("ig onf", 128, F32), ("ie ce", SAVE // 2, B16),
-        ("cid cidn cidh c37 cb cbh cb2 cb4 cbn cbn4 cbw cq1 cq3 tma ctm wb onb", 128, B16), ("isl sel selk seln", 2048, B16),
-        ("dg dd", 640, B16), ("ic bl b256", 12, F32), ("bas", 24, B16), ("lim", 192, B16)):
+        ("mi", 12, I32), ("dvs", 5, B16), ("wts", 1, B16), ("zb0", 192, B16), ("ze", 64, B16), ("zw", 68, F16),
+        ("d00 d01 d02", 2 * SAVE, B16), ("d1 ss", 6144, B16), ("ind", 3072, B16), ("ol", 192, U16), ("gg mb gi sg hh yy", 192, B16),
+        ("oh", ROWS[3], B16), ("zt", 128 * len(TURNS), B16), ("st", 128, B16), ("q1 q3", 192, F16), ("mal", 12, F16),
+        ("tm ys mf0", 12, F32), ("lst", 24, F32), ("acc sm", 2, F32), ("ev sum", 1, F32), ("thr", 8, F32), ("ml sl la", 12, U16),
+        ("of fd fw", 192, F32), ("f1 f2 f3 f4", 192, I32),
+        ("pi", 4, I32), ("pf", 4, F32), ("k37 kw kwa ohb qb1 qb3 pw", 1, F32), ("pwi iw", 16, F32), ("onf", 128, F32),
+        ("ie ce", 1024, B16), ("cbm", 8, B16), ("ig cid cidn cidm c37 cb cb2 cb6 cb43 cbn cbw cq1 cq3 tri wb onb lim ha hb", 128, B16),
+        ("isl sel seln", 2048, B16), ("dg dd", 640, B16), ("ic bl top", 12, F32), ("bas", ROWS[3] // 16, B16)):
     for _n in _names.split():
         SCRATCH[_n] = ("sbuf", [128, _cols], _type)
-for _b, (_a, _e) in enumerate(BLOCKS):
-    SCRATCH["d0%d" % _b] = ("sbuf", [128, SAVE + 32 * (_e - _a)], B16)
-SCRATCH["tg"] = ("sbuf", [128, 2, 192], B16)
-SCRATCH["eb"] = ("sbuf", [128, 12, 192], B16)
-for _t in range(STEPS):
-    SCRATCH["zb%d" % _t] = ("sbuf", [128, 192], B16)
-    SCRATCH["mf%d" % _t] = ("sbuf", [128, 12], F32)
-    SCRATCH["ms%d" % _t] = ("sbuf", [128, 12], F32)
-    if _t < STEPS - 1:
-        SCRATCH["zs%d" % _t] = ("sbuf", [128, 192], B16)
-for _b in BANKS:
+SCRATCH["tg"] = ("sbuf", [128, 2, 192], F16)
+SCRATCH["yo"] = ("sbuf", [128, 3, 68], F32)
+SCRATCH["eb"] = ("sbuf", [128, 12, 128], B16)
+for _t in range(1, STEPS):
+    SCRATCH["zb%d" % _t] = ("sbuf", [128, 3, 72], F16)
+    SCRATCH["zs%d" % _t] = ("sbuf", [128, 3, 72], F16)
+SCRATCH["p0"] = ("psum", [128, 1024], F32)
+for _b in BANKS[2:]:
     SCRATCH[_b] = ("psum", [128, 512], F32)
 LOADS = ["mc", "m0", "z0", "ad", "gl", "pr", "wt", "dv"]
 SEMAPHORES = ["cv", "cs", "ct", "cg", "outz", "outm", "outa", "snd"] + ["ld_" + n for n in LOADS]
-SEMAPHORES += ["%s%d_%d" % (x, t, b) for x in ("mr", "zr") for t in range(1, STEPS) for b in range(len(BLOCKS))]
+SEMAPHORES += ["ze"] + ["zr%d_%d" % (t, b) for t in range(1, STEPS) for b in range(len(BLOCKS))]
 
-CYCLE, PE_CYCLE, CALL, WAKE, LOOK = 0.83, 0.42, 20.0, 70.0, 0.0
-GATHER, SCATTER, SEND, FLIGHT = 1.56, 3.8, 600.0, {"m": 1700.0, "z": 2250.0}
-FIRST = 3600.0
+CYCLE, PE_CYCLE, CALL, WAKE, LOOK = 0.83, 0.42, 20.0, 66.0, 0.19
+GATHER, SCATTER, SEND, FLIGHT = 1.56, 3.8, 570.0, 2300.0
+FIRST, PCALL, SCALL, GCALL = 3400.0, 0.0, 0.0, 40.0
 ORDER, DAG = [], []
-PERIOD = 16.3
-DUE = {'lists': (-17.7, 5.5, -44.5), 'ops': (5.3, 9.7, 22.1), 'adds': (-5.9, 10.0, 13.9), 'needs': (39.4, 13.2, 41.6), 'scan': (-0.9, -24.3, -0.3), 'goal': (-56.1, -25.9, 28.4), 'mod': (-7.0, 9.7, 7.7), 'first': (-4.6, -15.3, -14.4), 'count': (16.2,), 'lost': (38.5,), 'new': (-25.1, -31.6, 34.1), 'use': (1.5, 3.5, -18.0), 'write': (24.7, 29.1, 13.2), 'met': (-3.4, 6.4, 18.0), 'cmp': (-33.5, -13.1, 13.6), 'pass': (-26.6, 0.6, -21.5), 'move': (11.3, 1.8, 10.5)}
+PERIOD = 17.1
+DUE = {'place': (-15.5, -3.2, -18.1), 'lists': (-30.3, -32.7, -14.9), 'ops': (-11.3, -19.0, -16.2), 'adds': (-0.8, -2.9, 8.6, -3.1, -0.4, 3.5), 'needs': (-3.4, 1.9, 9.2, 3.6, -3.4, 6.4), 'scan': (-19.3, -6.9, -20.0), 'goal': (-34.6, -17.3, -24.9), 'mod': (-6.0, -22.8, -19.5), 'first': (1.8, 2.0, -4.2), 'count': (26.5,), 'room': (-18.5, -23.6, -25.4), 'lost': (-28.5, -17.8, -17.3), 'new': (8.7,), 'use': (11.3, -5.7, -35.7), 'write': (0.7, 21.2, -32.3), 'met': (-23.1, -11.5, -31.7), 'cmp': (-17.8, -13.7, -21.6), 'pass': (-26.6, -28.3, -19.9), 'move': (-26.2, -33.4, -37.6), 'spread': (-18.6, -19.5, -22.8), 'dist': (38.2,), 'row': (-28.1, -18.8, -25.0), 'place0': (-29.0, -22.2, -9.6), 'lists0': (-53.2, -63.3, -63.9), 'ops0': (-63.9, -47.0, -78.9), 'adds0': (-47.1, -44.7, -35.6, -48.4, -59.5, -45.5), 'needs0': (-45.3, -47.2, -31.7, -47.5, -42.9, -26.9), 'scan0': (-62.7, -34.5, -20.1), 'goal0': (-36.2, -44.2, -30.5), 'mod0': (-36.3, -27.5, -17.7), 'first0': (-37.2, -47.2, -22.8), 'count0': (11.4,), 'room0': (-15.8, -12.3, -3.3), 'lost0': (-34.0, -42.8, -22.4), 'new0': (-15.3,), 'use0': (-26.2, -20.6, -30.3), 'write0': (-6.6, -1.3, -18.5), 'met0': (-52.6, -39.9, -13.2), 'cmp0': (-46.7, -26.7, -10.6), 'pass0': (-41.8, -38.1, -16.8), 'move0': (-49.6, -42.5, -28.9), 'spread0': (-47.3, -31.3, -24.8), 'dist0': (-38.5,), 'row0': (-43.3, -39.3, -32.6), 'ahead0': (-20.4,), 'c1': (-68.9,), 'c2': (-67.4,), 'c3': (-41.5,), 'c4': (-36.8,), 'c5': (-37.5,), 'c6': (-10.4,), 'c7': (-55.7,), 'c8': (-58.8,), 'c9': (-35.9,), 'c10': (21.1,)}
+OLD2 = {'place': (-14.0, -11.6, -19.6), 'lists': (-30.3, -32.7, -15.7), 'ops': (-11.5, -19.9, -16.2), 'adds': (-0.8, -2.9, 8.6, -3.8, -0.4, 3.5), 'needs': (-1.4, 1.9, 9.2, 3.6, -3.4, 5.6), 'scan': (-19.3, -6.9, -19.0), 'goal': (-34.6, -17.3, -28.4), 'mod': (-15.1, -22.8, -18.8), 'first': (2.9, 2.4, -1.9), 'count': (24.9,), 'room': (-16.9, -23.4, -25.4), 'lost': (-23.5, -17.8, -17.3), 'new': (8.7,), 'use': (11.3, -5.7, -36.8), 'write': (-0.5, 18.0, -32.3), 'met': (-25.9, -14.4, -31.7), 'cmp': (-20.3, -13.7, -21.6), 'pass': (-27.4, -28.3, -20.2), 'move': (-26.2, -33.4, -36.4), 'spread': (-21.5, -19.5, -22.8), 'dist': (36.7,), 'row': (-28.1, -20.5, -25.0), 'place0': (-30.3, -20.6, -9.1), 'lists0': (-55.6, -65.3, -63.8), 'ops0': (-63.9, -47.0, -78.9), 'adds0': (-47.6, -44.7, -36.8, -44.7, -59.5, -44.9), 'needs0': (-43.2, -47.2, -30.6, -47.5, -42.9, -26.9), 'scan0': (-64.0, -34.5, -20.1), 'goal0': (-36.9, -44.2, -32.2), 'mod0': (-36.3, -27.5, -17.7), 'first0': (-32.2, -47.2, -21.4), 'count0': (14.3,), 'room0': (-18.1, -14.1, -3.3), 'lost0': (-32.8, -42.9, -18.9), 'new0': (-12.3,), 'use0': (-26.2, -20.6, -30.3), 'write0': (-6.6, -1.1, -18.2), 'met0': (-52.6, -41.7, -16.7), 'cmp0': (-46.7, -29.0, -8.3), 'pass0': (-42.8, -41.2, -19.7), 'move0': (-49.6, -41.8, -28.9), 'spread0': (-47.3, -24.7, -27.0), 'dist0': (-35.3,), 'row0': (-43.3, -39.3, -32.7), 'ahead0': (-19.0,), 'c1': (-68.5,), 'c2': (-69.5,), 'c3': (-40.8,), 'c4': (-36.8,), 'c5': (-37.5,), 'c6': (-13.1,), 'c7': (-55.7,), 'c8': (-56.0,), 'c9': (-36.1,), 'c10': (18.9,)}
+OLD1 = {'place': (-17.2, -14.9, -21.9), 'lists': (-23.2, -25.1, -18.8), 'ops': (-12.7, -23.6, -15.3), 'adds': (0, -3.2, 1.4, -1.3, 1.1, 4.2), 'needs': (-4.0, 0.3, 6.6, -0.3, 1.3, 5.1), 'scan': (-16.3, -11.5, -17.0), 'goal': (-27.0, -22.5, -20.4), 'mod': (-22.7, -20.6, -20), 'first': (-5.3, -10.5, -10.6), 'count': (20.4,), 'room': (-22.3, -20.6, -22.7), 'lost': (-22.9, -20, -11.2), 'new': (4.6,), 'use': (5.7, -2.1, -35.0), 'write': (3.9, 12.0, -30.1), 'met': (-23.4, -10.3, -19.8), 'cmp': (-12.7, -12.4, -14.0), 'pass': (-26.7, -26.9, -21.9), 'move': (-23.0, -28.4, -27.5), 'spread': (-19.6, -19.8, -19.7), 'dist': (21.7,), 'row': (-21.7, -20.2, -21.0), 'place0': (-27.5, -23.7, -14.6), 'lists0': (-60.3, -60.8, -67.5), 'ops0': (-63.8, -56.5, -73.7), 'adds0': (-47.8, -47.2, -45.1, -50.0, -53.2, -48.4), 'needs0': (-45.4, -50.9, -30.9, -42.4, -47.2, -35.2), 'scan0': (-49.7, -34.5, -27.7), 'goal0': (-40.7, -42.7, -29.3), 'mod0': (-35.3, -35.2, -20.6), 'first0': (-26.9, -39.6, -24.7), 'count0': (6.3,), 'room0': (-16.1, -11.8, -10.9), 'lost0': (-25.9, -40.9, -27.1), 'new0': (-15.6,), 'use0': (-18.7, -19.9, -31.1), 'write0': (-12.4, -9.7, -24.4), 'met0': (-44.4, -48.4, -24.9), 'cmp0': (-46.0, -29.8, -7.1), 'pass0': (-44.4, -35.7, -19.2), 'move0': (-45.1, -37.7, -30.0), 'spread0': (-47.1, -38.1, -27.3), 'dist0': (-31.4,), 'row0': (-38.3, -40.7, -34.5), 'ahead0': (-28.1,), 'c1': (-64.7,), 'c2': (-65.9,), 'c3': (-44.7,), 'c4': (-41.4,), 'c5': (-36.1,), 'c6': (-19.1,), 'c7': (-53.1,), 'c8': (-53.1,), 'c9': (-44.4,), 'c10': (15.6,)}
 
 
 def scheduler(g, T, now):
@@ -94,7 +95,31 @@ def scheduler(g, T, now):
         for i, n in enumerate(left):
             if n == 0:
                 ready.setdefault(calls[i]["q"], []).append(i)
-        free, bank, start, out = {}, {}, {}, []
+        free, bank, start, out, clock = {}, {}, {}, [], {}
+
+        def eta(u, depth):
+            t = can[u]
+            for p in pre[u]:
+                if p not in start:
+                    if depth == 0:
+                        return 1e18
+                    t = max(t, max(eta(p, depth - 1), free.get(calls[p]["q"], 0.0)) + calls[p]["ns"] + calls[p]["late"] + WAKE)
+            return t
+
+        def urgent(q, i):
+            found = [j for j in ready[q] if due[j] < due[i]]
+            seen, front = set(), [j for k, r in ready.items() if k != q for j in r]
+            for _ in range(3):
+                behind = []
+                for u in (u for j in front for u in users[j]):
+                    if u not in seen:
+                        seen.add(u)
+                        if calls[u]["q"] != q:
+                            behind.append(u)
+                        elif due[u] < due[i]:
+                            found.append(u)
+                front = behind
+            return found
 
         def first(i):
             o = calls[i]
@@ -105,11 +130,18 @@ def scheduler(g, T, now):
                         t = e + WAKE
             return t
         while len(out) < len(calls):
-            t, q = min((min(first(i) for i in r), str(q)) for q, r in ready.items() if r)
-            q = None if q == "None" else q
-            i = min((j for j in ready[q] if first(j) <= t + look), key=lambda j: (due[j], j))
+            t, q = min(((max(min(first(i) for i in r), clock.get(q, 0.0)), q) for q, r in ready.items() if r), key=lambda x: x[0])
+            i = min((j for j in ready[q] if first(j) <= t + 1), key=lambda j: (due[j], j))
+            if q and calls[i]["ns"] > 150:
+                soon = min([first(u) if left[u] == 0 else eta(u, 3) for u in urgent(q, i)] + [1e18])
+                if t < soon < t + look * calls[i]["ns"]:
+                    short = [j for j in ready[q] if first(j) <= t + 1 and t + calls[j]["ns"] <= soon + 30]
+                    if not short:
+                        clock[q] = min([soon] + [x for x in map(first, ready[q]) if x > t + 1])
+                        continue
+                    i = min(short, key=lambda j: (due[j], j))
             o = calls[i]
-            start[i] = first(i)
+            start[i] = max(first(i), t)
             end = start[i] + o["ns"]
             if q:
                 free[q] = end
@@ -205,16 +237,22 @@ def size(ap):
     return n
 
 
+def shares(plan):
+    out = []
+    for b, ((a, e), word) in enumerate(zip(BLOCKS, plan.split())):
+        out += [(b, a, e, word, 0)] if len(word) == 1 else [(b, a + 32, e, word[0], 0), (b, a, a + 32, word[1], 1)]
+    return out
+
+
 def rank_program(g, core, T, topo):
     rank = T.rank_of(core)
     if rank is None:
         return
-    now = [0.0, -1, None, 0]
+    now = [-1000.0, -1, None, 0]
     op, emit = scheduler(g, T, now)
-    n_ranks = len(T.cores)
-    nxt = T.cores[(rank + 1) % n_ranks]
-    n_eng = 8
-    mask_out = sum(1 << e for e in topo.engines(core, nxt)[:n_eng])
+    nxt = T.cores[(rank + 1) % len(T.cores)]
+    mask_out = topo.mask(core, nxt)
+    n_out, n_in = len(topo.engines(core, nxt)), len(topo.engines(T.cores[rank - 1], core))
     rid, pid = topo.addr(nxt)[:2]
 
     def V(fn, r=(), w=()):
@@ -242,321 +280,365 @@ def rank_program(g, core, T, topo):
         return (lambda Q: Q.tensor_copy(out, a)), ns(size(out), rate)
 
     def act(out, a, f, **k):
-        return (lambda Q: Q.activation(out, a, f, **k)), ns(size(out)) + 100.0 * ("accum_out" in k)
+        return (lambda Q: Q.activation(out, a, f, **k)), ns(size(out)) + SCALL + 20.0 * ("accum_out" in k)
 
-    def ms(out, c):
-        return (lambda Q: Q.memset(out, c)), ns(size(out), 0.5)
+    def either(name, out, a, f, scale, bias, v, r, w):
+        if name in ON_V or name + w[0][-2:] in ON_V:
+            V(ts(out, a, *v), r, w)
+        else:
+            S(act(out, a, f, scale=scale, bias=bias), r, w)
 
-    def gather(call, n, rate=GATHER):
-        return call[0], 60 + n * rate * CYCLE + CALL
+    def ms(out, c, rate=0.5):
+        return (lambda Q: Q.memset(out, c)), ns(size(out), rate)
+
+    def gather(call, n, rate=GATHER, q="v"):
+        return call[0], 50 + (15 + SCALL) * (q == "s") + n * rate * CYCLE + CALL
 
     def mm(out, *terms):
         def fn(Q):
             for i, x in enumerate(terms):
                 ins = Q.matmul(x[2] if len(x) > 2 else out, x[0], x[1], i == 0, i == len(terms) - 1)
             return ins
-        return fn, sum(max(min(64, size(x[0])), size(x[1])) for x in terms) * PE_CYCLE
+        return fn, sum(max(min(64, size(x[0])), size(x[1])) for x in terms) * PE_CYCLE + PCALL * len(terms)
 
     def iota(out, pattern, base=0, cm=0):
-        return (lambda Q: Q.iota(out, pattern, base, cm, allow_small_or_imprecise_dtypes=True)), 130 + 2 * size(out) * CYCLE
+        return (lambda Q: Q.iota(out, pattern, base, cm, allow_small_or_imprecise_dtypes=True)), 130 + GCALL + 2 * size(out) * CYCLE
 
-    def move(q, out, a, r, w):
-        if q == "g":
-            G(((lambda Q: Q.affine_select(out, a, [[0, size(out)]], A.is_ge, 0.0, 0, 0)), 170 + 2 * size(out) * CYCLE), r, w)
-        elif q == "v":
-            V(cp(out, a), r, w)
-        else:
-            S(act(out, a, AF.Copy), r, w)
+    def pick(out, a, pattern, o, cm):
+        return (lambda Q: Q.affine_select(out, a, pattern, o, 0.0, 0, cm)), 170 + GCALL + 2 * size(out) * CYCLE
+
+    def move(out, a):
+        return pick(out, a, [[0, size(out)]], A.is_ge, 0)
+
+    def copy(q, out, a, r, w):
+        op(q, move(out, a) if q == "g" else cp(out, a) if q == "v" else act(out, a, AF.Copy), r, w)
 
     behind = {}
 
     def dma(q, out, a, r, w, sem, late):
         behind[q] = op(q, ((lambda Q: Q.dma_start(out, a)), 100.0, late), r, w, (sem, 16, True), behind.get(q))
 
-    for q, name, buf, late in (("s", "m0", "mi", 1600), ("y", "mc", "mci", 3300), ("y", "ad", "adw", 7400), ("s", "gl", "glw", 2100), ("s", "z0", "zb0", 2300),
-                               ("s", "wt", "wts", 2300), ("s", "dv", "dvs", 2300), ("y", "pr", "prw", 11500)):
-        dma(q, T[buf][:], T[name][:], [], regs("z0", 0, 192) if name == "z0" else [buf], "ld_" + name, late)
+    for q, name, buf, late in (("s", "m0", "mi", 1050), ("y", "mc", "mci", 1800), ("y", "ad", "adw", 3600), ("s", "gl", "glw", 1350), ("s", "z0", "zb0", 1400),
+                               ("s", "wt", "wts", 1400), ("s", "dv", "dvs", 1400), ("y", "pr", "prw", 5400)):
+        dma(q, T[buf][:], T[name][:], [], every("z0") if name == "z0" else [buf], "ld_" + name, late)
 
-    now[0] = -100.0
-    G(((lambda Q: Q.iota(T.pi[:], [[0, 1]], 0, 1)), 140.0), [], ["pi"])
+    def const(what):
+        now[:] = [DUE[what][0], 0, what, 0]
+    kkf, grf, odf, hf = [T.pf[:, i:i + 1] for i in range(4)]
+    const("c1")
+    G(((lambda Q: Q.iota(T.pi[:], [[0, 4]], 0, 1)), 140.0), [], ["pi"])
     G(iota(T.ig[:], [[1, 8], [0, 16]]), [], ["ig"])
-    G(iota(T.iw[:], [[1, 192]]), [], ["iw"])
-    G(iota(T.ic[:], [[16, 12]]), [], ["ic"])
+    V(ms(T.onb[:], 1.0), [], ["onb"])
+    G(pick(T.cid[:], T.onb[:], [[-1, 128]], A.is_equal, 1), ["onb"], ["cid"])
+    for i, (c, o) in enumerate(((15, A.bitwise_and), (4, A.arith_shift_right), (1, A.bitwise_and), (63, A.bitwise_and))):
+        V(ts(T.pi[:, i:i + 1], T.pi[:, i:i + 1], c, None, o), ["pi"], ["pi%d" % i])
+    V(cp(T.pf[:], T.pi[:]), ["pi0", "pi1", "pi2", "pi3"], ["pf"])
+    V(ts(T.cb[:], T.ig[:], grf, None, A.is_equal, rate=0.5), ["ig", "pf"], ["cb"])
+    const("c7")
     G(iota(T.imw[:, 0:256], [[1, 256]]), [], ["imwa"])
     G(iota(T.imw[:, 256:512], [[1, 256]], -256), [], ["imwb"])
-    G(iota(T.isl[:], [[-100, 16], [1, 8], [100, 16]]), [], ["isl"])
-    G(iota(T.ie[:], [[1, SAVE // 32], [0, 16]]), [], ["ie"])
+    const("c8")
+    for i in range(4):
+        G(iota(T.isl[:, 512 * i:512 * i + 512], [[-100, 4], [1, 8], [100, 16]], -400 * i), [], ["isl%d" % i])
+    V(ts(T.sel[:], T.isl[:], grf, None, A.is_equal, rate=0.5), ["isl0", "isl1", "isl2", "isl3", "pf"], ["sel"])
+    const("c2")
     for b, (a, e) in enumerate(BLOCKS):
-        V(ms(T["d0%d" % b][:, 0:32 * (e - a):2], 0.0), [], ["d0z%d" % b])
-        S(act(T.d1[:, 32 * a + 1:32 * e:2], T["d0%d" % b][:, 0:32 * (e - a):2], AF.Copy), ["d0z%d" % b], regs("r15", a, e))
-    V(ts(T.kki[:], T.pi[:], 15, None, A.bitwise_and), ["pi"], ["kki"])
-    V(ts(T.gri[:], T.pi[:], 4, None, A.arith_shift_right), ["pi"], ["gri"])
-    V(ts(T.odi[:], T.pi[:], 1, None, A.bitwise_and), ["pi"], ["odi"])
-    for a, b in (("pf", "pi"), ("kkf", "kki"), ("grf", "gri"), ("odf", "odi")):
-        V(cp(T[a][:], T[b][:]), [b], [a])
-    V(ts(T.cb[:], T.ig[:], T.grf[:], None, A.is_equal), ["ig", "grf"], ["cb"])
-    V(ts(T.sel[:], T.isl[:], T.grf[:], None, A.is_equal, rate=0.5), ["isl", "grf"], ["sel"])
-    V(ts(T.kwa[:], T.kkf[:], 15.0, SAVE - 31.0, A.is_equal, A.mult), ["kkf"], ["kwa"])
-    V(ts(T.kw[:], T.kkf[:], 2.0, 1.0, A.mult, A.add), ["kkf"], ["kw"])
-    V(tt(T.kw[:], T.kw[:], T.kwa[:], A.add), ["kw", "kwa"], ["kw"])
-    S(act(T.seln[:], T.sel[:], AF.Copy, scale=-1.0), ["sel"], ["seln"])
-    S(act(T.selk[:], T.sel[:], AF.Copy, scale=T.kw[:]), ["sel", "kw"], ["selk"])
-    V(ts(T.k37[:], T.kkf[:], 37.0, None, A.mult), ["kkf"], ["k37"])
-    V(ts(T.ohb[:], T.kkf[:], -14.5, 1024.0, A.add, A.mult), ["kkf"], ["ohb"])
-    V(ts(T.qb1[:], T.odf[:], 2560.0, -1280.5 + 2.0 ** -13, A.mult, A.add), ["odf"], ["qb1"])
-    V(ts(T.qb3[:], T.odf[:], 2560.0, -1280.5 + 2.0 ** -10, A.mult, A.add), ["odf"], ["qb3"])
-    V(ts(T.cid[:], T.iw[:, 0:128], T.pf[:], None, A.is_equal), ["iw", "pf"], ["cid"])
-    V(ts(T.ce[:], T.ie[:], T.pf[:], None, A.is_equal, rate=0.5), ["ie", "pf"], ["ce"])
-    for name, src, c in (("cidn", "cid", -1.0), ("cidh", "cid", 0.5), ("c37", "cid", 37.0), ("cbh", "cb", 0.5), ("cb2", "cb", -2.0), ("cb4", "cb", 4.0),
-                         ("cbn", "cb", -4.0), ("cbn4", "cb", -0.25), ("cq1", "cb", -256.0), ("cq3", "cb", -32.0)):
-        V(ts(T[name][:], T[src][:], c, None, A.mult), [src], [name])
-    V(ts(T.tma[:], T.iw[:, 0:128], T.pf[:], None, A.is_lt), ["iw", "pf"], ["tma"])
-    V(tt(T.tma[:], T.tma[:], T.cb[:], A.mult), ["tma", "cb"], ["tma"])
-    V(tt(T.ctm[:], T.cidh[:], T.tma[:], A.subtract), ["tma", "cidh"], ["ctm"])
-    V(ms(T.onb[:], 1.0), [], ["onb"])
-    V(ms(T.onf[:], 1.0), [], ["onf"])
-    V(ms(T.fw[:], 0.5), [], every("fw"))
-    V(ms(T.fw[:, 0::16], 0.0), [], every("fw"))
-    V(ms(T.fd[:], 0.0), [], every("fd"))
-    V(ms(T.fd[:, 0::16], -0.125), [], every("fd"))
-    V(((lambda Q: Q.tensor_tensor_scan(T.lim[:], T.fw[:], T.fd[:], 0.0, A.mult, A.add)), ns(192)), every("fw") + every("fd"), ["lim"])
-    V(ts(T.pwi[:], T.iw[:, 0:16], T.kkf[:], -8.0, A.is_equal, A.mult), ["iw", "kkf"], ["pwi"])
+        V(ms(T["d0%d" % b][:, 1:SAVE:2], 0.0), [], ["d0z%d" % b])
+        S(act(T.d1[:, 6144 - 32 * e:6144 - 32 * a:2], T.d00[:, 1:SAVE:2], AF.Copy), ["d0z0"], regs("r15", a, e))
+    const("c3")
+    V(ts(T.qb1[:], odf, 2560.0, -1280.5 + 2.0 ** -13, A.mult, A.add), ["pf"], ["qb1"])
+    V(ts(T.qb3[:], odf, 2560.0, -1280.5 + 2.0 ** -10, A.mult, A.add), ["pf"], ["qb3"])
+    for name, src, c in (("cidn", "cid", -1.0), ("c37", "cid", 37.0), ("cb6", "cb", -6 / 16), ("cq1", "cb", -256.0), ("cq3", "cb", -32.0)):
+        V(ts(T[name][:], T[src][:], c, None, A.mult, rate=0.5), [src], [name])
+    V(ts(T.wb[:], T.cb[:], T.wts[:], None, A.mult, rate=0.5), ["cb", "wts"], ["wb"])
+    V(ts(T.k37[:], kkf, 37.0, None, A.mult), ["pf"], ["k37"])
+    const("c4")
+    G(iota(T.ic[:], [[16, 12]]), [], ["ic"])
+    G(iota(T.iw[:], [[1, 16]]), [], ["iw"])
+    V(ms(T.ha[:], 0.5), [], ["ha"])
+    V(ms(T.ha[:, 0::16], 0.0), [], ["ha"])
+    V(ms(T.hb[:], 0.0), [], ["hb"])
+    V(ms(T.hb[:, 0::16], -1 / 32), [], ["hb"])
+    V(((lambda Q: Q.tensor_tensor_scan(T.lim[:], T.ha[:], T.hb[:], 0.0, A.mult, A.add)), ns(128, 0.5)), ["ha", "hb"], ["lim"])
+    V(ts(T.pwi[:], T.iw[:], kkf, -8.0, A.is_equal, A.mult), ["iw", "pf"], ["pwi"])
     V(tt(T.pwi[:], T.pwi[:], T.lim[:, 0:16], A.mult), ["pwi", "lim"], ["pwi"])
     V(((lambda Q: Q.tensor_reduce(T.pw[:], T.pwi[:], AxisListType.X, A.add)), ns(16)), ["pwi"], ["pw"])
-    V(ts(T.cbw[:], T.cb[:], T.pw[:], None, A.mult), ["cb", "pw"], ["cbw"])
-    V(ts(T.bl[:], T.ic[:], T.kkf[:], None, A.add), ["ic", "kkf"], ["bl"])
-    V(ts(T.b256[:], T.bl[:], 256.0, None, A.add), ["bl"], ["b256"])
+    V(ts(T.cbw[:], T.cb[:], T.pw[:], None, A.mult, rate=0.5), ["cb", "pw"], ["cbw"])
+    V(ts(T.cbn[:], T.cb[:], -1 / 16, None, A.mult, rate=0.5), ["cb"], ["cbn"])
+    V(ts(T.bl[:], T.ic[:], kkf, None, A.add), ["ic", "pf"], ["bl"])
+    V(ts(T.top[:], T.bl[:], 513.0, None, A.add), ["bl"], ["top"])
+    const("c9")
+    for i in range(2):
+        G(iota(T.ie[:, 512 * i:512 * i + 512], [[1, 32], [0, 16]], 32 * i), [], ["ie%d" % i])
+    V(ts(T.ce[:], T.ie[:], hf, None, A.is_equal, rate=0.5), ["ie0", "ie1", "pf"], ["ce"])
+    const("c5")
+    V(ts(T.kwa[:], kkf, 15.0, SAVE + 31.0, A.is_equal, A.mult), ["pf"], ["kwa"])
+    V(ts(T.kw[:], kkf, -2.0, -1.0, A.mult, A.add), ["pf"], ["kw"])
+    V(tt(T.kw[:], T.kw[:], T.kwa[:], A.add), ["kw", "kwa"], ["kw"])
+    V(ts(T.ohb[:], kkf, -14.5, 1024.0, A.add, A.mult), ["pf"], ["ohb"])
+    for name, src, c in (("cb2", "cb", -2.0), ("cb43", "cb", -43 / 16)):
+        V(ts(T[name][:], T[src][:], c, None, A.mult, rate=0.5), [src], [name])
+    G(pick(T.tri[:], T.cb2[:], [[-1, 128]], A.is_gt, 1), ["cb2"], ["tri"])
+    V(tt(T.tri[:], T.tri[:], T.cid[:], A.add, rate=2.0), ["tri", "cid"], ["tri"])
+    V(ms(T.bas[:], 0.0), [], ["bas"])
     for b, (a, e) in enumerate(BLOCKS):
-        n = (e - a) // 16
-        V(ms(T.bas[:, a // 8:a // 8 + n], -256.0), [], ["basa%d" % b])
-        V(ts(T.bas[:, a // 8 + n:a // 8 + 2 * n], T.bl[:, 0:n], 32768.0, None, A.mult), ["bl"], ["basb%d" % b])
-    for i, c in enumerate((-2.5, -42.5, -34.5)):
-        V(ms(T.th0[:, i:i + 1], c), [], ["th0%d" % i])
-    V(ts(T.wb[:], T.cb[:], T.wts[:], None, A.mult), ["cb", "wts"], ["wb"])
-    for t in range(STEPS):
-        V(ts(T.dg[:, 128 * t:128 * t + 128], T.cid[:], T.dvs[:, t:t + 1], None, A.mult), ["cid", "dvs"], ["dg%d" % t])
-    P(mm(T.p0[:], (T.cb[:], T.dg[:, 0:512])), ["cb", "dg0", "dg1", "dg2", "dg3"], ["p0"])
-    P(mm(T.p1[:, 0:128], (T.cb[:], T.dg[:, 512:640])), ["cb", "dg4"], ["p1"])
-    S(act(T.dd[:, 0:512], T.p0[:], AF.Copy, scale=2.0 ** -10), ["p0"], ["dd0", "dd1", "dd2", "dd3"])
-    S(act(T.dd[:, 512:640], T.p1[:, 0:128], AF.Copy, scale=2.0 ** -10), ["p1"], ["dd4"])
-    V(cp(T.tb[:, 0:512], T.mci[:]), ["mci"], ["tb"])
-    V(cp(T.mf0[:], T.mi[:]), ["mi"], regs("m0", 0, 192))
+        V(ms(T.bas[:, ROWS[b] // 16:ROWS[b] // 16 + 4], 1.0), ["bas"], regs("one", a, e))
+        V(ts(T.bas[:, ROWS[b] // 16 + 4:ROWS[b] // 16 + 8], T.bl[:, 0:4], -32768.0, None, A.mult), ["bl", "bas"], regs("bas", a, e))
+    G(move(T.mf0[:], T.mi[:]), ["mi"], every("m0"))
+    const("c6")
+    V(ts(T.cbm[:], T.cb[:, 0::16], -1.0, None, A.mult), ["cb"], ["cbm"])
+    V(ts(T.cidm[:], T.cid[:, ::-1], 4096.0, None, A.mult), ["cid"], ["cidm"])
+    V(ms(T.onf[:], 1 / 32, 1.0), [], ["onf"])
+    G(move(T.tb[:, 0:512], T.mci[:]), ["mci"], ["tb"])
+    const("c10")
+    for i in range(4):
+        S(act(T.seln[:, 512 * i:512 * i + 512], T.sel[:, 512 * i:512 * i + 512], AF.Copy, scale=-1.0), ["sel"], ["seln%d" % i])
 
-    def listmm(out, mats, buf, a, b, base=()):
-        return mm(out, *(list(base) + [(T[mats][:, 128 * i:128 * i + 128], T[buf][:, a + i:b:16]) for i in range(16)]))
+    def listmm(out, buf, a, b, base=()):
+        return mm(out, *(list(base) + [(T.sel[:, 128 * i:128 * i + 128], T[buf][:, a + i:b:16]) for i in range(16)]))
 
     sends = [0]
 
     def send(name, src, dst, r, w):
         sends[0] += 1
         i = op("g", ((lambda Q: Q.remote_dma(dst, src, T.sem[name], T.sem.snd, pid, rid, mask_out)), SEND), r, [], ("snd%d" % sends[0], 0, False))
-        op(None, (None, 0.0, FLIGHT[name[0]] + FIRST * (sends[0] == 1)), [], w, (name, n_eng, False), i)
+        op(None, (None, 0.0, FLIGHT + FIRST * (sends[0] == 1)), [], w, (name, n_in, False), i)
 
-    def back(a, b):
-        return slice(b - 1, a - 1 if a else None, -1)
+    def back(a, b, step, total):
+        stop = total - 1 - a - step * len(range(a, b, step))
+        return slice(total - 1 - a, stop if stop >= 0 else None, -step)
 
-    def home(a):
-        b = [i for i, x in enumerate(BLOCKS) if x[0] <= a < x[1]][0]
-        return b, T["d0%d" % b], BLOCKS[b][0]
+    def gg(a, e):
+        return T.gg[:, back(a, e, 1, 192)]
 
-    def quotient(out, a, scale, bias, r, w):
-        if Q_MOD == "s":
-            S(act(out, a, AF.Identity, scale=scale, bias=bias), r, w)
-        else:
-            V(ts(out, a, scale, bias, A.mult, A.add), r, w)
+    def part(buf, a, e, lo, hi):
+        return buf[:, a // 64, lo:hi] if e - a == 64 else buf[:, a // 64:e // 64, lo:hi]
 
     def step(t):
         lastt = t == STEPS - 1
-        mf, z = T["mf%d" % t], T["zb%d" % t]
-        mfn, zn = "m%d" % t, "z%d" % t
-        th = [T.thr[:, 3 * t + i:3 * t + i + 1] if t else T.th0[:, i:i + 1] for i in range(3)]
-        thn = ["thr%d" % t] if t else ["th00", "th01", "th02"]
+        mfn, zn = ("y%d" % t if t else "m0"), "z%d" % t
+        th, thn = (T.thr[:, t:t + 1], ["thr%d" % t]) if t else (0.5, [])
 
-        def when(what, a=0):
-            now[1:] = [t, what, home(a)[0] if len(DUE[what]) > 1 else 0]
+        def z(a, e):
+            return part(T["zb%d" % t], a, e, 0, 64) if t else T.zb0[:, a:e]
+
+        def mf(a, e):
+            return part(T["zb%d" % t], a, e, 64, 68) if t else T.mf0[:, a // 16:e // 16]
+
+        def when(what, a=0, second=0):
+            what = what + "0" * (t == 0)
+            now[1:] = [t, what, 2 - a // 64 + len(BLOCKS) * second if len(DUE[what]) > 1 else 0]
             now[0] = PERIOD * t + DUE[what][now[3]]
 
-        for b, (a, e) in enumerate(BLOCKS):
+        if t == 0:
+            when("ahead")
+            send("ze", z(*BLOCKS[0]), T.ze[:], regs(zn, *BLOCKS[0]), ["ze"])
+        if t == 1:
+            a, e = BLOCKS[0]
+            when("goal", a)
+            P(mm(T.p2[:, 384:448], (T.cid[:], T.ze[:]), (T.cid[:], T.zw[:, 0:64])), ["cid", "ze"] + regs("w1", a, e), ["p2.z"])
+            S(act(z(a, e), T.p2[:, 384:448], AF.Abs), ["p2.z"], regs(zn, a, e))
+            V(cp(mf(a, e), T.zw[:, 64:68]), regs("w1", a, e), regs(mfn, a, e))
+
+        for a, e in BLOCKS:
             c = slice(a // 16, e // 16)
             when("lists", a)
-            move(Q_ML if t else "v", T.ml[:, c], mf[:, c] if t else T.mi[:, c], regs(mfn, a, e) if t else ["mi"], regs("ml", a, e))
-            S(gather(act(T.gg[:, a:e], T.glw[:].indirect(T.ml[:, c]), AF.Copy), e - a), ["glw"] + regs("ml", a, e), regs("gg", a, e))
-            S(gather(act(T.mb[:, a:e], T.imw[:].indirect(T.ml[:, c]), AF.Copy), e - a), ["imwa", "imwb"] + regs("ml", a, e), regs("mb", a, e))
+            if t == 0:
+                V(cp(T.ml[:, c], T.mi[:, c]), ["mi"], regs("ml", a, e))
+            elif t == 1 and (a, e) == BLOCKS[0]:
+                copy(Q_ML, T.ml[:, c], T.zw[:, 64:68], regs("w1", a, e), regs("ml", a, e))
+            else:
+                copy(Q_ML, T.ml[:, c], mf(a, e), regs(mfn, a, e), regs("ml", a, e))
+            S(gather(act(gg(a, e), T.glw[:].indirect(T.ml[:, c]), AF.Copy), e - a, q="s"), ["glw"] + regs("ml", a, e), regs("gg", a, e))
+            when("row", a)
+            S(gather(act(T.mb[:, a:e], T.imw[:].indirect(T.ml[:, c]), AF.Copy), e - a, q="s"), ["imwa", "imwb"] + regs("ml", a, e), regs("mb", a, e))
             when("ops", a)
             win = T.tb[:, 0:512] if t else T.mci[:]
             V(gather(cp(T.ol[:, a:e], win.indirect(T.ml[:, c])), e - a), ["tb" if t else "mci"] + regs("ml", a, e), regs("ol", a, e))
 
-        for a, e, q in ADDS[min(t, 1)]:
-            b, d0, o = home(a)
-            when("adds", a)
-            out, win = d0[:, 32 * (a - o) + 1:32 * (e - o):2], T.adw[:].indirect(T.ol[:, a:e])
+        for b, a, e, q, half in shares(ADDS[min(t, 1)]):
+            when("adds", a, half)
+            o = BLOCKS[b][0]
+            out, win = T["d0%d" % b][:, back(32 * (a - o) + 1, 32 * (e - o), 2, SAVE)], T.adw[:].indirect(T.ol[:, a:e])
             call = ts(out, win, -1.0, None, A.mult) if q == "v" else act(out, win, AF.Copy, scale=-1.0)
-            op(q, gather(call, 16 * (e - a)), ["adw"] + regs("ol", a, e), regs("d0", a, e) + regs("cut", a, e))
-        for a, e, q in NEEDS[min(t, 1)]:
-            when("needs", a)
-            out, win = T.d1[:, 32 * a:32 * e:2], T.prw[:].indirect(T.ol[:, a:e])
-            op(q, gather(cp(out, win) if q == "v" else act(out, win, AF.Copy), 16 * (e - a)), ["prw"] + regs("ol", a, e), regs("d1", a, e))
+            op(q, gather(call, 16 * (e - a), q=q), ["adw"] + regs("ol", a, e), regs("d0", a, e) + regs("cut", a, e))
+        for b, a, e, q, half in shares(NEEDS[min(t, 1)]):
+            when("needs", a, half)
+            out, win = T.d1[:, back(32 * a, 32 * e, 2, 6144)], T.prw[:].indirect(T.ol[:, a:e])
+            op(q, gather(cp(out, win) if q == "v" else act(out, win, AF.Copy), 16 * (e - a), q=q), ["prw"] + regs("ol", a, e), regs("d1", a, e))
         for b, (a, e) in enumerate(BLOCKS):
-            d0, n = T["d0%d" % b], e - a
+            d0 = T["d0%d" % b]
             when("scan", a)
-            first, kept = d0[:, 31:32 * n:32], d0[:, SAVE:SAVE + 32 * n:32]
-            P(mm(T.p4[:, 384:384 + n], (T.cid[:], T.gg[:, a:e]), (T.cid[:], first)), ["cid"] + regs("gg", a, e) + regs("cut", a, e), ["p4.r"])
-            if Q_R15 == "v":
-                V(ts(T.d1[:, 32 * a + 31:32 * e:32], T.p4[:, 384:384 + n], 0.0, None, A.max), ["p4.r"], regs("r15", a, e))
-            else:
-                S(act(T.d1[:, 32 * a + 31:32 * e:32], T.p4[:, 384:384 + n], AF.Relu), ["p4.r"], regs("r15", a, e))
-            move(Q_SAVE, kept, first, regs("cut", a, e), regs("a15", a, e))
-            if Q_SAVE == "g":
-                G(iota(first, [[0, n]], -1024), [], regs("cut", a, e))
-            else:
-                V(ms(first, -1024.0), [], regs("cut", a, e))
-            j, k = back(32 * a, 32 * e), back(0, 32 * n)
-            V(((lambda Q, j=j, k=k, d0=d0: Q.tensor_tensor_scan(T.ss[:, j], d0[:, k], T.d1[:, j], 0.0, A.add, A.max)), ns(32 * n, 0.5)),
+            first, kept = d0[:, 0:SAVE:32], d0[:, SAVE + 31:2 * SAVE:32]
+            P(mm(T.p4[:, 384:448], (T.cid[:], gg(a, e)), (T.cid[:], d0[:, back(31, SAVE, 32, SAVE)])), ["cid"] + regs("gg", a, e) + regs("cut", a, e), ["p4.r"])
+            either("r15", T.d1[:, back(32 * a + 31, 32 * e, 32, 6144)], T.p4[:, 384:448], AF.Relu, 1.0, 0.0, (0.0, None, A.max), ["p4.r"], regs("r15", a, e))
+            copy(Q_SAVE, kept, first, regs("cut", a, e), regs("a15", a, e))
+            op(Q_CUT, iota(first, [[0, 64]], -1024) if Q_CUT == "g" else ms(first, -1024.0), [], regs("cut", a, e))
+            j, k = slice(6144 - 32 * e, 6144 - 32 * a), slice(0, SAVE)
+            V(((lambda Q, j=j, k=k, d0=d0: Q.tensor_tensor_scan(T.ss[:, j], d0[:, k], T.d1[:, j], 0.0, A.add, A.max)), ns(SAVE, 0.5)),
               ["d0z%d" % b] + regs("d0", a, e) + regs("cut", a, e) + regs("d1", a, e) + regs("r15", a, e), regs("ss", a, e))
 
-        for b, (a, e) in enumerate(BLOCKS):
+        for i, (a, e) in enumerate(GOALS):
             when("goal", a)
-            P(mm(T.p5[:, 128 + a:128 + e], (T.cid[:], z[:, a:e]), (T.cidn[:], T.gg[:, a:e])), ["cid", "cidn"] + regs(zn, a, e) + regs("gg", a, e), regs("p5.d", a, e))
+            P(mm(T.p5[:, 128 + a:128 + e], (T.cid[:], z(a, e)), (T.cidn[:], gg(a, e))), ["cid", "cidn"] + regs(zn, a, e) + regs("gg", a, e), regs("p5.d", a, e))
             S(act(T.gi[:, a:e], T.p5[:, 128 + a:128 + e], AF.Sign, bias=0.5), regs("p5.d", a, e), regs("gi", a, e))
-            P(mm(T.p5[:, 320 + a:320 + e], (T.cbh[:], T.gi[:, a:e])), ["cbh"] + regs("gi", a, e), regs("p5.c", a, e))
-            S(act(T.tg[:, 1, a:e], T.p5[:, 320 + a:320 + e], AF.Sign, bias=th[0]), regs("p5.c", a, e) + thn, regs("goal", a, e))
+            P(mm(T.p5[:, 320 + a:320 + e], (T.cb[:], T.gi[:, a:e]), (T.cb6[:], T.onb[:, 0:e - a])), ["cb", "cb6", "onb"] + regs("gi", a, e), regs("p5.c", a, e))
+            S(act(T.tg[:, 1, a:e], T.p5[:, 320 + a:320 + e], AF.Sign, scale=0.5, bias=th, accum_out=T.acc[:, i:i + 1]), regs("p5.c", a, e) + thn,
+              regs("goal", a, e) + ["acc%d" % i])
+            when("room", a)
+            either("hh", T.hh[:, a:e], z(a, e), AF.Copy, 1.0, -255.0, (-255.0, None, A.add), regs(zn, a, e), regs("hh", a, e))
 
-        for i, (a, e) in enumerate(MODS):
+        for a, e in MODS:
             when("mod", a)
             c, l0, w = slice(a // 16, e // 16), 384 + a // 8, (e - a) // 16
-            x = [(T.wb[:], z[:, a:e]), (T.cq1[:], T.q1[:, a:e]), (T.c37[:], T.mb[:, a:e]), (T.cq3[:], T.q3[:, a:e])]
+            x = [(T.wb[:], z(a, e)), (T.cq1[:], T.q1[:, a:e]), (T.c37[:], T.mb[:, a:e]), (T.cq3[:], T.q3[:, a:e])]
             xn = [["wb"] + regs(zn, a, e), ["cq1"] + regs("q1", a, e), ["c37"] + regs("mb", a, e), ["cq3"] + regs("q3", a, e)]
             P(mm(T.p6[:, a:e], *x[:1]), xn[0], regs("p6.x", a, e))
-            quotient(T.q1[:, a:e], T.p6[:, a:e], 2.0 ** -12, T.qb1[:], regs("p6.x", a, e) + ["qb1"], regs("q1", a, e))
+            either("q1", T.q1[:, a:e], T.p6[:, a:e], AF.Identity, 2.0 ** -12, T.qb1[:], (2.0 ** -12, T.qb1[:], A.mult, A.add), regs("p6.x", a, e) + ["qb1"], regs("q1", a, e))
             P(mm(T.p7[:, a:e], *x[:3]), sum(xn[:3], []), regs("p7.x", a, e))
             P(mm(T.p6[:, 192 + a:192 + e], *x[:2]), sum(xn[:2], []), regs("p6.u", a, e))
-            quotient(T.q3[:, a:e], T.p7[:, a:e], 2.0 ** -9, T.qb3[:], regs("p7.x", a, e) + ["qb3"], regs("q3", a, e))
+            either("q3", T.q3[:, a:e], T.p7[:, a:e], AF.Identity, 2.0 ** -9, T.qb3[:], (2.0 ** -9, T.qb3[:], A.mult, A.add), regs("p7.x", a, e) + ["qb3"], regs("q3", a, e))
             P(mm(T.p7[:, 192 + a:192 + e], *x), sum(xn, []), regs("p7.m", a, e))
-            S(act(T.tg[:, 0, a:e], T.p7[:, 192 + a:192 + e], AF.Copy, bias=-256.0), regs("p7.m", a, e), regs("to", a, e))
+            either("to", T.tg[:, 0, a:e], T.p7[:, 192 + a:192 + e], AF.Copy, 1.0, 1.0, (1.0, None, A.add), regs("p7.m", a, e), regs("to", a, e))
             P(mm(T.p6[:, l0:l0 + 2 * w], *[(T.sel[:, 128 * j:128 * j + 128], T.tg[:, :, a + j:e:16]) for j in range(16)]),
               ["sel"] + regs("to", a, e) + regs("goal", a, e), regs("p6.l", a, e))
-            S(act(T.mal[:, c], T.p6[:, l0:l0 + w], AF.Copy, scale=0.0625), regs("p6.l", a, e), regs("mal", a, e))
-            S(act(T.ngl[:, c], T.p6[:, l0 + w:l0 + 2 * w], AF.Copy, scale=-32.0, bias=512.0, accum_out=T.acc[:, i:i + 1]), regs("p6.l", a, e),
-              regs("ngl", a, e) + ["acc%d" % i])
+            either("lst", T.lst[:, 2 * c.start:2 * c.stop], T.p6[:, l0:l0 + 2 * w], AF.Copy, 0.0625, 0.0, (0.0625, None, A.mult), regs("p6.l", a, e), regs("lst", a, e))
+            copy(Q_MAL, T.mal[:, c], T.lst[:, 2 * c.start:2 * c.start + w], regs("lst", a, e), regs("mal", a, e))
             when("first", a)
-            V(tt(T.kl[:, c], T.mal[:, c], T.ngl[:, c], A.add), regs("mal", a, e) + regs("ngl", a, e), regs("kl", a, e))
             for k in range(a // 16, e // 16):
-                V(ts(T.eb[:, k, 0:192 - 16 * k], T.tg[:, 0, 16 * k:192], T.kl[:, k:k + 1], None, A.is_equal, rate=0.5), regs("to", a, 192) + regs("kl", a, e), ["eb%d" % k])
+                lk, end = k + a // 16, [y for x, y in USES if x <= 16 * k < y][0]
+                V(ts(T.eb[:, k, 0:end - 16 * k], T.tg[:, 0, 16 * k:end], T.lst[:, lk + w:lk + w + 1], T.lst[:, lk:lk + 1], A.mult, A.is_equal, rate=0.5),
+                  regs("to", a, end) + regs("lst", a, e), ["eb%d" % k])
         if not lastt:
             when("count")
-            sums = mm(T.p6[:, 408:409], *[(T.onf[:], T.acc[:, i:i + 1]) for i in range(len(MODS))])
-            P((sums[0], 4 * sums[1]), ["onf"] + ["acc%d" % i for i in range(len(MODS))], ["p6.a"])
-            V(ts(T.ai[:], T.p6[:, 408:409], 2.0 ** -10, None, A.mult), ["p6.a"], ["ai"])
-            V(ts(T.ai2[:], T.ai[:], 1, None, A.bitwise_and), ["ai"], ["ai2"])
-            V(cp(T.aif[:], T.ai2[:]), ["ai2"], ["aif"])
-            V(ts(T.thr[:, 3 * t + 3:3 * t + 6], T.th0[:], T.aif[:], None, A.subtract), ["aif", "th00", "th01", "th02"], ["thr%d" % (t + 1)])
+            sums = mm(T.p6[:, 408:410], (T.onf[:], T.acc[:]))
+            P((sums[0], 4 * sums[1]), ["onf", "acc0", "acc1"], ["p6.a"])
+            S(act(T.sm[:], T.p6[:, 408:410], AF.Copy, bias=-0.25, accum_out=T.sum[:]), ["p6.a"], ["sum"])
+            S(act(T.ev[:], T.sum[:], AF.Copy, bias=MAGIC), ["sum"], ["ev"])
+            V(ts(T.thr[:, t + 1:t + 2], T.ev[:], MAGIC, T.sum[:], A.subtract, A.subtract), ["ev", "sum"], ["thr%d" % (t + 1)])
 
-        when("lost")
-        P(mm(T.p7[:, 0:192], (T.cbn4[:], T.tg[:, 1, :]), (T.cb[:], T.lim[:]), (T.cbw[:], T.eb[:, :, 0:16]),
-             *[(T.cb4[:], T.eb[:, c, 16:192 - 16 * c], T.p7[:, 16 * c + 16:192]) for c in range(11)]),
-          ["cbn4", "cb", "cbw", "cb4", "lim"] + every("goal") + ["eb%d" % c for c in range(12)], every("p7.x"))
-        S(act(T.wn[:], T.p7[:, 0:192], AF.Relu, scale=2.0 ** 26, bias=2.0 ** 28 + 1024.0), every("p7.x"), ["wn"])
-        P(listmm(T.p6[:, 416:428], "sel", "wn", 0, 192, [(T.cid[:], T.mal[:])]), ["sel", "cid", "wn"] + every("mal"), ["p6.s"])
-        V(tt(T.ys[:], T.b256[:], T.p6[:, 416:428], A.min), ["b256", "p6.s"], ["ys"])
-        V(ts(T.sl[:], T.ys[:], 256.0, None, A.add), ["ys"], ["sl"])
+        for b, (a, e) in enumerate(USES):
+            when("lost", a)
+            c, ks = slice(a // 16, e // 16), range(a // 16, e // 16)
+            P(mm(T.p7[:, a:e], (T.cbn[:], T.tg[:, 1, a:e]), (T.cb[:], T.lim[:, 0:e - a]), (T.cbw[:], T.eb[:, c, 0:16]),
+                 *[(T.cb[:], T.eb[:, k, 16:e - 16 * k], T.p7[:, 16 * k + 16:e]) for k in ks[:-1]]),
+              ["cbn", "cb", "cbw", "lim"] + regs("goal", a, e) + ["eb%d" % k for k in ks], regs("p7.x", a, e))
+            either("wn", T.oh[:, ROWS[b] + 128:ROWS[b + 1]], T.p7[:, a:e], AF.Relu, 2.0 ** 28, 2.0 ** 28 + 1024.0, (-1.0, 1024.0, A.is_ge, A.mult),
+                   regs("p7.x", a, e), regs("wn", a, e))
 
-        for a, e in NEWS:
-            when("new", a)
-            if Q_OF == "s":
-                S(gather(act(T.of[:, a:e], T.tb[:, 0:512].indirect(T.ml[:, a // 16:e // 16]), AF.Copy), e - a), ["tb"] + regs("ml", a, e), regs("of", a, e))
+        when("new")
+        G(move(T.of[:], T.ol[:]), every("ol"), ["of"])
+        either("ok", T.p2[:, 192:384], T.of[:], AF.Identity, 1.0, T.k37[:], (T.k37[:], None, A.add), ["of", "k37"], ["p2.k"])
+        V(tt(T.f1[:], T.of[:], T.p6[:, 192:384], A.mult), ["of"] + every("p6.u"), ["f1"])
+        V(ts(T.f2[:], T.f1[:], 5, None, A.arith_shift_right), ["f1"], ["f2"])
+        V(tt(T.f3[:], T.f2[:], T.p2[:, 192:384], A.add), ["f2", "p2.k"], ["f3"])
+        V(ts(T.f4[:], T.f3[:], 4095, None, A.bitwise_and), ["f3"], ["f4"])
+
+        if t < 2:
+            when("dist")
+            a, e = (1, STEPS) if t else (0, 1)
+            out, names = (T.p3[:], every("p3.c") + ["p3.y"]) if t else (T.p2[:, 0:128], ["p2.d"])
+            for i in range(a, e):
+                V(ts(T.dg[:, 128 * i:128 * i + 128], T.cid[:], T.dvs[:, i:i + 1], None, A.mult, rate=0.5), ["cid", "dvs"], ["dg%d" % i])
+            P(mm(out, (T.cb[:], T.dg[:, 128 * a:128 * e])), ["cb"] + ["dg%d" % i for i in range(a, e)], names)
+            S(act(T.dd[:, 128 * a:128 * e], out, AF.Copy, scale=-2.0 ** -10), names, ["dd%d" % t])
+
+        for b, (a, e) in enumerate(TURNS):
+            n = e - a
+            when("met", a)
+            zt = T.zt[0:n, 128 * b:128 * b + 128]
+            for s in range(a, e, 64):
+                P(mm(T.p5[s - a:s - a + 64, 0:128], (z(s, s + 64), T.cid[:])), ["cid"] + regs(zn, s, s + 64), ["p5.t%d" % (s - a)])
+            either("zt", zt, T.p5[0:n, 0:128], AF.Copy, 1.0, 0.0, (0.0, None, A.add), ["p5.t%d" % s for s in range(0, n, 64)], ["zt%d" % b])
+            for s in range(e - 64, a - 64, -64):
+                when("spread", s)
+                for h in range(2):
+                    P(mm(T.p0[:, 512 * h:512 * h + 512], (T.zt[s - a:s - a + 64, 128 * b:128 * b + 128], T.ce[s - a:s - a + 64, 512 * h:512 * h + 512])),
+                      ["zt%d" % b, "ce"], ["p0.%d" % h])
+                when("cmp", s)
+                V(tt(T.ind[:, 16 * s:16 * s + 1024], T.ss[:, back(32 * s, 32 * s + 2048, 2, 6144)], T.p0[:], A.is_le), regs("ss", s, s + 64) + ["p0.0", "p0.1"], regs("ind", s, s + 64))
+
+        for b, (a, e) in enumerate(BLOCKS):
+            c, o, end = slice(a // 16, e // 16), ROWS[b], ROWS[b + 1]
+            when("pass", a)
+            P(mm(T.p3[:, a:e], (T.cb2[:], T.tg[:, 1, a:e]), (T.cb43[:], T.onb[:, 0:64]),
+                 *[(T.sel[:, 128 * k:128 * k + 128], T.ind[:, 16 * a + k:16 * e:16]) for k in range(16)]),
+              ["sel", "cb2", "cb43", "onb"] + regs("goal", a, e) + regs("ind", a, e), regs("p3.c", a, e))
+            S(act(T.sg[:, a:e], T.p3[:, a:e], AF.Sign, bias=th), regs("p3.c", a, e) + thn, regs("sg", a, e))
+            P(mm(T.p3[:, 192:256], (T.tri[:], T.sg[:, a:e])), ["tri"] + regs("sg", a, e), ["p3.y"])
+            S(act(T.oh[:, o:o + 64], T.p3[:, 192:256], AF.Relu, scale=512.0, bias=T.ohb[:]), ["p3.y", "ohb"], regs("oh", a, e))
+            either("ow", T.oh[:, o + 64:o + 128], T.oh[:, o:o + 64], AF.Copy, T.kw[:], 0.0, (T.kw[:], None, A.mult), ["kw"] + regs("oh", a, e), regs("ow", a, e))
+            l0, l1 = 384 + o // 16, 384 + end // 16
+            terms, names = [(T.cid[:], T.bas[:, o // 16:end // 16]), (T.cidn[:], T.mal[:, c], T.p7[:, l0:l0 + 4])], []
+            if b < len(USES):
+                x, y = USES[b]
+                terms, names = terms + [(T.cid[:], T.mal[:, x // 16:y // 16], T.p7[:, l0 + 8:l1])], regs("wn", x, y) + regs("mal", x, y)
+            P(listmm(T.p7[:, l0:l1], "oh", o, end, terms),
+              ["sel", "cid", "cidn"] + names + regs("bas", a, e) + regs("one", a, e) + regs("mal", a, e) + regs("ow", a, e) + regs("oh", a, e), regs("p7.l", a, e))
+            if b < len(USES):
+                when("place", x)
+                V(tt(T.ys[:, x // 16:y // 16], T.top[:, x // 16:y // 16], T.p7[:, l0 + 8:l1], A.min), ["top"] + regs("p7.l", a, e), regs("ys", x, y))
+                V(ts(T.sl[:, x // 16:y // 16], T.ys[:, x // 16:y // 16], -1.0, None, A.add), regs("ys", x, y), regs("sl", x, y))
+                when("pass", a)
+            out, ahead = T.yo if lastt else T["zs%d" % (t + 1)], t == 0 and b == 0
+            V(tt(T.tm[:, c] if ahead else T.p2[:, 448:452], mf(a, e), T.p7[:, l0:l0 + 4], A.min), regs(mfn, a, e) + regs("p7.l", a, e), ["tm" if ahead else "p2.m"])
+            when("move", a)
+            V(ts(T.la[:, c], T.p7[:, l0 + 4:l0 + 8], 2.0 ** -10, SAVE - 1.0, A.mult, A.add), regs("p7.l", a, e), regs("la", a, e))
+            V(gather(tt(T.yy[:, a:e], T["d0%d" % b][:].indirect(T.la[:, c]), T.hh[:, a:e], A.max), 64),
+              ["d0z%d" % b] + regs("la", a, e) + regs("hh", a, e) + regs("d0", a, e) + regs("cut", a, e) + regs("a15", a, e), regs("yy", a, e))
+            P(mm(T.p2[:, 384:448], (T.dd[:, 128 * t:128 * t + 128], T.oh[:, o:o + 64]), (T.cidn[:], T.yy[:, a:e]), *[(T.cid[:], z(a, e))] * (not ahead)),
+              ["dd%d" % min(t, 1), "cid", "cidn"] + regs("oh", a, e) + regs("yy", a, e) + regs(zn, a, e), ["p2.z"])
+            if ahead:
+                S(act(part(out, a, e, 64, 68), T.tm[:, c], AF.Abs), ["tm"], ["ms"])
+                S(act(part(out, a, e, 0, 64), T.p2[:, 384:448], AF.Copy), ["p2.z"], regs("zs%d" % t, a, e))
             else:
-                move(Q_OF, T.of[:, a:e], T.ol[:, a:e], regs("ol", a, e), regs("of", a, e))
-            S(act(T.p2[:, a:e], T.of[:, a:e], AF.Copy), regs("of", a, e), regs("p2.o", a, e))
-            S(act(T.p2[:, 192 + a:192 + e], T.of[:, a:e], AF.Identity, bias=T.k37[:]), regs("of", a, e) + ["k37"], regs("p2.k", a, e))
-            V(tt(T.f1[:, a:e], T.of[:, a:e], T.p6[:, 192 + a:192 + e], A.mult), regs("of", a, e) + regs("p6.u", a, e), regs("f1", a, e))
-            V(ts(T.f2[:, a:e], T.f1[:, a:e], 5, None, A.arith_shift_right), regs("f1", a, e), regs("f2", a, e))
-            V(tt(T.f3[:, a:e], T.f2[:, a:e], T.p2[:, 192 + a:192 + e], A.add), regs("f2", a, e) + regs("p2.k", a, e), regs("f3", a, e))
-            V(ts(T.f4[:, a:e], T.f3[:, a:e], 4095, None, A.bitwise_and), regs("f3", a, e), regs("f4", a, e))
-            V(tt(T.fd[:, a:e], T.f4[:, a:e], T.p2[:, a:e], A.subtract), regs("f4", a, e) + regs("p2.o", a, e), regs("fd", a, e))
+                S(act(part(out, a, e, 0, 68), T.p2[:, 384:452], AF.Abs), ["p2.z", "p2.m"], regs("zs%d" % t, a, e))
+            if not lastt:
+                send("zr%d_%d" % (t + 1, b), part(out, a, e, 0, 68), T.zw[:] if ahead else part(T["zb%d" % (t + 1)], a, e, 0, 68), regs("zs%d" % t, a, e) + ["ms"] * ahead,
+                     regs("w1", a, e) if ahead else regs("y%d" % (t + 1), a, e) + regs("z%d" % (t + 1), a, e))
 
         for a, e in USES:
             n = e - a
             c = slice(a // 16, e // 16)
             when("use", a)
-            ends = [(T.ss[:, 32 * a + 2 * k + 2:32 * e:32] if k < 15 else T.gg[:, a:e], T.ss[:, 32 * a + 2 * k + 1:32 * e:32]) for k in range(16)]
+            ends = [(T.ss[:, back(32 * a + 2 * k + 2, 32 * e, 32, 6144)] if k < 15 else gg(a, e), T.ss[:, back(32 * a + 2 * k + 1, 32 * e, 32, 6144)])
+                    for k in range(16)]
             mask = T.p4[:, 192 + a:192 + e]
-            if n > 64:
+            if n > 64 or t == 0:
+                x, y = 6144 - 32 * e, 6144 - 32 * a
+                ends = [(T.ss[:, x + 29 - 2 * k:y:32] if k < 15 else T.gg[:, 192 - e:192 - a], T.ss[:, x + 30 - 2 * k:y:32]) for k in range(16)]
+
                 def turned(Q, ends=ends, n=n):
                     for k, (hi, lo) in enumerate(ends):
-                        Q.matmul(T.p4[0:n, k:128:16], hi, T.sel[:, 0:128:16], True, False)
-                        ins = Q.matmul(T.p4[0:n, k:128:16], lo, T.seln[:, 0:128:16], False, True)
+                        Q.matmul(T.p4[0:n, k:128:16], hi, T.cb[:, 0::16], True, False)
+                        ins = Q.matmul(T.p4[0:n, k:128:16], lo, T.cbm[:], False, True)
                     return ins
-                P((turned, 32 * 64 * PE_CYCLE), ["sel", "seln"] + regs("gg", a, e) + regs("ss", a, e), ["p4.t"])
+                P((turned, 32 * (64 * PE_CYCLE + PCALL)), ["cb", "cbm"] + regs("gg", a, e) + regs("ss", a, e), ["p4.t"])
                 S(act(T.st[0:n, :], T.p4[0:n, 0:128], AF.Sign, scale=-1.0, bias=253.5), ["p4.t"], ["st"])
-                P(mm(mask, (T.st[0:n, :], T.cidh[0:n, 0:n]), (T.onb[0:n, :], T.cidh[0:n, 0:n])), ["st", "cidh", "onb"], regs("p4.m", a, e))
+                P(mm(mask, (T.st[0:n, :], T.cidm[0:n, 128 - n:128]), (T.onb[0:n, :], T.cidm[0:n, 128 - n:128])), ["st", "cidm", "onb"], regs("p4.m", a, e))
+                when("write", a)
+                V(tt(T.fw[:, a:e], T.f4[:, a:e], mask, A.min), ["f4"] + regs("p4.m", a, e), regs("fw", a, e))
+                V(tt(T.fd[:, a:e], T.of[:, a:e], mask, A.subtract), ["of"] + regs("p4.m", a, e), regs("fd", a, e))
+                V(gather(tt(T.tb[:].indirect(T.sl[:, c]), T.fw[:, a:e], T.fd[:, a:e], A.max), n, SCATTER), regs("sl", a, e) + regs("fd", a, e) + regs("fw", a, e), ["tb"])
             else:
                 P(mm(T.p4[:, 128:128 + n], *[(T[m][:, 128 * k:128 * k + 128], x[i]) for k, x in enumerate(ends) for i, m in enumerate(("sel", "seln"))]),
-                  ["sel", "seln"] + regs("gg", a, e) + regs("ss", a, e), ["p4.u"])
+                  ["sel", "seln0", "seln1", "seln2", "seln3"] + regs("gg", a, e) + regs("ss", a, e), ["p4.u"])
                 V(ts(mask, T.p4[:, 128:128 + n], 254.0, None, A.is_lt), ["p4.u"], regs("p4.m", a, e))
-            when("write", a)
-            V(tt(T.fw[:, a:e], T.fd[:, a:e], mask, A.mult), regs("fd", a, e) + regs("p4.m", a, e), regs("fw", a, e))
-            V(gather(tt(T.tb[:].indirect(T.sl[:, c]), T.fw[:, a:e], T.of[:, a:e], A.add), n, SCATTER), ["sl"] + regs("of", a, e) + regs("fw", a, e), ["tb"])
-
-        for b, (a, e) in enumerate(BLOCKS):
-            n = e - a
-            c = slice(a // 16, e // 16)
-            d0 = T["d0%d" % b]
-            when("met", a)
-            zt = T.zt[0:n, 128 * b:128 * b + 128]
-            P(mm(T.p5[0:n, 0:128], (z[:, a:e], T.cid[:])), ["cid"] + regs(zn, a, e), ["p5.t"])
-            S(act(zt, T.p5[0:n, 0:128], AF.Copy), ["p5.t"], ["zt%d" % b])
-            when("cmp", a)
-            for s in range(a, e, 32):
-                pb = "p%d" % (s // 32 % 2)
-                spread, kk = (zt, T.ce[0:n, 16 * (s - a):16 * (s - a) + 512]), T.ss[:, 32 * s:32 * s + 1024:2]
-                if Q_MET[b] == "v":
-                    P(mm(T[pb][:], spread), ["zt%d" % b, "ce"], [pb])
-                    V(tt(T.ind[:, 16 * s:16 * s + 512], kk, T[pb][:], A.is_le), regs("ss", s, s + 32) + [pb], regs("ind", s, s + 32))
-                else:
-                    P(mm(T[pb][:], spread, (T.cidn[:], kk)), ["zt%d" % b, "ce", "cidn"] + regs("ss", s, s + 32), [pb])
-                    S(act(T.ind[:, 16 * s:16 * s + 512], T[pb][:], AF.Sign, bias=0.5), [pb], regs("ind", s, s + 32))
-            when("pass", a)
-            off = "cb2" if Q_MET[b] == "v" else "cbn"
-            P(mm(T.p3[:, a:e], (T[off][:], T.tg[:, 1, a:e]), *[(T.sel[:, 128 * k:128 * k + 128], T.ind[:, 16 * a + k:16 * e:16]) for k in range(16)]),
-              ["sel", off] + regs("goal", a, e) + regs("ind", a, e), regs("p3.c", a, e))
-            if Q_MET[b] == "v":
-                S(act(T.sg[:, a:e], T.p3[:, a:e], AF.Sign, bias=th[1]), regs("p3.c", a, e) + thn, regs("sg", a, e))
-            else:
-                S(act(T.sg[:, a:e], T.p3[:, a:e], AF.Sign, scale=0.5, bias=th[2]), regs("p3.c", a, e) + thn, regs("sg", a, e))
-            P(mm(T.p3[:, 192:192 + n], (T.ctm[:], T.sg[:, a:e])), ["ctm"] + regs("sg", a, e), ["p3.y"])
-            P(mm(T.p3[:, 192 + n:192 + 2 * n], (T.ctm[:], T.sg[:, a:e])), ["ctm"] + regs("sg", a, e), ["p3.w"])
-            S(act(T.oh[:, 2 * a:2 * e], T.p3[:, 192:192 + 2 * n], AF.Relu, scale=1024.0, bias=T.ohb[:]), ["p3.y", "p3.w", "ohb"], regs("oh", a, e))
-            l0, w = 384 + a // 8, n // 16
-            P(listmm(T.p7[:, l0:l0 + 2 * w], "selk", "oh", 2 * a, 2 * e, [(T.cid[:], T.bas[:, a // 8:e // 8]), (T.cidn[:], T.mal[:, c], T.p7[:, l0:l0 + w])]),
-              ["selk", "cid", "cidn", "basa%d" % b, "basb%d" % b] + regs("mal", a, e) + regs("oh", a, e), regs("p7.l", a, e))
-            V(tt(T.tm[:, c], mf[:, c], T.p7[:, l0:l0 + w], A.min), regs(mfn, a, e) + regs("p7.l", a, e), regs("tm", a, e))
-            S(act(T["ms%d" % t][:, c], T.tm[:, c], AF.Abs), regs("tm", a, e), regs("ms%d" % t, a, e))
-            if not lastt:
-                send("mr%d_%d" % (t + 1, b), T["ms%d" % t][:, c], T["mf%d" % (t + 1)][:, c], regs("ms%d" % t, a, e), regs("m%d" % (t + 1), a, e))
-            when("move", a)
-            V(ts(T.la[:, c], T.p7[:, l0 + w:l0 + 2 * w], 2.0 ** -10, None, A.mult), regs("p7.l", a, e), regs("la", a, e))
-            V(gather(tt(T.yy[:, a:e], d0[:].indirect(T.la[:, c]), z[:, a:e], A.subtract), n),
-              ["d0z%d" % b] + regs("la", a, e) + regs(zn, a, e) + regs("d0", a, e) + regs("cut", a, e) + regs("a15", a, e), regs("yy", a, e))
-            if Q_CLIP == "v":
-                V(ts(T.xx[:, a:e], T.yy[:, a:e], -255.0, None, A.max, rate=0.5), regs("yy", a, e), regs("xx", a, e))
-            else:
-                S(act(T.xx[:, a:e], T.yy[:, a:e], AF.Relu, bias=255.0), regs("yy", a, e), regs("xx", a, e))
-            P(mm(T.p2[:, 384:384 + n], (T.dd[:, 128 * t:128 * t + 128], T.oh[:, 2 * a:2 * a + n]), (T.cid[:], T.xx[:, a:e])),
-              ["dd%d" % t, "cid"] + regs("oh", a, e) + regs("xx", a, e), ["p2.z"])
-            zs = T.yzs if lastt else T["zs%d" % t]
-            S(act(zs[:, a:e], T.p2[:, 384:384 + n], AF.Abs, bias=0.0 if Q_CLIP == "v" else -255.0), ["p2.z"], regs("zs%d" % t, a, e))
-            if not lastt:
-                send("zr%d_%d" % (t + 1, b), zs[:, a:e], T["zb%d" % (t + 1)][:, a:e], regs("zs%d" % t, a, e), regs("z%d" % (t + 1), a, e))
+                when("new")
+                V(tt(T.fd[:, a:e], T.f4[:, a:e], T.of[:, a:e], A.subtract, rate=2.0), ["f4", "of"], regs("fd", a, e))
+                when("write", a)
+                V(tt(T.fw[:, a:e], T.fd[:, a:e], mask, A.mult), regs("fd", a, e) + regs("p4.m", a, e), regs("fw", a, e))
+                V(gather(tt(T.tb[:].indirect(T.sl[:, c]), T.fw[:, a:e], T.of[:, a:e], A.add), n, SCATTER), regs("sl", a, e) + ["of"] + regs("fw", a, e), ["tb"])
 
     for t in range(STEPS):
         step(t)
     t = STEPS - 1
     now[:] = [1000.0, -1, None, 0]
-    dma("y", T.ym[:], T["ms%d" % t][:], regs("ms%d" % t, 0, 192), ["ym"], "outm", 1600)
-    dma("s", T.yz[:], T.yzs[:], regs("zs%d" % t, 0, 192), ["yz"], "outz", 2000)
+    dma("y", T.ym[:], T.yo[:, :, 64:68], regs("zs%d" % t, 0, 192), ["ym"], "outm", 1050)
+    dma("s", T.yz[:], T.yo[:, :, 0:64], regs("zs%d" % t, 0, 192), ["yz"], "outz", 1200)
     behind.clear()
-    dma("y", T.ymc[:], T.tb[:, 0:512], ["tb"], ["ymc"], "outa", 2600)
+    dma("y", T.ymc[:], T.tb[:, 0:512], ["tb"], ["ymc"], "outa", 1500)
     emit()
     for s in ("outm", "outz", "outa"):
         g.wait_ge(T.sem[s], 16)
-    g.wait_ge(T.sem.snd, n_eng * sends[0])
+    g.wait_ge(T.sem.snd, n_out * sends[0])

@@ -9,61 +9,87 @@ F16 = "float16"
 I32 = "int32"
 U16 = "uint16"
 BLOCKS = [(128, 192), (64, 128), (0, 64)]
-MODS = [(64, 192), (0, 64)]
-GOALS = MODS
-TURNS = MODS
-USES = [(64, 192), (0, 64)]
-NEEDS = ["v s vs", "v vs s"]
-ADDS = ["s v vs", "s s s"]
-ON_V = "".split()
-Q_ML, Q_SAVE, Q_CUT, Q_MAL = "ggvg"
-ROWS = [0, 256, 448, 576]
-SAVE = 32 * 64
+PAIRED = [(64, 192), (0, 64)]
+USES = PAIRED
+PLAN = {"goal": BLOCKS, "mod": PAIRED, "lists": BLOCKS, "row": PAIRED, "ops": BLOCKS, "spread": BLOCKS, "head": BLOCKS, "scan": BLOCKS, "cmp": BLOCKS,
+        "needs": ["vs sv ss", "sv v v ss"], "adds": ["ss vv sv", "vs ss ss"],
+        "ml": "v", "save": "g", "cut": "g", "mal": "g", "hh": "s", "sl": "g", "la": "v", "masks": PAIRED[:1], "halve": True, "early": False, "ahead": [(0, 1, 2), (1, 2)]}
+MAIN, ZERO, MID = 64, 2112, 1600
 MAGIC = 1.5 * 2.0 ** 24
 BANKS = ["p%d" % b for b in range(8)]
 SCRATCH = {}
 for _names, _cols, _type in (
-        ("prw adw", 4096, B16), ("glw imw", 512, B16), ("mci", 512, I32), ("tb", 704, F32),
-        ("mi", 12, I32), ("dvs", 5, B16), ("wts", 1, B16), ("zb0", 192, B16), ("ze", 64, B16), ("zw", 68, F16),
-        ("d00 d01 d02", 2 * SAVE, B16), ("d1 ss", 6144, B16), ("ind", 3072, B16), ("ol", 192, U16), ("gg mb gi sg hh yy", 192, B16),
-        ("oh", ROWS[3], B16), ("zt", 128 * len(TURNS), B16), ("st", 128, B16), ("q1 q3", 192, F16), ("mal", 12, F16),
-        ("tm ys mf0", 12, F32), ("lst", 24, F32), ("acc sm", 2, F32), ("ev sum", 1, F32), ("thr", 8, F32), ("ml sl la", 12, U16),
-        ("of fd fw", 192, F32), ("f1 f2 f3 f4", 192, I32),
-        ("pi", 4, I32), ("pf", 4, F32), ("k37 kw kwa ohb qb1 qb3 pw", 1, F32), ("pwi iw", 16, F32), ("onf", 128, F32),
-        ("ie ce", 1024, B16), ("cbm", 8, B16), ("ig cid cidn cidm c37 cb cb2 cb6 cb43 cbn cbw cq1 cq3 tri wb onb lim ha hb", 128, B16),
-        ("isl sel seln", 2048, B16), ("dg dd", 640, B16), ("ic bl top", 12, F32), ("bas", ROWS[3] // 16, B16)):
+        ("prw adw", 4096, B16), ("glw imw", 512, B16), ("mci", 512, I32), ("tb", 1472, F32),
+        ("mi", 12, I32), ("dvs", 5, B16), ("dvf", 5, F32), ("wts", 1, B16), ("zb0", 192, B16), ("ze", 64, B16), ("zw", 64, F16),
+        ("d00 d01 d02 ft", ZERO + 16, B16), ("d1 ss", 3072, B16), ("ol", 192, U16), ("gg mb gi hh yy fd", 192, B16),
+        ("zt", 128 * 3, F16), ("q1 q3", 192, F16), ("mal", 24, F16), ("mf0", 12, F16), ("lst", 24, F32), ("acc", 3, F32), ("ev", 1, F32),
+        ("ml sl la", 12, U16), ("kr wk yo", 216, F32), ("zb1 zb2 zb3 zb4 zs1 zs2 zs3 zs4", 216, F16),
+        ("eb wd ws", 1280, F16), ("of dl fw", 192, F32), ("f1 f2 f3 f4", 192, I32),
+        ("pi", 4, I32), ("pf", 4, F32), ("kk k37 qb1 qb3 r16 g16 zbias cew l127 l63 h32", 1, F32), ("onf st", 128, B16), ("acb", 3, B16), ("c68", 68, F32), ("wi", 216, F32),
+        ("kb", 72, F16), ("ie", 512, B16), ("ce", 1024, B16), ("edge", 256, F16), ("ib", 256, B16), ("big", 144, B16), ("ic top", 12, F32),
+        ("ig cid cidn c37 cb cq1 cq3 wb onb c8kn c4k c384 c384n c512n bigp", 128, B16)):
     for _n in _names.split():
         SCRATCH[_n] = ("sbuf", [128, _cols], _type)
 SCRATCH["tg"] = ("sbuf", [128, 2, 192], F16)
-SCRATCH["yo"] = ("sbuf", [128, 3, 68], F32)
-SCRATCH["eb"] = ("sbuf", [128, 12, 128], B16)
-for _t in range(1, STEPS):
-    SCRATCH["zb%d" % _t] = ("sbuf", [128, 3, 72], F16)
-    SCRATCH["zs%d" % _t] = ("sbuf", [128, 3, 72], F16)
-SCRATCH["p0"] = ("psum", [128, 1024], F32)
-for _b in BANKS[2:]:
-    SCRATCH[_b] = ("psum", [128, 512], F32)
+SCRATCH["ind"] = ("sbuf", [128, 192, 18], B16)
+SCRATCH["thw"] = ("sbuf", [128, 4 * STEPS, 18], B16)
+for _b, _n in (("p0", 1024), ("p2", 1024), ("p4", 512), ("p5", 512), ("p6", 512), ("p7", 512)):
+    SCRATCH[_b] = ("psum", [128, _n], F32)
+PSUM = {"use": ("p4", 0), "old": ("p4", 192), "mask": ("p4", 384), "turn": ("p5", 0), "goal": ("p5", 256), "sum": ("p6", 0), "u": ("p6", 192),
+        "met": ("p7", 0), "z": ("p7", 216), "r": ("p7", 280), "list": ("p7", 344), "all": ("p7", 368)}
 LOADS = ["mc", "m0", "z0", "ad", "gl", "pr", "wt", "dv"]
-SEMAPHORES = ["cv", "cs", "ct", "cg", "outz", "outm", "outa", "snd"] + ["ld_" + n for n in LOADS]
-SEMAPHORES += ["ze"] + ["zr%d_%d" % (t, b) for t in range(1, STEPS) for b in range(len(BLOCKS))]
+SEMAPHORES = ["cv", "cs", "ct", "cg", "outa", "snd", "ze", "ebs", "wd0", "wd64"] + ["ld_" + n for n in LOADS] + ["out%s%d" % (x, b) for x in "zm" for b in range(len(BLOCKS))]
+SEMAPHORES += ["%sr%d_%d" % (x, t, b) for x in "zm" for t in range(1, STEPS) for b in range(len(BLOCKS))]
 
-CYCLE, PE_CYCLE, CALL, WAKE, LOOK = 0.83, 0.42, 20.0, 66.0, 0.19
-GATHER, SCATTER, SEND, FLIGHT = 1.56, 3.8, 570.0, 2300.0
-FIRST, PCALL, SCALL, GCALL = 3400.0, 0.0, 0.0, 40.0
+COST = {"cycle": 0.83, "pe": 0.42, "call": 55.0, "wake": 100.0, "gather": 1.56, "scatter": 3.8, "send": 570.0, "flight": 2300.0, "wire": 300.0,
+        "first": 3400.0, "pcall": 8.0, "scall": 15.0, "gcall": 60.0, "psum": 40.0}
+EARLY = {}
+PERIOD = 14.0
+PHASE = "0g0u0h0W7ubJ9r0IdA3Rd35ee1e7eLeFdUaTf2fWh9hs0c0e0f0d8g72cSf0dkab9Acp8786b05D5A0T1m8jhbda9N4e7R7W7x9u8ncQ8c8R60bC8F8r92bp9d1U3Nbr7ZctcPdbdNfcdobm98aJe0c0eI3D31blgges46djepcu9ycTe8eVe3fycxdXanafcy9DeMeAgKdSh2hci9gphWiwiBbVdvdPeBg3hjeWfOg0h0f9eXfYeEgFfAgidFfkflewg5fqfrhwhCi0hUhViqcrczccaYdudHdl8EaOb99payfefBeOf4a0aPdYbEc8d4dfe5cMcWeRcBf7c6dreYeDfdetezgDeihtdggnfofHgPfzgJc1fT7hi6cedWbvdRhihzc5bOcwcl9T5VePdVegdmdGb2edddbaejdOdL97aEbsbTdp4kaFaGaKcOhrffgBhyf3eKfLg4huhDgtfIg6f5fxeQene9gkfjfifpfUfDgwiifMgLh5fVgQgvh1f8gWhqhvgMibkwjohJizjnjmjli2iDiKjHhnjtcVdIcddBdDdCdte4gbg99hfueZfghkhZdyftfXgagmhmd2dz4adig1cEotj6idk8wteHeSf1exeJfafCfZgcgydZgHhSgjicimhXiviohgihhlgzhPiyiFbBcN9ZeNcFaZfb1Ld0e2d1gogRcXadcn85eueaeqecfQgxhNh6i1ixfFbigrgSarfRj9ijiPhagXgdfKhFiRjehOh7iShLhMi5jkjMjTiH"
+_OLD5 = "0k0o0m0l1vbU9B0nd92bcq3Gerekecf4dWeuf8fZgaho5Q5h6F5L8O7WdXf2efa88ueB8v86bL6J6P3y7iaohC9Lbf0p717n7fb2bt8I9AaL7ZdV91araJbNaw426N5T3YcmcpaqfChkfBdpcjbieqeSeU4Z7Pdlghf75NcVepegaVdkbMcidsfEeDed99cacXcSb6eVibg0gwjLhMiwiOcBc8afcfd4dQfbeHgfdmfPglgnhgfOgrfSdDePfyfIeCgyfofTgcj7hJhxiZgei2gdidcEdfc6bqdZdOdNe9abbK7U5WeIg6fufGcg9Te49zbnen94eXc3dEdCd8fnczdIfhebfsf0f6hbgthUeEgYhrgghug9h2cdgDcZipcRaXccfzeyhAcnc5dndh8S7dfdeseWdFe2apeRdudKeAelbId29MbAcodT15aSctaDbzfjeLgIh9eJfwfNg7gXhGethfeifxfmg3g1flgFg5fAgufVfRiYf9b8hpdxhHgNgZfqheh7evhshnk0kehOiHiLh4i1hvkxj0jcjlhQjRdjejcydedbe1dzeNg8gEeYfFeQfQhNiCfYbufJgigRgVcscT5EbHimgPmDtelgnlrLeOdBewf1fafvgve8gMgJgTh1h0iGi4hPdLiFi3hiikhwiagKi6iXbOdi95fedH4bfrdwd7eMd5ckeodMdvcF7yeKeegLezh5gGftgbe6gQisiIfDfHjefii8hmjhjriNhcjohzhIhRk3k5k9gp"
+_OLD4 = "0j0M0h0f84bZ8Z0idu2vdF4Pe9eFe7ew7aaTfygcffhF0e0d0b0c8H7QdyfudH9wa4do9L9Fb75C7G0v0g98hjebbh6h8i8k7Fbe8Bbd97997Icp9O9M9gab9H1N7Tcm8Cc3c5bpdAgQf1c1a3c0e1eeeA4442ddgjfa58cs8henbJejdtbSdUemcxdq71czdRdje8cRhPfvg5iahTisiGdxdCf6eSgdhgfGfVfFgMfdfIfCfHgyfegGeyfOfBdsfifXhahzhnhZhVioetcncPcdc9dEdNdmdlaJbt9GaAfnfPeGfrbBbLdP8QcedkaGelcKaseLcXfpdaeqeXbgf8eoeCgKefhefzgkfRgqh7fQgSc4gf7KhxaQe5dzf9gZhEbobUcQcv9T7Mf0e2dpdrdGb9eidicZdfdQc6969Y9kc7cN45byac93cceJeTgEcSeEeKfLdMh8hIgBfAfof2fqfwdWf4glfWfDg2g7fNhDhwcLgOgYdIeYgwgAezh0eghpgXjOjJjmgxi0jjjtjgjhixiBj1j9jkcMdOc8dJd8dKd1ecfKgnawbDeRfEh9i8e0fbgegCgHgLcicq52dYg3g4nIkhhAkUwgepeaeQeBeWfhg0bAgigIgrgPi3hKi9ifeDiwh4gti4h5joiEgVj7bwd59XeZcTb0fs1UdveIeNf7h1d2a9cgbFeMerf5dLgUgzhHg8hch2i6iues9zhigDcahbiNhXi1iygRhoiJjbhRhliLg9hUibjdhhjuhM"
+_OLD3 = "150p0x0z7NbQbY0wdh84cu8Xe7eLe1f3cbbefxbxcfhv0q0s0t0u947YdcfecH8D8eeibn8E9Q6v7J0Q4M95gYew9V45680y8Kbt4paJaF8H8OdX9R9IagbKbv3p83da53cBbZ9Eejfkbjd9ctcddVepey4j6ReeeSeZ4Vcidtefbrd7dPaKdSeJdzaVe6c9dUeld8drh0cRhWijhzitiEdydje4fGdOgRflfWgffAenfKfLexeOfwgbfggwgsfvfCeEh2gpgehRhTh7ipbWcnbRcwdkdDcMdo9Oboa09GfmfyfqfM8W54e8au9udB9Peacm9HcEdNePd6eqecf6fXdKeTeNeVgyfsfpfDg5gVdMgFbDfddQhYbzdLbMaWgChqbpbTc5co9e7PdReocxd5dEaxe9cKd1f7dJdHdd9XbIc0dn4Fave5b0anhUeFfEgEfuetcyf2evhxg7f89weMf0gmaTcOffeBbwfjfIeHhnhjesgqgxdCgrgl6wdGh1fnhogGjHiQiDhygDgUi7iPjKhLiwifhgiNdedIc3dsd0dFdqdYfZg6b1c4fBfQgNiufbg0fNgceKgubqdb0v87h3jylihHmYcNoVeIdZc1fceuf48Ld2fYgighg9i8hSgoixi5irhfgzhOh4fthmfOiCbscz9meAc8b5ez4ob7eDe3gngZdicLcG9seddTgjeWgBfSemgQi2iFggeCbcfogMgkeGgTiShPinjzdAhaikiahbhsi0hhhNi1jsjCjgjJ"
+_OLD2 = "2G3765647Qbhaw54cAaL8U9Yd0dWdmdUbab8eAehgpgaXSXJYmXT8X8Kcf9kcu808t9laU8laQ820d4D8r9Afsd7bg8L6q8sah9jaS8Z9w8na09H9h9gabav9G6K817g6ebpbmc3dXcyaiaxaYb7d2dwbu6I7ecV7qdv6DcodxaI9ocxdqag95embrbUbbae6na59UcQereRgThqgZhAhOdjcYdBd5cbfDexeDeyf8dLf2ekdKejdJdPdddRdzdfeJf9e7g4g5fUgBghfw9Vc8bNbTc9cjaVbW8aaTaBa7d8ewdee88Gc1dradbtcRcic2cIcEdh9feoaMbdd1cTePdacNfvfagRfefGezeTfTeSftbkc0dygQaccWdGeeeifgbcbjbSbn7B8zcSd6cwbIcC9pctbQckcacUd4dn9ybebHdc8jascBbfbRcPcneFf0bFdbdZe5dYgqeYeLdte0dEcObwbEdodVe6eGeqeagcgEg8amdQfKg6g3dAfFebfEf6fQi6i7ineHhkgYhshxiIhIfLhLhRhNbKcDbYbXdIczcHf4eQdNeOdTffgmgvgFdlfueUfcg1eEgb8dbC6pcZdOedlPhzglhXise1dkdu9vdFb2alfofMeXf3dMgIfOgJhnh3fzgLfpfBeChugwhDh2b4bO9id3bZaKd99FcmegdCfVfS7FcJcdaNcLcvese9eVdpcXf5gGh7gAgriehFgCfRhbgth1hCfdhBigh5"
+_OLD = "7f7wa99Mg79O6HfiebgFdShRi2hSfXitj8jsjZlg4v5d623W2u5jdvcUcRcVcQdtdedxa5a0589D7HiJdGh1bFcfflbHbTdrdKezffcv926Q7h6d5e6edQbnbCfT9ZeWfRe27FkadWdu7I64gkgmgT9bbqfkavgdapi7g9gYhEi8jghsi6j9jFjhh9hKhXljhekbgsemhTiyk5lukOkBjHjyliktkolkiah2hghAhOi9hUhGjNjdg2kll7lcl4lmeqf2dgerepgyg39jg1gjfPg4iSgginjneAfKfAeLfBdDfZihgShjeBh0hngrhWj6jaizgtiYiuiDjSiojcjEiHlhjikJhafujoeXk4lxhyifgQikkgee9Cf7bU8LeyfxfQ8Ki1iKgWdFfCfYgldEeJeVfmf5fDgugIhmhufqfWhDgZgzjufEiVjqkid9i5eFiUiclCijj5ivibhMhYjek0kIk6jbiCiFhJiiimiIkdjvghiwjVhzlFkuhQjXk7kekfjpkNkThxgJj3kUneninhn9kQmJhHkSmSmQmgncmKn3eZgUhhgnidgRk1h5jCixiRjlk3j4jGlfkzfMkylykmcIgLfyiPmMn1ltmwgwknhPhdhFi4fNfvjjbPiQiMeUkAkrirkCkDmIiZm6l9mklNj7lUmDmUlMcufjcyeSfFiNePfLi3ish7hChBgPiGkZgcedh4gojPhljwkpdIkqiLlzlamvm1mGk9kKnul6kcmonlnonxmT"
+DUE = {"lists1": -4, "room1": -4, "keep1": -3, "lists3": -2.5, "room3": -2.5, "keep3": -1, "row3": -2.4, "goal3": -2.5, "mod3": -2.3, "spread3": -2.2,
+       "row1": -3.9, "goal1": -4, "mod1": -3.8, "spread1": -3.7, "ops1": -0.6,
+       "fill1": -1, "ops3": -0.5, "adds0": -0.05, "adds1": 0, "needs0": -0.05, "needs1": 0, "head1": -0.2, "scan1": -0.2, "less1": -0.2, "cmp1": 1, "pass1": 1, "move1": 1,
+       "needs2": 1.5, "adds2": 1.4, "adds3": 1.5, "needs3": 2.5, "head3": 1.2, "scan3": 2, "fill3": 2, "less3": 2, "cmp3": 2.5, "pass3": 2.6, "move3": 2.6,
+       "lists5": 2.7, "room5": 2.7, "row5": 2.8, "goal5": 2.8, "mod5": 2.9, "spread5": 2.9, "keep5": 5, "ops5": 2.6, "adds4": 3.9, "adds5": 4, "needs4": 4.9, "needs5": 5,
+       "head4": 4.4, "head5": 4.5, "scan4": 4.4, "scan5": 4.5, "fill4": 4.4, "fill5": 4.5, "less4": 4.4, "less5": 4.5, "cmp4": 4.9, "cmp5": 5, "use5": 5, "write5": 5.5,
+       "pass5": 6, "move5": 6,
+       "first3": 3.5, "place3": 5.2, "first5": 5.3, "place5": 5.35, "new5": 5.1, "use3": 5, "write3": 5.4, "count5": 7,
+       "const0": -9, "const1": -8, "const2": -7, "const3": -6, "const4": -1, "const5": 3, "const6": 4, "out1": 1, "out3": 2.6, "out5": 6, "out9": 6}
 ORDER, DAG = [], []
-PERIOD = 17.1
-DUE = {'place': (-15.5, -3.2, -18.1), 'lists': (-30.3, -32.7, -14.9), 'ops': (-11.3, -19.0, -16.2), 'adds': (-0.8, -2.9, 8.6, -3.1, -0.4, 3.5), 'needs': (-3.4, 1.9, 9.2, 3.6, -3.4, 6.4), 'scan': (-19.3, -6.9, -20.0), 'goal': (-34.6, -17.3, -24.9), 'mod': (-6.0, -22.8, -19.5), 'first': (1.8, 2.0, -4.2), 'count': (26.5,), 'room': (-18.5, -23.6, -25.4), 'lost': (-28.5, -17.8, -17.3), 'new': (8.7,), 'use': (11.3, -5.7, -35.7), 'write': (0.7, 21.2, -32.3), 'met': (-23.1, -11.5, -31.7), 'cmp': (-17.8, -13.7, -21.6), 'pass': (-26.6, -28.3, -19.9), 'move': (-26.2, -33.4, -37.6), 'spread': (-18.6, -19.5, -22.8), 'dist': (38.2,), 'row': (-28.1, -18.8, -25.0), 'place0': (-29.0, -22.2, -9.6), 'lists0': (-53.2, -63.3, -63.9), 'ops0': (-63.9, -47.0, -78.9), 'adds0': (-47.1, -44.7, -35.6, -48.4, -59.5, -45.5), 'needs0': (-45.3, -47.2, -31.7, -47.5, -42.9, -26.9), 'scan0': (-62.7, -34.5, -20.1), 'goal0': (-36.2, -44.2, -30.5), 'mod0': (-36.3, -27.5, -17.7), 'first0': (-37.2, -47.2, -22.8), 'count0': (11.4,), 'room0': (-15.8, -12.3, -3.3), 'lost0': (-34.0, -42.8, -22.4), 'new0': (-15.3,), 'use0': (-26.2, -20.6, -30.3), 'write0': (-6.6, -1.3, -18.5), 'met0': (-52.6, -39.9, -13.2), 'cmp0': (-46.7, -26.7, -10.6), 'pass0': (-41.8, -38.1, -16.8), 'move0': (-49.6, -42.5, -28.9), 'spread0': (-47.3, -31.3, -24.8), 'dist0': (-38.5,), 'row0': (-43.3, -39.3, -32.6), 'ahead0': (-20.4,), 'c1': (-68.9,), 'c2': (-67.4,), 'c3': (-41.5,), 'c4': (-36.8,), 'c5': (-37.5,), 'c6': (-10.4,), 'c7': (-55.7,), 'c8': (-58.8,), 'c9': (-35.9,), 'c10': (21.1,)}
-OLD2 = {'place': (-14.0, -11.6, -19.6), 'lists': (-30.3, -32.7, -15.7), 'ops': (-11.5, -19.9, -16.2), 'adds': (-0.8, -2.9, 8.6, -3.8, -0.4, 3.5), 'needs': (-1.4, 1.9, 9.2, 3.6, -3.4, 5.6), 'scan': (-19.3, -6.9, -19.0), 'goal': (-34.6, -17.3, -28.4), 'mod': (-15.1, -22.8, -18.8), 'first': (2.9, 2.4, -1.9), 'count': (24.9,), 'room': (-16.9, -23.4, -25.4), 'lost': (-23.5, -17.8, -17.3), 'new': (8.7,), 'use': (11.3, -5.7, -36.8), 'write': (-0.5, 18.0, -32.3), 'met': (-25.9, -14.4, -31.7), 'cmp': (-20.3, -13.7, -21.6), 'pass': (-27.4, -28.3, -20.2), 'move': (-26.2, -33.4, -36.4), 'spread': (-21.5, -19.5, -22.8), 'dist': (36.7,), 'row': (-28.1, -20.5, -25.0), 'place0': (-30.3, -20.6, -9.1), 'lists0': (-55.6, -65.3, -63.8), 'ops0': (-63.9, -47.0, -78.9), 'adds0': (-47.6, -44.7, -36.8, -44.7, -59.5, -44.9), 'needs0': (-43.2, -47.2, -30.6, -47.5, -42.9, -26.9), 'scan0': (-64.0, -34.5, -20.1), 'goal0': (-36.9, -44.2, -32.2), 'mod0': (-36.3, -27.5, -17.7), 'first0': (-32.2, -47.2, -21.4), 'count0': (14.3,), 'room0': (-18.1, -14.1, -3.3), 'lost0': (-32.8, -42.9, -18.9), 'new0': (-12.3,), 'use0': (-26.2, -20.6, -30.3), 'write0': (-6.6, -1.1, -18.2), 'met0': (-52.6, -41.7, -16.7), 'cmp0': (-46.7, -29.0, -8.3), 'pass0': (-42.8, -41.2, -19.7), 'move0': (-49.6, -41.8, -28.9), 'spread0': (-47.3, -24.7, -27.0), 'dist0': (-35.3,), 'row0': (-43.3, -39.3, -32.7), 'ahead0': (-19.0,), 'c1': (-68.5,), 'c2': (-69.5,), 'c3': (-40.8,), 'c4': (-36.8,), 'c5': (-37.5,), 'c6': (-13.1,), 'c7': (-55.7,), 'c8': (-56.0,), 'c9': (-36.1,), 'c10': (18.9,)}
-OLD1 = {'place': (-17.2, -14.9, -21.9), 'lists': (-23.2, -25.1, -18.8), 'ops': (-12.7, -23.6, -15.3), 'adds': (0, -3.2, 1.4, -1.3, 1.1, 4.2), 'needs': (-4.0, 0.3, 6.6, -0.3, 1.3, 5.1), 'scan': (-16.3, -11.5, -17.0), 'goal': (-27.0, -22.5, -20.4), 'mod': (-22.7, -20.6, -20), 'first': (-5.3, -10.5, -10.6), 'count': (20.4,), 'room': (-22.3, -20.6, -22.7), 'lost': (-22.9, -20, -11.2), 'new': (4.6,), 'use': (5.7, -2.1, -35.0), 'write': (3.9, 12.0, -30.1), 'met': (-23.4, -10.3, -19.8), 'cmp': (-12.7, -12.4, -14.0), 'pass': (-26.7, -26.9, -21.9), 'move': (-23.0, -28.4, -27.5), 'spread': (-19.6, -19.8, -19.7), 'dist': (21.7,), 'row': (-21.7, -20.2, -21.0), 'place0': (-27.5, -23.7, -14.6), 'lists0': (-60.3, -60.8, -67.5), 'ops0': (-63.8, -56.5, -73.7), 'adds0': (-47.8, -47.2, -45.1, -50.0, -53.2, -48.4), 'needs0': (-45.4, -50.9, -30.9, -42.4, -47.2, -35.2), 'scan0': (-49.7, -34.5, -27.7), 'goal0': (-40.7, -42.7, -29.3), 'mod0': (-35.3, -35.2, -20.6), 'first0': (-26.9, -39.6, -24.7), 'count0': (6.3,), 'room0': (-16.1, -11.8, -10.9), 'lost0': (-25.9, -40.9, -27.1), 'new0': (-15.6,), 'use0': (-18.7, -19.9, -31.1), 'write0': (-12.4, -9.7, -24.4), 'met0': (-44.4, -48.4, -24.9), 'cmp0': (-46.0, -29.8, -7.1), 'pass0': (-44.4, -35.7, -19.2), 'move0': (-45.1, -37.7, -30.0), 'spread0': (-47.1, -38.1, -27.3), 'dist0': (-31.4,), 'row0': (-38.3, -40.7, -34.5), 'ahead0': (-28.1,), 'c1': (-64.7,), 'c2': (-65.9,), 'c3': (-44.7,), 'c4': (-41.4,), 'c5': (-36.1,), 'c6': (-19.1,), 'c7': (-53.1,), 'c8': (-53.1,), 'c9': (-44.4,), 'c10': (15.6,)}
+
+
+def kind(o):
+    t, what, b = o["cls"]
+    return "%s%d%s" % (what, b, "'" * (t == 0))
+
+
+def sort(o):
+    return kind(o) + (o["q"] if o["fn"] else "")
+
+
+def names(calls):
+    seen, out = {}, []
+    for o in calls:
+        k = (o["cls"][0], sort(o))
+        seen[k] = seen.get(k, 0) + 1
+        out.append(k[1] + (str(seen[k]) if seen[k] > 1 else ""))
+    return out
 
 
 def scheduler(g, T, now):
     queues = {"g": g, "v": g.vector, "s": g.scalar, "t": g.tensor, "y": g.sync}
     calls = []
+    WAKE = COST["wake"]
 
     def op(q, call, r=(), w=(), ext=None, after=None):
-        calls.append({"q": q, "fn": call[0], "ns": call[1], "late": call[2] if len(call) > 2 else 0.0, "r": list(r), "w": list(w), "ext": ext,
-                      "after": after, "due": now[0], "cls": tuple(now[1:]), "banks": {x[:2] for x in list(r) + list(w) if x[:2] in BANKS}})
+        banks = {x[:2] for x in list(r) + list(w) if x[:2] in BANKS}
+        calls.append({"q": q, "fn": call[0], "ns": call[1] + COST["psum"] * (q in ("v", "s") and len(banks) > 0), "late": call[2] if len(call) > 2 else 0.0,
+                      "r": list(r), "w": list(w), "ext": ext, "after": after, "cls": tuple(now), "banks": banks})
         return len(calls) - 1
 
     def needs(ops, banks):
@@ -95,7 +121,8 @@ def scheduler(g, T, now):
         for i, n in enumerate(left):
             if n == 0:
                 ready.setdefault(calls[i]["q"], []).append(i)
-        free, bank, start, out, clock = {}, {}, {}, [], {}
+        free, start, out, clock = {}, {}, [], {}
+        bank = {x: (None, 0.0) for x in BANKS}
 
         def eta(u, depth):
             t = can[u]
@@ -108,45 +135,45 @@ def scheduler(g, T, now):
 
         def urgent(q, i):
             found = [j for j in ready[q] if due[j] < due[i]]
-            seen, front = set(), [j for k, r in ready.items() if k != q for j in r]
+            seen, front = set(), [j for k, r in ready.items() if k != q for j in r if due[j] < due[i]]
             for _ in range(3):
-                behind = []
-                for u in (u for j in front for u in users[j]):
-                    if u not in seen:
-                        seen.add(u)
-                        if calls[u]["q"] != q:
-                            behind.append(u)
-                        elif due[u] < due[i]:
-                            found.append(u)
-                front = behind
+                behind = {u for j in front for u in users[j] if due[u] < due[i]} - seen
+                seen |= behind
+                found += [u for u in behind if calls[u]["q"] == q]
+                front = [u for u in behind if calls[u]["q"] != q]
             return found
 
         def first(i):
-            o = calls[i]
-            t = max(can[i], free.get(o["q"], 0.0))
-            for x in o["banks"]:
-                for k, e in bank.get(x, {}).items():
-                    if k != o["q"] and e + WAKE > t:
-                        t = e + WAKE
+            t = can[i]
+            for x in calls[i]["banks"]:
+                k, e = bank[x]
+                if e > t and k != calls[i]["q"]:
+                    t = e
             return t
         while len(out) < len(calls):
-            t, q = min(((max(min(first(i) for i in r), clock.get(q, 0.0)), q) for q, r in ready.items() if r), key=lambda x: x[0])
-            i = min((j for j in ready[q] if first(j) <= t + 1), key=lambda j: (due[j], j))
-            if q and calls[i]["ns"] > 150:
+            t = 1e18
+            for k, r in ready.items():
+                if r:
+                    x = max(min(map(first, r)), clock.get(k, 0.0), free.get(k, 0.0))
+                    if x < t:
+                        t, q = x, k
+            can_go = [j for j in ready[q] if first(j) <= t + 1]
+            i = min(can_go, key=lambda j: due[j])
+            if q and calls[i]["ns"] > 300:
                 soon = min([first(u) if left[u] == 0 else eta(u, 3) for u in urgent(q, i)] + [1e18])
                 if t < soon < t + look * calls[i]["ns"]:
-                    short = [j for j in ready[q] if first(j) <= t + 1 and t + calls[j]["ns"] <= soon + 30]
+                    short = [j for j in can_go if t + calls[j]["ns"] <= soon + 30]
                     if not short:
                         clock[q] = min([soon] + [x for x in map(first, ready[q]) if x > t + 1])
                         continue
-                    i = min(short, key=lambda j: (due[j], j))
+                    i = min(short, key=lambda j: due[j])
             o = calls[i]
-            start[i] = max(first(i), t)
-            end = start[i] + o["ns"]
+            start[i] = t
+            end = t + o["ns"]
             if q:
                 free[q] = end
             for x in o["banks"]:
-                bank.setdefault(x, {})[q] = end
+                bank[x] = (q, end + WAKE)
             out.append(i)
             ready[q].remove(i)
             for u in users[i]:
@@ -164,8 +191,28 @@ def scheduler(g, T, now):
             for i, p in enumerate(pre):
                 for d in p:
                     users[d].add(i)
-            DAG.append((calls, pre, users, place))
-            ORDER[:] = place([o["due"] for o in calls], pre, users, LOOK)[0]
+            chain = [0.0] * len(calls)
+            for i in range(len(calls) - 1, -1, -1):
+                chain[i] = calls[i]["ns"] + calls[i]["late"] + WAKE + max([chain[u] for u in users[i]] + [0.0])
+            due = [1000 * (PERIOD * o["cls"][0] + DUE.get(kind(o), DUE.get(kind(o)[:-1], 0.0))) - chain[i] / 1000 - EARLY.get(sort(o), 0.0) for i, o in enumerate(calls)]
+            DAG.append((calls, pre, users, place, due))
+            if PHASE:
+                AB = "0123456789abcdefghijklmnopqrstuvwxyzABCDEFGHIJKLMNOPQRSTUVWXYZ"
+                ks = sorted(set(names(calls)))
+                phase = {k: ((AB.index(PHASE[2 * i]) * 62 + AB.index(PHASE[2 * i + 1]) + 800) % 3844) * PERIOD / len(ks) for i, k in enumerate(ks)}
+                key = [PERIOD * max(0, o["cls"][0]) + phase[n] for o, n in zip(calls, names(calls))]
+                left = [len(p) for p in pre]
+                ready = [i for i, n in enumerate(left) if n == 0]
+                while ready:
+                    i = min(ready, key=lambda j: (key[j], j))
+                    ready.remove(i)
+                    ORDER.append(i)
+                    for u in users[i]:
+                        left[u] -= 1
+                        if left[u] == 0:
+                            ready.append(u)
+            else:
+                ORDER[:] = place(due, pre, users, EARLY.get("look", 1900) / 1e4)[0]
         return [calls[i] for i in ORDER]
 
     def emit():
@@ -238,22 +285,31 @@ def size(ap):
 
 
 def shares(plan):
-    out = []
-    for b, ((a, e), word) in enumerate(zip(BLOCKS, plan.split())):
-        out += [(b, a, e, word, 0)] if len(word) == 1 else [(b, a + 32, e, word[0], 0), (b, a, a + 32, word[1], 1)]
+    out, e, before = [], 192, " "
+    for x in plan:
+        if x != " ":
+            out[len(out) - (x == before):] = [(e - 32, out[-1][1] if x == before else e, x)]
+            e -= 32
+        before = x
     return out
+
+
+def down(a, n, step=1):
+    stop = a - n * step
+    return slice(a, stop if stop >= 0 else None, -step)
 
 
 def rank_program(g, core, T, topo):
     rank = T.rank_of(core)
     if rank is None:
         return
-    now = [-1000.0, -1, None, 0]
+    now = [-1, None, 0]
     op, emit = scheduler(g, T, now)
     nxt = T.cores[(rank + 1) % len(T.cores)]
     mask_out = topo.mask(core, nxt)
     n_out, n_in = len(topo.engines(core, nxt)), len(topo.engines(T.cores[rank - 1], core))
     rid, pid = topo.addr(nxt)[:2]
+    CYCLE, CALL = COST["cycle"], COST["call"]
 
     def V(fn, r=(), w=()):
         op("v", fn, r, w)
@@ -279,33 +335,31 @@ def rank_program(g, core, T, topo):
     def cp(out, a, rate=1.0):
         return (lambda Q: Q.tensor_copy(out, a)), ns(size(out), rate)
 
-    def act(out, a, f, **k):
-        return (lambda Q: Q.activation(out, a, f, **k)), ns(size(out)) + SCALL + 20.0 * ("accum_out" in k)
+    def scan(out, a, b, o0, o1, rate):
+        return (lambda Q: Q.tensor_tensor_scan(out, a, b, 0.0, o0, o1)), ns(size(out), rate)
 
-    def either(name, out, a, f, scale, bias, v, r, w):
-        if name in ON_V or name + w[0][-2:] in ON_V:
-            V(ts(out, a, *v), r, w)
-        else:
-            S(act(out, a, f, scale=scale, bias=bias), r, w)
+    def act(out, a, f, **k):
+        return (lambda Q: Q.activation(out, a, f, **k)), ns(size(out)) + COST["scall"] + 20.0 * ("accum_out" in k)
 
     def ms(out, c, rate=0.5):
         return (lambda Q: Q.memset(out, c)), ns(size(out), rate)
 
-    def gather(call, n, rate=GATHER, q="v"):
-        return call[0], 50 + (15 + SCALL) * (q == "s") + n * rate * CYCLE + CALL
+    def gather(call, n, rate=COST["gather"], q="v"):
+        return call[0], 70 + 15 * (q == "s") + n * rate * CYCLE
 
-    def mm(out, *terms):
+    def mm(*groups, start=True, stop=True):
         def fn(Q):
-            for i, x in enumerate(terms):
-                ins = Q.matmul(x[2] if len(x) > 2 else out, x[0], x[1], i == 0, i == len(terms) - 1)
+            for x in groups:
+                for i, y in enumerate(x[1:]):
+                    ins = Q.matmul(y[2] if len(y) > 2 else x[0], y[0], y[1], start and i == 0, stop and i == len(x) - 2)
             return ins
-        return fn, sum(max(min(64, size(x[0])), size(x[1])) for x in terms) * PE_CYCLE + PCALL * len(terms)
+        return fn, sum(max(min(64, size(y[0])), size(y[1])) * COST["pe"] + COST["pcall"] for x in groups for y in x[1:])
 
     def iota(out, pattern, base=0, cm=0):
-        return (lambda Q: Q.iota(out, pattern, base, cm, allow_small_or_imprecise_dtypes=True)), 130 + GCALL + 2 * size(out) * CYCLE
+        return (lambda Q: Q.iota(out, pattern, base, cm, allow_small_or_imprecise_dtypes=True)), 130 + COST["gcall"] + 2 * size(out) * CYCLE
 
     def pick(out, a, pattern, o, cm):
-        return (lambda Q: Q.affine_select(out, a, pattern, o, 0.0, 0, cm)), 170 + GCALL + 2 * size(out) * CYCLE
+        return (lambda Q: Q.affine_select(out, a, pattern, o, 0.0, 0, cm)), 170 + COST["gcall"] + 2 * size(out) * CYCLE
 
     def move(out, a):
         return pick(out, a, [[0, size(out)]], A.is_ge, 0)
@@ -315,330 +369,346 @@ def rank_program(g, core, T, topo):
 
     behind = {}
 
-    def dma(q, out, a, r, w, sem, late):
-        behind[q] = op(q, ((lambda Q: Q.dma_start(out, a)), 100.0, late), r, w, (sem, 16, True), behind.get(q))
+    def dma(q, out, a, r, w, sem, late, n=1):
+        behind[q] = op(q, ((lambda Q: Q.dma_start(out, a)), 100.0, late), r, w, (sem, 16 * n, True), behind.get(q))
 
     for q, name, buf, late in (("s", "m0", "mi", 1050), ("y", "mc", "mci", 1800), ("y", "ad", "adw", 3600), ("s", "gl", "glw", 1350), ("s", "z0", "zb0", 1400),
                                ("s", "wt", "wts", 1400), ("s", "dv", "dvs", 1400), ("y", "pr", "prw", 5400)):
         dma(q, T[buf][:], T[name][:], [], every("z0") if name == "z0" else [buf], "ld_" + name, late)
+    behind.clear()
 
-    def const(what):
-        now[:] = [DUE[what][0], 0, what, 0]
-    kkf, grf, odf, hf = [T.pf[:, i:i + 1] for i in range(4)]
-    const("c1")
-    G(((lambda Q: Q.iota(T.pi[:], [[0, 4]], 0, 1)), 140.0), [], ["pi"])
-    G(iota(T.ig[:], [[1, 8], [0, 16]]), [], ["ig"])
+    def const(b):
+        now[:] = [0, "const", b]
+
+    def scaled(out, a, scale, bias, r, w):
+        S(act(out, a, AF.Copy, scale=scale, bias=bias), r, w)
+
+    def fill(out, c, r, w):
+        scaled(out, T.onb[0:out.shape[0], 0:size(out)], c, 0.0, ["onb"] + r, w)
+    const(0)
+    k4, grf, odf, hf = [T.pf[:, i:i + 1] for i in range(4)]
+    for i, cm in enumerate((64, 1, 512, 16)):
+        G(((lambda Q, i=i, cm=cm: Q.iota(T.pi[:, i:i + 1], [[0, 1]], 0, cm)), 130.0 + COST["gcall"]), [], ["pi%d" % i])
+    V(ts(T.pi[:], T.pi[:], 4, 63, A.arith_shift_right, A.bitwise_and), ["pi0", "pi1", "pi2", "pi3"], ["pi"])
+    V(cp(T.pf[:], T.pi[:]), ["pi"], ["pf"])
     V(ms(T.onb[:], 1.0), [], ["onb"])
     G(pick(T.cid[:], T.onb[:], [[-1, 128]], A.is_equal, 1), ["onb"], ["cid"])
-    for i, (c, o) in enumerate(((15, A.bitwise_and), (4, A.arith_shift_right), (1, A.bitwise_and), (63, A.bitwise_and))):
-        V(ts(T.pi[:, i:i + 1], T.pi[:, i:i + 1], c, None, o), ["pi"], ["pi%d" % i])
-    V(cp(T.pf[:], T.pi[:]), ["pi0", "pi1", "pi2", "pi3"], ["pf"])
+    G(iota(T.ig[:], [[1, 8], [0, 16]]), [], ["ig"])
     V(ts(T.cb[:], T.ig[:], grf, None, A.is_equal, rate=0.5), ["ig", "pf"], ["cb"])
-    const("c7")
-    G(iota(T.imw[:, 0:256], [[1, 256]]), [], ["imwa"])
-    G(iota(T.imw[:, 256:512], [[1, 256]], -256), [], ["imwb"])
-    const("c8")
-    for i in range(4):
-        G(iota(T.isl[:, 512 * i:512 * i + 512], [[-100, 4], [1, 8], [100, 16]], -400 * i), [], ["isl%d" % i])
-    V(ts(T.sel[:], T.isl[:], grf, None, A.is_equal, rate=0.5), ["isl0", "isl1", "isl2", "isl3", "pf"], ["sel"])
-    const("c2")
-    for b, (a, e) in enumerate(BLOCKS):
-        V(ms(T["d0%d" % b][:, 1:SAVE:2], 0.0), [], ["d0z%d" % b])
-        S(act(T.d1[:, 6144 - 32 * e:6144 - 32 * a:2], T.d00[:, 1:SAVE:2], AF.Copy), ["d0z0"], regs("r15", a, e))
-    const("c3")
-    V(ts(T.qb1[:], odf, 2560.0, -1280.5 + 2.0 ** -13, A.mult, A.add), ["pf"], ["qb1"])
-    V(ts(T.qb3[:], odf, 2560.0, -1280.5 + 2.0 ** -10, A.mult, A.add), ["pf"], ["qb3"])
-    for name, src, c in (("cidn", "cid", -1.0), ("c37", "cid", 37.0), ("cb6", "cb", -6 / 16), ("cq1", "cb", -256.0), ("cq3", "cb", -32.0)):
+    for name, src, scale, bias in (("kk", k4, 0.25, 0.0), ("k37", k4, 296.0, -2.0 ** 18), ("r16", k4, -4.0, 0.0), ("g16", grf, 16.0, 15.0), ("l127", k4, -0.25, 127.0),
+                                   ("l63", k4, -0.25, 63.0), ("h32", hf, 1.0, -32.0), ("qb1", odf, 80.0, -1280.5 + 2.0 ** -13), ("qb3", odf, 80.0, -1280.5 + 2.0 ** -10)):
+        scaled(T[name][:], src, scale, bias, ["pf"], [name])
+    const(1)
+    G(iota(T.ib[:], [[1, 256]]), [], ["ib"])
+    V(ts(T.big[:], T.ib[:, 0:144], T.g16[:], -16.0, A.is_equal, A.mult, rate=0.5), ["ib", "g16"], ["sel"])
+    scaled(T.bigp[:], T.big[:, 0:128], -1.0, 0.0, ["sel"], ["bigp"])
+
+    def sel(k):
+        return T.big[:, 15 - k:143 - k]
+    for name, src, c in (("cidn", "cid", -1.0), ("c37", "cid", 37.0), ("c8kn", "cid", -8192.0), ("c4k", "cid", 4096.0), ("c384", "cid", 384.0),
+                         ("c384n", "cid", -384.0), ("c512n", "cid", -512.0), ("cq1", "cb", -256.0), ("cq3", "cb", -32.0)):
         V(ts(T[name][:], T[src][:], c, None, A.mult, rate=0.5), [src], [name])
     V(ts(T.wb[:], T.cb[:], T.wts[:], None, A.mult, rate=0.5), ["cb", "wts"], ["wb"])
-    V(ts(T.k37[:], kkf, 37.0, None, A.mult), ["pf"], ["k37"])
-    const("c4")
-    G(iota(T.ic[:], [[16, 12]]), [], ["ic"])
-    G(iota(T.iw[:], [[1, 16]]), [], ["iw"])
-    V(ms(T.ha[:], 0.5), [], ["ha"])
-    V(ms(T.ha[:, 0::16], 0.0), [], ["ha"])
-    V(ms(T.hb[:], 0.0), [], ["hb"])
-    V(ms(T.hb[:, 0::16], -1 / 32), [], ["hb"])
-    V(((lambda Q: Q.tensor_tensor_scan(T.lim[:], T.ha[:], T.hb[:], 0.0, A.mult, A.add)), ns(128, 0.5)), ["ha", "hb"], ["lim"])
-    V(ts(T.pwi[:], T.iw[:], kkf, -8.0, A.is_equal, A.mult), ["iw", "pf"], ["pwi"])
-    V(tt(T.pwi[:], T.pwi[:], T.lim[:, 0:16], A.mult), ["pwi", "lim"], ["pwi"])
-    V(((lambda Q: Q.tensor_reduce(T.pw[:], T.pwi[:], AxisListType.X, A.add)), ns(16)), ["pwi"], ["pw"])
-    V(ts(T.cbw[:], T.cb[:], T.pw[:], None, A.mult, rate=0.5), ["cb", "pw"], ["cbw"])
-    V(ts(T.cbn[:], T.cb[:], -1 / 16, None, A.mult, rate=0.5), ["cb"], ["cbn"])
-    V(ts(T.bl[:], T.ic[:], kkf, None, A.add), ["ic", "pf"], ["bl"])
-    V(ts(T.top[:], T.bl[:], 513.0, None, A.add), ["bl"], ["top"])
-    const("c9")
-    for i in range(2):
-        G(iota(T.ie[:, 512 * i:512 * i + 512], [[1, 32], [0, 16]], 32 * i), [], ["ie%d" % i])
-    V(ts(T.ce[:], T.ie[:], hf, None, A.is_equal, rate=0.5), ["ie0", "ie1", "pf"], ["ce"])
-    const("c5")
-    V(ts(T.kwa[:], kkf, 15.0, SAVE + 31.0, A.is_equal, A.mult), ["pf"], ["kwa"])
-    V(ts(T.kw[:], kkf, -2.0, -1.0, A.mult, A.add), ["pf"], ["kw"])
-    V(tt(T.kw[:], T.kw[:], T.kwa[:], A.add), ["kw", "kwa"], ["kw"])
-    V(ts(T.ohb[:], kkf, -14.5, 1024.0, A.add, A.mult), ["pf"], ["ohb"])
-    for name, src, c in (("cb2", "cb", -2.0), ("cb43", "cb", -43 / 16)):
-        V(ts(T[name][:], T[src][:], c, None, A.mult, rate=0.5), [src], [name])
-    G(pick(T.tri[:], T.cb2[:], [[-1, 128]], A.is_gt, 1), ["cb2"], ["tri"])
-    V(tt(T.tri[:], T.tri[:], T.cid[:], A.add, rate=2.0), ["tri", "cid"], ["tri"])
-    V(ms(T.bas[:], 0.0), [], ["bas"])
-    for b, (a, e) in enumerate(BLOCKS):
-        V(ms(T.bas[:, ROWS[b] // 16:ROWS[b] // 16 + 4], 1.0), ["bas"], regs("one", a, e))
-        V(ts(T.bas[:, ROWS[b] // 16 + 4:ROWS[b] // 16 + 8], T.bl[:, 0:4], -32768.0, None, A.mult), ["bl", "bas"], regs("bas", a, e))
+    S(act(T.dvf[:], T.dvs[:], AF.Copy), ["dvs"], ["dvf"])
+    const(2)
+    V(cp(T.imw[:, 0:256], T.ib[:], 0.5), ["ib"], ["imwa"])
+    V(ts(T.imw[:, 256:512], T.ib[:], -256.0, None, A.add, rate=0.5), ["ib"], ["imwb"])
     G(move(T.mf0[:], T.mi[:]), ["mi"], every("m0"))
-    const("c6")
-    V(ts(T.cbm[:], T.cb[:, 0::16], -1.0, None, A.mult), ["cb"], ["cbm"])
-    V(ts(T.cidm[:], T.cid[:, ::-1], 4096.0, None, A.mult), ["cid"], ["cidm"])
-    V(ms(T.onf[:], 1 / 32, 1.0), [], ["onf"])
-    G(move(T.tb[:, 0:512], T.mci[:]), ["mci"], ["tb"])
-    const("c10")
-    for i in range(4):
-        S(act(T.seln[:, 512 * i:512 * i + 512], T.sel[:, 512 * i:512 * i + 512], AF.Copy, scale=-1.0), ["sel"], ["seln%d" % i])
-
-    def listmm(out, buf, a, b, base=()):
-        return mm(out, *(list(base) + [(T.sel[:, 128 * i:128 * i + 128], T[buf][:, a + i:b:16]) for i in range(16)]))
+    const(3)
+    G(iota(T.cew[:], [[0, 1]], 128), [], ["cewa"])
+    G(((lambda Q: Q.affine_select(T.cew[:], T.cew[:], [[0, 1]], A.is_ge, 1.0, -64, 1)), 170.0 + COST["gcall"]), ["cewa"], ["cewa", "cewb"])
+    fill(T.zbias[:], 0.0, [], ["zbias"])
+    fill(T.zbias[0:64, :], -0.5, ["zbias"], ["zbias"])
+    G(iota(T.ie[:], [[1, 32], [0, 16]]), [], ["ie"])
+    for i, h in enumerate((hf, T.h32[:])):
+        V(ts(T.ce[:, 512 * i:512 * i + 512], T.ie[:], h, T.cew[:], A.is_equal, A.mult, rate=0.5), ["ie", "pf", "h32", "cewa", "cewb"], ["ce%d" % i])
+    fill(T.thw[:, :, 0], 0.0, [], ["thwz"])
+    fill(T.thw[:, 0:4, 1:18], -2.0, [], ["thw0"])
+    const(4)
+    for b in range(len(BLOCKS)):
+        G(iota(T["d0%d" % b][:, MAIN + 1024:ZERO + 1:ZERO - MAIN - 1024], [[0, 2]]), [], ["d0z%d" % b])
+    G(iota(T.ft[:, ZERO:ZERO + 16], [[0, 16]]), [], ["ftb"])
+    V(ms(T.ft[:, 0:MAIN + 1024], 1.0), [], ["fta"])
+    G(iota(T.ind[:, :, 0], [[0, 192]]), [], ["indz"])
+    G(iota(T.wi[:], [[0, 3], [-256, 4], [1, 18]], MAIN + 1007), [], ["wi"])
+    G(iota(T.ic[:], [[0, 3], [16, 4]]), [], ["ic"])
+    S(act(T.wk[:], T.wi[:], AF.Identity, bias=T.r16[:]), ["wi", "r16"], ["wk"])
+    S(act(T.wk[:, 1::18], T.ic[:], AF.Identity, scale=-1.0, bias=T.l63[:]), ["ic", "l63", "wk"], ["wk"])
+    fill(T.wk[:, 17::18], float(ZERO), ["wk"], ["wk"])
+    fill(T.kb[:], -2056.0, [], ["kb"])
+    fill(T.kb[:, 17::18], 60000.0, ["kb"], ["kb"])
+    fill(T.kb[:, 0::18], (4096 + 1152 - MID) / 8192, ["kb"], ["kb"])
+    fill(T.c68[:], -MAGIC - 2.0, [], ["c68"])
+    fill(T.onf[:], 1 / 32, [], ["onf"])
+    const(5)
+    G(iota(T.top[:], [[16, 12]], 1280), [], ["top"])
+    V(ts(T.edge[:], T.ib[:], T.l127[:], 2000.0, A.is_ge, A.mult, rate=0.5), ["ib", "l127"], ["edge"])
+    waves, o = [], 0
+    for a, e in USES:
+        n = e - a
+        waves.append(o)
+        for k in range(n // 16):
+            dma("y", T.wd[:, o + k * n:o + k * n + n], T.edge[:, 112 - 16 * k:112 - 16 * k + n], ["edge"], ["wd%d" % a] * (k == n // 16 - 1), "wd%d" % a, 1500, k + 1)
+        S(act(T.wd[:, down(o + n * n // 16 - 1, n // 16, n)], T.top[:, a // 16:e // 16], AF.Identity, bias=T.kk[:]), ["top", "kk", "wd%d" % a], ["wd%d" % a])
+        o += n * n // 16
+    dma("y", T.eb[:], T.wd[:], ["wd%d" % a for a, e in USES], ["eb%d" % k for k in range(12)], "ebs", 1500)
+    const(6)
+    G(move(T.tb[:, 768:1280], T.mci[:]), ["mci"], ["tb"])
 
     sends = [0]
 
     def send(name, src, dst, r, w):
         sends[0] += 1
-        i = op("g", ((lambda Q: Q.remote_dma(dst, src, T.sem[name], T.sem.snd, pid, rid, mask_out)), SEND), r, [], ("snd%d" % sends[0], 0, False))
-        op(None, (None, 0.0, FLIGHT + FIRST * (sends[0] == 1)), [], w, (name, n_in, False), i)
+        i = op("g", ((lambda Q: Q.remote_dma(dst, src, T.sem[name], T.sem.snd, pid, rid, mask_out)), COST["send"]), r, [], ("snd%d" % sends[0], 0, False))
+        op("d", (None, COST["wire"], COST["flight"] - COST["wire"] + COST["first"] * (sends[0] == 1)), [], w, (name, n_in, False), i)
 
-    def back(a, b, step, total):
-        stop = total - 1 - a - step * len(range(a, b, step))
-        return slice(total - 1 - a, stop if stop >= 0 else None, -step)
+    def up(a, e):
+        return down(191 - a, e - a)
 
-    def gg(a, e):
-        return T.gg[:, back(a, e, 1, 192)]
+    def rv(a, e):
+        return slice(192 - e, 192 - a)
 
-    def part(buf, a, e, lo, hi):
-        return buf[:, a // 64, lo:hi] if e - a == 64 else buf[:, a // 64:e // 64, lo:hi]
+    def ps(name, a, e):
+        bank, o = PSUM[name]
+        return T[bank][:, o + a:o + e]
+
+    def pn(name, a=0, e=32):
+        return regs(PSUM[name][0] + name, a, e)
+
+    def split(a, e):
+        return [(max(a, x), min(e, y)) for x, y in BLOCKS if max(a, x) < min(e, y)]
+
+    def slots(a, e, shift=0, step=1):
+        y = a // 64 * 64 + 64
+        return T["d0%d" % (2 - a // 64)][:, MAIN + 16 * (y - e) + shift:MAIN + 16 * (y - a) + shift:step]
 
     def step(t):
         lastt = t == STEPS - 1
+
+        def batches(what):
+            return PLAN[what] if t else [(0, 192)]
+
+        def lists(buf, a, e):
+            x, y = [m for m in batches("mod") if m[0] <= a < m[1]][0]
+            o = x // 8 + (a - x) // 16
+            return buf[:, o:o + (e - a) // 16], buf[:, o + (y - x) // 16:o + (y - x + e - a) // 16]
         mfn, zn = ("y%d" % t if t else "m0"), "z%d" % t
-        th, thn = (T.thr[:, t:t + 1], ["thr%d" % t]) if t else (0.5, [])
+        thw, thn = T.thw[:, 4 * t:4 * t + 4, :], "thw%d" % t
 
         def z(a, e):
-            return part(T["zb%d" % t], a, e, 0, 64) if t else T.zb0[:, a:e]
+            o = a // 64 * 8
+            return T["zb%d" % t][:, o + a:o + e] if t else T.zb0[:, a:e]
 
         def mf(a, e):
-            return part(T["zb%d" % t], a, e, 64, 68) if t else T.mf0[:, a // 16:e // 16]
+            o = 9 * a // 8 + 64
+            return T["zb%d" % t][:, o:o + 4] if t else T.mf0[:, a // 16:e // 16]
 
-        def when(what, a=0, second=0):
-            what = what + "0" * (t == 0)
-            now[1:] = [t, what, 2 - a // 64 + len(BLOCKS) * second if len(DUE[what]) > 1 else 0]
-            now[0] = PERIOD * t + DUE[what][now[3]]
+        def when(what, a=0):
+            now[:] = [t, what, 5 - a // 32]
 
-        if t == 0:
-            when("ahead")
-            send("ze", z(*BLOCKS[0]), T.ze[:], regs(zn, *BLOCKS[0]), ["ze"])
-        if t == 1:
+        if PLAN["early"] and t < 2:
             a, e = BLOCKS[0]
-            when("goal", a)
-            P(mm(T.p2[:, 384:448], (T.cid[:], T.ze[:]), (T.cid[:], T.zw[:, 0:64])), ["cid", "ze"] + regs("w1", a, e), ["p2.z"])
-            S(act(z(a, e), T.p2[:, 384:448], AF.Abs), ["p2.z"], regs(zn, a, e))
-            V(cp(mf(a, e), T.zw[:, 64:68]), regs("w1", a, e), regs(mfn, a, e))
+            when("early", a)
+            if t == 0:
+                send("ze", z(a, e), T.ze[:], regs(zn, a, e), ["ze"])
+            else:
+                P(mm((ps("z", 0, 64), (T.cid[:], T.ze[:]), (T.cid[:], T.zw[:]))), ["cid", "ze", "zw"], pn("z"))
+                S(act(z(a, e), ps("z", 0, 64), AF.Abs), pn("z"), regs(zn, a, e))
 
-        for a, e in BLOCKS:
+        for a, e in BLOCKS if t else [(0, 192)]:
             c = slice(a // 16, e // 16)
             when("lists", a)
             if t == 0:
                 V(cp(T.ml[:, c], T.mi[:, c]), ["mi"], regs("ml", a, e))
-            elif t == 1 and (a, e) == BLOCKS[0]:
-                copy(Q_ML, T.ml[:, c], T.zw[:, 64:68], regs("w1", a, e), regs("ml", a, e))
             else:
-                copy(Q_ML, T.ml[:, c], mf(a, e), regs(mfn, a, e), regs("ml", a, e))
-            S(gather(act(gg(a, e), T.glw[:].indirect(T.ml[:, c]), AF.Copy), e - a, q="s"), ["glw"] + regs("ml", a, e), regs("gg", a, e))
+                copy(PLAN["ml"], T.ml[:, c], mf(a, e), regs(mfn, a, e), regs("ml", a, e))
+            when("keep", a)
+            scaled(T.wk[:, 18 * c.start:18 * c.stop:18], mf(a, e), -1.0, float(MID), ["wk"] + regs(mfn, a, e), regs("keep", a, e))
+        for a, e in batches("lists"):
+            when("lists", a)
+            S(gather(act(T.gg[:, up(a, e)], T.glw[:].indirect(T.ml[:, a // 16:e // 16]), AF.Copy), e - a, q="s"), ["glw"] + regs("ml", a, e), regs("gg", a, e))
+        for a, e in batches("row"):
             when("row", a)
-            S(gather(act(T.mb[:, a:e], T.imw[:].indirect(T.ml[:, c]), AF.Copy), e - a, q="s"), ["imwa", "imwb"] + regs("ml", a, e), regs("mb", a, e))
+            S(gather(act(T.mb[:, a:e], T.imw[:].indirect(T.ml[:, a // 16:e // 16]), AF.Copy), e - a, q="s"), ["imwa", "imwb"] + regs("ml", a, e), regs("mb", a, e))
+        for a, e in batches("ops"):
             when("ops", a)
-            win = T.tb[:, 0:512] if t else T.mci[:]
-            V(gather(cp(T.ol[:, a:e], win.indirect(T.ml[:, c])), e - a), ["tb" if t else "mci"] + regs("ml", a, e), regs("ol", a, e))
-
-        for b, a, e, q, half in shares(ADDS[min(t, 1)]):
-            when("adds", a, half)
-            o = BLOCKS[b][0]
-            out, win = T["d0%d" % b][:, back(32 * (a - o) + 1, 32 * (e - o), 2, SAVE)], T.adw[:].indirect(T.ol[:, a:e])
-            call = ts(out, win, -1.0, None, A.mult) if q == "v" else act(out, win, AF.Copy, scale=-1.0)
-            op(q, gather(call, 16 * (e - a), q=q), ["adw"] + regs("ol", a, e), regs("d0", a, e) + regs("cut", a, e))
-        for b, a, e, q, half in shares(NEEDS[min(t, 1)]):
-            when("needs", a, half)
-            out, win = T.d1[:, back(32 * a, 32 * e, 2, 6144)], T.prw[:].indirect(T.ol[:, a:e])
-            op(q, gather(cp(out, win) if q == "v" else act(out, win, AF.Copy), 16 * (e - a), q=q), ["prw"] + regs("ol", a, e), regs("d1", a, e))
-        for b, (a, e) in enumerate(BLOCKS):
-            d0 = T["d0%d" % b]
-            when("scan", a)
-            first, kept = d0[:, 0:SAVE:32], d0[:, SAVE + 31:2 * SAVE:32]
-            P(mm(T.p4[:, 384:448], (T.cid[:], gg(a, e)), (T.cid[:], d0[:, back(31, SAVE, 32, SAVE)])), ["cid"] + regs("gg", a, e) + regs("cut", a, e), ["p4.r"])
-            either("r15", T.d1[:, back(32 * a + 31, 32 * e, 32, 6144)], T.p4[:, 384:448], AF.Relu, 1.0, 0.0, (0.0, None, A.max), ["p4.r"], regs("r15", a, e))
-            copy(Q_SAVE, kept, first, regs("cut", a, e), regs("a15", a, e))
-            op(Q_CUT, iota(first, [[0, 64]], -1024) if Q_CUT == "g" else ms(first, -1024.0), [], regs("cut", a, e))
-            j, k = slice(6144 - 32 * e, 6144 - 32 * a), slice(0, SAVE)
-            V(((lambda Q, j=j, k=k, d0=d0: Q.tensor_tensor_scan(T.ss[:, j], d0[:, k], T.d1[:, j], 0.0, A.add, A.max)), ns(SAVE, 0.5)),
-              ["d0z%d" % b] + regs("d0", a, e) + regs("cut", a, e) + regs("d1", a, e) + regs("r15", a, e), regs("ss", a, e))
-
-        for i, (a, e) in enumerate(GOALS):
-            when("goal", a)
-            P(mm(T.p5[:, 128 + a:128 + e], (T.cid[:], z(a, e)), (T.cidn[:], gg(a, e))), ["cid", "cidn"] + regs(zn, a, e) + regs("gg", a, e), regs("p5.d", a, e))
-            S(act(T.gi[:, a:e], T.p5[:, 128 + a:128 + e], AF.Sign, bias=0.5), regs("p5.d", a, e), regs("gi", a, e))
-            P(mm(T.p5[:, 320 + a:320 + e], (T.cb[:], T.gi[:, a:e]), (T.cb6[:], T.onb[:, 0:e - a])), ["cb", "cb6", "onb"] + regs("gi", a, e), regs("p5.c", a, e))
-            S(act(T.tg[:, 1, a:e], T.p5[:, 320 + a:320 + e], AF.Sign, scale=0.5, bias=th, accum_out=T.acc[:, i:i + 1]), regs("p5.c", a, e) + thn,
-              regs("goal", a, e) + ["acc%d" % i])
+            win = T.tb[:, 768:1280] if t else T.mci[:]
+            V(gather(cp(T.ol[:, a:e], win.indirect(T.ml[:, a // 16:e // 16])), e - a), ["tb" if t else "mci"] + regs("ml", a, e), regs("ol", a, e))
+        for a, e in BLOCKS if t else [(0, 192)]:
             when("room", a)
-            either("hh", T.hh[:, a:e], z(a, e), AF.Copy, 1.0, -255.0, (-255.0, None, A.add), regs(zn, a, e), regs("hh", a, e))
+            out = T.hh[:, up(a, e)]
+            op(PLAN["hh"], ts(out, z(a, e), -255.0, None, A.add) if PLAN["hh"] == "v" else act(out, z(a, e), AF.Copy, bias=-255.0), regs(zn, a, e), regs("hh", a, e))
 
-        for a, e in MODS:
-            when("mod", a)
-            c, l0, w = slice(a // 16, e // 16), 384 + a // 8, (e - a) // 16
-            x = [(T.wb[:], z(a, e)), (T.cq1[:], T.q1[:, a:e]), (T.c37[:], T.mb[:, a:e]), (T.cq3[:], T.q3[:, a:e])]
-            xn = [["wb"] + regs(zn, a, e), ["cq1"] + regs("q1", a, e), ["c37"] + regs("mb", a, e), ["cq3"] + regs("q3", a, e)]
-            P(mm(T.p6[:, a:e], *x[:1]), xn[0], regs("p6.x", a, e))
-            either("q1", T.q1[:, a:e], T.p6[:, a:e], AF.Identity, 2.0 ** -12, T.qb1[:], (2.0 ** -12, T.qb1[:], A.mult, A.add), regs("p6.x", a, e) + ["qb1"], regs("q1", a, e))
-            P(mm(T.p7[:, a:e], *x[:3]), sum(xn[:3], []), regs("p7.x", a, e))
-            P(mm(T.p6[:, 192 + a:192 + e], *x[:2]), sum(xn[:2], []), regs("p6.u", a, e))
-            either("q3", T.q3[:, a:e], T.p7[:, a:e], AF.Identity, 2.0 ** -9, T.qb3[:], (2.0 ** -9, T.qb3[:], A.mult, A.add), regs("p7.x", a, e) + ["qb3"], regs("q3", a, e))
-            P(mm(T.p7[:, 192 + a:192 + e], *x), sum(xn, []), regs("p7.m", a, e))
-            either("to", T.tg[:, 0, a:e], T.p7[:, 192 + a:192 + e], AF.Copy, 1.0, 1.0, (1.0, None, A.add), regs("p7.m", a, e), regs("to", a, e))
-            P(mm(T.p6[:, l0:l0 + 2 * w], *[(T.sel[:, 128 * j:128 * j + 128], T.tg[:, :, a + j:e:16]) for j in range(16)]),
-              ["sel"] + regs("to", a, e) + regs("goal", a, e), regs("p6.l", a, e))
-            either("lst", T.lst[:, 2 * c.start:2 * c.stop], T.p6[:, l0:l0 + 2 * w], AF.Copy, 0.0625, 0.0, (0.0625, None, A.mult), regs("p6.l", a, e), regs("lst", a, e))
-            copy(Q_MAL, T.mal[:, c], T.lst[:, 2 * c.start:2 * c.start + w], regs("lst", a, e), regs("mal", a, e))
-            when("first", a)
-            for k in range(a // 16, e // 16):
-                lk, end = k + a // 16, [y for x, y in USES if x <= 16 * k < y][0]
-                V(ts(T.eb[:, k, 0:end - 16 * k], T.tg[:, 0, 16 * k:end], T.lst[:, lk + w:lk + w + 1], T.lst[:, lk:lk + 1], A.mult, A.is_equal, rate=0.5),
-                  regs("to", a, end) + regs("lst", a, e), ["eb%d" % k])
+        for i, (a, e) in enumerate(batches("goal")):
+            when("goal", a)
+            x, xn = ps("goal", a, e), pn("goal", a, e)
+            P(mm((x, (T.cid[:], T.hh[:, rv(a, e)]), (T.cidn[:], T.gg[:, rv(a, e)]))), ["cid", "cidn"] + regs("hh", a, e) + regs("gg", a, e), xn)
+            S(act(T.gi[:, a:e], x, AF.Sign, bias=255.5), xn, regs("gi", a, e))
+            P(mm((x, (T.cb[:], T.gi[:, a:e]))), ["cb"] + regs("gi", a, e), xn)
+            S(act(T.tg[:, 1, rv(a, e)], x, AF.Sign, scale=0.45, bias=thw[:, 0, 1:2], accum_out=T.acc[:, i:i + 1]), xn + [thn], regs("goal", a, e) + ["acc%d" % i])
         if not lastt:
             when("count")
-            sums = mm(T.p6[:, 408:410], (T.onf[:], T.acc[:]))
-            P((sums[0], 4 * sums[1]), ["onf", "acc0", "acc1"], ["p6.a"])
-            S(act(T.sm[:], T.p6[:, 408:410], AF.Copy, bias=-0.25, accum_out=T.sum[:]), ["p6.a"], ["sum"])
-            S(act(T.ev[:], T.sum[:], AF.Copy, bias=MAGIC), ["sum"], ["ev"])
-            V(ts(T.thr[:, t + 1:t + 2], T.ev[:], MAGIC, T.sum[:], A.subtract, A.subtract), ["ev", "sum"], ["thr%d" % (t + 1)])
+            n = len(batches("goal"))
+            x = ps("all", 0, 1)
+            G(move(T.acb[:, 0:n], T.acc[:, 0:n]), ["acc%d" % i for i in range(n)], ["acb"])
+            P(mm((x, *[(T.onf[:], T.acb[:, i:i + 1]) for i in range(n)])), ["onf", "acb"], pn("all"))
+            V(ts(T.ev[:], x, -0.5, MAGIC, A.add, A.add), pn("all"), ["ev"])
+            V(ts(T.thw[:, 4 * t + 4:4 * t + 8, 1:18], T.c68[:], T.ev[:], x, A.add, A.subtract), ["c68", "ev"] + pn("all"), ["thw%d" % (t + 1)])
 
-        for b, (a, e) in enumerate(USES):
-            when("lost", a)
-            c, ks = slice(a // 16, e // 16), range(a // 16, e // 16)
-            P(mm(T.p7[:, a:e], (T.cbn[:], T.tg[:, 1, a:e]), (T.cb[:], T.lim[:, 0:e - a]), (T.cbw[:], T.eb[:, c, 0:16]),
-                 *[(T.cb[:], T.eb[:, k, 16:e - 16 * k], T.p7[:, 16 * k + 16:e]) for k in ks[:-1]]),
-              ["cbn", "cb", "cbw", "lim"] + regs("goal", a, e) + ["eb%d" % k for k in ks], regs("p7.x", a, e))
-            either("wn", T.oh[:, ROWS[b] + 128:ROWS[b + 1]], T.p7[:, a:e], AF.Relu, 2.0 ** 28, 2.0 ** 28 + 1024.0, (-1.0, 1024.0, A.is_ge, A.mult),
-                   regs("p7.x", a, e), regs("wn", a, e))
+        for a, e in batches("mod"):
+            when("mod", a)
+            w = (e - a) // 16
+            xn = [["wb"] + regs(zn, a, e), ["cq1"] + regs("q1", a, e), ["c37"] + regs("mb", a, e), ["cq3"] + regs("q3", a, e), ["c384n"] + regs("goal", a, e)]
+
+            def terms(n, name):
+                wz = [(T.wb[:], z(x, y), ps(name, x, y)) for x, y in (split(a, e) if t else [(a, e)])]
+                rest = [(T.cq1[:], T.q1[:, a:e]), (T.c37[:], T.mb[:, a:e]), (T.cq3[:], T.q3[:, a:e]), (T.c384n[:], T.tg[:, 1, up(a, e)])][:n - 1]
+                P(mm(*([(ps(name, a, e), *rest, *wz)] if rest else [(x[2], x) for x in wz])), sum(xn[:n], []), pn(name, a, e))
+            terms(1, "sum")
+            S(act(T.q1[:, a:e], ps("sum", a, e), AF.Identity, scale=2.0 ** -12, bias=T.qb1[:]), pn("sum", a, e) + ["qb1"], regs("q1", a, e))
+            terms(3, "sum")
+            terms(2, "u")
+            S(act(T.q3[:, a:e], ps("sum", a, e), AF.Identity, scale=2.0 ** -9, bias=T.qb3[:]), pn("sum", a, e) + ["qb3"], regs("q3", a, e))
+            terms(5, "sum")
+            S(act(T.tg[:, 0, up(a, e)], ps("sum", a, e), AF.Copy, bias=1152.0), pn("sum", a, e), regs("to", a, e))
+            both = ps("list", a // 8, e // 8)
+            P(mm((both, *[(sel(j), T.tg[:, :, down(191 - a - j, w, 16)]) for j in range(16)])), ["sel"] + regs("to", a, e) + regs("goal", a, e), pn("list", a, e))
+            S(act(T.lst[:, a // 8:e // 8], both, AF.Copy, scale=-2.0 ** -8), pn("list", a, e), regs("lst", a, e))
+            copy(PLAN["mal"], T.mal[:, a // 8:e // 8], T.lst[:, a // 8:e // 8], regs("lst", a, e), regs("mal", a, e))
+
+        for (a, e), o in zip(USES, waves):
+            n = e - a
+            when("first", a)
+            for k in range(a // 16, e // 16):
+                own, end = lists(T.lst, 16 * k, 16 * k + 16)[0], o + (e // 16 - k) * n
+                V(ts(T.eb[:, end - (16 * k + 16 - a):end], T.tg[:, 0, rv(a, 16 * k + 16)], own, own, A.is_equal, A.mult, rate=0.5),
+                  regs("to", a, 16 * k + 16) + regs("lst", 16 * k, 16 * k + 16), ["eb%d" % k])
+            when("place", a)
+            c = slice(o, o + n * n // 16)
+            V(scan(T.ws[:, c], T.eb[:, c], T.wd[:, c], A.add, A.min, 0.5), ["wd%d" % a] + ["eb%d" % k for k in range(a // 16, e // 16)], ["ws%d" % a])
+            copy(PLAN["sl"], T.sl[:, a // 16:e // 16], T.ws[:, down(c.stop - 1, n // 16, n)], ["ws%d" % a], regs("sl", a, e))
 
         when("new")
         G(move(T.of[:], T.ol[:]), every("ol"), ["of"])
-        either("ok", T.p2[:, 192:384], T.of[:], AF.Identity, 1.0, T.k37[:], (T.k37[:], None, A.add), ["of", "k37"], ["p2.k"])
-        V(tt(T.f1[:], T.of[:], T.p6[:, 192:384], A.mult), ["of"] + every("p6.u"), ["f1"])
-        V(ts(T.f2[:], T.f1[:], 5, None, A.arith_shift_right), ["f1"], ["f2"])
-        V(tt(T.f3[:], T.f2[:], T.p2[:, 192:384], A.add), ["f2", "p2.k"], ["f3"])
-        V(ts(T.f4[:], T.f3[:], 4095, None, A.bitwise_and), ["f3"], ["f4"])
+        S(act(ps("old", 0, 192), T.of[:], AF.Identity, scale=32.0, bias=T.k37[:]), ["of", "k37"], pn("old"))
+        V(tt(T.f1[:], T.of[:], ps("u", 0, 192), A.mult), ["of"] + pn("u", 0, 192), ["f1"])
+        V(tt(T.f3[:], T.f1[:], ps("old", 0, 192), A.add), ["f1"] + pn("old"), ["f3"])
+        V(ts(T.f4[:], T.f3[:], 5, 4095, A.arith_shift_right, A.bitwise_and), ["f3"], ["f4"])
 
-        if t < 2:
-            when("dist")
-            a, e = (1, STEPS) if t else (0, 1)
-            out, names = (T.p3[:], every("p3.c") + ["p3.y"]) if t else (T.p2[:, 0:128], ["p2.d"])
-            for i in range(a, e):
-                V(ts(T.dg[:, 128 * i:128 * i + 128], T.cid[:], T.dvs[:, i:i + 1], None, A.mult, rate=0.5), ["cid", "dvs"], ["dg%d" % i])
-            P(mm(out, (T.cb[:], T.dg[:, 128 * a:128 * e])), ["cb"] + ["dg%d" % i for i in range(a, e)], names)
-            S(act(T.dd[:, 128 * a:128 * e], out, AF.Copy, scale=-2.0 ** -10), names, ["dd%d" % t])
+        for a, e, q in shares(PLAN["adds"][min(t, 1)]):
+            when("adds", a)
+            out, win = slots(a, e)[:, ::-1], T.adw[:].indirect(T.ol[:, a:e])
+            call = ts(out, win, -1.0, None, A.mult) if q == "v" else act(out, win, AF.Copy, scale=-1.0)
+            op(q, gather(call, 16 * (e - a), q=q), ["adw"] + regs("ol", a, e), regs("d0", a, e) + regs("cut", a, e))
+        for a, e, q in shares(PLAN["needs"][min(t, 1)]):
+            when("needs", a)
+            out, win = T.d1[:, down(3071 - 16 * a, 16 * (e - a))], T.prw[:].indirect(T.ol[:, a:e])
+            op(q, gather(cp(out, win) if q == "v" else act(out, win, AF.Copy), 16 * (e - a), q=q), ["prw"] + regs("ol", a, e), regs("d1", a, e))
 
-        for b, (a, e) in enumerate(TURNS):
-            n = e - a
-            when("met", a)
-            zt = T.zt[0:n, 128 * b:128 * b + 128]
-            for s in range(a, e, 64):
-                P(mm(T.p5[s - a:s - a + 64, 0:128], (z(s, s + 64), T.cid[:])), ["cid"] + regs(zn, s, s + 64), ["p5.t%d" % (s - a)])
-            either("zt", zt, T.p5[0:n, 0:128], AF.Copy, 1.0, 0.0, (0.0, None, A.add), ["p5.t%d" % s for s in range(0, n, 64)], ["zt%d" % b])
-            for s in range(e - 64, a - 64, -64):
-                when("spread", s)
-                for h in range(2):
-                    P(mm(T.p0[:, 512 * h:512 * h + 512], (T.zt[s - a:s - a + 64, 128 * b:128 * b + 128], T.ce[s - a:s - a + 64, 512 * h:512 * h + 512])),
-                      ["zt%d" % b, "ce"], ["p0.%d" % h])
-                when("cmp", s)
-                V(tt(T.ind[:, 16 * s:16 * s + 1024], T.ss[:, back(32 * s, 32 * s + 2048, 2, 6144)], T.p0[:], A.is_le), regs("ss", s, s + 64) + ["p0.0", "p0.1"], regs("ind", s, s + 64))
+        for a, e in PLAN["head"]:
+            y = a // 64 * 64 + 64
+            when("head", a)
+            first, head, r = slots(a, e, 0, 16), T.d1[:, 3072 - 16 * e:3072 - 16 * a:16], ps("r", 0, e - a)
+            P(mm((r, (T.cid[:], T.gg[:, rv(a, e)]), (T.cid[:], first))), ["cid"] + regs("gg", a, e) + regs("cut", a, e), pn("r"))
+            S(act(T.ind[:, rv(a, e), 17], r, AF.Relu), pn("r"), regs("r15", a, e))
+            copy(PLAN["save"], T["d0%d" % (2 - a // 64)][:, y - e:y - a], first, regs("cut", a, e), regs("a15", a, e))
+            op(PLAN["cut"], iota(first, [[0, e - a]], -1024) if PLAN["cut"] == "g" else ms(first, -1024.0, 1.0), [], regs("cut", a, e))
+            V(tt(head, head, r, A.max), pn("r") + regs("d1", a, e), regs("d1", a, e))
+        for a, e in PLAN["scan"]:
+            when("scan", a)
+            j = slice(3072 - 16 * e, 3072 - 16 * a)
+            V(scan(T.ss[:, j], slots(a, e), T.d1[:, j], A.add, A.max, 0.5), regs("d0", a, e) + regs("cut", a, e) + regs("d1", a, e), regs("ss", a, e))
+        for a, e in PLAN["spread"] if t else PAIRED:
+            when("spread", a)
+            groups, o = [], 128 * (a != 64)
+            out, names = ps("turn", o, o + 2 * (e - a)), pn("turn", o // 4, o // 4 + (e - a) // 2)
+            for x in range(a, e, 64):
+                y, tgb = slice(2 * (x - a), 2 * (x - a) + 128), (T.tg[:, 1, rv(x, x + 64)], T.c512n[:])
+                groups += [(out[0:64, y], (T.hh[:, rv(x, x + 64)], T.cid[:]), tgb), (out[64:128, y], tgb)]
+            P(mm(*groups), ["cid", "c512n"] + regs("hh", a, e) + regs("goal", a, e), names)
+            S(act(T.zt[:, 2 * a:2 * e], out, AF.Relu, bias=T.zbias[:]), names + ["zbias"], regs("zt", a, e))
+        for a, e in PLAN["cmp"]:
+            x = a // 64 * 64
+            halves = [(512 * h, x + 32 - 32 * h) for h in range(2) if a <= x + 32 - 32 * h < e]
+            pair = 2 * ((t + a // 64) % 2)
+            py, names = T["p%d" % pair], ["p%d.y" % (pair + o // 512) for o, s in halves]
+            when("fill", a)
+            P(mm(*[(py[:, o:o + 512], (T.zt[:, 2 * x:2 * x + 128], T.ce[:, o:o + 512])) for o, s in halves], stop=False), regs("zt", a, e) + ["ce0", "ce1"], names)
+            when("less", a)
+            P(mm(*[(py[:, o:o + 512], (T.cidn[:], T.ss[:, 2560 - 16 * s:3072 - 16 * s])) for o, s in halves], start=False), ["cidn"] + names + regs("ss", a, e), names)
+            when("cmp", a)
+            V(tt(T.ind[:, rv(a, e), 1:17], slots(a, e, 1), py[:, halves[0][0]:halves[-1][0] + 512], A.max),
+              ["d0z%d" % (2 - a // 64)] + names + regs("d0", a, e) + regs("cut", max(x, a - 32), e), regs("ind", a, e))
 
         for b, (a, e) in enumerate(BLOCKS):
-            c, o, end = slice(a // 16, e // 16), ROWS[b], ROWS[b + 1]
+            d0, c, o = T["d0%d" % b], slice(a // 16, e // 16), 9 * a // 8
             when("pass", a)
-            P(mm(T.p3[:, a:e], (T.cb2[:], T.tg[:, 1, a:e]), (T.cb43[:], T.onb[:, 0:64]),
-                 *[(T.sel[:, 128 * k:128 * k + 128], T.ind[:, 16 * a + k:16 * e:16]) for k in range(16)]),
-              ["sel", "cb2", "cb43", "onb"] + regs("goal", a, e) + regs("ind", a, e), regs("p3.c", a, e))
-            S(act(T.sg[:, a:e], T.p3[:, a:e], AF.Sign, bias=th), regs("p3.c", a, e) + thn, regs("sg", a, e))
-            P(mm(T.p3[:, 192:256], (T.tri[:], T.sg[:, a:e])), ["tri"] + regs("sg", a, e), ["p3.y"])
-            S(act(T.oh[:, o:o + 64], T.p3[:, 192:256], AF.Relu, scale=512.0, bias=T.ohb[:]), ["p3.y", "ohb"], regs("oh", a, e))
-            either("ow", T.oh[:, o + 64:o + 128], T.oh[:, o:o + 64], AF.Copy, T.kw[:], 0.0, (T.kw[:], None, A.mult), ["kw"] + regs("oh", a, e), regs("ow", a, e))
-            l0, l1 = 384 + o // 16, 384 + end // 16
-            terms, names = [(T.cid[:], T.bas[:, o // 16:end // 16]), (T.cidn[:], T.mal[:, c], T.p7[:, l0:l0 + 4])], []
-            if b < len(USES):
-                x, y = USES[b]
-                terms, names = terms + [(T.cid[:], T.mal[:, x // 16:y // 16], T.p7[:, l0 + 8:l1])], regs("wn", x, y) + regs("mal", x, y)
-            P(listmm(T.p7[:, l0:l1], "oh", o, end, terms),
-              ["sel", "cid", "cidn"] + names + regs("bas", a, e) + regs("one", a, e) + regs("mal", a, e) + regs("ow", a, e) + regs("oh", a, e), regs("p7.l", a, e))
-            if b < len(USES):
-                when("place", x)
-                V(tt(T.ys[:, x // 16:y // 16], T.top[:, x // 16:y // 16], T.p7[:, l0 + 8:l1], A.min), ["top"] + regs("p7.l", a, e), regs("ys", x, y))
-                V(ts(T.sl[:, x // 16:y // 16], T.ys[:, x // 16:y // 16], -1.0, None, A.add), regs("ys", x, y), regs("sl", x, y))
-                when("pass", a)
-            out, ahead = T.yo if lastt else T["zs%d" % (t + 1)], t == 0 and b == 0
-            V(tt(T.tm[:, c] if ahead else T.p2[:, 448:452], mf(a, e), T.p7[:, l0:l0 + 4], A.min), regs(mfn, a, e) + regs("p7.l", a, e), ["tm" if ahead else "p2.m"])
+            x = slice(18 * c.start, 18 * c.stop)
+            cnt, kr = ps("met", x.start, x.stop), T.kr[:, x]
+            tol, tgl = lists(T.mal, a, e)
+            P(mm((cnt, (T.c8kn[:], T.kb[:]), (T.c8kn[:], thw), (T.c4k[:], T.onb[:, 0:72]), (T.cid[:], tol, cnt[:, 0::18]), (T.c384[:], tgl, cnt[:, 0::18]),
+                  *[(sel(r), T.ind[:, down(191 - a - r, 4, 16), :]) for r in range(16)])),
+              ["sel", "c8kn", "c4k", "cid", "c384", "onb", "kb", "thwz", "indz", thn] + regs("ind", a, e) + regs("r15", a, e) + regs("mal", a, e), pn("met", a, e))
+            V(scan(kr[:, ::-1], cnt[:, ::-1], T.wk[:, x][:, ::-1], A.min, A.max, 1.0), ["wk"] + pn("met", a, e) + regs("keep", a, e), regs("kr", a, e))
+            copy(PLAN["la"], T.la[:, c], kr[:, 1::18], regs("kr", a, e), regs("la", a, e))
             when("move", a)
-            V(ts(T.la[:, c], T.p7[:, l0 + 4:l0 + 8], 2.0 ** -10, SAVE - 1.0, A.mult, A.add), regs("p7.l", a, e), regs("la", a, e))
-            V(gather(tt(T.yy[:, a:e], T["d0%d" % b][:].indirect(T.la[:, c]), T.hh[:, a:e], A.max), 64),
+            out = (T.yo if lastt else T["zs%d" % (t + 1)])[:, o:o + 68]
+            S(act(out[:, 64:68], kr[:, 0::18], AF.Abs, bias=-float(MID)), regs("kr", a, e), regs("ms%d" % t, a, e))
+            V(gather(tt(T.yy[:, a:e], d0[:].indirect(T.la[:, c]), T.hh[:, up(a, e)], A.max), 64),
               ["d0z%d" % b] + regs("la", a, e) + regs("hh", a, e) + regs("d0", a, e) + regs("cut", a, e) + regs("a15", a, e), regs("yy", a, e))
-            P(mm(T.p2[:, 384:448], (T.dd[:, 128 * t:128 * t + 128], T.oh[:, o:o + 64]), (T.cidn[:], T.yy[:, a:e]), *[(T.cid[:], z(a, e))] * (not ahead)),
-              ["dd%d" % min(t, 1), "cid", "cidn"] + regs("oh", a, e) + regs("yy", a, e) + regs(zn, a, e), ["p2.z"])
-            if ahead:
-                S(act(part(out, a, e, 64, 68), T.tm[:, c], AF.Abs), ["tm"], ["ms"])
-                S(act(part(out, a, e, 0, 64), T.p2[:, 384:448], AF.Copy), ["p2.z"], regs("zs%d" % t, a, e))
+            S(gather(act(T.fd[:, a:e], T.ft[:].indirect(T.la[:, c]), AF.Copy, scale=T.dvf[:, t:t + 1]), 64, q="s"), ["fta", "ftb", "dvf"] + regs("la", a, e), regs("fd", a, e))
+            change = PLAN["early"] and t == 0 and b == 0
+            P(mm((ps("z", 0, 64), (T.cidn[:], T.fd[:, a:e]), (T.cidn[:], T.yy[:, a:e]), *[(T.cid[:], z(a, e))] * (not change))),
+              ["cid", "cidn"] + regs("fd", a, e) + regs("yy", a, e) + regs(zn, a, e), pn("z"))
+            S(act(out[:, 0:64], ps("z", 0, 64), AF.Copy if change else AF.Abs), pn("z"), regs("zs%d" % t, a, e))
+            if lastt:
+                when("out", a)
+                dma("y", T.ym[:, c], out[:, 64:68], regs("ms%d" % t, a, e), [], "outm%d" % b, 1050)
+                dma("y", T.yz[:, a:e], out[:, 0:64], regs("zs%d" % t, a, e), [], "outz%d" % b, 1200)
             else:
-                S(act(part(out, a, e, 0, 68), T.p2[:, 384:452], AF.Abs), ["p2.z", "p2.m"], regs("zs%d" % t, a, e))
-            if not lastt:
-                send("zr%d_%d" % (t + 1, b), part(out, a, e, 0, 68), T.zw[:] if ahead else part(T["zb%d" % (t + 1)], a, e, 0, 68), regs("zs%d" % t, a, e) + ["ms"] * ahead,
-                     regs("w1", a, e) if ahead else regs("y%d" % (t + 1), a, e) + regs("z%d" % (t + 1), a, e))
+                far, ms_, mr = T["zb%d" % (t + 1)][:, o:o + 68], regs("ms%d" % t, a, e), regs("y%d" % (t + 1), a, e)
+                if b in PLAN["ahead"][min(t, 1)]:
+                    when("tell", a)
+                    send("mr%d_%d" % (t + 1, b), out[:, 64:68], far[:, 64:68], ms_, mr)
+                    out, far, ms_, mr = out[:, 0:64], far[:, 0:64], [], []
+                when("move", a)
+                send("zr%d_%d" % (t + 1, b), out, T.zw[:] if change else far, regs("zs%d" % t, a, e) + ms_, ["zw"] if change else regs("z%d" % (t + 1), a, e) + mr)
 
         for a, e in USES:
-            n = e - a
-            c = slice(a // 16, e // 16)
             when("use", a)
-            ends = [(T.ss[:, back(32 * a + 2 * k + 2, 32 * e, 32, 6144)] if k < 15 else gg(a, e), T.ss[:, back(32 * a + 2 * k + 1, 32 * e, 32, 6144)])
-                    for k in range(16)]
-            mask = T.p4[:, 192 + a:192 + e]
-            if n > 64 or t == 0:
-                x, y = 6144 - 32 * e, 6144 - 32 * a
-                ends = [(T.ss[:, x + 29 - 2 * k:y:32] if k < 15 else T.gg[:, 192 - e:192 - a], T.ss[:, x + 30 - 2 * k:y:32]) for k in range(16)]
-
-                def turned(Q, ends=ends, n=n):
-                    for k, (hi, lo) in enumerate(ends):
-                        Q.matmul(T.p4[0:n, k:128:16], hi, T.cb[:, 0::16], True, False)
-                        ins = Q.matmul(T.p4[0:n, k:128:16], lo, T.cbm[:], False, True)
-                    return ins
-                P((turned, 32 * (64 * PE_CYCLE + PCALL)), ["cb", "cbm"] + regs("gg", a, e) + regs("ss", a, e), ["p4.t"])
-                S(act(T.st[0:n, :], T.p4[0:n, 0:128], AF.Sign, scale=-1.0, bias=253.5), ["p4.t"], ["st"])
-                P(mm(mask, (T.st[0:n, :], T.cidm[0:n, 128 - n:128]), (T.onb[0:n, :], T.cidm[0:n, 128 - n:128])), ["st", "cidm", "onb"], regs("p4.m", a, e))
-                when("write", a)
-                V(tt(T.fw[:, a:e], T.f4[:, a:e], mask, A.min), ["f4"] + regs("p4.m", a, e), regs("fw", a, e))
-                V(tt(T.fd[:, a:e], T.of[:, a:e], mask, A.subtract), ["of"] + regs("p4.m", a, e), regs("fd", a, e))
-                V(gather(tt(T.tb[:].indirect(T.sl[:, c]), T.fw[:, a:e], T.fd[:, a:e], A.max), n, SCATTER), regs("sl", a, e) + regs("fd", a, e) + regs("fw", a, e), ["tb"])
+            use = mask = ps("use", a, e)
+            names, slot = pn("use", a, e), [15 - k if k < 15 else 17 for k in range(16)]
+            when("sum", a)
+            if e - a == 128:
+                groups = [(use[:, k::16], (T.ind[:, rv(a, e), slot[k]], T.big[:, 15:143:16])) for k in range(16)]
+                groups[15] += ((T.gg[:, rv(a, e)], T.bigp[:, 15::16]),)
             else:
-                P(mm(T.p4[:, 128:128 + n], *[(T[m][:, 128 * k:128 * k + 128], x[i]) for k, x in enumerate(ends) for i, m in enumerate(("sel", "seln"))]),
-                  ["sel", "seln0", "seln1", "seln2", "seln3"] + regs("gg", a, e) + regs("ss", a, e), ["p4.u"])
-                V(ts(mask, T.p4[:, 128:128 + n], 254.0, None, A.is_lt), ["p4.u"], regs("p4.m", a, e))
-                when("new")
-                V(tt(T.fd[:, a:e], T.f4[:, a:e], T.of[:, a:e], A.subtract, rate=2.0), ["f4", "of"], regs("fd", a, e))
+                groups = [(use, (T.bigp[:], T.gg[:, up(a, e)]), *[(sel(k), T.ind[:, up(a, e), slot[k]]) for k in range(16)])]
+            P(mm(*groups), ["sel", "bigp"] + regs("gg", a, e) + regs("ind", a, e) + regs("r15", a, e), names)
+            when("use", a)
+            to = T.tb[:].indirect(T.sl[:, a // 16:e // 16])
+            if e - a == 128:
+                S(act(T.st[:], use, AF.Relu, scale=-512.0, bias=512 * 16 * 253.5), names, ["st"])
+                P(mm((ps("mask", 0, 128), (T.st[:], T.cid[:]))), ["st", "cid"], pn("mask"))
+                mask, names = ps("mask", 0, 128)[:, ::-1], pn("mask")
                 when("write", a)
-                V(tt(T.fw[:, a:e], T.fd[:, a:e], mask, A.mult), regs("fd", a, e) + regs("p4.m", a, e), regs("fw", a, e))
-                V(gather(tt(T.tb[:].indirect(T.sl[:, c]), T.fw[:, a:e], T.of[:, a:e], A.add), n, SCATTER), regs("sl", a, e) + ["of"] + regs("fw", a, e), ["tb"])
+                V(tt(T.fw[:, a:e], T.f4[:, a:e], mask, A.min), ["f4"] + names, regs("fw", a, e))
+                V(tt(T.dl[:, a:e], T.of[:, a:e], mask, A.subtract), ["of"] + names, regs("dl", a, e))
+                V(gather(tt(to, T.fw[:, a:e], T.dl[:, a:e], A.max), e - a, COST["scatter"]), regs("sl", a, e) + regs("dl", a, e) + regs("fw", a, e), ["tb"])
+            else:
+                V(ts(mask, use, 16 * 253.5, None, A.is_lt), names, names)
+                when("new", a)
+                V(tt(T.dl[:, a:e], T.f4[:, a:e], T.of[:, a:e], A.subtract, rate=2.0), ["f4", "of"], regs("dl", a, e))
+                when("write", a)
+                V(tt(T.fw[:, a:e], T.dl[:, a:e], mask, A.mult), regs("dl", a, e) + names, regs("fw", a, e))
+                V(gather(tt(to, T.fw[:, a:e], T.of[:, a:e], A.add), e - a, COST["scatter"]), regs("sl", a, e) + ["of"] + regs("fw", a, e), ["tb"])
 
     for t in range(STEPS):
         step(t)
-    t = STEPS - 1
-    now[:] = [1000.0, -1, None, 0]
-    dma("y", T.ym[:], T.yo[:, :, 64:68], regs("zs%d" % t, 0, 192), ["ym"], "outm", 1050)
-    dma("s", T.yz[:], T.yo[:, :, 0:64], regs("zs%d" % t, 0, 192), ["yz"], "outz", 1200)
-    behind.clear()
-    dma("y", T.ymc[:], T.tb[:, 0:512], ["tb"], ["ymc"], "outa", 1500)
+    now[:] = [STEPS - 1, "out", 9]
+    dma("s", T.ymc[:], T.tb[:, 768:1280], ["tb"], [], "outa", 1500)
     emit()
-    for s in ("outm", "outz", "outa"):
-        g.wait_ge(T.sem[s], 16)
+    for s in SEMAPHORES:
+        if s[:3] == "out":
+            g.wait_ge(T.sem[s], 16)
     g.wait_ge(T.sem.snd, n_out * sends[0])

@@ -3,93 +3,91 @@ from concourse.mybir import dt, AluOpType, AxisListType, ActivationFunctionType
 A = AluOpType
 AF = ActivationFunctionType
 STEPS = 5
-B16 = "bfloat16"
-F32 = "float32"
-F16 = "float16"
-I32 = "int32"
-U16 = "uint16"
+B16, F16, F32, I32, U16 = "bfloat16", "float16", "float32", "int32", "uint16"
 BLOCKS = [(128, 192), (64, 128), (0, 64)]
 PAIRED = [(64, 192), (0, 64)]
-USES = PAIRED
-PLAN = {"goal": BLOCKS, "mod": PAIRED, "lists": BLOCKS, "row": PAIRED, "ops": BLOCKS, "spread": BLOCKS, "head": BLOCKS, "scan": BLOCKS, "cmp": BLOCKS,
-        "needs": ["vs sv ss", "sv v v ss"], "adds": ["ss vv sv", "vs ss ss"],
-        "ml": "v", "save": "g", "cut": "g", "mal": "g", "hh": "s", "sl": "g", "la": "v", "masks": PAIRED[:1], "halve": True, "early": False, "ahead": [(0, 1, 2), (1, 2)]}
-MAIN, ZERO, MID = 64, 2112, 1600
+WHOLE = [(0, 192)]
+NEEDS = ["vs vs ss", "sv v v ss"]
+ADDS = ["ss vv ss", "vs ss ss"]
+AHEAD = [(0, 1, 2), (1, 2)]
+MAIN, TOP, ZERO = 64, 2112, 4160
 MAGIC = 1.5 * 2.0 ** 24
-BANKS = ["p%d" % b for b in range(8)]
 SCRATCH = {}
 for _names, _cols, _type in (
         ("prw adw", 4096, B16), ("glw imw", 512, B16), ("mci", 512, I32), ("tb", 1472, F32),
-        ("mi", 12, I32), ("dvs", 5, B16), ("dvf", 5, F32), ("wts", 1, B16), ("zb0", 192, B16), ("ze", 64, B16), ("zw", 64, F16),
-        ("d00 d01 d02 ft", ZERO + 16, B16), ("d1 ss", 3072, B16), ("ol", 192, U16), ("gg mb gi hh yy fd", 192, B16),
-        ("zt", 128 * 3, F16), ("q1 q3", 192, F16), ("mal", 24, F16), ("mf0", 12, F16), ("lst", 24, F32), ("acc", 3, F32), ("ev", 1, F32),
+        ("mi", 12, I32), ("dvs", 5, B16), ("dvf", 5, F32), ("wts", 1, B16), ("zb0", 192, B16),
+        ("d00 d01 d02 ft", ZERO + 16, B16), ("d1 ss", 3072, B16), ("ol", 192, U16), ("gg mb gi hh yy fd", 192, B16), ("st", 128, B16),
+        ("zt", 384, F16), ("q1 q3", 192, F16), ("mf0", 12, F16), ("lst", 12, F32), ("acc", 3, F32), ("acb", 4, B16), ("ev", 1, F32),
         ("ml sl la", 12, U16), ("kr wk yo", 216, F32), ("zb1 zb2 zb3 zb4 zs1 zs2 zs3 zs4", 216, F16),
-        ("eb wd ws", 1280, F16), ("of dl fw", 192, F32), ("f1 f2 f3 f4", 192, I32),
-        ("pi", 4, I32), ("pf", 4, F32), ("kk k37 qb1 qb3 r16 g16 zbias cew l127 l63 h32", 1, F32), ("onf st", 128, B16), ("acb", 3, B16), ("c68", 68, F32), ("wi", 216, F32),
-        ("kb", 72, F16), ("ie", 512, B16), ("ce", 1024, B16), ("edge", 256, F16), ("ib", 256, B16), ("big", 144, B16), ("ic top", 12, F32),
-        ("ig cid cidn c37 cb cq1 cq3 wb onb c8kn c4k c384 c384n c512n bigp", 128, B16)):
+        ("eb wd ws", 748, F16), ("of dl fw", 192, F32), ("f1 f3 f4", 192, I32),
+        ("pi", 4, I32), ("pf", 4, F32), ("kk k37 qb1 qb3 r16 g16 zbias cew l127 l63 h32", 1, F32), ("c68", 68, F32), ("wi", 216, F32),
+        ("kb", 72, F16), ("ie", 512, B16), ("ce", 1024, B16), ("edge", 256, F16), ("ib", 256, B16), ("big", 144, B16), ("ic top tops", 12, F32),
+        ("ig cid cidn c37 cb cq1 cq3 wb onb onf c8k c384n c512n bign", 128, B16)):
     for _n in _names.split():
         SCRATCH[_n] = ("sbuf", [128, _cols], _type)
 SCRATCH["tg"] = ("sbuf", [128, 2, 192], F16)
+SCRATCH["mal"] = ("sbuf", [128, 2, 12], F16)
 SCRATCH["ind"] = ("sbuf", [128, 192, 18], B16)
 SCRATCH["thw"] = ("sbuf", [128, 4 * STEPS, 18], B16)
+BANKS = ["p%d" % b for b in range(8)]
 for _b, _n in (("p0", 1024), ("p2", 1024), ("p4", 512), ("p5", 512), ("p6", 512), ("p7", 512)):
     SCRATCH[_b] = ("psum", [128, _n], F32)
-PSUM = {"use": ("p4", 0), "old": ("p4", 192), "mask": ("p4", 384), "turn": ("p5", 0), "goal": ("p5", 256), "sum": ("p6", 0), "u": ("p6", 192),
-        "met": ("p7", 0), "z": ("p7", 216), "r": ("p7", 280), "list": ("p7", 344), "all": ("p7", 368)}
-LOADS = ["mc", "m0", "z0", "ad", "gl", "pr", "wt", "dv"]
-SEMAPHORES = ["cv", "cs", "ct", "cg", "outa", "snd", "ze", "ebs", "wd0", "wd64"] + ["ld_" + n for n in LOADS] + ["out%s%d" % (x, b) for x in "zm" for b in range(len(BLOCKS))]
-SEMAPHORES += ["%sr%d_%d" % (x, t, b) for x in "zm" for t in range(1, STEPS) for b in range(len(BLOCKS))]
+PSUM = {"use": ("p4", 0), "old": ("p4", 192), "mask": ("p4", 384), "turn": ("p5", 0), "goal": ("p5", 256), "r": ("p5", 448),
+        "sum": ("p6", 0), "u": ("p6", 192), "z": ("p6", 384), "met": ("p7", 0), "own": ("p7", 216), "all": ("p7", 472)}
+LOADS = [("s", "m0", "mi"), ("y", "mc", "mci"), ("y", "ad", "adw"), ("s", "gl", "glw"), ("s", "z0", "zb0"), ("s", "wt", "wts"), ("s", "dv", "dvs"), ("y", "pr", "prw")]
+SEMAPHORES = ["cv", "cs", "ct", "cg", "outa", "snd", "ebs", "wd0", "wd64"] + ["ld_" + n for _, n, _ in LOADS]
+SEMAPHORES += ["out%s%d" % (x, b) for x in "zm" for b in range(3)] + ["%sr%d_%d" % (x, t, b) for x in "zm" for t in range(1, STEPS) for b in range(3)]
 
-COST = {"cycle": 0.83, "pe": 0.42, "call": 55.0, "wake": 100.0, "gather": 1.56, "scatter": 3.8, "send": 570.0, "flight": 2300.0, "wire": 300.0,
-        "first": 3400.0, "pcall": 8.0, "scall": 15.0, "gcall": 60.0, "psum": 40.0}
-EARLY = {}
-PERIOD = 14.0
-PHASE = "0g0u0h0W7ubJ9r0IdA3Rd35ee1e7eLeFdUaTf2fWh9hs0c0e0f0d8g72cSf0dkab9Acp8786b05D5A0T1m8jhbda9N4e7R7W7x9u8ncQ8c8R60bC8F8r92bp9d1U3Nbr7ZctcPdbdNfcdobm98aJe0c0eI3D31blgges46djepcu9ycTe8eVe3fycxdXanafcy9DeMeAgKdSh2hci9gphWiwiBbVdvdPeBg3hjeWfOg0h0f9eXfYeEgFfAgidFfkflewg5fqfrhwhCi0hUhViqcrczccaYdudHdl8EaOb99payfefBeOf4a0aPdYbEc8d4dfe5cMcWeRcBf7c6dreYeDfdetezgDeihtdggnfofHgPfzgJc1fT7hi6cedWbvdRhihzc5bOcwcl9T5VePdVegdmdGb2edddbaejdOdL97aEbsbTdp4kaFaGaKcOhrffgBhyf3eKfLg4huhDgtfIg6f5fxeQene9gkfjfifpfUfDgwiifMgLh5fVgQgvh1f8gWhqhvgMibkwjohJizjnjmjli2iDiKjHhnjtcVdIcddBdDdCdte4gbg99hfueZfghkhZdyftfXgagmhmd2dz4adig1cEotj6idk8wteHeSf1exeJfafCfZgcgydZgHhSgjicimhXiviohgihhlgzhPiyiFbBcN9ZeNcFaZfb1Ld0e2d1gogRcXadcn85eueaeqecfQgxhNh6i1ixfFbigrgSarfRj9ijiPhagXgdfKhFiRjehOh7iShLhMi5jkjMjTiH"
-_OLD5 = "0k0o0m0l1vbU9B0nd92bcq3Gerekecf4dWeuf8fZgaho5Q5h6F5L8O7WdXf2efa88ueB8v86bL6J6P3y7iaohC9Lbf0p717n7fb2bt8I9AaL7ZdV91araJbNaw426N5T3YcmcpaqfChkfBdpcjbieqeSeU4Z7Pdlghf75NcVepegaVdkbMcidsfEeDed99cacXcSb6eVibg0gwjLhMiwiOcBc8afcfd4dQfbeHgfdmfPglgnhgfOgrfSdDePfyfIeCgyfofTgcj7hJhxiZgei2gdidcEdfc6bqdZdOdNe9abbK7U5WeIg6fufGcg9Te49zbnen94eXc3dEdCd8fnczdIfhebfsf0f6hbgthUeEgYhrgghug9h2cdgDcZipcRaXccfzeyhAcnc5dndh8S7dfdeseWdFe2apeRdudKeAelbId29MbAcodT15aSctaDbzfjeLgIh9eJfwfNg7gXhGethfeifxfmg3g1flgFg5fAgufVfRiYf9b8hpdxhHgNgZfqheh7evhshnk0kehOiHiLh4i1hvkxj0jcjlhQjRdjejcydedbe1dzeNg8gEeYfFeQfQhNiCfYbufJgigRgVcscT5EbHimgPmDtelgnlrLeOdBewf1fafvgve8gMgJgTh1h0iGi4hPdLiFi3hiikhwiagKi6iXbOdi95fedH4bfrdwd7eMd5ckeodMdvcF7yeKeegLezh5gGftgbe6gQisiIfDfHjefii8hmjhjriNhcjohzhIhRk3k5k9gp"
-_OLD4 = "0j0M0h0f84bZ8Z0idu2vdF4Pe9eFe7ew7aaTfygcffhF0e0d0b0c8H7QdyfudH9wa4do9L9Fb75C7G0v0g98hjebbh6h8i8k7Fbe8Bbd97997Icp9O9M9gab9H1N7Tcm8Cc3c5bpdAgQf1c1a3c0e1eeeA4442ddgjfa58cs8henbJejdtbSdUemcxdq71czdRdje8cRhPfvg5iahTisiGdxdCf6eSgdhgfGfVfFgMfdfIfCfHgyfegGeyfOfBdsfifXhahzhnhZhVioetcncPcdc9dEdNdmdlaJbt9GaAfnfPeGfrbBbLdP8QcedkaGelcKaseLcXfpdaeqeXbgf8eoeCgKefhefzgkfRgqh7fQgSc4gf7KhxaQe5dzf9gZhEbobUcQcv9T7Mf0e2dpdrdGb9eidicZdfdQc6969Y9kc7cN45byac93cceJeTgEcSeEeKfLdMh8hIgBfAfof2fqfwdWf4glfWfDg2g7fNhDhwcLgOgYdIeYgwgAezh0eghpgXjOjJjmgxi0jjjtjgjhixiBj1j9jkcMdOc8dJd8dKd1ecfKgnawbDeRfEh9i8e0fbgegCgHgLcicq52dYg3g4nIkhhAkUwgepeaeQeBeWfhg0bAgigIgrgPi3hKi9ifeDiwh4gti4h5joiEgVj7bwd59XeZcTb0fs1UdveIeNf7h1d2a9cgbFeMerf5dLgUgzhHg8hch2i6iues9zhigDcahbiNhXi1iygRhoiJjbhRhliLg9hUibjdhhjuhM"
-_OLD3 = "150p0x0z7NbQbY0wdh84cu8Xe7eLe1f3cbbefxbxcfhv0q0s0t0u947YdcfecH8D8eeibn8E9Q6v7J0Q4M95gYew9V45680y8Kbt4paJaF8H8OdX9R9IagbKbv3p83da53cBbZ9Eejfkbjd9ctcddVepey4j6ReeeSeZ4Vcidtefbrd7dPaKdSeJdzaVe6c9dUeld8drh0cRhWijhzitiEdydje4fGdOgRflfWgffAenfKfLexeOfwgbfggwgsfvfCeEh2gpgehRhTh7ipbWcnbRcwdkdDcMdo9Oboa09GfmfyfqfM8W54e8au9udB9Peacm9HcEdNePd6eqecf6fXdKeTeNeVgyfsfpfDg5gVdMgFbDfddQhYbzdLbMaWgChqbpbTc5co9e7PdReocxd5dEaxe9cKd1f7dJdHdd9XbIc0dn4Fave5b0anhUeFfEgEfuetcyf2evhxg7f89weMf0gmaTcOffeBbwfjfIeHhnhjesgqgxdCgrgl6wdGh1fnhogGjHiQiDhygDgUi7iPjKhLiwifhgiNdedIc3dsd0dFdqdYfZg6b1c4fBfQgNiufbg0fNgceKgubqdb0v87h3jylihHmYcNoVeIdZc1fceuf48Ld2fYgighg9i8hSgoixi5irhfgzhOh4fthmfOiCbscz9meAc8b5ez4ob7eDe3gngZdicLcG9seddTgjeWgBfSemgQi2iFggeCbcfogMgkeGgTiShPinjzdAhaikiahbhsi0hhhNi1jsjCjgjJ"
-_OLD2 = "2G3765647Qbhaw54cAaL8U9Yd0dWdmdUbab8eAehgpgaXSXJYmXT8X8Kcf9kcu808t9laU8laQ820d4D8r9Afsd7bg8L6q8sah9jaS8Z9w8na09H9h9gabav9G6K817g6ebpbmc3dXcyaiaxaYb7d2dwbu6I7ecV7qdv6DcodxaI9ocxdqag95embrbUbbae6na59UcQereRgThqgZhAhOdjcYdBd5cbfDexeDeyf8dLf2ekdKejdJdPdddRdzdfeJf9e7g4g5fUgBghfw9Vc8bNbTc9cjaVbW8aaTaBa7d8ewdee88Gc1dradbtcRcic2cIcEdh9feoaMbdd1cTePdacNfvfagRfefGezeTfTeSftbkc0dygQaccWdGeeeifgbcbjbSbn7B8zcSd6cwbIcC9pctbQckcacUd4dn9ybebHdc8jascBbfbRcPcneFf0bFdbdZe5dYgqeYeLdte0dEcObwbEdodVe6eGeqeagcgEg8amdQfKg6g3dAfFebfEf6fQi6i7ineHhkgYhshxiIhIfLhLhRhNbKcDbYbXdIczcHf4eQdNeOdTffgmgvgFdlfueUfcg1eEgb8dbC6pcZdOedlPhzglhXise1dkdu9vdFb2alfofMeXf3dMgIfOgJhnh3fzgLfpfBeChugwhDh2b4bO9id3bZaKd99FcmegdCfVfS7FcJcdaNcLcvese9eVdpcXf5gGh7gAgriehFgCfRhbgth1hCfdhBigh5"
-_OLD = "7f7wa99Mg79O6HfiebgFdShRi2hSfXitj8jsjZlg4v5d623W2u5jdvcUcRcVcQdtdedxa5a0589D7HiJdGh1bFcfflbHbTdrdKezffcv926Q7h6d5e6edQbnbCfT9ZeWfRe27FkadWdu7I64gkgmgT9bbqfkavgdapi7g9gYhEi8jghsi6j9jFjhh9hKhXljhekbgsemhTiyk5lukOkBjHjyliktkolkiah2hghAhOi9hUhGjNjdg2kll7lcl4lmeqf2dgerepgyg39jg1gjfPg4iSgginjneAfKfAeLfBdDfZihgShjeBh0hngrhWj6jaizgtiYiuiDjSiojcjEiHlhjikJhafujoeXk4lxhyifgQikkgee9Cf7bU8LeyfxfQ8Ki1iKgWdFfCfYgldEeJeVfmf5fDgugIhmhufqfWhDgZgzjufEiVjqkid9i5eFiUiclCijj5ivibhMhYjek0kIk6jbiCiFhJiiimiIkdjvghiwjVhzlFkuhQjXk7kekfjpkNkThxgJj3kUneninhn9kQmJhHkSmSmQmgncmKn3eZgUhhgnidgRk1h5jCixiRjlk3j4jGlfkzfMkylykmcIgLfyiPmMn1ltmwgwknhPhdhFi4fNfvjjbPiQiMeUkAkrirkCkDmIiZm6l9mklNj7lUmDmUlMcufjcyeSfFiNePfLi3ish7hChBgPiGkZgcedh4gojPhljwkpdIkqiLlzlamvm1mGk9kKnul6kcmonlnonxmT"
-DUE = {"lists1": -4, "room1": -4, "keep1": -3, "lists3": -2.5, "room3": -2.5, "keep3": -1, "row3": -2.4, "goal3": -2.5, "mod3": -2.3, "spread3": -2.2,
-       "row1": -3.9, "goal1": -4, "mod1": -3.8, "spread1": -3.7, "ops1": -0.6,
-       "fill1": -1, "ops3": -0.5, "adds0": -0.05, "adds1": 0, "needs0": -0.05, "needs1": 0, "head1": -0.2, "scan1": -0.2, "less1": -0.2, "cmp1": 1, "pass1": 1, "move1": 1,
-       "needs2": 1.5, "adds2": 1.4, "adds3": 1.5, "needs3": 2.5, "head3": 1.2, "scan3": 2, "fill3": 2, "less3": 2, "cmp3": 2.5, "pass3": 2.6, "move3": 2.6,
-       "lists5": 2.7, "room5": 2.7, "row5": 2.8, "goal5": 2.8, "mod5": 2.9, "spread5": 2.9, "keep5": 5, "ops5": 2.6, "adds4": 3.9, "adds5": 4, "needs4": 4.9, "needs5": 5,
-       "head4": 4.4, "head5": 4.5, "scan4": 4.4, "scan5": 4.5, "fill4": 4.4, "fill5": 4.5, "less4": 4.4, "less5": 4.5, "cmp4": 4.9, "cmp5": 5, "use5": 5, "write5": 5.5,
-       "pass5": 6, "move5": 6,
-       "first3": 3.5, "place3": 5.2, "first5": 5.3, "place5": 5.35, "new5": 5.1, "use3": 5, "write3": 5.4, "count5": 7,
-       "const0": -9, "const1": -8, "const2": -7, "const3": -6, "const4": -1, "const5": 3, "const6": 4, "out1": 1, "out3": 2.6, "out5": 6, "out9": 6}
-ORDER, DAG = [], []
-
-
-def kind(o):
-    t, what, b = o["cls"]
-    return "%s%d%s" % (what, b, "'" * (t == 0))
-
-
-def sort(o):
-    return kind(o) + (o["q"] if o["fn"] else "")
+START = """
+pi_3 pi_ pi_4 pi_2 thwz_ onb_ c68_ half_ thw0_ zbias_ onf_ loady loady2 zbias_2 loads loads2 loads3 loads4 loads5 pi_5 kb_ lists5v lists5s room5s pf_
+cid_ cidn_ c384n_ c512n_ l127_ qb3_ g16_ ops5v ib_ imw_2 c8k_ ig_ h32_ goal5t qb1_ loady3 goal5s imw_ row5s cb_ goal5t2 goal5s2 sel_ wb_ mod5t mod5s
+ie_ edge_ wd_ wd_2 top_ count5g count5t c37_ adds1s cq3_ cq1_ mod5t3 mod5s2 d0z_ adds3v spread3t cew_ cew_2 ce_ ce_2 needs0v head1t count5v wd_3 ft_
+spread3s wi_ needs1s head1v ic_ wd_4 wd_5 count5v2 head1g head1g2 scan1v l63_ mod5t4 mod5s3 fill1t spread5t needs3s needs2v m0_ own5t kk_ less1t cmp1v
+head1s head3t own5s kb_2 r16_ tops_ kb_3 bign_ indz_ wk_ wk_2 wk_3 new5g own3t head3g head3g2 wd_6 wd_7 wd_8 wd_11 wd_12 wd_13 wd_14 wd_9 wd_15 wd_10
+fill3t own3s pass1t adds5s head3v scan3v less3t keep5g pass1v move1s wd_16 eb_ spread5s fill5t head3s own5g pass1s needs5s ft_2 d0z_2 cmp3v move1v
+dvf_ first5v2 tell1g tell1 head5g mod5t2 new5v head5t head5v own3g first3v2 pass3t move1s2 move1t k37_ new5s head5g2 scan5v less5t d0z_3 pass3v
+move1s3 move1g first3v5 new5v2 pass3s move3v move3s tell3g move1 tell3 move3s2 move3t cmp5v first5v4 first5v move3s3 move3g move3 first3v3 first3v4
+head5s sum3t first3v6 sum5t use5s pass5t new5v3 first3v tb_ lists1g+ room1s+ use3s use3t lists1s+ first3v8 first3v7 first5v3 place3v place3g place5v
+goal1t+ lists3g+ pass5v move5s pass5s goal1s+ goal1t2+ write5v2 place3g2 lists3s+ write3v2 write3v row3s+ mod3t+ write5v place5g2 place5g tell5g
+goal1s2+ spread1t+ write3v3 write5v3 room3s+ goal3t+ mod3s+ mod3t2+ mod3t3+ ops3v+ move5s2 spread1s+ goal3s+ goal3t2+ move5v move5t adds0v+ needs1v+
+adds1s+ head1g+ fill1t+ move5s3 goal3s2+ mod3s2+ head1t+ needs0s+ tell5 move5g move5"""
+ROUND = """
+ops3v mod3t2 spread1s goal3s move5v- goal3t2 move5t- adds1s adds0v tell5g- fill1t needs1v tell5- move5s3- goal3s2 move5g- head1g mod3s2 head1t head1g2
+mod3t4 needs0s needs2v spread3t move5- mod3s3 own3t adds3s head1v scan1v less1t lists5g ops5v new5g needs3v spread3s head1s head3t own3s room5s keep5g
+cmp1v own3g fill3t first3v3 head3g head3g2 lists5s goal5t head3v row5s mod5t pass1t adds5s keep1g first3v6 first3v5 scan3v mod5s head3s less3t pass1v
+pass1s goal5s move1s2 move1s goal5t2 goal5s2 first3v7 first3v first3v4 new5s move1v mod5t3 cmp3v mod5t2 move1t move1s3 count5g new5v first3v2 move1g
+needs5s new5v2 spread5t move1 first3v8 head5g new5v3 head5t count5t pass3t head5g2 pass3v spread5s sum3t fill5t pass3s place3v head5v move3s tell3g
+use3s move3v mod5s2 move3s2 scan5v use3t count5v mod5t4 move3t move3s3 move3g write3v2 mod5s3 write3v count5v2 less5t lists1g+ own5t head5s cmp5v
+place3g2 tell3 place3g write3v3 room1s+ lists1s+ own5s own5g goal1t+ move3 sum5t lists3g+ first5v2 first5v3 goal1s+ goal1t2+ first5v first5v4 pass5t
+mod3t+ use5s row3s+ goal1s2+ lists3s+ place5v room3s+ mod3s+ place5g2 place5g write5v2 spread1t+ keep3g+ goal3t+ write5v pass5v pass5s move5s mod3t3+
+move5s2 write5v3"""
+BUILT = {}
 
 
 def names(calls):
     seen, out = {}, []
     for o in calls:
-        k = (o["cls"][0], sort(o))
+        k = (o["step"], o["name"])
         seen[k] = seen.get(k, 0) + 1
         out.append(k[1] + (str(seen[k]) if seen[k] > 1 else ""))
     return out
 
 
+def places(calls):
+    start, turns = START.split(), ROUND.split()
+    first = {(x.count("+"), x.strip("+")): i for i, x in enumerate(start)}
+    later = {x.strip("+-"): i + len(turns) * (x.count("-") - x.count("+")) for i, x in enumerate(turns)}
+    return [first.get((o["step"], n), len(start) + len(turns) * o["step"] + later.get(n, 0)) for o, n in zip(calls, names(calls))]
+
+
 def scheduler(g, T, now):
     queues = {"g": g, "v": g.vector, "s": g.scalar, "t": g.tensor, "y": g.sync}
     calls = []
-    WAKE = COST["wake"]
 
-    def op(q, call, r=(), w=(), ext=None, after=None):
-        banks = {x[:2] for x in list(r) + list(w) if x[:2] in BANKS}
-        calls.append({"q": q, "fn": call[0], "ns": call[1] + COST["psum"] * (q in ("v", "s") and len(banks) > 0), "late": call[2] if len(call) > 2 else 0.0,
-                      "r": list(r), "w": list(w), "ext": ext, "after": after, "cls": tuple(now), "banks": banks})
+    def op(q, fn, r=(), w=(), ext=None, after=None):
+        name = now[1] + (q if fn else "") if now[1] else (list(w) + ["wd"])[0].split(".")[0] + "_"
+        calls.append({"q": q, "fn": fn, "r": list(r), "w": list(w), "ext": ext, "after": after, "step": now[0], "name": name,
+                      "banks": {x[:2] for x in list(r) + list(w) if x[:2] in BANKS}})
         return len(calls) - 1
 
     def needs(ops, banks):
@@ -114,106 +112,19 @@ def scheduler(g, T, now):
             deps.discard(i)
             o["deps"] = deps
 
-    def place(due, pre, users, look):
-        left = [len(p) for p in pre]
-        can = [0.0] * len(calls)
-        ready = {}
-        for i, n in enumerate(left):
-            if n == 0:
-                ready.setdefault(calls[i]["q"], []).append(i)
-        free, start, out, clock = {}, {}, [], {}
-        bank = {x: (None, 0.0) for x in BANKS}
-
-        def eta(u, depth):
-            t = can[u]
-            for p in pre[u]:
-                if p not in start:
-                    if depth == 0:
-                        return 1e18
-                    t = max(t, max(eta(p, depth - 1), free.get(calls[p]["q"], 0.0)) + calls[p]["ns"] + calls[p]["late"] + WAKE)
-            return t
-
-        def urgent(q, i):
-            found = [j for j in ready[q] if due[j] < due[i]]
-            seen, front = set(), [j for k, r in ready.items() if k != q for j in r if due[j] < due[i]]
-            for _ in range(3):
-                behind = {u for j in front for u in users[j] if due[u] < due[i]} - seen
-                seen |= behind
-                found += [u for u in behind if calls[u]["q"] == q]
-                front = [u for u in behind if calls[u]["q"] != q]
-            return found
-
-        def first(i):
-            t = can[i]
-            for x in calls[i]["banks"]:
-                k, e = bank[x]
-                if e > t and k != calls[i]["q"]:
-                    t = e
-            return t
-        while len(out) < len(calls):
-            t = 1e18
-            for k, r in ready.items():
-                if r:
-                    x = max(min(map(first, r)), clock.get(k, 0.0), free.get(k, 0.0))
-                    if x < t:
-                        t, q = x, k
-            can_go = [j for j in ready[q] if first(j) <= t + 1]
-            i = min(can_go, key=lambda j: due[j])
-            if q and calls[i]["ns"] > 300:
-                soon = min([first(u) if left[u] == 0 else eta(u, 3) for u in urgent(q, i)] + [1e18])
-                if t < soon < t + look * calls[i]["ns"]:
-                    short = [j for j in can_go if t + calls[j]["ns"] <= soon + 30]
-                    if not short:
-                        clock[q] = min([soon] + [x for x in map(first, ready[q]) if x > t + 1])
-                        continue
-                    i = min(short, key=lambda j: due[j])
-            o = calls[i]
-            start[i] = t
-            end = t + o["ns"]
-            if q:
-                free[q] = end
-            for x in o["banks"]:
-                bank[x] = (q, end + WAKE)
-            out.append(i)
-            ready[q].remove(i)
-            for u in users[i]:
-                can[u] = max(can[u], end + (0.0 if calls[u]["after"] == i else o["late"] + WAKE))
-                left[u] -= 1
-                if left[u] == 0:
-                    ready.setdefault(calls[u]["q"], []).append(u)
-        return out, start
-
     def order():
-        if not ORDER:
+        if not BUILT:
             needs(calls, False)
-            pre = [set(o["deps"]) | ({o["after"]} if o["after"] is not None else set()) for o in calls]
-            users = [set() for _ in calls]
-            for i, p in enumerate(pre):
-                for d in p:
-                    users[d].add(i)
-            chain = [0.0] * len(calls)
-            for i in range(len(calls) - 1, -1, -1):
-                chain[i] = calls[i]["ns"] + calls[i]["late"] + WAKE + max([chain[u] for u in users[i]] + [0.0])
-            due = [1000 * (PERIOD * o["cls"][0] + DUE.get(kind(o), DUE.get(kind(o)[:-1], 0.0))) - chain[i] / 1000 - EARLY.get(sort(o), 0.0) for i, o in enumerate(calls)]
-            DAG.append((calls, pre, users, place, due))
-            if PHASE:
-                AB = "0123456789abcdefghijklmnopqrstuvwxyzABCDEFGHIJKLMNOPQRSTUVWXYZ"
-                ks = sorted(set(names(calls)))
-                phase = {k: ((AB.index(PHASE[2 * i]) * 62 + AB.index(PHASE[2 * i + 1]) + 800) % 3844) * PERIOD / len(ks) for i, k in enumerate(ks)}
-                key = [PERIOD * max(0, o["cls"][0]) + phase[n] for o, n in zip(calls, names(calls))]
-                left = [len(p) for p in pre]
-                ready = [i for i, n in enumerate(left) if n == 0]
-                while ready:
-                    i = min(ready, key=lambda j: (key[j], j))
-                    ready.remove(i)
-                    ORDER.append(i)
-                    for u in users[i]:
-                        left[u] -= 1
-                        if left[u] == 0:
-                            ready.append(u)
-            else:
-                ORDER[:] = place(due, pre, users, EARLY.get("look", 1900) / 1e4)[0]
-        return [calls[i] for i in ORDER]
+            pre = [o["deps"] | ({o["after"]} - {None}) for o in calls]
+            place, done, out = places(calls), set(), []
+            left = sorted(range(len(calls)), key=lambda i: (place[i], i))
+            while left:
+                i = next(j for j in left if pre[j] <= done)
+                left.remove(i)
+                done.add(i)
+                out.append(i)
+            BUILT.update(calls=calls, pre=pre, order=out)
+        return [calls[i] for i in BUILT["order"]]
 
     def emit():
         ops = order()
@@ -237,11 +148,7 @@ def scheduler(g, T, now):
                 k[key] = max(k.get(key, 0), val)
             waits.append(mine)
             snap.append(dict(k))
-        last = {}
-        for i, o in enumerate(ops):
-            if not o["ext"]:
-                last[o["q"]] = i
-        need.update(last.values())
+        need.update({o["q"]: i for i, o in enumerate(ops) if not o["ext"]}.values())
         count = {}
         for i, o in enumerate(ops):
             if i in need and not o["ext"]:
@@ -269,12 +176,8 @@ def scheduler(g, T, now):
     return op, emit
 
 
-def regs(name, a, b):
+def regs(name, a=0, b=192):
     return ["%s.%d" % (name, c) for c in range(a // 32, (b + 31) // 32)]
-
-
-def every(name):
-    return regs(name, 0, 192)
 
 
 def size(ap):
@@ -299,174 +202,75 @@ def down(a, n, step=1):
     return slice(a, stop if stop >= 0 else None, -step)
 
 
+def up(a, e):
+    return down(191 - a, e - a)
+
+
+def rv(a, e):
+    return slice(192 - e, 192 - a)
+
+
+def ts(out, in0, s1, s2, *o):
+    return lambda Q: Q.tensor_scalar(out, in0, s1, s2, *o)
+
+
+def tt(out, a, b, o):
+    return lambda Q: Q.tensor_tensor(out, a, b, o)
+
+
+def cp(out, a):
+    return lambda Q: Q.tensor_copy(out, a)
+
+
+def scan(out, a, b, o0, o1):
+    return lambda Q: Q.tensor_tensor_scan(out, a, b, 0.0, o0, o1)
+
+
+def act(out, a, f=AF.Copy, **k):
+    return lambda Q: Q.activation(out, a, f, **k)
+
+
+def ms(out, c):
+    return lambda Q: Q.memset(out, c)
+
+
+def mm(*groups, start=True, stop=True):
+    def fn(Q):
+        for x in groups:
+            for i, y in enumerate(x[1:]):
+                ins = Q.matmul(y[2] if len(y) > 2 else x[0], y[0], y[1], start and i == 0, stop and i == len(x) - 2)
+        return ins
+    return fn
+
+
+def iota(out, pattern, base=0, cm=0):
+    return lambda Q: Q.iota(out, pattern, base, cm, allow_small_or_imprecise_dtypes=True)
+
+
+def move(out, a):
+    return lambda Q: Q.affine_select(out, a, [[0, size(out)]], A.is_ge, 0.0, 0, 0)
+
+
 def rank_program(g, core, T, topo):
     rank = T.rank_of(core)
     if rank is None:
         return
-    now = [-1, None, 0]
+    now = [0, "load"]
     op, emit = scheduler(g, T, now)
     nxt = T.cores[(rank + 1) % len(T.cores)]
     mask_out = topo.mask(core, nxt)
     n_out, n_in = len(topo.engines(core, nxt)), len(topo.engines(T.cores[rank - 1], core))
     rid, pid = topo.addr(nxt)[:2]
-    CYCLE, CALL = COST["cycle"], COST["call"]
+    V, S, P, G = [lambda fn, r, w, q=q: op(q, fn, r, w) for q in "vstg"]
+    behind, sends = {}, [0]
 
-    def V(fn, r=(), w=()):
-        op("v", fn, r, w)
-
-    def S(fn, r=(), w=()):
-        op("s", fn, r, w)
-
-    def P(fn, r=(), w=()):
-        op("t", fn, r, w)
-
-    def G(fn, r=(), w=()):
-        op("g", fn, r, w)
-
-    def ns(n, rate=1.0):
-        return max(64, n * rate) * CYCLE + CALL
-
-    def ts(out, in0, s1, s2, *o, rate=1.0):
-        return (lambda Q: Q.tensor_scalar(out, in0, s1, s2, *o)), ns(size(out), rate)
-
-    def tt(out, a, b, o, rate=1.0):
-        return (lambda Q: Q.tensor_tensor(out, a, b, o)), ns(size(b), rate)
-
-    def cp(out, a, rate=1.0):
-        return (lambda Q: Q.tensor_copy(out, a)), ns(size(out), rate)
-
-    def scan(out, a, b, o0, o1, rate):
-        return (lambda Q: Q.tensor_tensor_scan(out, a, b, 0.0, o0, o1)), ns(size(out), rate)
-
-    def act(out, a, f, **k):
-        return (lambda Q: Q.activation(out, a, f, **k)), ns(size(out)) + COST["scall"] + 20.0 * ("accum_out" in k)
-
-    def ms(out, c, rate=0.5):
-        return (lambda Q: Q.memset(out, c)), ns(size(out), rate)
-
-    def gather(call, n, rate=COST["gather"], q="v"):
-        return call[0], 70 + 15 * (q == "s") + n * rate * CYCLE
-
-    def mm(*groups, start=True, stop=True):
-        def fn(Q):
-            for x in groups:
-                for i, y in enumerate(x[1:]):
-                    ins = Q.matmul(y[2] if len(y) > 2 else x[0], y[0], y[1], start and i == 0, stop and i == len(x) - 2)
-            return ins
-        return fn, sum(max(min(64, size(y[0])), size(y[1])) * COST["pe"] + COST["pcall"] for x in groups for y in x[1:])
-
-    def iota(out, pattern, base=0, cm=0):
-        return (lambda Q: Q.iota(out, pattern, base, cm, allow_small_or_imprecise_dtypes=True)), 130 + COST["gcall"] + 2 * size(out) * CYCLE
-
-    def pick(out, a, pattern, o, cm):
-        return (lambda Q: Q.affine_select(out, a, pattern, o, 0.0, 0, cm)), 170 + COST["gcall"] + 2 * size(out) * CYCLE
-
-    def move(out, a):
-        return pick(out, a, [[0, size(out)]], A.is_ge, 0)
-
-    def copy(q, out, a, r, w):
-        op(q, move(out, a) if q == "g" else cp(out, a) if q == "v" else act(out, a, AF.Copy), r, w)
-
-    behind = {}
-
-    def dma(q, out, a, r, w, sem, late, n=1):
-        behind[q] = op(q, ((lambda Q: Q.dma_start(out, a)), 100.0, late), r, w, (sem, 16 * n, True), behind.get(q))
-
-    for q, name, buf, late in (("s", "m0", "mi", 1050), ("y", "mc", "mci", 1800), ("y", "ad", "adw", 3600), ("s", "gl", "glw", 1350), ("s", "z0", "zb0", 1400),
-                               ("s", "wt", "wts", 1400), ("s", "dv", "dvs", 1400), ("y", "pr", "prw", 5400)):
-        dma(q, T[buf][:], T[name][:], [], every("z0") if name == "z0" else [buf], "ld_" + name, late)
-    behind.clear()
-
-    def const(b):
-        now[:] = [0, "const", b]
-
-    def scaled(out, a, scale, bias, r, w):
-        S(act(out, a, AF.Copy, scale=scale, bias=bias), r, w)
-
-    def fill(out, c, r, w):
-        scaled(out, T.onb[0:out.shape[0], 0:size(out)], c, 0.0, ["onb"] + r, w)
-    const(0)
-    k4, grf, odf, hf = [T.pf[:, i:i + 1] for i in range(4)]
-    for i, cm in enumerate((64, 1, 512, 16)):
-        G(((lambda Q, i=i, cm=cm: Q.iota(T.pi[:, i:i + 1], [[0, 1]], 0, cm)), 130.0 + COST["gcall"]), [], ["pi%d" % i])
-    V(ts(T.pi[:], T.pi[:], 4, 63, A.arith_shift_right, A.bitwise_and), ["pi0", "pi1", "pi2", "pi3"], ["pi"])
-    V(cp(T.pf[:], T.pi[:]), ["pi"], ["pf"])
-    V(ms(T.onb[:], 1.0), [], ["onb"])
-    G(pick(T.cid[:], T.onb[:], [[-1, 128]], A.is_equal, 1), ["onb"], ["cid"])
-    G(iota(T.ig[:], [[1, 8], [0, 16]]), [], ["ig"])
-    V(ts(T.cb[:], T.ig[:], grf, None, A.is_equal, rate=0.5), ["ig", "pf"], ["cb"])
-    for name, src, scale, bias in (("kk", k4, 0.25, 0.0), ("k37", k4, 296.0, -2.0 ** 18), ("r16", k4, -4.0, 0.0), ("g16", grf, 16.0, 15.0), ("l127", k4, -0.25, 127.0),
-                                   ("l63", k4, -0.25, 63.0), ("h32", hf, 1.0, -32.0), ("qb1", odf, 80.0, -1280.5 + 2.0 ** -13), ("qb3", odf, 80.0, -1280.5 + 2.0 ** -10)):
-        scaled(T[name][:], src, scale, bias, ["pf"], [name])
-    const(1)
-    G(iota(T.ib[:], [[1, 256]]), [], ["ib"])
-    V(ts(T.big[:], T.ib[:, 0:144], T.g16[:], -16.0, A.is_equal, A.mult, rate=0.5), ["ib", "g16"], ["sel"])
-    scaled(T.bigp[:], T.big[:, 0:128], -1.0, 0.0, ["sel"], ["bigp"])
-
-    def sel(k):
-        return T.big[:, 15 - k:143 - k]
-    for name, src, c in (("cidn", "cid", -1.0), ("c37", "cid", 37.0), ("c8kn", "cid", -8192.0), ("c4k", "cid", 4096.0), ("c384", "cid", 384.0),
-                         ("c384n", "cid", -384.0), ("c512n", "cid", -512.0), ("cq1", "cb", -256.0), ("cq3", "cb", -32.0)):
-        V(ts(T[name][:], T[src][:], c, None, A.mult, rate=0.5), [src], [name])
-    V(ts(T.wb[:], T.cb[:], T.wts[:], None, A.mult, rate=0.5), ["cb", "wts"], ["wb"])
-    S(act(T.dvf[:], T.dvs[:], AF.Copy), ["dvs"], ["dvf"])
-    const(2)
-    V(cp(T.imw[:, 0:256], T.ib[:], 0.5), ["ib"], ["imwa"])
-    V(ts(T.imw[:, 256:512], T.ib[:], -256.0, None, A.add, rate=0.5), ["ib"], ["imwb"])
-    G(move(T.mf0[:], T.mi[:]), ["mi"], every("m0"))
-    const(3)
-    G(iota(T.cew[:], [[0, 1]], 128), [], ["cewa"])
-    G(((lambda Q: Q.affine_select(T.cew[:], T.cew[:], [[0, 1]], A.is_ge, 1.0, -64, 1)), 170.0 + COST["gcall"]), ["cewa"], ["cewa", "cewb"])
-    fill(T.zbias[:], 0.0, [], ["zbias"])
-    fill(T.zbias[0:64, :], -0.5, ["zbias"], ["zbias"])
-    G(iota(T.ie[:], [[1, 32], [0, 16]]), [], ["ie"])
-    for i, h in enumerate((hf, T.h32[:])):
-        V(ts(T.ce[:, 512 * i:512 * i + 512], T.ie[:], h, T.cew[:], A.is_equal, A.mult, rate=0.5), ["ie", "pf", "h32", "cewa", "cewb"], ["ce%d" % i])
-    fill(T.thw[:, :, 0], 0.0, [], ["thwz"])
-    fill(T.thw[:, 0:4, 1:18], -2.0, [], ["thw0"])
-    const(4)
-    for b in range(len(BLOCKS)):
-        G(iota(T["d0%d" % b][:, MAIN + 1024:ZERO + 1:ZERO - MAIN - 1024], [[0, 2]]), [], ["d0z%d" % b])
-    G(iota(T.ft[:, ZERO:ZERO + 16], [[0, 16]]), [], ["ftb"])
-    V(ms(T.ft[:, 0:MAIN + 1024], 1.0), [], ["fta"])
-    G(iota(T.ind[:, :, 0], [[0, 192]]), [], ["indz"])
-    G(iota(T.wi[:], [[0, 3], [-256, 4], [1, 18]], MAIN + 1007), [], ["wi"])
-    G(iota(T.ic[:], [[0, 3], [16, 4]]), [], ["ic"])
-    S(act(T.wk[:], T.wi[:], AF.Identity, bias=T.r16[:]), ["wi", "r16"], ["wk"])
-    S(act(T.wk[:, 1::18], T.ic[:], AF.Identity, scale=-1.0, bias=T.l63[:]), ["ic", "l63", "wk"], ["wk"])
-    fill(T.wk[:, 17::18], float(ZERO), ["wk"], ["wk"])
-    fill(T.kb[:], -2056.0, [], ["kb"])
-    fill(T.kb[:, 17::18], 60000.0, ["kb"], ["kb"])
-    fill(T.kb[:, 0::18], (4096 + 1152 - MID) / 8192, ["kb"], ["kb"])
-    fill(T.c68[:], -MAGIC - 2.0, [], ["c68"])
-    fill(T.onf[:], 1 / 32, [], ["onf"])
-    const(5)
-    G(iota(T.top[:], [[16, 12]], 1280), [], ["top"])
-    V(ts(T.edge[:], T.ib[:], T.l127[:], 2000.0, A.is_ge, A.mult, rate=0.5), ["ib", "l127"], ["edge"])
-    waves, o = [], 0
-    for a, e in USES:
-        n = e - a
-        waves.append(o)
-        for k in range(n // 16):
-            dma("y", T.wd[:, o + k * n:o + k * n + n], T.edge[:, 112 - 16 * k:112 - 16 * k + n], ["edge"], ["wd%d" % a] * (k == n // 16 - 1), "wd%d" % a, 1500, k + 1)
-        S(act(T.wd[:, down(o + n * n // 16 - 1, n // 16, n)], T.top[:, a // 16:e // 16], AF.Identity, bias=T.kk[:]), ["top", "kk", "wd%d" % a], ["wd%d" % a])
-        o += n * n // 16
-    dma("y", T.eb[:], T.wd[:], ["wd%d" % a for a, e in USES], ["eb%d" % k for k in range(12)], "ebs", 1500)
-    const(6)
-    G(move(T.tb[:, 768:1280], T.mci[:]), ["mci"], ["tb"])
-
-    sends = [0]
+    def dma(q, out, a, r, w, sem, n=1):
+        behind[q] = op(q, lambda Q: Q.dma_start(out, a), r, w, (sem, 16 * n, True), behind.get(q))
 
     def send(name, src, dst, r, w):
         sends[0] += 1
-        i = op("g", ((lambda Q: Q.remote_dma(dst, src, T.sem[name], T.sem.snd, pid, rid, mask_out)), COST["send"]), r, [], ("snd%d" % sends[0], 0, False))
-        op("d", (None, COST["wire"], COST["flight"] - COST["wire"] + COST["first"] * (sends[0] == 1)), [], w, (name, n_in, False), i)
-
-    def up(a, e):
-        return down(191 - a, e - a)
-
-    def rv(a, e):
-        return slice(192 - e, 192 - a)
+        i = op("g", lambda Q: Q.remote_dma(dst, src, T.sem[name], T.sem.snd, pid, rid, mask_out), r, [], ("snd%d" % sends[0], 0, False))
+        op("d", None, [], w, (name, n_in, False), i)
 
     def ps(name, a, e):
         bank, o = PSUM[name]
@@ -475,23 +279,88 @@ def rank_program(g, core, T, topo):
     def pn(name, a=0, e=32):
         return regs(PSUM[name][0] + name, a, e)
 
-    def split(a, e):
-        return [(max(a, x), min(e, y)) for x, y in BLOCKS if max(a, x) < min(e, y)]
-
     def slots(a, e, shift=0, step=1):
         y = a // 64 * 64 + 64
         return T["d0%d" % (2 - a // 64)][:, MAIN + 16 * (y - e) + shift:MAIN + 16 * (y - a) + shift:step]
 
+    def sel(k):
+        return T.big[:, 15 - k:143 - k]
+
+    for q, name, buf in LOADS:
+        dma(q, T[buf][:], T[name][:], [], regs("z0") if name == "z0" else [buf], "ld_" + name)
+    behind.clear()
+
+    now[1] = None
+    k4, grf, odf, hf = [T.pf[:, i:i + 1] for i in range(4)]
+    for i, cm in enumerate((64, 1, 512, 16)):
+        G(lambda Q, i=i, cm=cm: Q.iota(T.pi[:, i:i + 1], [[0, 1]], 0, cm), [], ["pi.%d" % i])
+    V(ts(T.pi[:], T.pi[:], 4, 63, A.arith_shift_right, A.bitwise_and), regs("pi", 0, 128), ["pi"])
+    V(cp(T.pf[:], T.pi[:]), ["pi"], ["pf"])
+    V(ms(T.onb[:], 1.0), [], ["onb"])
+    G(lambda Q: Q.affine_select(T.cid[:], T.onb[:], [[-1, 128]], A.is_equal, 0.0, 0, 1), ["onb"], ["cid"])
+    G(iota(T.ig[:], [[1, 8], [0, 16]]), [], ["ig"])
+    V(ts(T.cb[:], T.ig[:], grf, None, A.is_equal), ["ig", "pf"], ["cb"])
+    for name, src, scale, bias in (("kk", k4, 0.25, 0.0), ("k37", k4, 296.0, -2.0 ** 18), ("qb1", odf, 80.0, -1280.5 + 2.0 ** -13),
+                                   ("qb3", odf, 80.0, -1280.5 + 2.0 ** -10), ("g16", grf, 16.0, 15.0),
+                                   ("r16", k4, 4.0, 0.0), ("l127", k4, -0.25, 127.0), ("l63", k4, 0.25, TOP - 63.0), ("h32", hf, 1.0, -32.0)):
+        S(act(T[name][:], src, scale=scale, bias=bias), ["pf"], [name])
+    G(iota(T.ib[:], [[1, 256]]), [], ["ib"])
+    V(ts(T.big[:], T.ib[:, 0:144], T.g16[:], 16.0, A.is_equal, A.mult), ["ib", "g16"], ["sel"])
+    for name, src, c in (("bign", "big", -1.0), ("cidn", "cid", -1.0), ("c37", "cid", 37.0), ("c8k", "cid", 8192.0), ("c384n", "cid", -384.0),
+                         ("c512n", "cid", -512.0), ("cq1", "cb", -256.0), ("cq3", "cb", -32.0)):
+        V(ts(T[name][:], T[src][:, 0:128], c, None, A.mult), ["sel" if src == "big" else src], [name])
+    V(ts(T.wb[:], T.cb[:], T.wts[:], None, A.mult), ["cb", "wts"], ["wb"])
+    S(act(T.dvf[:], T.dvs[:]), ["dvs"], ["dvf"])
+    V(cp(T.imw[:, 0:256], T.ib[:]), ["ib"], ["imw.0"])
+    V(ts(T.imw[:, 256:512], T.ib[:], -256.0, None, A.add), ["ib"], ["imw.1"])
+    G(move(T.mf0[:], T.mi[:]), ["mi"], regs("m0"))
+    G(iota(T.cew[:], [[0, 1]], 128), [], ["cew"])
+    G(lambda Q: Q.affine_select(T.cew[:], T.cew[:], [[0, 1]], A.is_ge, 1.0, -64, 1), ["cew"], ["cew"])
+    V(ms(T.zbias[:], 0.0), [], ["zbias"])
+    V(ms(T.zbias[0:64, :], -0.5), ["zbias"], ["zbias"])
+    G(iota(T.ie[:], [[1, 32], [0, 16]]), [], ["ie"])
+    for i, h in enumerate((hf, T.h32[:])):
+        V(ts(T.ce[:, 512 * i:512 * i + 512], T.ie[:], h, T.cew[:], A.is_equal, A.mult), ["ie", "pf", "h32", "cew"], ["ce.%d" % i])
+    V(ms(T.thw[:, :, 0], 0.0), [], ["thwz"])
+    V(ms(T.thw[:, 0:4, 1:18], -2.5), [], ["thw0"])
+    for b in range(3):
+        G(iota(T["d0%d" % b][:, MAIN + 1024:ZERO + 1:ZERO - MAIN - 1024], [[0, 2]]), [], ["d0z.%d" % b])
+    G(iota(T.ft[:, ZERO:ZERO + 16], [[0, 16]]), [], ["ft.0"])
+    V(ms(T.ft[:, 0:MAIN + 1024], 1.0), [], ["ft.1"])
+    G(iota(T.ind[:, :, 0], [[0, 192]]), [], ["indz"])
+    G(iota(T.wi[:], [[0, 3], [256, 4], [-1, 18]], TOP - MAIN - 1007), [], ["wi"])
+    G(iota(T.ic[:], [[0, 3], [16, 4]]), [], ["ic"])
+    S(act(T.wk[:], T.wi[:], AF.Identity, bias=T.r16[:]), ["wi", "r16"], ["wk"])
+    S(act(T.wk[:, 1::18], T.ic[:], AF.Identity, bias=T.l63[:]), ["ic", "l63", "wk"], ["wk"])
+    V(ms(T.wk[:, 17::18], float(TOP - ZERO)), ["wk"], ["wk"])
+    V(ms(T.acb[:, 3:4], 0.125), [], ["half"])
+    for x, c in ((T.kb[:], -2056.0), (T.kb[:, 17::18], 60000.0), (T.kb[:, 0::18], 1152 / 8192)):
+        S(act(x, T.onb[:, 0:size(x)], scale=c), ["onb", "kb"], ["kb"])
+    V(ms(T.c68[:], -MAGIC - 2.0), [], ["c68"])
+    V(ms(T.onf[:], 1 / 32), [], ["onf"])
+    G(iota(T.top[:], [[16, 12]], 1280), [], ["top"])
+    S(act(T.tops[:], T.top[:], AF.Identity, bias=T.kk[:]), ["top", "kk"], ["tops"])
+    V(ts(T.edge[:], T.ib[:], T.l127[:], 2000.0, A.is_ge, A.mult), ["ib", "l127"], ["edge"])
+    waves, o = [], 0
+    for a, e in PAIRED:
+        n, c = e - a, a // 16
+        h, ends = n // 32, {}
+        for i in range(h):
+            ends[c + 2 * h - 1 - i], ends[c + i] = o + (n + 2) * i + n + 1, o + (n + 18) * (i + 1)
+        tails = [(slice(c, c + h), slice(o + n + 17, o + (n + 18) * h, n + 18)), (slice(c + h, c + 2 * h), down(o + (n + 2) * (h - 1) + n, h, n + 2))]
+        waves.append((slice(o, o + (n + 18) * h), ends, tails))
+        for i, k in enumerate(ends):
+            w = 16 * (k - c) + 17
+            dma("y", T.wd[:, ends[k] - w:ends[k]], T.edge[:, 111:111 + w], ["edge"], ["wd.%d" % a] * (i == 2 * h - 1), "wd%d" % a, i + 1)
+        for x, y in tails:
+            G(move(T.wd[:, y], T.tops[:, x]), ["tops", "wd.%d" % a], ["wd.%d" % a])
+        o += (n + 18) * h
+    dma("y", T.eb[:], T.wd[:], ["wd.0", "wd.64"], ["eb.%d" % k for k in range(12)], "ebs")
+    G(move(T.tb[:, 768:1280], T.mci[:]), ["mci"], ["tb"])
+
     def step(t):
-        lastt = t == STEPS - 1
-
-        def batches(what):
-            return PLAN[what] if t else [(0, 192)]
-
-        def lists(buf, a, e):
-            x, y = [m for m in batches("mod") if m[0] <= a < m[1]][0]
-            o = x // 8 + (a - x) // 16
-            return buf[:, o:o + (e - a) // 16], buf[:, o + (y - x) // 16:o + (y - x + e - a) // 16]
+        lastt, later = t == STEPS - 1, min(t, 1)
+        blocks, paired = (BLOCKS, PAIRED) if t else (WHOLE, WHOLE)
         mfn, zn = ("y%d" % t if t else "m0"), "z%d" % t
         thw, thn = T.thw[:, 4 * t:4 * t + 4, :], "thw%d" % t
 
@@ -501,212 +370,188 @@ def rank_program(g, core, T, topo):
 
         def mf(a, e):
             o = 9 * a // 8 + 64
-            return T["zb%d" % t][:, o:o + 4] if t else T.mf0[:, a // 16:e // 16]
+            return T["zb%d" % t][:, o:o + 4] if t else T.mf0[:]
 
         def when(what, a=0):
-            now[:] = [t, what, 5 - a // 32]
+            now[:] = [t, "%s%d" % (what, 5 - a // 32)]
 
-        if PLAN["early"] and t < 2:
-            a, e = BLOCKS[0]
-            when("early", a)
-            if t == 0:
-                send("ze", z(a, e), T.ze[:], regs(zn, a, e), ["ze"])
-            else:
-                P(mm((ps("z", 0, 64), (T.cid[:], T.ze[:]), (T.cid[:], T.zw[:]))), ["cid", "ze", "zw"], pn("z"))
-                S(act(z(a, e), ps("z", 0, 64), AF.Abs), pn("z"), regs(zn, a, e))
-
-        for a, e in BLOCKS if t else [(0, 192)]:
+        for a, e in blocks:
             c = slice(a // 16, e // 16)
             when("lists", a)
             if t == 0:
-                V(cp(T.ml[:, c], T.mi[:, c]), ["mi"], regs("ml", a, e))
+                V(cp(T.ml[:], T.mi[:]), ["mi"], regs("ml"))
             else:
-                copy(PLAN["ml"], T.ml[:, c], mf(a, e), regs(mfn, a, e), regs("ml", a, e))
+                G(move(T.ml[:, c], mf(a, e)), regs(mfn, a, e), regs("ml", a, e))
             when("keep", a)
-            scaled(T.wk[:, 18 * c.start:18 * c.stop:18], mf(a, e), -1.0, float(MID), ["wk"] + regs(mfn, a, e), regs("keep", a, e))
-        for a, e in batches("lists"):
+            G(move(T.wk[:, 18 * c.start:18 * c.stop:18], mf(a, e)), ["wk"] + regs(mfn, a, e), regs("keep", a, e))
+        for a, e in blocks:
             when("lists", a)
-            S(gather(act(T.gg[:, up(a, e)], T.glw[:].indirect(T.ml[:, a // 16:e // 16]), AF.Copy), e - a, q="s"), ["glw"] + regs("ml", a, e), regs("gg", a, e))
-        for a, e in batches("row"):
+            S(act(T.gg[:, up(a, e)], T.glw[:].indirect(T.ml[:, a // 16:e // 16])), ["glw"] + regs("ml", a, e), regs("gg", a, e))
+        for a, e in paired:
             when("row", a)
-            S(gather(act(T.mb[:, a:e], T.imw[:].indirect(T.ml[:, a // 16:e // 16]), AF.Copy), e - a, q="s"), ["imwa", "imwb"] + regs("ml", a, e), regs("mb", a, e))
-        for a, e in batches("ops"):
+            S(act(T.mb[:, a:e], T.imw[:].indirect(T.ml[:, a // 16:e // 16])), regs("imw", 0, 64) + regs("ml", a, e), regs("mb", a, e))
+        for a, e in paired:
             when("ops", a)
             win = T.tb[:, 768:1280] if t else T.mci[:]
-            V(gather(cp(T.ol[:, a:e], win.indirect(T.ml[:, a // 16:e // 16])), e - a), ["tb" if t else "mci"] + regs("ml", a, e), regs("ol", a, e))
-        for a, e in BLOCKS if t else [(0, 192)]:
+            V(cp(T.ol[:, a:e], win.indirect(T.ml[:, a // 16:e // 16])), ["tb" if t else "mci"] + regs("ml", a, e), regs("ol", a, e))
+        for a, e in blocks:
             when("room", a)
-            out = T.hh[:, up(a, e)]
-            op(PLAN["hh"], ts(out, z(a, e), -255.0, None, A.add) if PLAN["hh"] == "v" else act(out, z(a, e), AF.Copy, bias=-255.0), regs(zn, a, e), regs("hh", a, e))
+            S(act(T.hh[:, up(a, e)], z(a, e), bias=-255.0), regs(zn, a, e), regs("hh", a, e))
 
-        for i, (a, e) in enumerate(batches("goal")):
+        for i, (a, e) in enumerate(blocks):
             when("goal", a)
             x, xn = ps("goal", a, e), pn("goal", a, e)
             P(mm((x, (T.cid[:], T.hh[:, rv(a, e)]), (T.cidn[:], T.gg[:, rv(a, e)]))), ["cid", "cidn"] + regs("hh", a, e) + regs("gg", a, e), xn)
             S(act(T.gi[:, a:e], x, AF.Sign, bias=255.5), xn, regs("gi", a, e))
             P(mm((x, (T.cb[:], T.gi[:, a:e]))), ["cb"] + regs("gi", a, e), xn)
-            S(act(T.tg[:, 1, rv(a, e)], x, AF.Sign, scale=0.45, bias=thw[:, 0, 1:2], accum_out=T.acc[:, i:i + 1]), xn + [thn], regs("goal", a, e) + ["acc%d" % i])
+            S(act(T.tg[:, 1, rv(a, e)], x, AF.Sign, scale=0.5, bias=thw[:, 0, 1:2], accum_out=T.acc[:, i:i + 1]), xn + [thn], regs("goal", a, e) + ["acc%d" % i])
         if not lastt:
             when("count")
-            n = len(batches("goal"))
-            x = ps("all", 0, 1)
+            n, x = len(blocks), ps("all", 0, 1)
             G(move(T.acb[:, 0:n], T.acc[:, 0:n]), ["acc%d" % i for i in range(n)], ["acb"])
-            P(mm((x, *[(T.onf[:], T.acb[:, i:i + 1]) for i in range(n)])), ["onf", "acb"], pn("all"))
-            V(ts(T.ev[:], x, -0.5, MAGIC, A.add, A.add), pn("all"), ["ev"])
+            P(mm((x, *[(T.onf[:], T.acb[:, i:i + 1]) for i in [3] + list(range(n))])), ["onf", "acb", "half"], pn("all"))
+            V(ts(T.ev[:], x, -1.0, MAGIC, A.add, A.add), pn("all"), ["ev"])
             V(ts(T.thw[:, 4 * t + 4:4 * t + 8, 1:18], T.c68[:], T.ev[:], x, A.add, A.subtract), ["c68", "ev"] + pn("all"), ["thw%d" % (t + 1)])
 
-        for a, e in batches("mod"):
+        for a, e in paired:
             when("mod", a)
-            w = (e - a) // 16
             xn = [["wb"] + regs(zn, a, e), ["cq1"] + regs("q1", a, e), ["c37"] + regs("mb", a, e), ["cq3"] + regs("q3", a, e), ["c384n"] + regs("goal", a, e)]
 
             def terms(n, name):
-                wz = [(T.wb[:], z(x, y), ps(name, x, y)) for x, y in (split(a, e) if t else [(a, e)])]
+                wz = [(T.wb[:], z(x, y), ps(name, x, y)) for x, y in blocks if a <= x < e]
                 rest = [(T.cq1[:], T.q1[:, a:e]), (T.c37[:], T.mb[:, a:e]), (T.cq3[:], T.q3[:, a:e]), (T.c384n[:], T.tg[:, 1, up(a, e)])][:n - 1]
                 P(mm(*([(ps(name, a, e), *rest, *wz)] if rest else [(x[2], x) for x in wz])), sum(xn[:n], []), pn(name, a, e))
             terms(1, "sum")
             S(act(T.q1[:, a:e], ps("sum", a, e), AF.Identity, scale=2.0 ** -12, bias=T.qb1[:]), pn("sum", a, e) + ["qb1"], regs("q1", a, e))
-            terms(3, "sum")
             terms(2, "u")
+            terms(3, "sum")
             S(act(T.q3[:, a:e], ps("sum", a, e), AF.Identity, scale=2.0 ** -9, bias=T.qb3[:]), pn("sum", a, e) + ["qb3"], regs("q3", a, e))
             terms(5, "sum")
-            S(act(T.tg[:, 0, up(a, e)], ps("sum", a, e), AF.Copy, bias=1152.0), pn("sum", a, e), regs("to", a, e))
-            both = ps("list", a // 8, e // 8)
-            P(mm((both, *[(sel(j), T.tg[:, :, down(191 - a - j, w, 16)]) for j in range(16)])), ["sel"] + regs("to", a, e) + regs("goal", a, e), pn("list", a, e))
-            S(act(T.lst[:, a // 8:e // 8], both, AF.Copy, scale=-2.0 ** -8), pn("list", a, e), regs("lst", a, e))
-            copy(PLAN["mal"], T.mal[:, a // 8:e // 8], T.lst[:, a // 8:e // 8], regs("lst", a, e), regs("mal", a, e))
+            S(act(T.tg[:, 0, up(a, e)], ps("sum", a, e), bias=1152.0), pn("sum", a, e), regs("to", a, e))
+        for a, e in PAIRED:
+            when("own", a)
+            c, x = slice(a // 16, e // 16), ps("own", a // 8, e // 8)
+            P(mm((x, *[(sel(j), T.tg[:, :, down(191 - a - j, (e - a) // 16, 16)]) for j in range(16)])), ["sel"] + regs("to", a, e) + regs("goal", a, e), pn("own", a, e))
+            S(act(T.mal[:, :, c], x, scale=2.0 ** -8), pn("own", a, e), regs("mal", a, e))
+            G(move(T.lst[:, c], T.mal[:, 0, c]), regs("mal", a, e), regs("lst", a, e))
 
-        for (a, e), o in zip(USES, waves):
-            n = e - a
+        for (a, e), (c, ends, tails) in zip(PAIRED, waves):
             when("first", a)
             for k in range(a // 16, e // 16):
-                own, end = lists(T.lst, 16 * k, 16 * k + 16)[0], o + (e // 16 - k) * n
-                V(ts(T.eb[:, end - (16 * k + 16 - a):end], T.tg[:, 0, rv(a, 16 * k + 16)], own, own, A.is_equal, A.mult, rate=0.5),
-                  regs("to", a, 16 * k + 16) + regs("lst", 16 * k, 16 * k + 16), ["eb%d" % k])
+                own = T.lst[:, k:k + 1]
+                V(ts(T.eb[:, ends[k] - (16 * k + 16 - a):ends[k]], T.tg[:, 0, rv(a, 16 * k + 16)], own, own, A.is_equal, A.mult),
+                  regs("to", a, 16 * k + 16) + regs("lst", 16 * k, 16 * k + 16), ["eb.%d" % k])
             when("place", a)
-            c = slice(o, o + n * n // 16)
-            V(scan(T.ws[:, c], T.eb[:, c], T.wd[:, c], A.add, A.min, 0.5), ["wd%d" % a] + ["eb%d" % k for k in range(a // 16, e // 16)], ["ws%d" % a])
-            copy(PLAN["sl"], T.sl[:, a // 16:e // 16], T.ws[:, down(c.stop - 1, n // 16, n)], ["ws%d" % a], regs("sl", a, e))
+            V(scan(T.ws[:, c], T.eb[:, c], T.wd[:, c], A.add, A.min), ["wd.%d" % a] + ["eb.%d" % k for k in ends], ["ws%d" % a])
+            for x, y in tails:
+                G(move(T.sl[:, x], T.ws[:, y]), ["ws%d" % a], regs("sl", 16 * x.start, 16 * x.stop))
 
         when("new")
-        G(move(T.of[:], T.ol[:]), every("ol"), ["of"])
+        G(move(T.of[:], T.ol[:]), regs("ol"), ["of"])
         S(act(ps("old", 0, 192), T.of[:], AF.Identity, scale=32.0, bias=T.k37[:]), ["of", "k37"], pn("old"))
         V(tt(T.f1[:], T.of[:], ps("u", 0, 192), A.mult), ["of"] + pn("u", 0, 192), ["f1"])
         V(tt(T.f3[:], T.f1[:], ps("old", 0, 192), A.add), ["f1"] + pn("old"), ["f3"])
         V(ts(T.f4[:], T.f3[:], 5, 4095, A.arith_shift_right, A.bitwise_and), ["f3"], ["f4"])
 
-        for a, e, q in shares(PLAN["adds"][min(t, 1)]):
+        for a, e, q in shares(ADDS[later]):
             when("adds", a)
             out, win = slots(a, e)[:, ::-1], T.adw[:].indirect(T.ol[:, a:e])
-            call = ts(out, win, -1.0, None, A.mult) if q == "v" else act(out, win, AF.Copy, scale=-1.0)
-            op(q, gather(call, 16 * (e - a), q=q), ["adw"] + regs("ol", a, e), regs("d0", a, e) + regs("cut", a, e))
-        for a, e, q in shares(PLAN["needs"][min(t, 1)]):
+            op(q, ts(out, win, -1.0, None, A.mult) if q == "v" else act(out, win, scale=-1.0), ["adw"] + regs("ol", a, e), regs("d0", a, e) + regs("cut", a, e))
+        for a, e, q in shares(NEEDS[later]):
             when("needs", a)
             out, win = T.d1[:, down(3071 - 16 * a, 16 * (e - a))], T.prw[:].indirect(T.ol[:, a:e])
-            op(q, gather(cp(out, win) if q == "v" else act(out, win, AF.Copy), 16 * (e - a), q=q), ["prw"] + regs("ol", a, e), regs("d1", a, e))
+            op(q, cp(out, win) if q == "v" else act(out, win), ["prw"] + regs("ol", a, e), regs("d1", a, e))
 
-        for a, e in PLAN["head"]:
-            y = a // 64 * 64 + 64
+        for b, (a, e) in enumerate(BLOCKS):
             when("head", a)
-            first, head, r = slots(a, e, 0, 16), T.d1[:, 3072 - 16 * e:3072 - 16 * a:16], ps("r", 0, e - a)
+            first, head, r = slots(a, e, 0, 16), T.d1[:, 3072 - 16 * e:3072 - 16 * a:16], ps("r", 0, 64)
             P(mm((r, (T.cid[:], T.gg[:, rv(a, e)]), (T.cid[:], first))), ["cid"] + regs("gg", a, e) + regs("cut", a, e), pn("r"))
             S(act(T.ind[:, rv(a, e), 17], r, AF.Relu), pn("r"), regs("r15", a, e))
-            copy(PLAN["save"], T["d0%d" % (2 - a // 64)][:, y - e:y - a], first, regs("cut", a, e), regs("a15", a, e))
-            op(PLAN["cut"], iota(first, [[0, e - a]], -1024) if PLAN["cut"] == "g" else ms(first, -1024.0, 1.0), [], regs("cut", a, e))
+            G(move(T["d0%d" % b][:, 0:64], first), regs("cut", a, e), regs("a15", a, e))
+            G(iota(first, [[0, 64]], -1024), [], regs("cut", a, e))
             V(tt(head, head, r, A.max), pn("r") + regs("d1", a, e), regs("d1", a, e))
-        for a, e in PLAN["scan"]:
+        for a, e in BLOCKS:
             when("scan", a)
             j = slice(3072 - 16 * e, 3072 - 16 * a)
-            V(scan(T.ss[:, j], slots(a, e), T.d1[:, j], A.add, A.max, 0.5), regs("d0", a, e) + regs("cut", a, e) + regs("d1", a, e), regs("ss", a, e))
-        for a, e in PLAN["spread"] if t else PAIRED:
+            V(scan(T.ss[:, j], slots(a, e), T.d1[:, j], A.add, A.max), regs("d0", a, e) + regs("cut", a, e) + regs("d1", a, e), regs("ss", a, e))
+        for a, e in BLOCKS if t else PAIRED:
             when("spread", a)
             groups, o = [], 128 * (a != 64)
-            out, names = ps("turn", o, o + 2 * (e - a)), pn("turn", o // 4, o // 4 + (e - a) // 2)
+            out, xn = ps("turn", o, o + 2 * (e - a)), pn("turn", o // 4, o // 4 + (e - a) // 2)
             for x in range(a, e, 64):
                 y, tgb = slice(2 * (x - a), 2 * (x - a) + 128), (T.tg[:, 1, rv(x, x + 64)], T.c512n[:])
                 groups += [(out[0:64, y], (T.hh[:, rv(x, x + 64)], T.cid[:]), tgb), (out[64:128, y], tgb)]
-            P(mm(*groups), ["cid", "c512n"] + regs("hh", a, e) + regs("goal", a, e), names)
-            S(act(T.zt[:, 2 * a:2 * e], out, AF.Relu, bias=T.zbias[:]), names + ["zbias"], regs("zt", a, e))
-        for a, e in PLAN["cmp"]:
-            x = a // 64 * 64
-            halves = [(512 * h, x + 32 - 32 * h) for h in range(2) if a <= x + 32 - 32 * h < e]
-            pair = 2 * ((t + a // 64) % 2)
-            py, names = T["p%d" % pair], ["p%d.y" % (pair + o // 512) for o, s in halves]
+            P(mm(*groups), ["cid", "c512n"] + regs("hh", a, e) + regs("goal", a, e), xn)
+            S(act(T.zt[:, 2 * a:2 * e], out, AF.Relu, bias=T.zbias[:]), xn + ["zbias"], regs("zt", a, e))
+        for b, (a, e) in enumerate(BLOCKS):
+            pair = 2 * ((t + b) % 2)
+            py, xn, j = T["p%d" % pair], ["p%d.y" % pair, "p%d.y" % (pair + 1)], 3072 - 16 * e
             when("fill", a)
-            P(mm(*[(py[:, o:o + 512], (T.zt[:, 2 * x:2 * x + 128], T.ce[:, o:o + 512])) for o, s in halves], stop=False), regs("zt", a, e) + ["ce0", "ce1"], names)
+            P(mm(*[(py[:, o:o + 512], (T.zt[:, 2 * a:2 * e], T.ce[:, o:o + 512])) for o in (0, 512)], stop=False), regs("zt", a, e) + regs("ce", 0, 64), xn)
             when("less", a)
-            P(mm(*[(py[:, o:o + 512], (T.cidn[:], T.ss[:, 2560 - 16 * s:3072 - 16 * s])) for o, s in halves], start=False), ["cidn"] + names + regs("ss", a, e), names)
+            P(mm(*[(py[:, o:o + 512], (T.cidn[:], T.ss[:, j + o:j + o + 512])) for o in (0, 512)], start=False), ["cidn"] + xn + regs("ss", a, e), xn)
             when("cmp", a)
-            V(tt(T.ind[:, rv(a, e), 1:17], slots(a, e, 1), py[:, halves[0][0]:halves[-1][0] + 512], A.max),
-              ["d0z%d" % (2 - a // 64)] + names + regs("d0", a, e) + regs("cut", max(x, a - 32), e), regs("ind", a, e))
+            V(tt(T.ind[:, rv(a, e), 1:17], slots(a, e, 1), py[:], A.max), ["d0z.%d" % b] + xn + regs("d0", a, e) + regs("cut", a, e), regs("ind", a, e))
 
         for b, (a, e) in enumerate(BLOCKS):
-            d0, c, o = T["d0%d" % b], slice(a // 16, e // 16), 9 * a // 8
+            c, o = slice(a // 16, e // 16), 9 * a // 8
             when("pass", a)
             x = slice(18 * c.start, 18 * c.stop)
             cnt, kr = ps("met", x.start, x.stop), T.kr[:, x]
-            tol, tgl = lists(T.mal, a, e)
-            P(mm((cnt, (T.c8kn[:], T.kb[:]), (T.c8kn[:], thw), (T.c4k[:], T.onb[:, 0:72]), (T.cid[:], tol, cnt[:, 0::18]), (T.c384[:], tgl, cnt[:, 0::18]),
+            P(mm((cnt, (T.c8k[:], T.kb[:]), (T.c8k[:], thw), (T.cidn[:], T.mal[:, 0, c], cnt[:, 0::18]), (T.c384n[:], T.mal[:, 1, c], cnt[:, 0::18]),
                   *[(sel(r), T.ind[:, down(191 - a - r, 4, 16), :]) for r in range(16)])),
-              ["sel", "c8kn", "c4k", "cid", "c384", "onb", "kb", "thwz", "indz", thn] + regs("ind", a, e) + regs("r15", a, e) + regs("mal", a, e), pn("met", a, e))
-            V(scan(kr[:, ::-1], cnt[:, ::-1], T.wk[:, x][:, ::-1], A.min, A.max, 1.0), ["wk"] + pn("met", a, e) + regs("keep", a, e), regs("kr", a, e))
-            copy(PLAN["la"], T.la[:, c], kr[:, 1::18], regs("kr", a, e), regs("la", a, e))
+              ["sel", "c8k", "cidn", "c384n", "kb", "thwz", "indz", thn] + regs("ind", a, e) + regs("r15", a, e) + regs("mal", a, e), pn("met", a, e))
+            V(scan(kr[:, ::-1], cnt[:, ::-1], T.wk[:, x][:, ::-1], A.max, A.min), ["wk"] + pn("met", a, e) + regs("keep", a, e), regs("kr", a, e))
+            S(act(T.la[:, c], kr[:, 1::18], scale=-1.0, bias=float(TOP)), regs("kr", a, e), regs("la", a, e))
             when("move", a)
             out = (T.yo if lastt else T["zs%d" % (t + 1)])[:, o:o + 68]
-            S(act(out[:, 64:68], kr[:, 0::18], AF.Abs, bias=-float(MID)), regs("kr", a, e), regs("ms%d" % t, a, e))
-            V(gather(tt(T.yy[:, a:e], d0[:].indirect(T.la[:, c]), T.hh[:, up(a, e)], A.max), 64),
-              ["d0z%d" % b] + regs("la", a, e) + regs("hh", a, e) + regs("d0", a, e) + regs("cut", a, e) + regs("a15", a, e), regs("yy", a, e))
-            S(gather(act(T.fd[:, a:e], T.ft[:].indirect(T.la[:, c]), AF.Copy, scale=T.dvf[:, t:t + 1]), 64, q="s"), ["fta", "ftb", "dvf"] + regs("la", a, e), regs("fd", a, e))
-            change = PLAN["early"] and t == 0 and b == 0
-            P(mm((ps("z", 0, 64), (T.cidn[:], T.fd[:, a:e]), (T.cidn[:], T.yy[:, a:e]), *[(T.cid[:], z(a, e))] * (not change))),
+            S(act(out[:, 64:68], kr[:, 0::18], AF.Abs), regs("kr", a, e), regs("ms%d" % t, a, e))
+            V(tt(T.yy[:, a:e], T["d0%d" % b][:].indirect(T.la[:, c]), T.hh[:, up(a, e)], A.max),
+              ["d0z.%d" % b] + regs("la", a, e) + regs("hh", a, e) + regs("d0", a, e) + regs("cut", a, e) + regs("a15", a, e), regs("yy", a, e))
+            S(act(T.fd[:, a:e], T.ft[:].indirect(T.la[:, c]), scale=T.dvf[:, t:t + 1]), regs("ft", 0, 64) + ["dvf"] + regs("la", a, e), regs("fd", a, e))
+            P(mm((ps("z", 0, 64), (T.cidn[:], T.fd[:, a:e]), (T.cidn[:], T.yy[:, a:e]), (T.cid[:], z(a, e)))),
               ["cid", "cidn"] + regs("fd", a, e) + regs("yy", a, e) + regs(zn, a, e), pn("z"))
-            S(act(out[:, 0:64], ps("z", 0, 64), AF.Copy if change else AF.Abs), pn("z"), regs("zs%d" % t, a, e))
+            S(act(out[:, 0:64], ps("z", 0, 64), AF.Abs), pn("z"), regs("zs%d" % t, a, e))
             if lastt:
                 when("out", a)
-                dma("y", T.ym[:, c], out[:, 64:68], regs("ms%d" % t, a, e), [], "outm%d" % b, 1050)
-                dma("y", T.yz[:, a:e], out[:, 0:64], regs("zs%d" % t, a, e), [], "outz%d" % b, 1200)
+                dma("y", T.ym[:, c], out[:, 64:68], regs("ms%d" % t, a, e), [], "outm%d" % b)
+                dma("y", T.yz[:, a:e], out[:, 0:64], regs("zs%d" % t, a, e), [], "outz%d" % b)
             else:
-                far, ms_, mr = T["zb%d" % (t + 1)][:, o:o + 68], regs("ms%d" % t, a, e), regs("y%d" % (t + 1), a, e)
-                if b in PLAN["ahead"][min(t, 1)]:
+                far, here, there = T["zb%d" % (t + 1)][:, o:o + 68], regs("ms%d" % t, a, e), regs("y%d" % (t + 1), a, e)
+                if b in AHEAD[later]:
                     when("tell", a)
-                    send("mr%d_%d" % (t + 1, b), out[:, 64:68], far[:, 64:68], ms_, mr)
-                    out, far, ms_, mr = out[:, 0:64], far[:, 0:64], [], []
+                    send("mr%d_%d" % (t + 1, b), out[:, 64:68], far[:, 64:68], here, there)
+                    out, far, here, there = out[:, 0:64], far[:, 0:64], [], []
                 when("move", a)
-                send("zr%d_%d" % (t + 1, b), out, T.zw[:] if change else far, regs("zs%d" % t, a, e) + ms_, ["zw"] if change else regs("z%d" % (t + 1), a, e) + mr)
+                send("zr%d_%d" % (t + 1, b), out, far, regs("zs%d" % t, a, e) + here, regs("z%d" % (t + 1), a, e) + there)
 
-        for a, e in USES:
-            when("use", a)
-            use = mask = ps("use", a, e)
-            names, slot = pn("use", a, e), [15 - k if k < 15 else 17 for k in range(16)]
+        for a, e in PAIRED:
+            use, xn, slot = ps("use", a, e), pn("use", a, e), [15 - k if k < 15 else 17 for k in range(16)]
+            to = T.tb[:].indirect(T.sl[:, a // 16:e // 16])
             when("sum", a)
             if e - a == 128:
                 groups = [(use[:, k::16], (T.ind[:, rv(a, e), slot[k]], T.big[:, 15:143:16])) for k in range(16)]
-                groups[15] += ((T.gg[:, rv(a, e)], T.bigp[:, 15::16]),)
-            else:
-                groups = [(use, (T.bigp[:], T.gg[:, up(a, e)]), *[(sel(k), T.ind[:, up(a, e), slot[k]]) for k in range(16)])]
-            P(mm(*groups), ["sel", "bigp"] + regs("gg", a, e) + regs("ind", a, e) + regs("r15", a, e), names)
-            when("use", a)
-            to = T.tb[:].indirect(T.sl[:, a // 16:e // 16])
-            if e - a == 128:
-                S(act(T.st[:], use, AF.Relu, scale=-512.0, bias=512 * 16 * 253.5), names, ["st"])
+                groups[15] += ((T.gg[:, rv(a, e)], T.bign[:, 15::16]),)
+                P(mm(*groups), ["sel", "bign"] + regs("gg", a, e) + regs("ind", a, e) + regs("r15", a, e), xn)
+                when("use", a)
+                S(act(T.st[:], use, AF.Relu, scale=512.0, bias=512 * 16 * 253.5), xn, ["st"])
                 P(mm((ps("mask", 0, 128), (T.st[:], T.cid[:]))), ["st", "cid"], pn("mask"))
-                mask, names = ps("mask", 0, 128)[:, ::-1], pn("mask")
-                when("write", a)
-                V(tt(T.fw[:, a:e], T.f4[:, a:e], mask, A.min), ["f4"] + names, regs("fw", a, e))
-                V(tt(T.dl[:, a:e], T.of[:, a:e], mask, A.subtract), ["of"] + names, regs("dl", a, e))
-                V(gather(tt(to, T.fw[:, a:e], T.dl[:, a:e], A.max), e - a, COST["scatter"]), regs("sl", a, e) + regs("dl", a, e) + regs("fw", a, e), ["tb"])
+                mask, xn = ps("mask", 0, 128)[:, ::-1], pn("mask")
             else:
-                V(ts(mask, use, 16 * 253.5, None, A.is_lt), names, names)
-                when("new", a)
-                V(tt(T.dl[:, a:e], T.f4[:, a:e], T.of[:, a:e], A.subtract, rate=2.0), ["f4", "of"], regs("dl", a, e))
-                when("write", a)
-                V(tt(T.fw[:, a:e], T.dl[:, a:e], mask, A.mult), regs("dl", a, e) + names, regs("fw", a, e))
-                V(gather(tt(to, T.fw[:, a:e], T.of[:, a:e], A.add), e - a, COST["scatter"]), regs("sl", a, e) + ["of"] + regs("fw", a, e), ["tb"])
+                P(mm((use, (T.bign[:], T.gg[:, up(a, e)]), *[(sel(k), T.ind[:, up(a, e), slot[k]]) for k in range(16)])),
+                  ["sel", "bign"] + regs("gg", a, e) + regs("ind", a, e) + regs("r15", a, e), xn)
+                when("use", a)
+                mask = use
+                S(act(mask, use, AF.Relu, scale=512.0, bias=512 * 16 * 253.5), xn, xn)
+            when("write", a)
+            V(tt(T.fw[:, a:e], T.f4[:, a:e], mask, A.min), ["f4"] + xn, regs("fw", a, e))
+            V(tt(T.dl[:, a:e], T.of[:, a:e], mask, A.subtract), ["of"] + xn, regs("dl", a, e))
+            V(tt(to, T.fw[:, a:e], T.dl[:, a:e], A.max), regs("sl", a, e) + regs("dl", a, e) + regs("fw", a, e), ["tb"])
 
     for t in range(STEPS):
         step(t)
-    now[:] = [STEPS - 1, "out", 9]
-    dma("s", T.ymc[:], T.tb[:, 768:1280], ["tb"], [], "outa", 1500)
+    now[1] = "out9"
+    dma("s", T.ymc[:], T.tb[:, 768:1280], ["tb"], [], "outa")
     emit()
     for s in SEMAPHORES:
         if s[:3] == "out":

@@ -4,63 +4,38 @@ A = AluOpType
 AF = ActivationFunctionType
 STEPS = 5
 B16, F16, F32, I32, U16 = "bfloat16", "float16", "float32", "int32", "uint16"
-BLOCKS = [(128, 192), (64, 128), (0, 64)]
-PAIRED = [(64, 192), (0, 64)]
+BLOCKS = [(64, 192), (0, 64)]
+PARTS = [(128, 192), (64, 128), (0, 64)]
 WHOLE = [(0, 192)]
-NEEDS = ["vs vs ss", "sv v v ss"]
-ADDS = ["ss vv ss", "vs ss ss"]
-AHEAD = [(0, 1, 2), (1, 2)]
-MAIN, TOP, ZERO = 64, 2112, 4160
+NEEDS = ["vs vs ss", "vv vv sv"]
+ADDS = ["ss vv ss", "ss ss ss"]
+MAIN, TOP, ZERO = 128, 2720, 3232
 MAGIC = 1.5 * 2.0 ** 24
+ROWS = [(0, 64), (65, 48), (114, 32), (147, 16)]
 SCRATCH = {}
-for _names, _cols, _type in (
-        ("prw adw", 4096, B16), ("glw imw", 512, B16), ("mci", 512, I32), ("tb", 1472, F32),
-        ("mi", 12, I32), ("dvs", 5, B16), ("dvf", 5, F32), ("wts", 1, B16), ("zb0", 192, B16),
-        ("d00 d01 d02 ft", ZERO + 16, B16), ("d1 ss", 3072, B16), ("ol", 192, U16), ("gg mb gi hh yy fd", 192, B16), ("st", 128, B16),
-        ("zt", 384, F16), ("q1 q3", 192, F16), ("mf0", 12, F16), ("lst", 12, F32), ("acc", 3, F32), ("acb", 4, B16), ("ev", 1, F32),
-        ("ml sl la", 12, U16), ("kr wk yo", 216, F32), ("zb1 zb2 zb3 zb4 zs1 zs2 zs3 zs4", 216, F16),
-        ("eb wd ws", 748, F16), ("of dl fw", 192, F32), ("f1 f3 f4", 192, I32),
-        ("pi", 4, I32), ("pf", 4, F32), ("kk k37 qb1 qb3 r16 g16 zbias cew l127 l63 h32", 1, F32), ("c68", 68, F32), ("wi", 216, F32),
-        ("kb", 72, F16), ("ie", 512, B16), ("ce", 1024, B16), ("edge", 256, F16), ("ib", 256, B16), ("big", 144, B16), ("ic top tops", 12, F32),
-        ("ig cid cidn c37 cb cq1 cq3 wb onb onf c8k c384n c512n bign", 128, B16)):
+for _names, _shape, _type in (
+        ("prw adw", [4096], B16), ("glw imw", [512], B16), ("mci", [512], I32), ("tb", [1280], F32), ("mi", [12], I32), ("dvs", [5], B16),
+        ("dvf pb", [5], F32), ("wts", [1], B16), ("zb0 zb1 zb2 zb3 zb4 zs1 zs2 zs3 zs4", [192], B16),
+        ("d00 d01", [ZERO + 16], B16), ("d1 ss", [3072], B16), ("ind", [192, 18], B16), ("ol", [192], U16), ("gg gi rr", [192], B16),
+        ("mb0 mb1 qq yy hh fd", [192], F16), ("st", [128], B16), ("zt", [384], F16), ("ot", [128], F16), ("acc", [2], F32), ("acb", [2], B16),
+        ("ev", [1], F32), ("ml0 ml1 ml2 ml3 ml4 ms1 ms2 ms3 ms4 la lf", [16], U16), ("sl", [32], U16), ("kr wk yo wi", [216], F32),
+        ("ab ws", [492], F32), ("f1 f3 f4", [192], I32), ("fo fw", [2, 192], F32),
+        ("pi", [4], I32), ("pf eq", [4], F32), ("kk ef k37 r16 g16 zbias cew l15 lsave h32 mg bt rv1 rv2", [1], F32), ("pb16", [1], F16),
+        ("kb big", [144], B16), ("ie", [512], B16), ("ce", [1024], B16), ("ib", [256], B16), ("it", [48], B16), ("eo", [4], U16),
+        ("bign", [8], B16), ("ic top", [12], F32), ("wd", [492], F16), ("w3", [3, 164], F16), ("ex ez", [2, 164], B16),
+        ("ig ij off cid cidn c37 cb cbh cab cx wb wx qu mt qt rk gk ona onc onb c8k c8kn", [128], B16)):
     for _n in _names.split():
-        SCRATCH[_n] = ("sbuf", [128, _cols], _type)
-SCRATCH["tg"] = ("sbuf", [128, 2, 192], F16)
-SCRATCH["mal"] = ("sbuf", [128, 2, 12], F16)
-SCRATCH["ind"] = ("sbuf", [128, 192, 18], B16)
-SCRATCH["thw"] = ("sbuf", [128, 4 * STEPS, 18], B16)
+        SCRATCH[_n] = ("sbuf", [128] + _shape, _type)
 BANKS = ["p%d" % b for b in range(8)]
 for _b, _n in (("p0", 1024), ("p2", 1024), ("p4", 512), ("p5", 512), ("p6", 512), ("p7", 512)):
     SCRATCH[_b] = ("psum", [128, _n], F32)
-PSUM = {"use": ("p4", 0), "old": ("p4", 192), "mask": ("p4", 384), "turn": ("p5", 0), "goal": ("p5", 256), "r": ("p5", 448),
-        "sum": ("p6", 0), "u": ("p6", 192), "z": ("p6", 384), "met": ("p7", 0), "own": ("p7", 216), "all": ("p7", 472)}
+PSUM = {"u": ("p4", 0), "old": ("p4", 192), "x": ("p4", 384), "met": ("p5", 0), "mask": ("p5", 144), "turn": ("p6", 0), "use": ("p6", 256), "z": ("p6", 384), "d": ("p7", 0), "r": ("p7", 328), "q": ("p7", 392), "all": ("p7", 456)}
 LOADS = [("s", "m0", "mi"), ("y", "mc", "mci"), ("y", "ad", "adw"), ("s", "gl", "glw"), ("s", "z0", "zb0"), ("s", "wt", "wts"), ("s", "dv", "dvs"), ("y", "pr", "prw")]
-SEMAPHORES = ["cv", "cs", "ct", "cg", "outa", "snd", "ebs", "wd0", "wd64"] + ["ld_" + n for _, n, _ in LOADS]
-SEMAPHORES += ["out%s%d" % (x, b) for x in "zm" for b in range(3)] + ["%sr%d_%d" % (x, t, b) for x in "zm" for t in range(1, STEPS) for b in range(3)]
+SEMAPHORES = ["cv", "cs", "ct", "cg", "outa", "snd", "wds"] + ["ld_" + n for _, n, _ in LOADS]
+SEMAPHORES += ["out%s%d" % (x, b) for x in "zm" for b in range(2)] + ["%sr%d_%d" % (x, t, b) for x in "zm" for t in range(1, STEPS) for b in range(2)]
 
-START = """
-pi_3 pi_ pi_4 pi_2 thwz_ onb_ c68_ half_ thw0_ zbias_ onf_ loady loady2 zbias_2 loads loads2 loads3 loads4 loads5 pi_5 kb_ lists5v lists5s room5s pf_
-cid_ cidn_ c384n_ c512n_ l127_ qb3_ g16_ ops5v ib_ imw_2 c8k_ ig_ h32_ goal5t qb1_ loady3 goal5s imw_ row5s cb_ goal5t2 goal5s2 sel_ wb_ mod5t mod5s
-ie_ edge_ wd_ wd_2 top_ count5g count5t c37_ adds1s cq3_ cq1_ mod5t3 mod5s2 d0z_ adds3v spread3t cew_ cew_2 ce_ ce_2 needs0v head1t count5v wd_3 ft_
-spread3s wi_ needs1s head1v ic_ wd_4 wd_5 count5v2 head1g head1g2 scan1v l63_ mod5t4 mod5s3 fill1t spread5t needs3s needs2v m0_ own5t kk_ less1t cmp1v
-head1s head3t own5s kb_2 r16_ tops_ kb_3 bign_ indz_ wk_ wk_2 wk_3 new5g own3t head3g head3g2 wd_6 wd_7 wd_8 wd_11 wd_12 wd_13 wd_14 wd_9 wd_15 wd_10
-fill3t own3s pass1t adds5s head3v scan3v less3t keep5g pass1v move1s wd_16 eb_ spread5s fill5t head3s own5g pass1s needs5s ft_2 d0z_2 cmp3v move1v
-dvf_ first5v2 tell1g tell1 head5g mod5t2 new5v head5t head5v own3g first3v2 pass3t move1s2 move1t k37_ new5s head5g2 scan5v less5t d0z_3 pass3v
-move1s3 move1g first3v5 new5v2 pass3s move3v move3s tell3g move1 tell3 move3s2 move3t cmp5v first5v4 first5v move3s3 move3g move3 first3v3 first3v4
-head5s sum3t first3v6 sum5t use5s pass5t new5v3 first3v tb_ lists1g+ room1s+ use3s use3t lists1s+ first3v8 first3v7 first5v3 place3v place3g place5v
-goal1t+ lists3g+ pass5v move5s pass5s goal1s+ goal1t2+ write5v2 place3g2 lists3s+ write3v2 write3v row3s+ mod3t+ write5v place5g2 place5g tell5g
-goal1s2+ spread1t+ write3v3 write5v3 room3s+ goal3t+ mod3s+ mod3t2+ mod3t3+ ops3v+ move5s2 spread1s+ goal3s+ goal3t2+ move5v move5t adds0v+ needs1v+
-adds1s+ head1g+ fill1t+ move5s3 goal3s2+ mod3s2+ head1t+ needs0s+ tell5 move5g move5"""
-ROUND = """
-ops3v mod3t2 spread1s goal3s move5v- goal3t2 move5t- adds1s adds0v tell5g- fill1t needs1v tell5- move5s3- goal3s2 move5g- head1g mod3s2 head1t head1g2
-mod3t4 needs0s needs2v spread3t move5- mod3s3 own3t adds3s head1v scan1v less1t lists5g ops5v new5g needs3v spread3s head1s head3t own3s room5s keep5g
-cmp1v own3g fill3t first3v3 head3g head3g2 lists5s goal5t head3v row5s mod5t pass1t adds5s keep1g first3v6 first3v5 scan3v mod5s head3s less3t pass1v
-pass1s goal5s move1s2 move1s goal5t2 goal5s2 first3v7 first3v first3v4 new5s move1v mod5t3 cmp3v mod5t2 move1t move1s3 count5g new5v first3v2 move1g
-needs5s new5v2 spread5t move1 first3v8 head5g new5v3 head5t count5t pass3t head5g2 pass3v spread5s sum3t fill5t pass3s place3v head5v move3s tell3g
-use3s move3v mod5s2 move3s2 scan5v use3t count5v mod5t4 move3t move3s3 move3g write3v2 mod5s3 write3v count5v2 less5t lists1g+ own5t head5s cmp5v
-place3g2 tell3 place3g write3v3 room1s+ lists1s+ own5s own5g goal1t+ move3 sum5t lists3g+ first5v2 first5v3 goal1s+ goal1t2+ first5v first5v4 pass5t
-mod3t+ use5s row3s+ goal1s2+ lists3s+ place5v room3s+ mod3s+ place5g2 place5g write5v2 spread1t+ keep3g+ goal3t+ write5v pass5v pass5s move5s mod3t3+
-move5s2 write5v3"""
+START = "pi_ d0y_ pi_4 pi_3 pi_2 loads lists5v pi_5 ib_ ig_ loads2 loads3 loads4 loads5 lists5s onb_ loady loady2 loady3 room3s pf_ eq_ kk_ pb0_ cb_ l15_ k37_ rv2_ g16_ bt_ ona_ imw_ w3_ rv1_ gk_ wb_ imw_2 pb0_2 cid_ it_ wa_ wa_3 cbh_ cab_ top_ cew_ wa_4 wx_ rv2_2 cx_ r16_ ef_ rk_ qu_ wa_2 qt_ rv1_2 pb0_3 cidn_ rv1_3 goal3t lsave_ row5s goal3s sel_ ops5v kb_ mg_ qt_2 qt_3 c37_ mod3t ef_2 cew_2 d0y_2 mt_ we_3 bign_ kb_2 mod3v u3t to3t goal5t adds3v ij_ off_ ie_ zbias_ we_ ef_3 h32_ adds1s goal5s spread3t spread3s ic_2 head1g head1t kb_3 ce_ ce_2 new5g head3t onc_ to3s ez_4 mod5t head1s needs1s needs3s head3g mod5v u5t to5t to5s spread5t head1v2 eo_ wi_ ez_ adds5s fill3t needs0v last_ needs2v head1v pb16_ fill1t own5t wi_2 wk_ needs5s we_4 ic_ own3t eo_2 we_2 wd_ ez_3 head3v2 head5g head3v count5g scan1v new5v wk_2 scan3v ez_2 less1t tb_ cmp1v c8kn_ spread5s room5s less3t cmp3v head5t ex_ ey_3 ey_ ey_2 ey_4 head5v2 count5t new5s c8k_ pass1t own3s head5v wk_3 keep5g count5v head3s scan5v pass3t pass3v pass3s tell3s tell3g new5v2 move3v head5s fill5t less5t cmp5v fire3s sum3t dvf_ fire3s2 move3t move3s move3g use3s new5v3 new5g2 first3t first3s own5s pass5t place3v place3s use3t write3v pass5v pass5s fire5s write3v2 first5t first5s sum5t use5s use5t move5v tell5s tell5g fire5s2 lists3s+ place5v place5s move5t move5s move5g goal3t+ goal3s+ count5v2 row3s+ write3v3 write5v write5v2"
+ROUND = "ops3s move5v- move5t- move5s- move5g- adds1s head1g mod3t mod3v to3t spread3t spread3s fill1t needs1v head1t fill3t needs3v head1v head1v2 scan1v adds3s head3g head3t head3v head3v2 to3s own3t lists5s keep5g ops5s new5g u3t row5s goal5t goal5s less1t scan3v mod5t mod5v own3s first3t less3t adds5s head5g spread5t head1s head3s to5t spread5s needs4s cmp1v room3s pass1t cmp3v needs5v room5s u5t new5v keep3g new5s to5s count5g head5t head5v2 head5v pass3t pass3v fire3s pass3s tell3s tell3g scan5v fire3s2 new5v2 head5s fill5t sum3t use3s first3s move3v new5v3 new5g2 less5t cmp5v move3t move3s own5t own5s count5t move3g place3v place3s use3t write3v write3v2 first5t first5s place5v sum5t use5s place5s pass5t count5v write3v3 use5t count5v2 lists3s+ pass5v tell5s tell5g write5v pass5s fire5s row3s+ fire5s2 goal3t+ goal3s+ write5v2"
 BUILT = {}
 
 
@@ -77,7 +52,7 @@ def places(calls):
     start, turns = START.split(), ROUND.split()
     first = {(x.count("+"), x.strip("+")): i for i, x in enumerate(start)}
     later = {x.strip("+-"): i + len(turns) * (x.count("-") - x.count("+")) for i, x in enumerate(turns)}
-    return [first.get((o["step"], n), len(start) + len(turns) * o["step"] + later.get(n, 0)) for o, n in zip(calls, names(calls))]
+    return [first.get((o["step"], n), len(start) + len(turns) * o["step"] + later[n] if n in later else -1) for o, n in zip(calls, names(calls))]
 
 
 def scheduler(g, T, now):
@@ -85,7 +60,7 @@ def scheduler(g, T, now):
     calls = []
 
     def op(q, fn, r=(), w=(), ext=None, after=None):
-        name = now[1] + (q if fn else "") if now[1] else (list(w) + ["wd"])[0].split(".")[0] + "_"
+        name = now[1] + (q if fn else "") if now[1] else list(w)[0].split(".")[0] + "_"
         calls.append({"q": q, "fn": fn, "r": list(r), "w": list(w), "ext": ext, "after": after, "step": now[0], "name": name,
                       "banks": {x[:2] for x in list(r) + list(w) if x[:2] in BANKS}})
         return len(calls) - 1
@@ -202,8 +177,8 @@ def down(a, n, step=1):
     return slice(a, stop if stop >= 0 else None, -step)
 
 
-def up(a, e):
-    return down(191 - a, e - a)
+def up(a, e, step=1):
+    return down(191 - a, (e - a + step - 1) // step, step)
 
 
 def rv(a, e):
@@ -247,8 +222,12 @@ def iota(out, pattern, base=0, cm=0):
     return lambda Q: Q.iota(out, pattern, base, cm, allow_small_or_imprecise_dtypes=True)
 
 
+def pick(out, a, pattern, how, fill=0.0, base=0, cm=0):
+    return lambda Q: Q.affine_select(out, a, pattern, how, fill, base, cm)
+
+
 def move(out, a):
-    return lambda Q: Q.affine_select(out, a, [[0, size(out)]], A.is_ge, 0.0, 0, 0)
+    return pick(out, a, [[0, size(out)]], A.is_ge)
 
 
 def rank_program(g, core, T, topo):
@@ -264,24 +243,26 @@ def rank_program(g, core, T, topo):
     V, S, P, G = [lambda fn, r, w, q=q: op(q, fn, r, w) for q in "vstg"]
     behind, sends = {}, [0]
 
-    def dma(q, out, a, r, w, sem, n=1):
-        behind[q] = op(q, lambda Q: Q.dma_start(out, a), r, w, (sem, 16 * n, True), behind.get(q))
+    def dma(q, out, a, r, w, sem):
+        behind[q] = op(q, lambda Q: Q.dma_start(out, a), r, w, (sem, 16, True), behind.get(q))
 
     def send(name, src, dst, r, w):
         sends[0] += 1
         i = op("g", lambda Q: Q.remote_dma(dst, src, T.sem[name], T.sem.snd, pid, rid, mask_out), r, [], ("snd%d" % sends[0], 0, False))
         op("d", None, [], w, (name, n_in, False), i)
 
-    def ps(name, a, e):
+    def ps(name, n, a=0):
         bank, o = PSUM[name]
-        return T[bank][:, o + a:o + e]
+        return T[bank][:, o + a:o + a + n]
 
     def pn(name, a=0, e=32):
         return regs(PSUM[name][0] + name, a, e)
 
     def slots(a, e, shift=0, step=1):
-        y = a // 64 * 64 + 64
-        return T["d0%d" % (2 - a // 64)][:, MAIN + 16 * (y - e) + shift:MAIN + 16 * (y - a) + shift:step]
+        b = int(a < 64)
+        y = BLOCKS[b][1]
+        o = MAIN + 16 * ((y - e) // 64) + shift
+        return T["d0%d" % b][:, o + 16 * (y - e):o + 16 * (y - a):step]
 
     def sel(k):
         return T.big[:, 15 - k:143 - k]
@@ -291,167 +272,160 @@ def rank_program(g, core, T, topo):
     behind.clear()
 
     now[1] = None
-    k4, grf, odf, hf = [T.pf[:, i:i + 1] for i in range(4)]
-    for i, cm in enumerate((64, 1, 512, 16)):
+    k4, grf, c16, hf = [T.pf[:, i:i + 1] for i in range(4)]
+    ea, eb, ec, ed = [T.eq[:, i:i + 1] for i in range(4)]
+    for i, cm in enumerate((64, 1, 256, 16)):
         G(lambda Q, i=i, cm=cm: Q.iota(T.pi[:, i:i + 1], [[0, 1]], 0, cm), [], ["pi.%d" % i])
     V(ts(T.pi[:], T.pi[:], 4, 63, A.arith_shift_right, A.bitwise_and), regs("pi", 0, 128), ["pi"])
     V(cp(T.pf[:], T.pi[:]), ["pi"], ["pf"])
+    G(iota(T.ib[:], [[1, 256]]), [], ["ib"])
+    V(ts(T.eq[:], T.ib[:, 0:64:16], c16, None, A.is_equal), ["ib", "pf"], ["eq"])
     V(ms(T.onb[:], 1.0), [], ["onb"])
-    G(lambda Q: Q.affine_select(T.cid[:], T.onb[:], [[-1, 128]], A.is_equal, 0.0, 0, 1), ["onb"], ["cid"])
+    G(pick(T.cid[:], T.onb[:], [[-1, 128]], A.is_equal, 0.0, 0, 1), ["onb"], ["cid"])
     G(iota(T.ig[:], [[1, 8], [0, 16]]), [], ["ig"])
     V(ts(T.cb[:], T.ig[:], grf, None, A.is_equal), ["ig", "pf"], ["cb"])
-    for name, src, scale, bias in (("kk", k4, 0.25, 0.0), ("k37", k4, 296.0, -2.0 ** 18), ("qb1", odf, 80.0, -1280.5 + 2.0 ** -13),
-                                   ("qb3", odf, 80.0, -1280.5 + 2.0 ** -10), ("g16", grf, 16.0, 15.0),
-                                   ("r16", k4, 4.0, 0.0), ("l127", k4, -0.25, 127.0), ("l63", k4, 0.25, TOP - 63.0), ("h32", hf, 1.0, -32.0)):
-        S(act(T[name][:], src, scale=scale, bias=bias), ["pf"], [name])
-    G(iota(T.ib[:], [[1, 256]]), [], ["ib"])
+    src = {"k": (k4, "pf"), "g": (grf, "pf"), "h": (hf, "pf"), "b": (eb, "eq")}
+    for name, x, scale, bias in (("kk", "k", 0.25, 0.0), ("ef", "k", -10.25, 515.0), ("k37", "k", 296.0, -2.0 ** 18), ("g16", "g", 16.0, 15.0),
+                                 ("r16", "k", 4.0, 0.0), ("l15", "k", -0.25, 15.0), ("lsave", "k", 0.25, TOP - 127.0), ("h32", "h", 1.0, -32.0),
+                                 ("mg", "b", -10.5 * 2.0 ** 27, 1.5 * 2.0 ** 30)):
+        S(act(T[name][:], src[x][0], scale=scale, bias=bias), [src[x][1]], [name])
+    V(ts(T.bt[:], c16, 24.0, 1 / 256, A.is_lt, A.mult), ["pf"], ["bt"])
+    for name, x, rest, terms in (("pb0", T.pb[:, 0:1], 1.0, ((ea, -55.34375), (eb, -41.5), (ec, 53.25))),
+                                 ("rv1", T.rv1[:], 0.0, ((ea, 294.0), (ec, 256.0), (ed, -2.0 ** 19))),
+                                 ("rv2", T.rv2[:], -16.0, ((ec, 256.0), (ed, 0.0))),
+                                 ("ef", T.ef[:], None, ((ea, -24.0), (ec, 8.0)))):
+        for i, (e, c) in enumerate(terms):
+            S(act(x, e, AF.Identity, scale=c - (rest or 0.0), bias=x) if i or rest is None else act(x, e, scale=c - rest, bias=rest), ["eq", name], [name])
+    G(move(T.pb16[:], T.pb[:, 0:1]), ["pb0"], ["pb16"])
     V(ts(T.big[:], T.ib[:, 0:144], T.g16[:], 16.0, A.is_equal, A.mult), ["ib", "g16"], ["sel"])
-    for name, src, c in (("bign", "big", -1.0), ("cidn", "cid", -1.0), ("c37", "cid", 37.0), ("c8k", "cid", 8192.0), ("c384n", "cid", -384.0),
-                         ("c512n", "cid", -512.0), ("cq1", "cb", -256.0), ("cq3", "cb", -32.0)):
-        V(ts(T[name][:], T[src][:, 0:128], c, None, A.mult), ["sel" if src == "big" else src], [name])
-    V(ts(T.wb[:], T.cb[:], T.wts[:], None, A.mult), ["cb", "wts"], ["wb"])
+    G(pick(T.cab[:], T.cb[:], [[0, 32], [-1, 4]], A.is_ge, 0.0, 1), ["cb"], ["cab"])
+    S(act(T.cbh[:], T.cb[:], scale=0.5), ["cb"], ["cbh"])
+    G(pick(T.cx[:], T.cbh[:], [[0, 32], [1, 4]], A.is_equal, 0.0, -2), ["cbh"], ["cx"])
+    for name, x, c in (("cidn", "cid", -1.0), ("c37", "cid", 37 / 32), ("c8k", "cid", 8192.0), ("c8kn", "cid", -8192.0)):
+        S(act(T[name][:], T[x][:], scale=c), [x], [name])
+    S(act(T.bign[:], T.big[:, 15:143:16], scale=-1.0), ["sel"], ["bign"])
+    for name, x, col, coln, c in (("wb", "cb", T.wts[:], "wts", 1.0), ("wx", "cab", T.wts[:], "wts", 1 / 32), ("qu", "cb", ea, "eq", -8.0),
+                                  ("mt", "cab", eb, "eq", 37 / 128), ("qt", "cab", eb, "eq", -0.25), ("rk", "cb", T.rv2[:], "rv2", 1.0),
+                                  ("gk", "cb", ec, "eq", -2.0), ("ona", "onb", ec, "eq", 0.25)):
+        V(ts(T[name][:], T[x][:], col, c, A.mult, A.mult), [x, coln], [name])
+    for i, c in ((2, -1 / 128), (3, 1 / 128)):
+        V(ts(T.qt[:, i::4], T.cb[:, i::4], ec, c, A.mult, A.mult), ["cb", "eq", "qt"], ["qt"])
+    G(pick(T.onc[:], T.ona[:], [[0, 32], [1, 4]], A.is_equal, 0.0, -2), ["ona"], ["onc"])
     S(act(T.dvf[:], T.dvs[:]), ["dvs"], ["dvf"])
-    V(cp(T.imw[:, 0:256], T.ib[:]), ["ib"], ["imw.0"])
-    V(ts(T.imw[:, 256:512], T.ib[:], -256.0, None, A.add), ["ib"], ["imw.1"])
-    G(move(T.mf0[:], T.mi[:]), ["mi"], regs("m0"))
+    for i in range(2):
+        V(ts(T.imw[:, 256 * i:256 * i + 256], T.ib[:], 256.0 * i - 256, eb, A.add, A.mult), ["ib", "eq"], ["imw.%d" % i])
     G(iota(T.cew[:], [[0, 1]], 128), [], ["cew"])
-    G(lambda Q: Q.affine_select(T.cew[:], T.cew[:], [[0, 1]], A.is_ge, 1.0, -64, 1), ["cew"], ["cew"])
-    V(ms(T.zbias[:], 0.0), [], ["zbias"])
-    V(ms(T.zbias[0:64, :], -0.5), ["zbias"], ["zbias"])
-    G(iota(T.ie[:], [[1, 32], [0, 16]]), [], ["ie"])
-    for i, h in enumerate((hf, T.h32[:])):
+    G(pick(T.cew[:], T.cew[:], [[0, 1]], A.is_ge, 1.0, -64, 1), ["cew"], ["cew"])
+    S(act(T.zbias[:], T.cew[:], scale=255.5 / 127, bias=256.5 - 255.5 / 127), ["cew"], ["zbias"])
+    G(iota(T.ie[:], [[-1, 32], [0, 16]], 31), [], ["ie"])
+    for i, h in enumerate((T.h32[:], hf)):
         V(ts(T.ce[:, 512 * i:512 * i + 512], T.ie[:], h, T.cew[:], A.is_equal, A.mult), ["ie", "pf", "h32", "cew"], ["ce.%d" % i])
-    V(ms(T.thw[:, :, 0], 0.0), [], ["thwz"])
-    V(ms(T.thw[:, 0:4, 1:18], -2.5), [], ["thw0"])
-    for b in range(3):
-        G(iota(T["d0%d" % b][:, MAIN + 1024:ZERO + 1:ZERO - MAIN - 1024], [[0, 2]]), [], ["d0z.%d" % b])
-    G(iota(T.ft[:, ZERO:ZERO + 16], [[0, 16]]), [], ["ft.0"])
-    V(ms(T.ft[:, 0:MAIN + 1024], 1.0), [], ["ft.1"])
-    G(iota(T.ind[:, :, 0], [[0, 192]]), [], ["indz"])
-    G(iota(T.wi[:], [[0, 3], [256, 4], [-1, 18]], TOP - MAIN - 1007), [], ["wi"])
-    G(iota(T.ic[:], [[0, 3], [16, 4]]), [], ["ic"])
-    S(act(T.wk[:], T.wi[:], AF.Identity, bias=T.r16[:]), ["wi", "r16"], ["wk"])
-    S(act(T.wk[:, 1::18], T.ic[:], AF.Identity, bias=T.l63[:]), ["ic", "l63", "wk"], ["wk"])
+    for b in range(2):
+        G(iota(T["d0%d" % b][:, MAIN + 1024:ZERO + 1:1040], [[0, 3]]), [], ["d0y.%d" % b])
+    for a, e in BLOCKS:
+        c, n = a // 16, (e - a) // 16
+        G(iota(T.wi[:, 18 * c:18 * (c + n)], [[1040, n // 4], [256, 4], [-1, 18]], TOP - MAIN - 260 * n + 33), [], regs("wi", a, e))
+        G(iota(T.ic[:, c:c + n], [[16, n]], 128 - 16 * n), [], regs("ic", a, e))
+    S(act(T.wk[:], T.wi[:], AF.Identity, bias=T.r16[:]), regs("wi") + ["r16"], ["wk"])
+    S(act(T.wk[:, 1::18], T.ic[:], AF.Identity, bias=T.lsave[:]), regs("ic") + ["lsave", "wk"], ["wk"])
     V(ms(T.wk[:, 17::18], float(TOP - ZERO)), ["wk"], ["wk"])
-    V(ms(T.acb[:, 3:4], 0.125), [], ["half"])
-    for x, c in ((T.kb[:], -2056.0), (T.kb[:, 17::18], 60000.0), (T.kb[:, 0::18], 1152 / 8192)):
-        S(act(x, T.onb[:, 0:size(x)], scale=c), ["onb", "kb"], ["kb"])
-    V(ms(T.c68[:], -MAGIC - 2.0), [], ["c68"])
-    V(ms(T.onf[:], 1 / 32), [], ["onf"])
-    G(iota(T.top[:], [[16, 12]], 1280), [], ["top"])
-    S(act(T.tops[:], T.top[:], AF.Identity, bias=T.kk[:]), ["top", "kk"], ["tops"])
-    V(ts(T.edge[:], T.ib[:], T.l127[:], 2000.0, A.is_ge, A.mult), ["ib", "l127"], ["edge"])
-    waves, o = [], 0
-    for a, e in PAIRED:
-        n, c = e - a, a // 16
-        h, ends = n // 32, {}
-        for i in range(h):
-            ends[c + 2 * h - 1 - i], ends[c + i] = o + (n + 2) * i + n + 1, o + (n + 18) * (i + 1)
-        tails = [(slice(c, c + h), slice(o + n + 17, o + (n + 18) * h, n + 18)), (slice(c + h, c + 2 * h), down(o + (n + 2) * (h - 1) + n, h, n + 2))]
-        waves.append((slice(o, o + (n + 18) * h), ends, tails))
-        for i, k in enumerate(ends):
-            w = 16 * (k - c) + 17
-            dma("y", T.wd[:, ends[k] - w:ends[k]], T.edge[:, 111:111 + w], ["edge"], ["wd.%d" % a] * (i == 2 * h - 1), "wd%d" % a, i + 1)
-        for x, y in tails:
-            G(move(T.wd[:, y], T.tops[:, x]), ["tops", "wd.%d" % a], ["wd.%d" % a])
-        o += (n + 18) * h
-    dma("y", T.eb[:], T.wd[:], ["wd.0", "wd.64"], ["eb.%d" % k for k in range(12)], "ebs")
+    V(ts(T.kb[:], T.ib[:, 0:144], 0.0, T.rv1[:], A.mult, A.add), ["ib", "rv1"], ["kb"])
+    for x, c in ((T.kb[:, 17::18], 2.0 ** 20), (T.kb[:, 0::18], -8.0)):
+        V(ts(x, T.onb[:, 0:8], ed, c, A.mult, A.mult), ["onb", "eq", "kb"], ["kb"])
+    G(iota(T.ind[:, :, 17], [[0, 192]]), [], ["last"])
+    G(iota(T.it[:], [[0, 3], [1, 16]]), [], ["it"])
+    G(iota(T.top[:], [[-64, 3], [-16, 4]], 432), [], ["top"])
+    V(ms(T.w3[:], 0.0), [], ["w3"])
+    G(iota(T.ij[:], [[0, 8], [1, 16]]), [], ["ij"])
+    V(ts(T.off[:], T.ij[:], T.l15[:], -4096.0, A.not_equal, A.mult), ["ij", "l15"], ["off"])
+    for r, (o, n) in enumerate(ROWS):
+        G(iota(T.ez[:, :, o:o + n + 1], [[4, 2], [0, n + 1]], r), [], ["ez.%d" % r])
+    V(ts(T.ex[:], T.ez[:], grf, -1.0, A.is_equal, A.mult), regs("ez", 0, 128) + ["pf"], ["ex"])
+    for r, (o, n) in enumerate(ROWS):
+        V(ts(T.w3[:, :, o:o + 16], T.it[:], T.l15[:], 4096.0, A.is_le, A.mult), ["it", "l15", "w3"], ["wa.%d" % r])
+        S(act(T.w3[:, :, o + n], T.top[:, r::4], AF.Identity, bias=T.kk[:]), ["top", "kk", "w3"], ["we.%d" % r])
+        S(act(T.ex[:, :, o + n], T.ex[:, :, o + n], scale=-2.0 ** -11), ["ex"], ["ey.%d" % r])
+    dma("y", T.wd[:], T.w3[:], regs("wa", 0, 128) + regs("we", 0, 128), ["wd"], "wds")
+    for b, (a, e) in enumerate(BLOCKS):
+        S(act(T.eo[:, 2 * b:2 * b + 1], T.ef[:], bias=41.0 * ((e - a) // 16 - 12)), ["ef", "eo"], ["eo"])
     G(move(T.tb[:, 768:1280], T.mci[:]), ["mci"], ["tb"])
 
     def step(t):
         lastt, later = t == STEPS - 1, min(t, 1)
-        blocks, paired = (BLOCKS, PAIRED) if t else (WHOLE, WHOLE)
-        mfn, zn = ("y%d" % t if t else "m0"), "z%d" % t
-        thw, thn = T.thw[:, 4 * t:4 * t + 4, :], "thw%d" % t
-
-        def z(a, e):
-            o = a // 64 * 8
-            return T["zb%d" % t][:, o + a:o + e] if t else T.zb0[:, a:e]
-
-        def mf(a, e):
-            o = 9 * a // 8 + 64
-            return T["zb%d" % t][:, o:o + 4] if t else T.mf0[:]
+        z, ml, mb = T["zb%d" % t], T["ml%d" % t], T["mb%d" % (t % 2)]
+        zn, mn, mbn = "z%d" % t, "m%d" % t, "mb%d" % (t % 2)
 
         def when(what, a=0):
             now[:] = [t, "%s%d" % (what, 5 - a // 32)]
 
-        for a, e in blocks:
-            c = slice(a // 16, e // 16)
-            when("lists", a)
-            if t == 0:
-                V(cp(T.ml[:], T.mi[:]), ["mi"], regs("ml"))
-            else:
-                G(move(T.ml[:, c], mf(a, e)), regs(mfn, a, e), regs("ml", a, e))
+        if t == 0:
+            when("lists")
+            V(cp(ml[:, 0:12], T.mi[:]), ["mi"], regs(mn))
+        for a, e in BLOCKS if t else WHOLE:
+            c, mr = slice(a // 16, e // 16), regs(mn, a, e)
             when("keep", a)
-            G(move(T.wk[:, 18 * c.start:18 * c.stop:18], mf(a, e)), ["wk"] + regs(mfn, a, e), regs("keep", a, e))
-        for a, e in blocks:
-            when("lists", a)
-            S(act(T.gg[:, up(a, e)], T.glw[:].indirect(T.ml[:, a // 16:e // 16])), ["glw"] + regs("ml", a, e), regs("gg", a, e))
-        for a, e in paired:
+            G(move(T.wk[:, 18 * c.start:18 * c.stop:18], ml[:, c]), ["wk"] + mr, regs("keep", a, e))
             when("row", a)
-            S(act(T.mb[:, a:e], T.imw[:].indirect(T.ml[:, a // 16:e // 16])), regs("imw", 0, 64) + regs("ml", a, e), regs("mb", a, e))
-        for a, e in paired:
+            S(act(mb[:, a:e], T.imw[:].indirect(ml[:, c]), AF.Identity, bias=T.pb[:, t:t + 1]), regs("imw", 0, 64) + mr + ["pb%d" % t], regs(mbn, a, e))
+            when("lists", a)
+            S(act(T.gg[:, up(a, e)], T.glw[:].indirect(ml[:, c])), ["glw"] + mr, regs("gg", a, e))
             when("ops", a)
-            win = T.tb[:, 768:1280] if t else T.mci[:]
-            V(cp(T.ol[:, a:e], win.indirect(T.ml[:, a // 16:e // 16])), ["tb" if t else "mci"] + regs("ml", a, e), regs("ol", a, e))
-        for a, e in blocks:
-            when("room", a)
-            S(act(T.hh[:, up(a, e)], z(a, e), bias=-255.0), regs(zn, a, e), regs("hh", a, e))
+            if t:
+                S(act(T.ol[:, a:e], T.tb[:, 768:1280].indirect(ml[:, c])), ["tb"] + mr, regs("ol", a, e))
+            else:
+                V(cp(T.ol[:], T.mci[:].indirect(ml[:, c])), ["mci"] + mr, regs("ol"))
 
-        for i, (a, e) in enumerate(blocks):
+        for a, e in BLOCKS:
+            n, zr, mr, qr = e - a, regs(zn, a, e), regs(mbn, a, e), regs("qq", a, e)
             when("goal", a)
-            x, xn = ps("goal", a, e), pn("goal", a, e)
-            P(mm((x, (T.cid[:], T.hh[:, rv(a, e)]), (T.cidn[:], T.gg[:, rv(a, e)]))), ["cid", "cidn"] + regs("hh", a, e) + regs("gg", a, e), xn)
-            S(act(T.gi[:, a:e], x, AF.Sign, bias=255.5), xn, regs("gi", a, e))
-            P(mm((x, (T.cb[:], T.gi[:, a:e]))), ["cb"] + regs("gi", a, e), xn)
-            S(act(T.tg[:, 1, rv(a, e)], x, AF.Sign, scale=0.5, bias=thw[:, 0, 1:2], accum_out=T.acc[:, i:i + 1]), xn + [thn], regs("goal", a, e) + ["acc%d" % i])
+            P(mm((ps("x", n), (T.cid[:], z[:, a:e]), (T.cidn[:], T.gg[:, up(a, e)]))), ["cid", "cidn"] + zr + regs("gg", a, e), pn("x"))
+            S(act(T.gi[:, a:e], ps("x", n), AF.Sign, bias=0.5), pn("x"), regs("gi", a, e))
+            when("mod", a)
+            P(mm((ps("x", n), (T.wx[:], z[:, a:e]), (T.c37[:], mb[:, a:e]), (T.cx[:], T.gi[:, a:e]))), ["wx", "c37", "cx"] + zr + mr + regs("gi", a, e), pn("x"))
+            V(ts(T.qq[:, a:e], ps("x", n), T.mg[:], T.mg[:], A.add, A.subtract), pn("x") + ["mg"], qr)
+            when("spread", a)
+            terms, out = [], ps("turn", 2 * n)
+            for x in range(a, e, 64):
+                y, goal = slice(2 * (x - a), 2 * (x - a) + 128), (T.qq[:, x:x + 64], T.gk[:])
+                terms += [(out[0:64, y], (z[:, x:x + 64], T.cid[:]), goal), (out[64:128, y], goal)]
+            P(mm(*terms), ["cid", "gk"] + zr + qr, pn("turn"))
+            S(act(T.zt[:, 2 * a:2 * e], out, AF.Relu, bias=T.zbias[:]), pn("turn") + ["zbias"], regs("zt", a, e))
+        for b, (a, e) in enumerate(BLOCKS):
+            n, zr, mr, qr, x = e - a, regs(zn, a, e), regs(mbn, a, e), regs("qq", a, e), "zx"[b]
+            when("u", a)
+            P(mm((ps("u", n, a), (T.wb[:], z[:, a:e]), (T.qu[:], T.qq[:, a:e]))), ["wb", "qu"] + zr + qr, pn("u", a, e))
+            when("to", a)
+            P(mm((ps(x, n), (T.wx[:], z[:, a:e]), (T.mt[:], mb[:, a:e]), (T.qt[:], T.qq[:, a:e]))), ["wx", "mt", "qt"] + zr + mr + qr, pn(x))
+            S(act(T.ind[:, up(a, e), 0], ps(x, n), AF.Identity, scale=-0.25, bias=T.bt[:], accum_out=T.acc[:, b:b + 1]), pn(x) + ["bt"], regs("to", a, e) + ["acc%d" % b])
+        for b, (a, e) in enumerate(BLOCKS):
+            n, x, w = e - a, "zx"[b], slice(164 * (192 - e) // 64, 164 * (192 - a) // 64)
+            own, d = ps(x, 128)[0:n, :], ps("d", w.stop - w.start)
+            when("own", a)
+            P(mm((own, (T.ind[:, rv(a, e), 0], T.rk[:]), (T.cid[0:n, 0:n], T.off[0:n, :]))), ["rk", "cid", "off"] + regs("to", a, e), pn(x))
+            S(act(T.ot[0:n, :], own, AF.Relu), pn(x), ["ot"])
+            when("first", a)
+            rows = [(T.rk[:], T.ind[:, rv(y, y + m), 0], d[:, 164 * i + o:164 * i + o + m]) for i, y in enumerate(range(e - 64, a - 1, -64)) for o, m in ROWS]
+            P(mm((d, (T.ot[0:n, :], T.ex[0:n, 0:n // 64, :]), *rows)), ["ot", "rk"] + regs("ey", 0, 128) + regs("to", a, e), pn("d"))
+            S(act(T.ab[:, w], d, AF.Abs, scale=2048.0), pn("d"), regs("ab", a, e))
+            when("place", a)
+            V(scan(T.ws[:, w], T.ab[:, w], T.wd[:, w], A.min, A.max), ["wd"] + regs("ab", a, e), regs("ws", a, e))
+            S(act(T.sl[:, 16 * b:16 * b + 16], T.ws[:, w].indirect(T.eo[:, 2 * b:2 * b + 1])), regs("ws", a, e) + ["eo"], regs("sl", a, e))
         if not lastt:
             when("count")
-            n, x = len(blocks), ps("all", 0, 1)
-            G(move(T.acb[:, 0:n], T.acc[:, 0:n]), ["acc%d" % i for i in range(n)], ["acb"])
-            P(mm((x, *[(T.onf[:], T.acb[:, i:i + 1]) for i in [3] + list(range(n))])), ["onf", "acb", "half"], pn("all"))
-            V(ts(T.ev[:], x, -1.0, MAGIC, A.add, A.add), pn("all"), ["ev"])
-            V(ts(T.thw[:, 4 * t + 4:4 * t + 8, 1:18], T.c68[:], T.ev[:], x, A.add, A.subtract), ["c68", "ev"] + pn("all"), ["thw%d" % (t + 1)])
-
-        for a, e in paired:
-            when("mod", a)
-            xn = [["wb"] + regs(zn, a, e), ["cq1"] + regs("q1", a, e), ["c37"] + regs("mb", a, e), ["cq3"] + regs("q3", a, e), ["c384n"] + regs("goal", a, e)]
-
-            def terms(n, name):
-                wz = [(T.wb[:], z(x, y), ps(name, x, y)) for x, y in blocks if a <= x < e]
-                rest = [(T.cq1[:], T.q1[:, a:e]), (T.c37[:], T.mb[:, a:e]), (T.cq3[:], T.q3[:, a:e]), (T.c384n[:], T.tg[:, 1, up(a, e)])][:n - 1]
-                P(mm(*([(ps(name, a, e), *rest, *wz)] if rest else [(x[2], x) for x in wz])), sum(xn[:n], []), pn(name, a, e))
-            terms(1, "sum")
-            S(act(T.q1[:, a:e], ps("sum", a, e), AF.Identity, scale=2.0 ** -12, bias=T.qb1[:]), pn("sum", a, e) + ["qb1"], regs("q1", a, e))
-            terms(2, "u")
-            terms(3, "sum")
-            S(act(T.q3[:, a:e], ps("sum", a, e), AF.Identity, scale=2.0 ** -9, bias=T.qb3[:]), pn("sum", a, e) + ["qb3"], regs("q3", a, e))
-            terms(5, "sum")
-            S(act(T.tg[:, 0, up(a, e)], ps("sum", a, e), bias=1152.0), pn("sum", a, e), regs("to", a, e))
-        for a, e in PAIRED:
-            when("own", a)
-            c, x = slice(a // 16, e // 16), ps("own", a // 8, e // 8)
-            P(mm((x, *[(sel(j), T.tg[:, :, down(191 - a - j, (e - a) // 16, 16)]) for j in range(16)])), ["sel"] + regs("to", a, e) + regs("goal", a, e), pn("own", a, e))
-            S(act(T.mal[:, :, c], x, scale=2.0 ** -8), pn("own", a, e), regs("mal", a, e))
-            G(move(T.lst[:, c], T.mal[:, 0, c]), regs("mal", a, e), regs("lst", a, e))
-
-        for (a, e), (c, ends, tails) in zip(PAIRED, waves):
-            when("first", a)
-            for k in range(a // 16, e // 16):
-                own = T.lst[:, k:k + 1]
-                V(ts(T.eb[:, ends[k] - (16 * k + 16 - a):ends[k]], T.tg[:, 0, rv(a, 16 * k + 16)], own, own, A.is_equal, A.mult),
-                  regs("to", a, 16 * k + 16) + regs("lst", 16 * k, 16 * k + 16), ["eb.%d" % k])
-            when("place", a)
-            V(scan(T.ws[:, c], T.eb[:, c], T.wd[:, c], A.add, A.min), ["wd.%d" % a] + ["eb.%d" % k for k in ends], ["ws%d" % a])
-            for x, y in tails:
-                G(move(T.sl[:, x], T.ws[:, y]), ["ws%d" % a], regs("sl", 16 * x.start, 16 * x.stop))
+            x, x2 = ps("all", 1), ps("all", 1, 1)
+            G(move(T.acb[:], T.acc[:]), ["acc0", "acc1"], ["acb"])
+            terms = [(T.onc[:], T.acb[:, i:i + 1]) for i in range(2)]
+            P(mm((x, *terms), (x2, (T.cidn[:], T.pb16[:]), *terms)), ["onc", "acb", "cidn", "pb16"], pn("all"))
+            V(ts(T.ev[:], x, -0.5, MAGIC, A.add, A.add), pn("all"), ["ev"])
+            V(ts(T.pb[:, t + 1:t + 2], T.ev[:], -MAGIC, x2, A.add, A.subtract), ["ev"] + pn("all"), ["pb%d" % (t + 1)])
 
         when("new")
-        G(move(T.of[:], T.ol[:]), regs("ol"), ["of"])
-        S(act(ps("old", 0, 192), T.of[:], AF.Identity, scale=32.0, bias=T.k37[:]), ["of", "k37"], pn("old"))
-        V(tt(T.f1[:], T.of[:], ps("u", 0, 192), A.mult), ["of"] + pn("u", 0, 192), ["f1"])
-        V(tt(T.f3[:], T.f1[:], ps("old", 0, 192), A.add), ["f1"] + pn("old"), ["f3"])
+        G(move(T.fo[:, 1, :], T.ol[:]), regs("ol"), ["of"])
+        S(act(ps("old", 192), T.fo[:, 1, :], AF.Identity, scale=32.0, bias=T.k37[:]), ["of", "k37"], pn("old"))
+        V(tt(T.f1[:], T.fo[:, 1, :], ps("u", 192), A.mult), ["of"] + pn("u", 0, 192), ["f1"])
+        V(tt(T.f3[:], T.f1[:], ps("old", 192), A.add), ["f1"] + pn("old"), ["f3"])
         V(ts(T.f4[:], T.f3[:], 5, 4095, A.arith_shift_right, A.bitwise_and), ["f3"], ["f4"])
+        G(move(T.fo[:, 0, :], T.f4[:]), ["f4"], ["nf"])
 
         for a, e, q in shares(ADDS[later]):
             when("adds", a)
@@ -462,91 +436,77 @@ def rank_program(g, core, T, topo):
             out, win = T.d1[:, down(3071 - 16 * a, 16 * (e - a))], T.prw[:].indirect(T.ol[:, a:e])
             op(q, cp(out, win) if q == "v" else act(out, win), ["prw"] + regs("ol", a, e), regs("d1", a, e))
 
-        for b, (a, e) in enumerate(BLOCKS):
+        for (a, e), x in zip(PARTS, "rqr"):
             when("head", a)
-            first, head, r = slots(a, e, 0, 16), T.d1[:, 3072 - 16 * e:3072 - 16 * a:16], ps("r", 0, 64)
-            P(mm((r, (T.cid[:], T.gg[:, rv(a, e)]), (T.cid[:], first))), ["cid"] + regs("gg", a, e) + regs("cut", a, e), pn("r"))
-            S(act(T.ind[:, rv(a, e), 17], r, AF.Relu), pn("r"), regs("r15", a, e))
-            G(move(T["d0%d" % b][:, 0:64], first), regs("cut", a, e), regs("a15", a, e))
-            G(iota(first, [[0, 64]], -1024), [], regs("cut", a, e))
-            V(tt(head, head, r, A.max), pn("r") + regs("d1", a, e), regs("d1", a, e))
-        for a, e in BLOCKS:
+            b = int(a < 64)
+            first, head, r, o = slots(a, e, 0, 16), T.d1[:, 3072 - 16 * e:3072 - 16 * a:16], ps(x, 64), BLOCKS[b][1] - e
+            P(mm((r, (T.cid[:], T.gg[:, rv(a, e)]), (T.cid[:], first))), ["cid"] + regs("gg", a, e) + regs("cut", a, e), pn(x))
+            V(tt(head, head, r, A.max), pn(x) + regs("d1", a, e), regs("d1", a, e))
+            S(act(T.rr[:, rv(a, e)], r, AF.Relu), pn(x), regs("r15", a, e))
+            G(move(T["d0%d" % b][:, o:o + 64], first), regs("cut", a, e), regs("a15", a, e))
+            V(ms(first, -1024.0), [], regs("cut", a, e))
+        for i, (a, e) in enumerate(PARTS):
             when("scan", a)
-            j = slice(3072 - 16 * e, 3072 - 16 * a)
-            V(scan(T.ss[:, j], slots(a, e), T.d1[:, j], A.add, A.max), regs("d0", a, e) + regs("cut", a, e) + regs("d1", a, e), regs("ss", a, e))
-        for a, e in BLOCKS if t else PAIRED:
-            when("spread", a)
-            groups, o = [], 128 * (a != 64)
-            out, xn = ps("turn", o, o + 2 * (e - a)), pn("turn", o // 4, o // 4 + (e - a) // 2)
-            for x in range(a, e, 64):
-                y, tgb = slice(2 * (x - a), 2 * (x - a) + 128), (T.tg[:, 1, rv(x, x + 64)], T.c512n[:])
-                groups += [(out[0:64, y], (T.hh[:, rv(x, x + 64)], T.cid[:]), tgb), (out[64:128, y], tgb)]
-            P(mm(*groups), ["cid", "c512n"] + regs("hh", a, e) + regs("goal", a, e), xn)
-            S(act(T.zt[:, 2 * a:2 * e], out, AF.Relu, bias=T.zbias[:]), xn + ["zbias"], regs("zt", a, e))
-        for b, (a, e) in enumerate(BLOCKS):
-            pair = 2 * ((t + b) % 2)
-            py, xn, j = T["p%d" % pair], ["p%d.y" % pair, "p%d.y" % (pair + 1)], 3072 - 16 * e
+            j = 3072 - 16 * e
+            V(scan(T.ss[:, j:j + 1024], slots(a, e), T.d1[:, j:j + 1024], A.add, A.max), regs("d0", a, e) + regs("cut", a, e) + regs("d1", a, e), regs("ss", a, e))
+            pair = 2 * ((t + i) % 2)
+            py, xn = T["p%d" % pair], ["p%d.y" % pair, "p%d.y" % (pair + 1)]
             when("fill", a)
-            P(mm(*[(py[:, o:o + 512], (T.zt[:, 2 * a:2 * e], T.ce[:, o:o + 512])) for o in (0, 512)], stop=False), regs("zt", a, e) + regs("ce", 0, 64), xn)
+            P(mm(*[(py[:, h:h + 512], (T.zt[:, 2 * a:2 * e], T.ce[:, h:h + 512])) for h in (0, 512)], stop=False), regs("zt", a, e) + regs("ce", 0, 64), xn)
             when("less", a)
-            P(mm(*[(py[:, o:o + 512], (T.cidn[:], T.ss[:, j + o:j + o + 512])) for o in (0, 512)], start=False), ["cidn"] + xn + regs("ss", a, e), xn)
+            P(mm(*[(py[:, h:h + 512], (T.cidn[:], T.ss[:, j + h:j + h + 512])) for h in (0, 512)], start=False), ["cidn"] + regs("ss", a, e) + xn, xn)
             when("cmp", a)
-            V(tt(T.ind[:, rv(a, e), 1:17], slots(a, e, 1), py[:], A.max), ["d0z.%d" % b] + xn + regs("d0", a, e) + regs("cut", a, e), regs("ind", a, e))
+            V(tt(T.ind[:, rv(a, e), 1:17], slots(a, e, 1), py[:], A.max), ["d0y.%d" % (a < 64)] + xn + regs("d0", a, e) + regs("cut", a, e), regs("ind", a, e))
 
         for b, (a, e) in enumerate(BLOCKS):
-            c, o = slice(a // 16, e // 16), 9 * a // 8
-            when("pass", a)
-            x = slice(18 * c.start, 18 * c.stop)
-            cnt, kr = ps("met", x.start, x.stop), T.kr[:, x]
-            P(mm((cnt, (T.c8k[:], T.kb[:]), (T.c8k[:], thw), (T.cidn[:], T.mal[:, 0, c], cnt[:, 0::18]), (T.c384n[:], T.mal[:, 1, c], cnt[:, 0::18]),
-                  *[(sel(r), T.ind[:, down(191 - a - r, 4, 16), :]) for r in range(16)])),
-              ["sel", "c8k", "cidn", "c384n", "kb", "thwz", "indz", thn] + regs("ind", a, e) + regs("r15", a, e) + regs("mal", a, e), pn("met", a, e))
-            V(scan(kr[:, ::-1], cnt[:, ::-1], T.wk[:, x][:, ::-1], A.max, A.min), ["wk"] + pn("met", a, e) + regs("keep", a, e), regs("kr", a, e))
+            c, n = slice(a // 16, e // 16), e - a
+            x, o = slice(18 * c.start, 18 * c.stop), min(a, 64)
+            cnt, kr = ps("met", x.stop - x.start), T.kr[:, x]
+            for l in range(e - 64, a - 1, -64):
+                when("pass", l)
+                y = 18 * (l - a) // 16
+                P(mm((cnt[:, y:y + 72], (mb[:, o:o + 128], T.kb[:, 0:72]), *[(sel(r), T.ind[:, up(l + r, l + 64, 16), :]) for r in range(16)])),
+                  ["sel", "kb", "last"] + regs(mbn, o, o + 128) + regs("ind", l, l + 64) + regs("to", l, l + 64), pn("met", l - a, l - a + 64))
+            V(scan(kr[:, ::-1], cnt[:, ::-1], T.wk[:, x][:, ::-1], A.max, A.min), ["wk"] + pn("met", 0, n) + regs("keep", a, e), regs("kr", a, e))
             S(act(T.la[:, c], kr[:, 1::18], scale=-1.0, bias=float(TOP)), regs("kr", a, e), regs("la", a, e))
-            when("move", a)
-            out = (T.yo if lastt else T["zs%d" % (t + 1)])[:, o:o + 68]
-            S(act(out[:, 64:68], kr[:, 0::18], AF.Abs), regs("kr", a, e), regs("ms%d" % t, a, e))
-            V(tt(T.yy[:, a:e], T["d0%d" % b][:].indirect(T.la[:, c]), T.hh[:, up(a, e)], A.max),
-              ["d0z.%d" % b] + regs("la", a, e) + regs("hh", a, e) + regs("d0", a, e) + regs("cut", a, e) + regs("a15", a, e), regs("yy", a, e))
-            S(act(T.fd[:, a:e], T.ft[:].indirect(T.la[:, c]), scale=T.dvf[:, t:t + 1]), regs("ft", 0, 64) + ["dvf"] + regs("la", a, e), regs("fd", a, e))
-            P(mm((ps("z", 0, 64), (T.cidn[:], T.fd[:, a:e]), (T.cidn[:], T.yy[:, a:e]), (T.cid[:], z(a, e)))),
-              ["cid", "cidn"] + regs("fd", a, e) + regs("yy", a, e) + regs(zn, a, e), pn("z"))
-            S(act(out[:, 0:64], ps("z", 0, 64), AF.Abs), pn("z"), regs("zs%d" % t, a, e))
+            when("tell", a)
+            out = T.yo[:, 192 + c.start:192 + c.stop] if lastt else T["ms%d" % (t + 1)][:, c]
+            S(act(out, kr[:, 0::18], AF.Abs), regs("kr", a, e), regs("ms%d" % t, a, e))
             if lastt:
-                when("out", a)
-                dma("y", T.ym[:, c], out[:, 64:68], regs("ms%d" % t, a, e), [], "outm%d" % b)
-                dma("y", T.yz[:, a:e], out[:, 0:64], regs("zs%d" % t, a, e), [], "outz%d" % b)
+                dma("y", T.ym[:, c], out, regs("ms%d" % t, a, e), [], "outm%d" % b)
             else:
-                far, here, there = T["zb%d" % (t + 1)][:, o:o + 68], regs("ms%d" % t, a, e), regs("y%d" % (t + 1), a, e)
-                if b in AHEAD[later]:
-                    when("tell", a)
-                    send("mr%d_%d" % (t + 1, b), out[:, 64:68], far[:, 64:68], here, there)
-                    out, far, here, there = out[:, 0:64], far[:, 0:64], [], []
-                when("move", a)
-                send("zr%d_%d" % (t + 1, b), out, far, regs("zs%d" % t, a, e) + here, regs("z%d" % (t + 1), a, e) + there)
+                send("mr%d_%d" % (t + 1, b), out, T["ml%d" % (t + 1)][:, c], regs("ms%d" % t, a, e), regs("m%d" % (t + 1), a, e))
+            when("room", a)
+            S(act(T.hh[:, a:e], z[:, a:e], bias=-255.0), regs(zn, a, e), regs("hh", a, e))
+            when("fire", a)
+            S(act(T.lf[:, c], kr[:, 1::18], AF.Sign), regs("kr", a, e), regs("lf", a, e))
+            S(act(T.fd[:, a:e], T.ib[:, 0:16].indirect(T.lf[:, c]), scale=T.dvf[:, t:t + 1]), ["ib", "dvf"] + regs("lf", a, e), regs("fd", a, e))
+            when("move", a)
+            out = (T.yo if lastt else T["zs%d" % (t + 1)])[:, a:e]
+            V(tt(T.yy[:, a:e], T["d0%d" % b][:].indirect(T.la[:, c]), T.hh[:, a:e], A.max),
+              ["d0y.%d" % b] + regs("la", a, e) + regs("d0", a, e) + regs("cut", a, e) + regs("a15", a, e) + regs("hh", a, e), regs("yy", a, e))
+            P(mm((ps("z", n), (T.cid[:], z[:, a:e]), (T.cidn[:], T.fd[:, a:e]), (T.cidn[:], T.yy[:, a:e]))),
+              ["cid", "cidn"] + regs("yy", a, e) + regs("fd", a, e) + regs(zn, a, e), pn("z"))
+            S(act(out, ps("z", n), AF.Abs), pn("z"), regs("zs%d" % t, a, e))
+            if lastt:
+                dma("y", T.yz[:, a:e], out, regs("zs%d" % t, a, e), [], "outz%d" % b)
+            else:
+                send("zr%d_%d" % (t + 1, b), out, T["zb%d" % (t + 1)][:, a:e], regs("zs%d" % t, a, e), regs("z%d" % (t + 1), a, e))
 
-        for a, e in PAIRED:
-            use, xn, slot = ps("use", a, e), pn("use", a, e), [15 - k if k < 15 else 17 for k in range(16)]
-            to = T.tb[:].indirect(T.sl[:, a // 16:e // 16])
+        for b, (a, e) in enumerate(BLOCKS):
+            n, ones = e - a, T.big[:, 15:143:16]
+            use, mask = ps("use", 128)[0:n, :], ps("mask", 2 * n)
             when("sum", a)
-            if e - a == 128:
-                groups = [(use[:, k::16], (T.ind[:, rv(a, e), slot[k]], T.big[:, 15:143:16])) for k in range(16)]
-                groups[15] += ((T.gg[:, rv(a, e)], T.bign[:, 15::16]),)
-                P(mm(*groups), ["sel", "bign"] + regs("gg", a, e) + regs("ind", a, e) + regs("r15", a, e), xn)
-                when("use", a)
-                S(act(T.st[:], use, AF.Relu, scale=512.0, bias=512 * 16 * 253.5), xn, ["st"])
-                P(mm((ps("mask", 0, 128), (T.st[:], T.cid[:]))), ["st", "cid"], pn("mask"))
-                mask, xn = ps("mask", 0, 128)[:, ::-1], pn("mask")
-            else:
-                P(mm((use, (T.bign[:], T.gg[:, up(a, e)]), *[(sel(k), T.ind[:, up(a, e), slot[k]]) for k in range(16)])),
-                  ["sel", "bign"] + regs("gg", a, e) + regs("ind", a, e) + regs("r15", a, e), xn)
-                when("use", a)
-                mask = use
-                S(act(mask, use, AF.Relu, scale=512.0, bias=512 * 16 * 253.5), xn, xn)
+            P(mm(*[(use[:, k::16], (T.ind[:, rv(a, e), 15 - k], ones)) for k in range(15)], (use[:, 15::16], (T.rr[:, rv(a, e)], ones), (T.gg[:, rv(a, e)], T.bign[:]))),
+              ["sel", "bign"] + regs("gg", a, e) + regs("ind", a, e) + regs("r15", a, e), pn("use"))
+            when("use", a)
+            S(act(T.st[0:n, :], use, AF.Sign, bias=16 * 253.5), pn("use"), ["st"])
+            P(mm(*[(mask[:, i * n:i * n + n], (T.st[0:n, :], T[x][0:n, 0:n])) for i, x in enumerate(("c8k", "c8kn"))]), ["st", "c8k", "c8kn"], pn("mask"))
             when("write", a)
-            V(tt(T.fw[:, a:e], T.f4[:, a:e], mask, A.min), ["f4"] + xn, regs("fw", a, e))
-            V(tt(T.dl[:, a:e], T.of[:, a:e], mask, A.subtract), ["of"] + xn, regs("dl", a, e))
-            V(tt(to, T.fw[:, a:e], T.dl[:, a:e], A.max), regs("sl", a, e) + regs("dl", a, e) + regs("fw", a, e), ["tb"])
+            V(tt(T.fw[:, :, down(e - 1, n)], T.fo[:, :, down(e - 1, n)], mask, A.min), ["nf", "of"] + pn("mask"), regs("fw", a, e))
+            for x in range(e - 64, a - 1, -64):
+                o = 16 * b + (x - a) // 16
+                V(tt(T.tb[:].indirect(T.sl[:, o:o + 4]), T.fw[:, 0, x:x + 64], T.fw[:, 1, x:x + 64], A.max), regs("sl", a, e) + regs("fw", a, e), ["tb"])
 
     for t in range(STEPS):
         step(t)

from concourse.mybir import dt, AluOpType, AxisListType, ActivationFunctionType

A = AluOpType
AF = ActivationFunctionType
STEPS = 5
B16, F16, F32, I32, U16 = "bfloat16", "float16", "float32", "int32", "uint16"
BLOCKS = [(64, 192), (0, 64)]
PARTS = [(128, 192), (64, 128), (0, 64)]
WHOLE = [(0, 192)]
NEEDS = ["vs vs ss", "vv vv sv"]
ADDS = ["ss vv ss", "ss ss ss"]
MAIN, TOP, ZERO = 128, 2720, 3232
MAGIC = 1.5 * 2.0 ** 24
ROWS = [(0, 64), (65, 48), (114, 32), (147, 16)]
SCRATCH = {}
for _names, _shape, _type in (
        ("prw adw", [4096], B16), ("glw imw", [512], B16), ("mci", [512], I32), ("tb", [1280], F32), ("mi", [12], I32), ("dvs", [5], B16),
        ("dvf pb", [5], F32), ("wts", [1], B16), ("zb0 zb1 zb2 zb3 zb4 zs1 zs2 zs3 zs4", [192], B16),
        ("d00 d01", [ZERO + 16], B16), ("d1 ss", [3072], B16), ("ind", [192, 18], B16), ("ol", [192], U16), ("gg gi rr", [192], B16),
        ("mb0 mb1 qq yy hh fd", [192], F16), ("st", [128], B16), ("zt", [384], F16), ("ot", [128], F16), ("acc", [2], F32), ("acb", [2], B16),
        ("ev", [1], F32), ("ml0 ml1 ml2 ml3 ml4 ms1 ms2 ms3 ms4 la lf", [16], U16), ("sl", [32], U16), ("kr wk yo wi", [216], F32),
        ("ab ws", [492], F32), ("f1 f3 f4", [192], I32), ("fo fw", [2, 192], F32),
        ("pi", [4], I32), ("pf eq", [4], F32), ("kk ef k37 r16 g16 zbias cew l15 lsave h32 mg bt rv1 rv2", [1], F32), ("pb16", [1], F16),
        ("kb big", [144], B16), ("ie", [512], B16), ("ce", [1024], B16), ("ib", [256], B16), ("it", [48], B16), ("eo", [4], U16),
        ("bign", [8], B16), ("ic top", [12], F32), ("wd", [492], F16), ("w3", [3, 164], F16), ("ex ez", [2, 164], B16),
        ("ig ij off cid cidn c37 cb cbh cab cx wb wx qu mt qt rk gk ona onc onb c8k c8kn", [128], B16)):
    for _n in _names.split():
        SCRATCH[_n] = ("sbuf", [128] + _shape, _type)
BANKS = ["p%d" % b for b in range(8)]
for _b, _n in (("p0", 1024), ("p2", 1024), ("p4", 512), ("p5", 512), ("p6", 512), ("p7", 512)):
    SCRATCH[_b] = ("psum", [128, _n], F32)
PSUM = {"u": ("p4", 0), "old": ("p4", 192), "x": ("p4", 384), "met": ("p5", 0), "mask": ("p5", 144), "turn": ("p6", 0), "use": ("p6", 256), "z": ("p6", 384), "d": ("p7", 0), "r": ("p7", 328), "q": ("p7", 392), "all": ("p7", 456)}
LOADS = [("s", "m0", "mi"), ("y", "mc", "mci"), ("y", "ad", "adw"), ("s", "gl", "glw"), ("s", "z0", "zb0"), ("s", "wt", "wts"), ("s", "dv", "dvs"), ("y", "pr", "prw")]
SEMAPHORES = ["cv", "cs", "ct", "cg", "outa", "snd", "wds"] + ["ld_" + n for _, n, _ in LOADS]
SEMAPHORES += ["out%s%d" % (x, b) for x in "zm" for b in range(2)] + ["%sr%d_%d" % (x, t, b) for x in "zm" for t in range(1, STEPS) for b in range(2)]

START = "pi_ d0y_ pi_4 pi_3 pi_2 loads lists5v pi_5 ib_ ig_ loads2 loads3 loads4 loads5 lists5s onb_ loady loady2 loady3 room3s pf_ eq_ kk_ pb0_ cb_ l15_ k37_ rv2_ g16_ bt_ ona_ imw_ w3_ rv1_ gk_ wb_ imw_2 pb0_2 cid_ it_ wa_ wa_3 cbh_ cab_ top_ cew_ wa_4 wx_ rv2_2 cx_ r16_ ef_ rk_ qu_ wa_2 qt_ rv1_2 pb0_3 cidn_ rv1_3 goal3t lsave_ row5s goal3s sel_ ops5v kb_ mg_ qt_2 qt_3 c37_ mod3t ef_2 cew_2 d0y_2 mt_ we_3 bign_ kb_2 mod3v u3t to3t goal5t adds3v ij_ off_ ie_ zbias_ we_ ef_3 h32_ adds1s goal5s spread3t spread3s ic_2 head1g head1t kb_3 ce_ ce_2 new5g head3t onc_ to3s ez_4 mod5t head1s needs1s needs3s head3g mod5v u5t to5t to5s spread5t head1v2 eo_ wi_ ez_ adds5s fill3t needs0v last_ needs2v head1v pb16_ fill1t own5t wi_2 wk_ needs5s we_4 ic_ own3t eo_2 we_2 wd_ ez_3 head3v2 head5g head3v count5g scan1v new5v wk_2 scan3v ez_2 less1t tb_ cmp1v c8kn_ spread5s room5s less3t cmp3v head5t ex_ ey_3 ey_ ey_2 ey_4 head5v2 count5t new5s c8k_ pass1t own3s head5v wk_3 keep5g count5v head3s scan5v pass3t pass3v pass3s tell3s tell3g new5v2 move3v head5s fill5t less5t cmp5v fire3s sum3t dvf_ fire3s2 move3t move3s move3g use3s new5v3 new5g2 first3t first3s own5s pass5t place3v place3s use3t write3v pass5v pass5s fire5s write3v2 first5t first5s sum5t use5s use5t move5v tell5s tell5g fire5s2 lists3s+ place5v place5s move5t move5s move5g goal3t+ goal3s+ count5v2 row3s+ write3v3 write5v write5v2"
ROUND = "ops3s move5v- move5t- move5s- move5g- adds1s head1g mod3t mod3v to3t spread3t spread3s fill1t needs1v head1t fill3t needs3v head1v head1v2 scan1v adds3s head3g head3t head3v head3v2 to3s own3t lists5s keep5g ops5s new5g u3t row5s goal5t goal5s less1t scan3v mod5t mod5v own3s first3t less3t adds5s head5g spread5t head1s head3s to5t spread5s needs4s cmp1v room3s pass1t cmp3v needs5v room5s u5t new5v keep3g new5s to5s count5g head5t head5v2 head5v pass3t pass3v fire3s pass3s tell3s tell3g scan5v fire3s2 new5v2 head5s fill5t sum3t use3s first3s move3v new5v3 new5g2 less5t cmp5v move3t move3s own5t own5s count5t move3g place3v place3s use3t write3v write3v2 first5t first5s place5v sum5t use5s place5s pass5t count5v write3v3 use5t count5v2 lists3s+ pass5v tell5s tell5g write5v pass5s fire5s row3s+ fire5s2 goal3t+ goal3s+ write5v2"
BUILT = {}


def names(calls):
    seen, out = {}, []
    for o in calls:
        k = (o["step"], o["name"])
        seen[k] = seen.get(k, 0) + 1
        out.append(k[1] + (str(seen[k]) if seen[k] > 1 else ""))
    return out


def places(calls):
    start, turns = START.split(), ROUND.split()
    first = {(x.count("+"), x.strip("+")): i for i, x in enumerate(start)}
    later = {x.strip("+-"): i + len(turns) * (x.count("-") - x.count("+")) for i, x in enumerate(turns)}
    return [first.get((o["step"], n), len(start) + len(turns) * o["step"] + later[n] if n in later else -1) for o, n in zip(calls, names(calls))]


def scheduler(g, T, now):
    queues = {"g": g, "v": g.vector, "s": g.scalar, "t": g.tensor, "y": g.sync}
    calls = []

    def op(q, fn, r=(), w=(), ext=None, after=None):
        name = now[1] + (q if fn else "") if now[1] else list(w)[0].split(".")[0] + "_"
        calls.append({"q": q, "fn": fn, "r": list(r), "w": list(w), "ext": ext, "after": after, "step": now[0], "name": name,
                      "banks": {x[:2] for x in list(r) + list(w) if x[:2] in BANKS}})
        return len(calls) - 1

    def needs(ops, banks):
        wr, rd, bank = {}, {}, {}
        for i, o in enumerate(ops):
            deps = set()
            if banks:
                for x in o["banks"]:
                    h = bank.setdefault(x, {})
                    deps.update(h[k] for k in h if k != o["q"])
                    h[o["q"]] = i
            for x in o["r"]:
                if x in wr:
                    deps.add(wr[x])
                rd.setdefault(x, []).append(i)
            for x in o["w"]:
                if x in wr:
                    deps.add(wr[x])
                deps.update(rd.get(x, []))
                wr[x] = i
                rd[x] = []
            deps.discard(i)
            o["deps"] = deps

    def order():
        if not BUILT:
            needs(calls, False)
            pre = [o["deps"] | ({o["after"]} - {None}) for o in calls]
            place, done, out = places(calls), set(), []
            left = sorted(range(len(calls)), key=lambda i: (place[i], i))
            while left:
                i = next(j for j in left if pre[j] <= done)
                left.remove(i)
                done.add(i)
                out.append(i)
            BUILT.update(calls=calls, pre=pre, order=out)
        return [calls[i] for i in BUILT["order"]]

    def emit():
        ops = order()
        needs(ops, True)
        pos, known, snap, need, waits = {}, {}, [], set(), []
        for i, o in enumerate(ops):
            q = o["q"]
            pos[q] = pos.get(q, 0) + 1
            o["pos"] = pos[q]
            k = known.setdefault(q, {})
            mine = []
            for d in sorted(o["deps"], reverse=True):
                e = ops[d]["ext"]
                key, val = (e[0], 1) if e else (ops[d]["q"], ops[d]["pos"])
                if k.get(key, 0) >= val or key == q == "t":
                    continue
                mine.append(d)
                need.add(d)
                for a, b in snap[d].items():
                    k[a] = max(k.get(a, 0), b)
                k[key] = max(k.get(key, 0), val)
            waits.append(mine)
            snap.append(dict(k))
        need.update({o["q"]: i for i, o in enumerate(ops) if not o["ext"]}.values())
        count = {}
        for i, o in enumerate(ops):
            if i in need and not o["ext"]:
                count[o["q"]] = count.get(o["q"], 0) + 1
                o["tok"] = ("c" + o["q"], count[o["q"]])
        for i, o in enumerate(ops):
            if o["fn"] is None:
                continue
            Q = queues[o["q"]]
            best = {}
            for d in waits[i]:
                s, n = (ops[d]["ext"] or ops[d]["tok"])[:2]
                best[s] = max(best.get(s, 0), n)
            for s, n in best.items():
                Q.wait_ge(T.sem[s], n)
            ins = o["fn"](Q)
            if o["ext"]:
                if o["ext"][2]:
                    ins.then_inc(T.sem[o["ext"][0]], 16)
            elif i in need:
                ins.then_inc(T.sem["c" + o["q"]], 1)
        for q, n in count.items():
            g.wait_ge(T.sem["c" + q], n)

    return op, emit


def regs(name, a=0, b=192):
    return ["%s.%d" % (name, c) for c in range(a // 32, (b + 31) // 32)]


def size(ap):
    n = 1
    for x in ap.shape[1:]:
        n *= x
    return n


def shares(plan):
    out, e, before = [], 192, " "
    for x in plan:
        if x != " ":
            out[len(out) - (x == before):] = [(e - 32, out[-1][1] if x == before else e, x)]
            e -= 32
        before = x
    return out


def down(a, n, step=1):
    stop = a - n * step
    return slice(a, stop if stop >= 0 else None, -step)


def up(a, e, step=1):
    return down(191 - a, (e - a + step - 1) // step, step)


def rv(a, e):
    return slice(192 - e, 192 - a)


def ts(out, in0, s1, s2, *o):
    return lambda Q: Q.tensor_scalar(out, in0, s1, s2, *o)


def tt(out, a, b, o):
    return lambda Q: Q.tensor_tensor(out, a, b, o)


def cp(out, a):
    return lambda Q: Q.tensor_copy(out, a)


def scan(out, a, b, o0, o1):
    return lambda Q: Q.tensor_tensor_scan(out, a, b, 0.0, o0, o1)


def act(out, a, f=AF.Copy, **k):
    return lambda Q: Q.activation(out, a, f, **k)


def ms(out, c):
    return lambda Q: Q.memset(out, c)


def mm(*groups, start=True, stop=True):
    def fn(Q):
        for x in groups:
            for i, y in enumerate(x[1:]):
                ins = Q.matmul(y[2] if len(y) > 2 else x[0], y[0], y[1], start and i == 0, stop and i == len(x) - 2)
        return ins
    return fn


def iota(out, pattern, base=0, cm=0):
    return lambda Q: Q.iota(out, pattern, base, cm, allow_small_or_imprecise_dtypes=True)


def pick(out, a, pattern, how, fill=0.0, base=0, cm=0):
    return lambda Q: Q.affine_select(out, a, pattern, how, fill, base, cm)


def move(out, a):
    return pick(out, a, [[0, size(out)]], A.is_ge)


def rank_program(g, core, T, topo):
    rank = T.rank_of(core)
    if rank is None:
        return
    now = [0, "load"]
    op, emit = scheduler(g, T, now)
    nxt = T.cores[(rank + 1) % len(T.cores)]
    mask_out = topo.mask(core, nxt)
    n_out, n_in = len(topo.engines(core, nxt)), len(topo.engines(T.cores[rank - 1], core))
    rid, pid = topo.addr(nxt)[:2]
    V, S, P, G = [lambda fn, r, w, q=q: op(q, fn, r, w) for q in "vstg"]
    behind, sends = {}, [0]

    def dma(q, out, a, r, w, sem):
        behind[q] = op(q, lambda Q: Q.dma_start(out, a), r, w, (sem, 16, True), behind.get(q))

    def send(name, src, dst, r, w):
        sends[0] += 1
        i = op("g", lambda Q: Q.remote_dma(dst, src, T.sem[name], T.sem.snd, pid, rid, mask_out), r, [], ("snd%d" % sends[0], 0, False))
        op("d", None, [], w, (name, n_in, False), i)

    def ps(name, n, a=0):
        bank, o = PSUM[name]
        return T[bank][:, o + a:o + a + n]

    def pn(name, a=0, e=32):
        return regs(PSUM[name][0] + name, a, e)

    def slots(a, e, shift=0, step=1):
        b = int(a < 64)
        y = BLOCKS[b][1]
        o = MAIN + 16 * ((y - e) // 64) + shift
        return T["d0%d" % b][:, o + 16 * (y - e):o + 16 * (y - a):step]

    def sel(k):
        return T.big[:, 15 - k:143 - k]

    for q, name, buf in LOADS:
        dma(q, T[buf][:], T[name][:], [], regs("z0") if name == "z0" else [buf], "ld_" + name)
    behind.clear()

    now[1] = None
    k4, grf, c16, hf = [T.pf[:, i:i + 1] for i in range(4)]
    ea, eb, ec, ed = [T.eq[:, i:i + 1] for i in range(4)]
    for i, cm in enumerate((64, 1, 256, 16)):
        G(lambda Q, i=i, cm=cm: Q.iota(T.pi[:, i:i + 1], [[0, 1]], 0, cm), [], ["pi.%d" % i])
    V(ts(T.pi[:], T.pi[:], 4, 63, A.arith_shift_right, A.bitwise_and), regs("pi", 0, 128), ["pi"])
    V(cp(T.pf[:], T.pi[:]), ["pi"], ["pf"])
    G(iota(T.ib[:], [[1, 256]]), [], ["ib"])
    V(ts(T.eq[:], T.ib[:, 0:64:16], c16, None, A.is_equal), ["ib", "pf"], ["eq"])
    V(ms(T.onb[:], 1.0), [], ["onb"])
    G(pick(T.cid[:], T.onb[:], [[-1, 128]], A.is_equal, 0.0, 0, 1), ["onb"], ["cid"])
    G(iota(T.ig[:], [[1, 8], [0, 16]]), [], ["ig"])
    V(ts(T.cb[:], T.ig[:], grf, None, A.is_equal), ["ig", "pf"], ["cb"])
    src = {"k": (k4, "pf"), "g": (grf, "pf"), "h": (hf, "pf"), "b": (eb, "eq")}
    for name, x, scale, bias in (("kk", "k", 0.25, 0.0), ("ef", "k", -10.25, 515.0), ("k37", "k", 296.0, -2.0 ** 18), ("g16", "g", 16.0, 15.0),
                                 ("r16", "k", 4.0, 0.0), ("l15", "k", -0.25, 15.0), ("lsave", "k", 0.25, TOP - 127.0), ("h32", "h", 1.0, -32.0),
                                 ("mg", "b", -10.5 * 2.0 ** 27, 1.5 * 2.0 ** 30)):
        S(act(T[name][:], src[x][0], scale=scale, bias=bias), [src[x][1]], [name])
    V(ts(T.bt[:], c16, 24.0, 1 / 256, A.is_lt, A.mult), ["pf"], ["bt"])
    for name, x, rest, terms in (("pb0", T.pb[:, 0:1], 1.0, ((ea, -55.34375), (eb, -41.5), (ec, 53.25))),
                                 ("rv1", T.rv1[:], 0.0, ((ea, 294.0), (ec, 256.0), (ed, -2.0 ** 19))),
                                 ("rv2", T.rv2[:], -16.0, ((ec, 256.0), (ed, 0.0))),
                                 ("ef", T.ef[:], None, ((ea, -24.0), (ec, 8.0)))):
        for i, (e, c) in enumerate(terms):
            S(act(x, e, AF.Identity, scale=c - (rest or 0.0), bias=x) if i or rest is None else act(x, e, scale=c - rest, bias=rest), ["eq", name], [name])
    G(move(T.pb16[:], T.pb[:, 0:1]), ["pb0"], ["pb16"])
    V(ts(T.big[:], T.ib[:, 0:144], T.g16[:], 16.0, A.is_equal, A.mult), ["ib", "g16"], ["sel"])
    G(pick(T.cab[:], T.cb[:], [[0, 32], [-1, 4]], A.is_ge, 0.0, 1), ["cb"], ["cab"])
    S(act(T.cbh[:], T.cb[:], scale=0.5), ["cb"], ["cbh"])
    G(pick(T.cx[:], T.cbh[:], [[0, 32], [1, 4]], A.is_equal, 0.0, -2), ["cbh"], ["cx"])
    for name, x, c in (("cidn", "cid", -1.0), ("c37", "cid", 37 / 32), ("c8k", "cid", 8192.0), ("c8kn", "cid", -8192.0)):
        S(act(T[name][:], T[x][:], scale=c), [x], [name])
    S(act(T.bign[:], T.big[:, 15:143:16], scale=-1.0), ["sel"], ["bign"])
    for name, x, col, coln, c in (("wb", "cb", T.wts[:], "wts", 1.0), ("wx", "cab", T.wts[:], "wts", 1 / 32), ("qu", "cb", ea, "eq", -8.0),
                                  ("mt", "cab", eb, "eq", 37 / 128), ("qt", "cab", eb, "eq", -0.25), ("rk", "cb", T.rv2[:], "rv2", 1.0),
                                  ("gk", "cb", ec, "eq", -2.0), ("ona", "onb", ec, "eq", 0.25)):
        V(ts(T[name][:], T[x][:], col, c, A.mult, A.mult), [x, coln], [name])
    for i, c in ((2, -1 / 128), (3, 1 / 128)):
        V(ts(T.qt[:, i::4], T.cb[:, i::4], ec, c, A.mult, A.mult), ["cb", "eq", "qt"], ["qt"])
    G(pick(T.onc[:], T.ona[:], [[0, 32], [1, 4]], A.is_equal, 0.0, -2), ["ona"], ["onc"])
    S(act(T.dvf[:], T.dvs[:]), ["dvs"], ["dvf"])
    for i in range(2):
        V(ts(T.imw[:, 256 * i:256 * i + 256], T.ib[:], 256.0 * i - 256, eb, A.add, A.mult), ["ib", "eq"], ["imw.%d" % i])
    G(iota(T.cew[:], [[0, 1]], 128), [], ["cew"])
    G(pick(T.cew[:], T.cew[:], [[0, 1]], A.is_ge, 1.0, -64, 1), ["cew"], ["cew"])
    S(act(T.zbias[:], T.cew[:], scale=255.5 / 127, bias=256.5 - 255.5 / 127), ["cew"], ["zbias"])
    G(iota(T.ie[:], [[-1, 32], [0, 16]], 31), [], ["ie"])
    for i, h in enumerate((T.h32[:], hf)):
        V(ts(T.ce[:, 512 * i:512 * i + 512], T.ie[:], h, T.cew[:], A.is_equal, A.mult), ["ie", "pf", "h32", "cew"], ["ce.%d" % i])
    for b in range(2):
        G(iota(T["d0%d" % b][:, MAIN + 1024:ZERO + 1:1040], [[0, 3]]), [], ["d0y.%d" % b])
    for a, e in BLOCKS:
        c, n = a // 16, (e - a) // 16
        G(iota(T.wi[:, 18 * c:18 * (c + n)], [[1040, n // 4], [256, 4], [-1, 18]], TOP - MAIN - 260 * n + 33), [], regs("wi", a, e))
        G(iota(T.ic[:, c:c + n], [[16, n]], 128 - 16 * n), [], regs("ic", a, e))
    S(act(T.wk[:], T.wi[:], AF.Identity, bias=T.r16[:]), regs("wi") + ["r16"], ["wk"])
    S(act(T.wk[:, 1::18], T.ic[:], AF.Identity, bias=T.lsave[:]), regs("ic") + ["lsave", "wk"], ["wk"])
    V(ms(T.wk[:, 17::18], float(TOP - ZERO)), ["wk"], ["wk"])
    V(ts(T.kb[:], T.ib[:, 0:144], 0.0, T.rv1[:], A.mult, A.add), ["ib", "rv1"], ["kb"])
    for x, c in ((T.kb[:, 17::18], 2.0 ** 20), (T.kb[:, 0::18], -8.0)):
        V(ts(x, T.onb[:, 0:8], ed, c, A.mult, A.mult), ["onb", "eq", "kb"], ["kb"])
    G(iota(T.ind[:, :, 17], [[0, 192]]), [], ["last"])
    G(iota(T.it[:], [[0, 3], [1, 16]]), [], ["it"])
    G(iota(T.top[:], [[-64, 3], [-16, 4]], 432), [], ["top"])
    V(ms(T.w3[:], 0.0), [], ["w3"])
    G(iota(T.ij[:], [[0, 8], [1, 16]]), [], ["ij"])
    V(ts(T.off[:], T.ij[:], T.l15[:], -4096.0, A.not_equal, A.mult), ["ij", "l15"], ["off"])
    for r, (o, n) in enumerate(ROWS):
        G(iota(T.ez[:, :, o:o + n + 1], [[4, 2], [0, n + 1]], r), [], ["ez.%d" % r])
    V(ts(T.ex[:], T.ez[:], grf, -1.0, A.is_equal, A.mult), regs("ez", 0, 128) + ["pf"], ["ex"])
    for r, (o, n) in enumerate(ROWS):
        V(ts(T.w3[:, :, o:o + 16], T.it[:], T.l15[:], 4096.0, A.is_le, A.mult), ["it", "l15", "w3"], ["wa.%d" % r])
        S(act(T.w3[:, :, o + n], T.top[:, r::4], AF.Identity, bias=T.kk[:]), ["top", "kk", "w3"], ["we.%d" % r])
        S(act(T.ex[:, :, o + n], T.ex[:, :, o + n], scale=-2.0 ** -11), ["ex"], ["ey.%d" % r])
    dma("y", T.wd[:], T.w3[:], regs("wa", 0, 128) + regs("we", 0, 128), ["wd"], "wds")
    for b, (a, e) in enumerate(BLOCKS):
        S(act(T.eo[:, 2 * b:2 * b + 1], T.ef[:], bias=41.0 * ((e - a) // 16 - 12)), ["ef", "eo"], ["eo"])
    G(move(T.tb[:, 768:1280], T.mci[:]), ["mci"], ["tb"])

    def step(t):
        lastt, later = t == STEPS - 1, min(t, 1)
        z, ml, mb = T["zb%d" % t], T["ml%d" % t], T["mb%d" % (t % 2)]
        zn, mn, mbn = "z%d" % t, "m%d" % t, "mb%d" % (t % 2)

        def when(what, a=0):
            now[:] = [t, "%s%d" % (what, 5 - a // 32)]

        if t == 0:
            when("lists")
            V(cp(ml[:, 0:12], T.mi[:]), ["mi"], regs(mn))
        for a, e in BLOCKS if t else WHOLE:
            c, mr = slice(a // 16, e // 16), regs(mn, a, e)
            when("keep", a)
            G(move(T.wk[:, 18 * c.start:18 * c.stop:18], ml[:, c]), ["wk"] + mr, regs("keep", a, e))
            when("row", a)
            S(act(mb[:, a:e], T.imw[:].indirect(ml[:, c]), AF.Identity, bias=T.pb[:, t:t + 1]), regs("imw", 0, 64) + mr + ["pb%d" % t], regs(mbn, a, e))
            when("lists", a)
            S(act(T.gg[:, up(a, e)], T.glw[:].indirect(ml[:, c])), ["glw"] + mr, regs("gg", a, e))
            when("ops", a)
            if t:
                S(act(T.ol[:, a:e], T.tb[:, 768:1280].indirect(ml[:, c])), ["tb"] + mr, regs("ol", a, e))
            else:
                V(cp(T.ol[:], T.mci[:].indirect(ml[:, c])), ["mci"] + mr, regs("ol"))

        for a, e in BLOCKS:
            n, zr, mr, qr = e - a, regs(zn, a, e), regs(mbn, a, e), regs("qq", a, e)
            when("goal", a)
            P(mm((ps("x", n), (T.cid[:], z[:, a:e]), (T.cidn[:], T.gg[:, up(a, e)]))), ["cid", "cidn"] + zr + regs("gg", a, e), pn("x"))
            S(act(T.gi[:, a:e], ps("x", n), AF.Sign, bias=0.5), pn("x"), regs("gi", a, e))
            when("mod", a)
            P(mm((ps("x", n), (T.wx[:], z[:, a:e]), (T.c37[:], mb[:, a:e]), (T.cx[:], T.gi[:, a:e]))), ["wx", "c37", "cx"] + zr + mr + regs("gi", a, e), pn("x"))
            V(ts(T.qq[:, a:e], ps("x", n), T.mg[:], T.mg[:], A.add, A.subtract), pn("x") + ["mg"], qr)
            when("spread", a)
            terms, out = [], ps("turn", 2 * n)
            for x in range(a, e, 64):
                y, goal = slice(2 * (x - a), 2 * (x - a) + 128), (T.qq[:, x:x + 64], T.gk[:])
                terms += [(out[0:64, y], (z[:, x:x + 64], T.cid[:]), goal), (out[64:128, y], goal)]
            P(mm(*terms), ["cid", "gk"] + zr + qr, pn("turn"))
            S(act(T.zt[:, 2 * a:2 * e], out, AF.Relu, bias=T.zbias[:]), pn("turn") + ["zbias"], regs("zt", a, e))
        for b, (a, e) in enumerate(BLOCKS):
            n, zr, mr, qr, x = e - a, regs(zn, a, e), regs(mbn, a, e), regs("qq", a, e), "zx"[b]
            when("u", a)
            P(mm((ps("u", n, a), (T.wb[:], z[:, a:e]), (T.qu[:], T.qq[:, a:e]))), ["wb", "qu"] + zr + qr, pn("u", a, e))
            when("to", a)
            P(mm((ps(x, n), (T.wx[:], z[:, a:e]), (T.mt[:], mb[:, a:e]), (T.qt[:], T.qq[:, a:e]))), ["wx", "mt", "qt"] + zr + mr + qr, pn(x))
            S(act(T.ind[:, up(a, e), 0], ps(x, n), AF.Identity, scale=-0.25, bias=T.bt[:], accum_out=T.acc[:, b:b + 1]), pn(x) + ["bt"], regs("to", a, e) + ["acc%d" % b])
        for b, (a, e) in enumerate(BLOCKS):
            n, x, w = e - a, "zx"[b], slice(164 * (192 - e) // 64, 164 * (192 - a) // 64)
            own, d = ps(x, 128)[0:n, :], ps("d", w.stop - w.start)
            when("own", a)
            P(mm((own, (T.ind[:, rv(a, e), 0], T.rk[:]), (T.cid[0:n, 0:n], T.off[0:n, :]))), ["rk", "cid", "off"] + regs("to", a, e), pn(x))
            S(act(T.ot[0:n, :], own, AF.Relu), pn(x), ["ot"])
            when("first", a)
            rows = [(T.rk[:], T.ind[:, rv(y, y + m), 0], d[:, 164 * i + o:164 * i + o + m]) for i, y in enumerate(range(e - 64, a - 1, -64)) for o, m in ROWS]
            P(mm((d, (T.ot[0:n, :], T.ex[0:n, 0:n // 64, :]), *rows)), ["ot", "rk"] + regs("ey", 0, 128) + regs("to", a, e), pn("d"))
            S(act(T.ab[:, w], d, AF.Abs, scale=2048.0), pn("d"), regs("ab", a, e))
            when("place", a)
            V(scan(T.ws[:, w], T.ab[:, w], T.wd[:, w], A.min, A.max), ["wd"] + regs("ab", a, e), regs("ws", a, e))
            S(act(T.sl[:, 16 * b:16 * b + 16], T.ws[:, w].indirect(T.eo[:, 2 * b:2 * b + 1])), regs("ws", a, e) + ["eo"], regs("sl", a, e))
        if not lastt:
            when("count")
            x, x2 = ps("all", 1), ps("all", 1, 1)
            G(move(T.acb[:], T.acc[:]), ["acc0", "acc1"], ["acb"])
            terms = [(T.onc[:], T.acb[:, i:i + 1]) for i in range(2)]
            P(mm((x, *terms), (x2, (T.cidn[:], T.pb16[:]), *terms)), ["onc", "acb", "cidn", "pb16"], pn("all"))
            V(ts(T.ev[:], x, -0.5, MAGIC, A.add, A.add), pn("all"), ["ev"])
            V(ts(T.pb[:, t + 1:t + 2], T.ev[:], -MAGIC, x2, A.add, A.subtract), ["ev"] + pn("all"), ["pb%d" % (t + 1)])

        when("new")
        G(move(T.fo[:, 1, :], T.ol[:]), regs("ol"), ["of"])
        S(act(ps("old", 192), T.fo[:, 1, :], AF.Identity, scale=32.0, bias=T.k37[:]), ["of", "k37"], pn("old"))
        V(tt(T.f1[:], T.fo[:, 1, :], ps("u", 192), A.mult), ["of"] + pn("u", 0, 192), ["f1"])
        V(tt(T.f3[:], T.f1[:], ps("old", 192), A.add), ["f1"] + pn("old"), ["f3"])
        V(ts(T.f4[:], T.f3[:], 5, 4095, A.arith_shift_right, A.bitwise_and), ["f3"], ["f4"])
        G(move(T.fo[:, 0, :], T.f4[:]), ["f4"], ["nf"])

        for a, e, q in shares(ADDS[later]):
            when("adds", a)
            out, win = slots(a, e)[:, ::-1], T.adw[:].indirect(T.ol[:, a:e])
            op(q, ts(out, win, -1.0, None, A.mult) if q == "v" else act(out, win, scale=-1.0), ["adw"] + regs("ol", a, e), regs("d0", a, e) + regs("cut", a, e))
        for a, e, q in shares(NEEDS[later]):
            when("needs", a)
            out, win = T.d1[:, down(3071 - 16 * a, 16 * (e - a))], T.prw[:].indirect(T.ol[:, a:e])
            op(q, cp(out, win) if q == "v" else act(out, win), ["prw"] + regs("ol", a, e), regs("d1", a, e))

        for (a, e), x in zip(PARTS, "rqr"):
            when("head", a)
            b = int(a < 64)
            first, head, r, o = slots(a, e, 0, 16), T.d1[:, 3072 - 16 * e:3072 - 16 * a:16], ps(x, 64), BLOCKS[b][1] - e
            P(mm((r, (T.cid[:], T.gg[:, rv(a, e)]), (T.cid[:], first))), ["cid"] + regs("gg", a, e) + regs("cut", a, e), pn(x))
            V(tt(head, head, r, A.max), pn(x) + regs("d1", a, e), regs("d1", a, e))
            S(act(T.rr[:, rv(a, e)], r, AF.Relu), pn(x), regs("r15", a, e))
            G(move(T["d0%d" % b][:, o:o + 64], first), regs("cut", a, e), regs("a15", a, e))
            V(ms(first, -1024.0), [], regs("cut", a, e))
        for i, (a, e) in enumerate(PARTS):
            when("scan", a)
            j = 3072 - 16 * e
            V(scan(T.ss[:, j:j + 1024], slots(a, e), T.d1[:, j:j + 1024], A.add, A.max), regs("d0", a, e) + regs("cut", a, e) + regs("d1", a, e), regs("ss", a, e))
            pair = 2 * ((t + i) % 2)
            py, xn = T["p%d" % pair], ["p%d.y" % pair, "p%d.y" % (pair + 1)]
            when("fill", a)
            P(mm(*[(py[:, h:h + 512], (T.zt[:, 2 * a:2 * e], T.ce[:, h:h + 512])) for h in (0, 512)], stop=False), regs("zt", a, e) + regs("ce", 0, 64), xn)
            when("less", a)
            P(mm(*[(py[:, h:h + 512], (T.cidn[:], T.ss[:, j + h:j + h + 512])) for h in (0, 512)], start=False), ["cidn"] + regs("ss", a, e) + xn, xn)
            when("cmp", a)
            V(tt(T.ind[:, rv(a, e), 1:17], slots(a, e, 1), py[:], A.max), ["d0y.%d" % (a < 64)] + xn + regs("d0", a, e) + regs("cut", a, e), regs("ind", a, e))

        for b, (a, e) in enumerate(BLOCKS):
            c, n = slice(a // 16, e // 16), e - a
            x, o = slice(18 * c.start, 18 * c.stop), min(a, 64)
            cnt, kr = ps("met", x.stop - x.start), T.kr[:, x]
            for l in range(e - 64, a - 1, -64):
                when("pass", l)
                y = 18 * (l - a) // 16
                P(mm((cnt[:, y:y + 72], (mb[:, o:o + 128], T.kb[:, 0:72]), *[(sel(r), T.ind[:, up(l + r, l + 64, 16), :]) for r in range(16)])),
                  ["sel", "kb", "last"] + regs(mbn, o, o + 128) + regs("ind", l, l + 64) + regs("to", l, l + 64), pn("met", l - a, l - a + 64))
            V(scan(kr[:, ::-1], cnt[:, ::-1], T.wk[:, x][:, ::-1], A.max, A.min), ["wk"] + pn("met", 0, n) + regs("keep", a, e), regs("kr", a, e))
            S(act(T.la[:, c], kr[:, 1::18], scale=-1.0, bias=float(TOP)), regs("kr", a, e), regs("la", a, e))
            when("tell", a)
            out = T.yo[:, 192 + c.start:192 + c.stop] if lastt else T["ms%d" % (t + 1)][:, c]
            S(act(out, kr[:, 0::18], AF.Abs), regs("kr", a, e), regs("ms%d" % t, a, e))
            if lastt:
                dma("y", T.ym[:, c], out, regs("ms%d" % t, a, e), [], "outm%d" % b)
            else:
                send("mr%d_%d" % (t + 1, b), out, T["ml%d" % (t + 1)][:, c], regs("ms%d" % t, a, e), regs("m%d" % (t + 1), a, e))
            when("room", a)
            S(act(T.hh[:, a:e], z[:, a:e], bias=-255.0), regs(zn, a, e), regs("hh", a, e))
            when("fire", a)
            S(act(T.lf[:, c], kr[:, 1::18], AF.Sign), regs("kr", a, e), regs("lf", a, e))
            S(act(T.fd[:, a:e], T.ib[:, 0:16].indirect(T.lf[:, c]), scale=T.dvf[:, t:t + 1]), ["ib", "dvf"] + regs("lf", a, e), regs("fd", a, e))
            when("move", a)
            out = (T.yo if lastt else T["zs%d" % (t + 1)])[:, a:e]
            V(tt(T.yy[:, a:e], T["d0%d" % b][:].indirect(T.la[:, c]), T.hh[:, a:e], A.max),
              ["d0y.%d" % b] + regs("la", a, e) + regs("d0", a, e) + regs("cut", a, e) + regs("a15", a, e) + regs("hh", a, e), regs("yy", a, e))
            P(mm((ps("z", n), (T.cid[:], z[:, a:e]), (T.cidn[:], T.fd[:, a:e]), (T.cidn[:], T.yy[:, a:e]))),
              ["cid", "cidn"] + regs("yy", a, e) + regs("fd", a, e) + regs(zn, a, e), pn("z"))
            S(act(out, ps("z", n), AF.Abs), pn("z"), regs("zs%d" % t, a, e))
            if lastt:
                dma("y", T.yz[:, a:e], out, regs("zs%d" % t, a, e), [], "outz%d" % b)
            else:
                send("zr%d_%d" % (t + 1, b), out, T["zb%d" % (t + 1)][:, a:e], regs("zs%d" % t, a, e), regs("z%d" % (t + 1), a, e))

        for b, (a, e) in enumerate(BLOCKS):
            n, ones = e - a, T.big[:, 15:143:16]
            use, mask = ps("use", 128)[0:n, :], ps("mask", 2 * n)
            when("sum", a)
            P(mm(*[(use[:, k::16], (T.ind[:, rv(a, e), 15 - k], ones)) for k in range(15)], (use[:, 15::16], (T.rr[:, rv(a, e)], ones), (T.gg[:, rv(a, e)], T.bign[:]))),
              ["sel", "bign"] + regs("gg", a, e) + regs("ind", a, e) + regs("r15", a, e), pn("use"))
            when("use", a)
            S(act(T.st[0:n, :], use, AF.Sign, bias=16 * 253.5), pn("use"), ["st"])
            P(mm(*[(mask[:, i * n:i * n + n], (T.st[0:n, :], T[x][0:n, 0:n])) for i, x in enumerate(("c8k", "c8kn"))]), ["st", "c8k", "c8kn"], pn("mask"))
            when("write", a)
            V(tt(T.fw[:, :, down(e - 1, n)], T.fo[:, :, down(e - 1, n)], mask, A.min), ["nf", "of"] + pn("mask"), regs("fw", a, e))
            for x in range(e - 64, a - 1, -64):
                o = 16 * b + (x - a) // 16
                V(tt(T.tb[:].indirect(T.sl[:, o:o + 4]), T.fw[:, 0, x:x + 64], T.fw[:, 1, x:x + 64], A.max), regs("sl", a, e) + regs("fw", a, e), ["tb"])

    for t in range(STEPS):
        step(t)
    now[1] = "out9"
    dma("s", T.ymc[:], T.tb[:, 768:1280], ["tb"], [], "outa")
    emit()
    for s in SEMAPHORES:
        if s[:3] == "out":
            g.wait_ge(T.sem[s], 16)
    g.wait_ge(T.sem.snd, n_out * sends[0])
